import numpy as np, ml_dtypes
CORES = [13,21,141,149]
N = 4
BF = ml_dtypes.bfloat16
def gentries(a):
    return np.ascontiguousarray(a.reshape(8, 16, -1).transpose(0, 2, 1)).reshape(8, -1)
def gtable(e):
    e = np.asarray(e); return np.ascontiguousarray(e.reshape(8, -1, 16).transpose(0, 2, 1)).reshape(128, -1).astype(np.int32)
L, LB, HB, J, CAP, M, S, RO = 512, 9, 11, 2048, 640, 96, 32, 3
H, W, T, TOP = N * L, 2 * L, 2 ** (20 - HB), 2 ** 20 - 1
def shelf(rng, n, full):
    a = np.arange(H).reshape(N, 1, 1, L); b = np.roll(a, 1, axis=0); m = n.reshape(1, 8, 1, 1)
    e = rng.integers(0, T >> 4, (N, 8, 16, W)) + (T >> 4) * np.arange(16).reshape(1, 1, 16, 1)
    k = np.concatenate([a + H * np.where(a < m, e[..., :L] & -2, e[..., :L]), b + H * (e[..., L:] | 1)], axis=3)
    k = np.take_along_axis(k, np.argsort(rng.random(k.shape), axis=2), 2)
    c = np.where(rng.random((N, 8, 1, W)) < full, 16, rng.integers(0, 17, (N, 8, 1, W)))
    k = np.where(np.argsort(rng.random(k.shape), axis=2) < c, k, -1)
    k[..., L:] = np.where(b < m, k[..., L:], -1)
    return k
def lack(rng, k, t, c, n):
    c = np.asarray(c); lo = c < L; a = np.where(lo, t * L + c, ((t - 1) % N) * L + c - L)
    e = rng.integers(0, T, c.shape); e = np.where(lo, np.where(a < n, e & -2, e), e | 1)
    x = a[:, None] + H * ((e[:, None] + 2 * np.arange(17)) % T)
    ok = ~np.any(x[:, :, None] == k[:, c].T[:, None, :], axis=2)
    return x[np.arange(c.size), np.argmax(ok, axis=1)]
def stored(rng, k, shape):
    s = k[k >= 0]
    return s[rng.integers(0, s.size, shape)] if s.size else rng.integers(0, 2 ** 20, shape)
def lanes(rng, k, n, w, miss):
    key = np.zeros((N, 8, J), np.int64)
    for g in range(8):
        u = np.add.accumulate(w[:, g], axis=1)
        t = np.minimum(np.sum(rng.random((N, J, 1)) * u[:, None, -1:] >= u[:, None, :], axis=2), N - 1)
        for d in range(N):
            at = t == d; z = int(np.sum(at)); v = stored(rng, k[d, g], z); m = rng.random(z) < miss[g]
            c = rng.integers(0, L, z); c = np.where((rng.random(z) < 0.5) & (((d - 1) % N) * L + c < n[g]), c + L, c)
            v[m] = lack(rng, k[d, g], d, c[m], n[g]); key[:, g][at] = v
    return key
def draws(rng, k, n, w, miss):
    return np.stack([lanes(rng, k, n, w, miss) for _ in range(RO)], axis=2)
def pays(rng, k, miss):
    p = rng.integers(0, 2 ** 20, k.shape)
    for g in range(8):
        p[:, g] = np.where(rng.random(p[:, g].shape) < miss[g], p[:, g], stored(rng, k[:, g], p[:, g].shape))
    return p
def images(rng, n):
    m = n.reshape(1, 8, 1); z = rng.integers(0, 4, (N, 8, J))
    return np.where(z == 0, 0, np.where(z == 1, m, np.minimum((rng.random((N, 8, J)) * (m + 1)).astype(np.int64), m)))
def pack(k, p, n, key, img, dr):
    return {"tk": np.ascontiguousarray(k.reshape(N, 128, W)).astype(np.int32), "tp": np.ascontiguousarray(p.reshape(N, 128, W)).astype(np.int32),
            "pn": np.tile(np.repeat(n, 16).reshape(1, 128, 1), (N, 1, 1)).astype(np.int32), "lk": np.stack([gtable(a) for a in key]),
            "li": np.stack([gtable(a) for a in img]), "dk": np.stack([gtable(a.reshape(8, -1)) for a in dr])}
def setup_inputs(rng):
    n = rng.permutation(8) * (H >> 3) + rng.integers(1, H >> 3, 8)
    miss = rng.permutation(np.array([0.01, 0.01, 0.02, 0.04, 0.1, 0.2, 0.3, 0.4])); full = rng.choice(np.array([0.2, 0.4, 0.6]), (1, 8, 1, 1))
    k = shelf(rng, n, full); w = np.exp2(rng.integers(-1, 2, (N, 8, N)))
    return pack(k, pays(rng, k, miss), n, lanes(rng, k, n, w, miss), images(rng, n), draws(rng, k, n, w, miss))
def setup_inputs_spread(rng):
    n = np.minimum((H * rng.random(8) ** 2).astype(np.int64), H); k = shelf(rng, n, 0.4); b = (N, 8, 1, W)
    wild = rng.integers(0, 2 ** 16, k.shape) + 65536 * ((np.arange(16).reshape(1, 1, 16, 1) + rng.integers(0, 16, b)) % 16)
    wild = np.where(rng.random(k.shape) < rng.random(b) * 1.3, wild, -1)
    k = np.where(rng.random(b) < 0.4, wild, k); miss = rng.choice(np.array([0.01, 0.05, 0.2]), 8); w = np.exp2(rng.integers(-3, 4, (N, 8, N)))
    p = np.where(rng.random(k.shape) < 0.4, np.minimum(np.exp2(20 * rng.random(k.shape)).astype(np.int64), TOP), pays(rng, k, miss))
    key = np.where(rng.random((N, 8, J)) < 0.2, np.minimum(np.exp2(20 * rng.random((N, 8, J))).astype(np.int64), TOP), lanes(rng, k, n, w, miss))
    return pack(k, p, n, key, images(rng, n), draws(rng, k, n, w, miss))
def setup_inputs_ends(rng):
    n = np.concatenate([rng.permutation(np.array([0, 0, H, H, H, H - 1, H >> 1])), np.array([0])])
    k = shelf(rng, n, 1.0); b = (N, 8, 1, W); x = np.arange(16)
    one = rng.integers(0, 32, b) == x.reshape(1, 1, 16, 1)
    k = np.where(rng.random(b) < 0.68, np.where(one, TOP, -1), k)
    for g in range(8):
        k[0, g, :, 0] = H * (x + 1); k[N - 1, g, :, L - 1] = TOP - H * (x + 1); k[0, g, :, W - 1] = TOP - 2 * H * (x + 1)
        if g % 2 == 1: k[0, g, 15, 0] = 0; k[N - 1, g, 15, L - 1] = TOP; k[0, g, 15, W - 1] = TOP
    q = rng.random(b); p = TOP * np.where(q < 0.3, 1, np.where(q > 0.8, 0, rng.integers(0, 2, k.shape)))
    p[..., W - 1] = TOP; p[..., 2] = TOP; p[..., 5] = 0
    p[N - 1, 1::2, 15, L - 1] = TOP; p[N - 1, 1::2, 0, L - 1] = 0
    w = np.ones((N, 8, N)); miss = np.full(8, 0.7)
    def mix(v):
        z = rng.random(v.shape); return np.where(z < 0.34, 0, np.where(z < 0.68, TOP, v))
    img = np.where(rng.random((N, 8, J)) < 0.5, 0, n.reshape(1, 8, 1))
    return pack(k, p, n, mix(lanes(rng, k, n, w, miss)), img, mix(draws(rng, k, n, w, miss)))
def setup_inputs_corners(rng):
    n = rng.permutation(np.array([0, 1, L - 1, L, H - S, H - 1, H, (N - 1) * L - (S >> 1)])); k = shelf(rng, n, 0.5)
    miss = np.full(8, 0.04); w = np.exp2(rng.integers(-1, 2, (N, 8, N))); p = pays(rng, k, miss)
    key = lanes(rng, k, n, w, miss); img = images(rng, n); dr = draws(rng, k, n, w, miss)
    kind = rng.permutation(np.array([0, 0, 0, 1, 1, 1, 2, 2])); nth = [0, 0, 0]
    for g in range(8):
        i = nth[kind[g]]; nth[kind[g]] += 1
        if kind[g] == 0:
            for q in range(N):
                t = (q + 1) % N; x = int(rng.choice(np.array([0, 1, CAP - 1, CAP, CAP + 1, J])))
                if q == 0: x = (CAP, CAP + 1, CAP - 1)[i]
                to = rng.permutation(np.concatenate([np.full(x, t), (t + 1 + rng.integers(0, N - 1, J - x)) % N])); c = rng.integers(0, L, J)
                v = k[to, g, rng.integers(0, 16, J), c]; v = np.where(v < 0, to * L + c + H * rng.integers(0, T, J), v)
                key[q, g] = v; img[q, g] = np.where(((v >> HB) & 1) == 1, 0, img[q, g])
        elif kind[g] == 1:
            img[:, g] = n[g]; to = np.stack([rng.permutation(np.arange(J) % N) for _ in range(N)]); tot = S + i - 1
            for t in range(N):
                qi, ji = np.nonzero(to == t); v = stored(rng, k[t, g], qi.size); x = (M - 1, M, M + 1)[(t + i) % 3]
                f = rng.permutation(np.flatnonzero(np.all(k[t, g, :, :L] >= 0, axis=0))); c = rng.permutation(np.flatnonzero(np.any(k[t, g, :, :L] < 0, axis=0)))[:x]
                y = tot // N + (tot % N if t == N - 1 else 0); c[rng.permutation(M - 1)[:y]] = f[:y]
                if x > M: c[M] = f[y]
                v[np.sort(rng.permutation(qi.size)[:x])] = lack(rng, k[t, g], t, c, n[g]); key[qi, g, ji] = v
        else:
            a = key[:, g] & (H - 1); z = rng.integers(0, 5, a.shape); m = n[g]
            img[:, g] = np.where(z == 0, 0, np.where(z == 1, m, np.where(z == 2, np.minimum(a, m), np.where(z == 3, np.minimum(a + 1, m), max(int(m) - 1, 0)))))
    return pack(k, p, n, key, img, dr)
def setup_inputs_crowd(rng):
    kd = rng.permutation(8); n = np.concatenate([rng.integers(1, H, 4), np.array([0, 0, H, H >> 1])])[kd]
    k = shelf(rng, n, np.where(kd >= 4, 1.0, 0.5).reshape(1, 8, 1, 1)); miss = np.full(8, 0.1); w = np.ones((N, 8, N)); p = pays(rng, k, miss)
    key = lanes(rng, k, n, w, miss); img = images(rng, n); dr = draws(rng, k, n, w, miss); x = np.arange(16)
    for g in range(8):
        q1, j1 = int(rng.integers(0, N)), int(rng.integers(0, J)); keep = key[q1, g, j1]
        if kd[g] < 4:
            t, c = int(rng.integers(0, N)), int(rng.integers(0, L))
            if kd[g] == 3: t, c = N - 1, L - 1
            a = t * L + c; k[t, g, :, c] = rng.permutation(a + 2 * H * x); other = a + 2 * H * rng.integers(16, T >> 1, (N, J))
            if kd[g] == 0: key[:, g] = k[t, g, 15, c]; p[t, g, 15, c] = k[t, g, 3, c]; p[t, g, 3, c] = other[0, 0]
            elif kd[g] == 2: key[:, g] = other; dr[:, g, 0] = other[:, ::-1]
            else: k[t, g, 15, c] = -1; key[:, g] = a + 32 * H; dr[:, g, 0] = other
            if kd[g] == 3: key[q1, g, j1] = keep
        elif kd[g] < 6:
            if kd[g] == 4:
                for c in (0, S - 1, RO * S - 1): k[0, g, :, c] = c + H * (2 * rng.permutation(16) + 1)
            for t in range(N):
                cols = RO * S + rng.permutation(L - RO * S); sp = cols[-RO:]; cols = cols[:-RO]
                if kd[g] == 5: k[t, g, rng.integers(0, 16, RO), sp] = -1
                for rnd in range(RO + 1):
                    c = np.roll(cols, 7 * rnd)[np.arange(J // N) % cols.size]
                    if kd[g] == 5 and rnd < RO: c[5] = sp[rnd]
                    for q in range(N):
                        v = lack(rng, k[t, g], t, c, 0)
                        if rnd == 0: key[q, g, t::N] = v
                        else: dr[q, g, rnd - 1, t::N] = v
        else:
            t = 0 if kd[g] == 6 else 1; cols = L + rng.integers(0, L, 3)
            if kd[g] == 6: cols[0] = W - 1
            v = np.concatenate([stored(rng, k[t, g][:, cols], 4), lack(rng, k[t, g], t, cols, n[g])])
            img[:, g] = 0; key[:, g] = v[rng.integers(0, v.size, (N, J))]; dr[:, g, 0] = v[rng.integers(0, v.size, (N, J))]
            if kd[g] == 6: k[N - 1, g, 0, cols[2] - L] = v[-1]
            if kd[g] == 7:
                low = rng.random((N, J)) < 0.5
                key[:, g] = np.where(low, stored(rng, k[t, g][:, :L], (N, J)), key[:, g])
                key[q1, g, J - 1] = keep; img[q1, g, J - 1] = n[g]
                j = int(np.flatnonzero(~low[N - 1])[CAP - 1]); z, y = int(k[t, g, 15, cols[0]]), int(k[t, g, 0, cols[0]])
                key[N - 1, g, j] = z; dr[N - 1, g, 0, j] = y; p[t, g, 15, cols[0]] = z; p[t, g, 0, cols[0]] = y
    return pack(k, p, n, key, img, dr)
def setup_inputs_calm(rng):
    v = rng.permutation(np.array([0, 1, 2, 3, 0, 1, 2, 3])); n = np.where(rng.random(8) < 0.5, L * rng.integers(1, N, 8) - 2, rng.integers(16, H - 32, 8))
    few = np.concatenate([np.flatnonzero(v == 0), np.flatnonzero(v == 1)[:1]]); n[few] = np.array([0, 3, 0]); n[np.flatnonzero(v == 3)[0]] = L * int(rng.integers(1, N)) - 2
    k = shelf(rng, n, 0.5)
    for g in few:
        for x in range(3):
            if x < n[g]: k[1, g, :, L + x] = x + H * (2 * rng.permutation(16) + 1)
            else: k[0, g, :, x] = x + H * rng.permutation(16)
    none = np.zeros(8); w = np.ones((N, 8, N)); p = pays(rng, k, none); key = lanes(rng, k, n, w, none); dr = draws(rng, k, n, w, none)
    img = np.where(rng.random((N, 8, J)) < 0.5, np.maximum(n.reshape(1, 8, 1) - rng.integers(0, 4, (N, 8, J)), 0), images(rng, n))
    for g in range(8):
        s = k[:, g][k[:, g] >= 0]; s = s[np.abs((s & (H - 1)) - n[g] - 3) < 9]
        if s.size:
            for a in (p, key): a[:, g] = np.where(rng.random(a[:, g].shape) < 0.15, s[rng.integers(0, s.size, a[:, g].shape)], a[:, g])
        for i in range(int(v[g])):
            t = (i + 1) % N; f = np.flatnonzero(np.all(k[t, g, :, :L] >= 0, axis=0)); f = rng.permutation(f[np.abs(t * L + f - n[g] - 4) > 12])[:RO + 1]
            u = lack(rng, k[t, g], t, f, n[g]); key[i, g, 0] = u[0]; dr[i, g, :, 0] = u[1:]
    for g in few:
        for x in range(3):
            key[:, g, 2 + x] = x + H; p[:, g] = np.where(k[:, g] == x + H, x + H, p[:, g])
    return pack(k, p, n, key, img, dr)
def check_inputs(d):
    bad = []
    for a, lo, hi in (("tk", -1, TOP), ("tp", 0, TOP), ("pn", 0, H), ("lk", 0, TOP), ("li", 0, H), ("dk", 0, TOP)):
        if np.min(d[a]) < lo or np.max(d[a]) > hi: bad.append("range of " + a)
    s = np.sort(d["tk"].reshape(N, 8, 16, W), axis=2)
    if np.any((s[:, :, 1:] == s[:, :, :-1]) & (s[:, :, 1:] >= 0)): bad.append("tk: keys of one bucket differ")
    m = d["pn"].reshape(N, 8, 16)
    if np.any(m != m[:1, :, :1]): bad.append("pn: alike in a group and on all ranks")
    if np.any(d["li"].reshape(N, 8, -1) > m[:, :, :1]): bad.append("li: at most the pointer")
    return bad
def reference(tk, tp, pn, lk, li, dk):
    k = tk.astype(np.int64).reshape(N, 8, 16, W); p = tp.astype(np.int64).reshape(N, 8, 16, W); n = pn[0].astype(np.int64).reshape(8, 16)[:, 0]
    key = np.stack([gentries(a) for a in lk]).astype(np.int64); img = np.stack([gentries(a) for a in li]).astype(np.int64)
    dr = np.stack([gentries(a) for a in dk]).astype(np.int64).reshape(N, 8, RO, J)
    src = np.arange(N).reshape(N, 1, 1); grp = np.arange(8).reshape(1, 8, 1)
    for rnd in range(RO):
        home = key & (H - 1); bit = ((key >> HB) & 1) == 1
        old = bit & (home < img); new = bit & (home < n.reshape(1, 8, 1)); fwd = new & ~old
        to = ((home >> LB) + old) % N
        own = ((home >> LB) + new) % N; col = (home & (L - 1)) + L * new
        place = np.zeros_like(key)
        for d in range(N):
            m = (to == d).astype(np.int64); place = place + m * (np.add.accumulate(m, axis=2) - m)
        go = place < CAP
        eq = k[own, grp, :, col] == key[..., None]; hit = np.any(eq, axis=3)
        val = np.sum(np.where(eq, p[own, grp, :, col], 0), axis=3)
        order = fwd * (N * CAP) + src * CAP + place; miss = go & ~hit; over = np.zeros(8, np.int64)
        for t in range(N):
            for g in range(8):
                m = miss[:, g] & (own[:, g] == t)
                o = np.argsort(order[:, g][m])[:M]; ks = key[:, g][m][o]
                c, first = np.unique(col[:, g][m][o], return_index=True); ks = ks[first]
                e = k[t, g][:, c] == -1; room = np.any(e, axis=0); s = np.argmax(e, axis=0)
                over[g] += np.sum(~room)
                s, c, ks = s[room], c[room], ks[room]
                k[t, g, s, c] = ks; p[t, g, s, c] = (ks & 1023) * 1024 + (ks >> 10)
        key = np.where(go, np.where(hit, val, dr[:, :, rnd]), key); img = np.where(go & fwd, home + 1, img)
        nn = np.minimum(n + np.minimum(over, S), H)
        for g in range(8):
            x = np.arange(n[g], nn[g]); t = x >> LB; c = x & (L - 1); t2 = (t + 1) % N
            kl = k[t, g, :, c]; pl = p[t, g, :, c]; mv = (kl >= 0) & (((kl >> HB) & 1) == 1)
            k[t2, g, :, L + c] = np.where(mv, kl, -1); p[t2, g, :, L + c] = np.where(mv, pl, 0)
            k[t, g, :, c] = np.where(mv, -1, kl); p[t, g, :, c] = np.where(mv, 0, pl)
        n = nn
    return {"yk": k.reshape(N, 128, W).astype(np.float32), "ys": np.sum(p, axis=2).astype(np.float32), "yn": np.tile(np.repeat(n, 16).reshape(1, 128, 1), (N, 1, 1)).astype(np.float32),
            "yl": np.stack([gtable(a) for a in key]).astype(np.float32), "yi": np.stack([gtable(a) for a in img]).astype(np.float32)}

@@ -1,0 +1,731 @@
+from concourse.bass import DstId, RemoteDMATransfer
+from concourse.mybir import AluOpType as OP, AxisListType, ActivationFunctionType as AF
+
+N, RO, NCORES = 4, 3, 256
+MW = 56
+TW = 8256
+BIG = float(2 ** 22)
+SEG = [97 - 16 * m for m in range(6)]
+SEGT = sum(SEG)
+F, H, B, I, U = "float32", "float16", "bfloat16", "int32", "uint16"
+
+
+def _sb(w, d):
+    return ("sbuf", [128, w], d)
+
+
+SCRATCH = {
+    "DT": _sb(TW, F), "PT": _sb(TW, F), "RB0": _sb(4 * MW, F), "RB1": _sb(4 * MW, F), "RB2": _sb(4 * MW, F),
+    "TKI": _sb(1024, I), "TPI": _sb(1024, I), "LKI": _sb(128, I), "LII": _sb(128, I), "DKI": _sb(384, I), "PNI": _sb(4, I),
+    "W1": _sb(2048, F), "W2": _sb(2048, F), "W3": _sb(2048, F), "W4": _sb(2048, F), "TM": _sb(128 * 20, F), "TN": _sb(128 * 8, I),
+    "IOTA": _sb(512, F), "PCI": _sb(8, I), "PC": _sb(24, F), "MI": _sb(128, I), "MG": _sb(128, I), "CODE": _sb(128, B),
+    "BOb": _sb(128, B), "BOh": _sb(1024, H), "Ib": _sb(128, B), "Ih": _sb(128, H), "If": _sb(128, F), "XM": _sb(128, B),
+    "EMB": _sb(128, B), "CE": _sb(256, B), "SEL": _sb(2048, H), "REDb": _sb(2048, B), "REDh": _sb(2048, H), "TB": _sb(1024, B),
+    "GS": _sb(16, F), "S16": _sb(16, F), "CK": _sb(8, F), "RS8": _sb(1024, B), "RS4": _sb(512, B), "KW": _sb(384, F),
+    "KX": _sb(384, F), "KR": _sb(96, F), "KRW": _sb(384, H), "KRC": _sb(24, H), "T256": _sb(24, B), "IDT": _sb(4 * MW, F),
+    "KP": _sb(4 * SEGT, B), "ENDS": _sb(2, U), "PERM": _sb(8, U), "PIU": _sb(8, U), "DUMP": _sb(64, F), "XO": _sb(8, F),
+    "VB": _sb(24, B), "BSH": _sb(24, H), "CT": _sb(384, F), "WT": _sb(32, F),
+    "KB": _sb(160, F), "YT": _sb(288, F), "IMG": _sb(128, F), "K2": _sb(128, I), "Z2": _sb(128, I), "HI": _sb(128, I),
+    "E1": _sb(128, I), "EH": _sb(128, H), "Q": _sb(128, I), "OG": _sb(512, B), "IG": _sb(512, B),
+    "OH": _sb(1024, B), "INC": _sb(1024, B), "GOB": _sb(512, B), "GO": _sb(128, F), "KPI": _sb(128, I),
+    "ZP": _sb(128, I), "HP": _sb(128, I), "OFF": _sb(128, U), "CLS": _sb(128, I), "TS": _sb(128, F), "CM": _sb(128, B),
+    "HT": _sb(1024, F), "ET": _sb(1024, F), "XS": _sb(1024, F), "E2": _sb(64, F), "BC": _sb(4, B), "C1": _sb(384, B),
+    "C2": _sb(384, B), "O1": _sb(24, U), "O2": _sb(24, U), "O3": _sb(24, U), "O4": _sb(24, U), "O5": _sb(24, U),
+    "MK": _sb(384, F), "MH": _sb(384, H), "ME": _sb(384, H), "MN": _sb(384, H), "MB": _sb(384, H), "M1": _sb(384, H),
+    "ED": _sb(24, F), "IX": _sb(384, F), "BS": _sb(32, F), "BD": _sb(128, F), "NE": _sb(4 * SEGT, B), "SS": _sb(4 * SEGT, B),
+    "EM": _sb(384, B), "TOT": _sb(32, F), "OV": _sb(32, B), "TT": _sb(64, F), "NN": _sb(32, F), "SG": _sb(4, U), "SO": _sb(4, U),
+    "SX": _sb(256, F), "SI": _sb(64, I), "SK": _sb(320, F), "YS": _sb(1024, F),
+}
+for _b in range(8):
+    SCRATCH["P%d" % _b] = ("psum", [128, 512], F)
+SEMAPHORES = (["cv", "cs", "ct", "cg", "tabD", "tabP", "hD", "hP", "rl0", "rl1", "rl2", "lo"] + ["m%d" % t for t in range(RO)]
+              + ["hm%d" % t for t in range(RO)] + ["ls%d" % i for i in range(7)] + ["ld%d" % i for i in range(8)]
+              + ["st%d" % i for i in range(8)])
+ROUTES = []
+CYC, PEC, WAKE = 1.0e-3, 0.6e-3, 0.12
+
+
+def _mask(engines):
+    return sum(1 << e for e in engines)
+
+
+def _routes(T, topo):
+    R = list(T.cores)
+    out = []
+    for s, c in enumerate(R):
+        peer = [d for d in range(N) if d != s and topo.may_write(c, R[d])]
+        cross = [d for d in range(N) if d != s and d not in peer]
+        helpers = [h for h in topo.cores_of(c) if h != c and all(topo.may_write(h, R[d]) for d in cross)]
+        slot = {h: [y for y in helpers if topo.die(y) == topo.die(h)].index(h) for h in helpers}
+        helpers.sort(key=lambda h: (slot[h], topo.die(h)))
+        near = [h for h in helpers if topo.die(h) == topo.die(c)]
+        relay = {}
+        for d in cross:
+            srcs = [x for x in range(N) if x != d and not topo.may_write(R[x], R[d])]
+            for h in helpers:
+                cand = [x for x in range(NCORES) if topo.mates(x, R[d]) and topo.may_write(x, R[d]) and topo.die(x) == topo.die(h)]
+                relay[(h, d)] = (cand[srcs.index(s)], slot[h])
+        out.append({"peer": peer, "cross": cross, "helpers": helpers, "near": near, "relay": relay})
+    return out
+
+
+def _chunk(s, i):
+    return (512 * s if i < 2 else 2048 + 512 * ((s - 1) % N)) + 256 * (i % 2)
+
+
+def _dst(topo, d, c):
+    rid, pid = topo.addr(d, c)
+    return DstId(rid=rid, pnc=pid)
+
+
+def helper_program(g, core, T, topo, routes):
+    R = list(T.cores)
+    total = 0
+    for s in range(N):
+        ro = routes[s]
+        if core in ro["helpers"]:
+            i = ro["helpers"].index(core)
+            a = _chunk(s, i)
+            eng = topo.engines(core, R[ro["peer"][0]])
+            half = len(eng) // 2
+            got = len(topo.engines(R[s], core))
+            g.wait_ge(T.sem.hD, got // 2)
+            ap = T.DT[:, a:a + 256]
+            g.remote_dma_fused([RemoteDMATransfer(dst_ids=[_dst(topo, ro["relay"][(core, d)][0], core)], dma_engine_mask=_mask(eng[k * half:(k + 1) * half]),
+                                                  remote_sem=T.sem["rl%d" % ro["relay"][(core, d)][1]], src=ap, dst=ap)
+                                for k, d in enumerate(ro["cross"])], local_sem=T.sem.lo)
+            rid, pid = topo.addr(R[ro["peer"][0]], core)
+            g.remote_dma(ap, ap, T.sem.tabD, T.sem.lo, pid, rid, _mask(eng))
+            g.wait_ge(T.sem.hP, got // 2)
+            ap = T.PT[:, a:a + 256]
+            if ro["relay"][(core, ro["cross"][0])][1] == 0:
+                g.remote_dma_fused([RemoteDMATransfer(dst_ids=[_dst(topo, ro["relay"][(core, d)][0], core)], dma_engine_mask=_mask(eng[k * half:(k + 1) * half]),
+                                                      remote_sem=T.sem.rl2, src=ap, dst=ap) for k, d in enumerate(ro["cross"])], local_sem=T.sem.lo)
+                g.remote_dma(ap, ap, T.sem.tabP, T.sem.lo, pid, rid, _mask(eng))
+                total += 4 * len(eng)
+            else:
+                ds = ro["cross"] + ro["peer"]
+                g.remote_dma_fused([RemoteDMATransfer(dst_ids=[_dst(topo, R[d], core) for d in ds], dma_engine_mask=_mask(eng),
+                                                      remote_sem=T.sem.tabP, srcs=[ap], dsts=[ap for d in ds])], local_sem=T.sem.lo)
+                total += 3 * len(eng)
+            if core in ro["near"]:
+                d = R[ro["cross"][ro["near"].index(core)]]
+                rid, pid = topo.addr(d, core)
+                for t in range(RO):
+                    g.wait_ge(T.sem["hm%d" % t], got // 4)
+                    ap = T["RB%d" % t][:, MW * s:MW * (s + 1)]
+                    g.remote_dma(ap, ap, T.sem["m%d" % t], T.sem.lo, pid, rid, _mask(eng))
+                    total += len(eng)
+        for (h, d), (x, slot) in sorted(ro["relay"].items(), key=lambda e: e[1][1]):
+            if x == core:
+                a = _chunk(s, ro["helpers"].index(h))
+                eng = topo.engines(core, R[d])
+                rid, pid = topo.addr(R[d], core)
+                g.wait_ge(T.sem["rl%d" % slot], len(eng) // 2)
+                ap = T.DT[:, a:a + 256]
+                g.remote_dma(ap, ap, T.sem.tabD, T.sem.lo, pid, rid, _mask(eng))
+                total += len(eng)
+        for (h, d), (x, slot) in ro["relay"].items():
+            if x == core and slot == 0:
+                a = _chunk(s, ro["helpers"].index(h))
+                g.wait_ge(T.sem.rl2, len(eng) // 2)
+                ap = T.PT[:, a:a + 256]
+                g.remote_dma(ap, ap, T.sem.tabP, T.sem.lo, pid, rid, _mask(eng))
+                total += len(eng)
+    if total:
+        g.wait_ge(T.sem.lo, total)
+
+
+def _issue(T, Q, ops):
+    n = len(ops)
+    succ = [[] for o in ops]
+    for i, o in enumerate(ops):
+        for j in o["dep"] | o["after"]:
+            succ[j].append(i)
+    level = [0.0] * n
+    for i in range(n - 1, -1, -1):
+        level[i] = ops[i]["cost"] + max([level[k] + (WAKE if i in ops[k]["dep"] else 0.0) for k in succ[i]] + [0.0])
+    for i, o in enumerate(ops):
+        if o["sem"] is not None and not o["dep"]:
+            level[i] += 1000.0
+    left = [len(o["dep"] | o["after"]) for o in ops]
+    ready = [0.0] * n
+    cand = {q: [] for q in list(Q) + ["a"]}
+    free = {q: 0.0 for q in cand}
+    for i, o in enumerate(ops):
+        if not left[i]:
+            cand[o["q"]].append(i)
+    clock = {q: {} for q in cand}
+    count = {q: 0 for q in cand}
+    event = [None] * n
+    final = {}
+    for step in range(n):
+        pick = None
+        for q, c in cand.items():
+            if not c:
+                continue
+            t = free[q]
+            best = max(c, key=lambda i: (level[i], -i))
+            if ready[best] > t:
+                fill = [i for i in c if max(ready[i], t) + ops[i]["busy"] <= ready[best] + 0.05 and i != best]
+                if fill:
+                    best = min(fill, key=lambda i: (max(ready[i], t), -level[i]))
+            st = max(t, ready[best])
+            if pick is None or st < pick[0]:
+                pick = (st, best)
+        st, i = pick
+        o = ops[i]
+        q = o["q"]
+        cand[q].remove(i)
+        free[q] = st + o["busy"]
+        for k in succ[i]:
+            if i in ops[k]["dep"]:
+                ready[k] = max(ready[k], st + o["cost"] + WAKE)
+            else:
+                ready[k] = max(ready[k], st + (o["cost"] if ops[k]["q"] == "a" else o["busy"]))
+            left[k] -= 1
+            if not left[k]:
+                cand[ops[k]["q"]].append(k)
+        if q == "a":
+            event[i] = (o["sem"], o["val"], {o["sem"]: o["val"]})
+            final[o["sem"]] = o["val"]
+            continue
+        ck = clock[q]
+        want = {}
+        for j in o["dep"]:
+            ev = event[j]
+            if ev[1] > want.get(ev[0], (0, 0))[1]:
+                want[ev[0]] = ev
+        for ev in sorted(want.values(), key=lambda e: -len(e[2])):
+            if ck.get(ev[0], 0) < ev[1]:
+                Q[q].wait_ge(T.sem[ev[0]], ev[1])
+                for k, x in ev[2].items():
+                    if ck.get(k, 0) < x:
+                        ck[k] = x
+        ins = o["fn"]()
+        if o["sem"] is None:
+            count[q] += 1
+            sem, val = "c" + q, count[q]
+            ins.then_inc(T.sem[sem], 1)
+        else:
+            sem, val = o["sem"], o["val"]
+        c2 = dict(ck)
+        c2[sem] = val
+        event[i] = (sem, val, c2)
+        final[sem] = val
+    for sem, val in final.items():
+        Q["g"].wait_ge(T.sem[sem], val)
+
+
+def rank_program(g, core, T, topo):
+    if not ROUTES:
+        ROUTES.extend(_routes(T, topo))
+    routes = ROUTES
+    r = T.rank_of(core)
+    if r is None:
+        helper_program(g, core, T, topo, routes)
+        return
+    R = list(T.cores)
+    ro = routes[r]
+    ops, hist, bank, gate = [], {}, {}, []
+
+    def A(n, a=0, b=None, st=1, p=128):
+        if b is None:
+            b = SCRATCH[n][1][1]
+        return (T[n][0:p, a:b:st] if st > 1 else T[n][0:p, a:b], [(n, a, b, st)], (b - a + st - 1) // st, False)
+
+    def X(win, off):
+        return (win[0].indirect(off[0]), win[1] + off[1], 16 * off[2], True)
+
+    def run(q, outs, ins, fn, cost, busy=None, sem=None, val=0, after=()):
+        rd = [s for x in ins if isinstance(x, tuple) for s in x[1]]
+        wr = []
+        for x in outs:
+            if isinstance(x, tuple):
+                wr.append(x[1][0])
+                rd.extend(x[1][1:])
+        me, dep, aft = len(ops), set(), set(after) | set(gate)
+        for spans, w in ((rd, False), (wr, True)):
+            for n, a, b, st in spans:
+                ps = SCRATCH[n][0] == "psum"
+                if ps and n in bank:
+                    aft.add(bank[n])
+                for a2, b2, s2, w2, q2, j in hist.get(n, []):
+                    if ps and q2 != q:
+                        dep.add(j)
+                    elif q == "t" and q2 == "t":
+                        continue
+                    elif (w or w2) and a < b2 and a2 < b and (st == 1 or st != s2 or (a - a2) % st == 0):
+                        dep.add(j)
+        for spans, w in ((rd, False), (wr, True)):
+            for n, a, b, st in spans:
+                h = hist.setdefault(n, [])
+                if w and st == 1:
+                    h[:] = [e for e in h if not (a <= e[0] and e[1] <= b)]
+                h.append((a, b, st, w, q, me))
+                if SCRATCH[n][0] == "psum":
+                    bank[n] = me
+        ops.append({"q": q, "fn": fn, "dep": dep, "after": aft - dep, "cost": cost, "busy": cost if busy is None else busy, "sem": sem, "val": val})
+        return me
+
+    def ap(x):
+        return x[0] if isinstance(x, tuple) else x
+
+    def cyc(o, ins, f=1.0):
+        if o[3]:
+            return 0.05 + 3.8 * o[2] * CYC
+        if ins[0][3]:
+            return 0.05 + 1.56 * o[2] * CYC
+        if f == 0.5 and not all(SCRATCH[x[1][0][0]][2] in (H, B, U) for x in [o] + ins):
+            f = 1.0
+        return max(64, f * o[2]) * CYC
+
+    def ts(o, i, s1, op0, s2=None, op1=None):
+        if op1 is None:
+            run("v", [o], [i, s1], lambda: g.vector.tensor_scalar(o[0], i[0], ap(s1), None, op0), cyc(o, [i], 0.5))
+        else:
+            run("v", [o], [i, s1, s2], lambda: g.vector.tensor_scalar(o[0], i[0], ap(s1), ap(s2), op0, op1), cyc(o, [i], 0.5))
+
+    def tt(o, a, b, op):
+        ps = any(SCRATCH[x[1][0][0]][0] == "psum" for x in (a, b))
+        run("v", [o], [a, b], lambda: g.vector.tensor_tensor(o[0], a[0], b[0], op), cyc(o, [a], 1.0 if ps else 2.0))
+
+    def cp(o, i):
+        run("v", [o], [i], lambda: g.vector.tensor_copy(o[0], i[0]), cyc(o, [i], 0.5))
+
+    def ms(o, c):
+        run("v", [o], [], lambda: g.vector.memset(o[0], c), cyc(o, [o], 0.5))
+
+    def scan(o, d0, d1, init, op0, op1):
+        run("v", [o], [d0, d1], lambda: g.vector.tensor_tensor_scan(o[0], d0[0], d1[0], init, op0, op1), cyc(o, [d0, d1], 0.5))
+
+    def turn(o, i):
+        run("v", [o], [i], lambda: g.vector.transpose(o[0], i[0]), cyc(o, [i]))
+
+    def rsum(o, i):
+        run("v", [o], [i], lambda: g.vector.tensor_reduce(o[0], i[0], AxisListType.X, OP.add), cyc(i, [i]))
+
+    def act(o, i, f=AF.Identity, bias=0.0, scale=1.0, acc=None):
+        if acc is None:
+            run("s", [o], [i, bias], lambda: g.scalar.activation(o[0], i[0], f, bias=ap(bias), scale=scale), cyc(o, [i]))
+        else:
+            run("s", [o, acc], [i, bias], lambda: g.scalar.activation(o[0], i[0], f, bias=ap(bias), scale=scale, accum_out=acc[0]), cyc(o, [i]))
+
+    def mm(o, terms, start=True, stop=True):
+        def fn():
+            for k, (l, x) in enumerate(terms):
+                last = g.tensor.matmul(o[0], l[0], x[0], start and k == 0, stop and k == len(terms) - 1)
+            return last
+        c = sum(max(min(64, l[2]), x[2]) * (4 if SCRATCH[l[1][0][0]][2] == F else 1) for l, x in terms) * PEC
+        run("t", [o], [x for tm in terms for x in tm], fn, c)
+
+    def red(mat, n, a, b):
+        return [(A(mat, 128 * i, 128 * i + 128), A(n, a + i, b, 16)) for i in range(16)]
+
+    Q = {"v": g.vector, "s": g.scalar, "t": g.tensor, "g": g, "y": g.sync}
+    dmas = {"s": [], "y": []}
+
+    def dma(q, sem, o, i, cost):
+        dmas[q].append(run(q, [o], [i], lambda: Q[q].dma_start(ap(o), ap(i)).then_inc(T.sem[sem], 16), cost, 0.1, sem, 16, dmas[q][-1:]))
+
+    def send(ls, items):
+        return run("g", [], [x for x, d, e, sem in items],
+                   lambda: g.remote_dma_fused([RemoteDMATransfer(dst_ids=[_dst(topo, d, core)], dma_engine_mask=_mask(e), remote_sem=T.sem[sem],
+                                                                 src=x[0], dst=x[0]) for x, d, e, sem in items], local_sem=T.sem[ls]),
+                   2.5, 0.6, ls, sum(len(e) for x, d, e, sem in items))
+
+    def arrive(sem, val, outs, after, cost):
+        run("a", outs, [], None, cost, 0.0, sem, val, [after])
+
+    def f(k):
+        return A("TM", 128 * k, 128 * k + 128)
+
+    def z(k):
+        return A("TN", 128 * k, 128 * k + 128)
+
+    off_eng = topo.engines(core, R[ro["peer"][0]])
+    on_eng = topo.engines(core, ro["helpers"][0])
+    rest = [e for e in on_eng if e not in off_eng]
+    others = [s for s in range(N) if s != r]
+    own = (_chunk(r, 0), _chunk(r, 2))
+
+    dma("y", "ld0", A("TKI", 0, 512), T.tk[:, 0:512], 2.8)
+    dma("s", "ld1", A("TKI", 512, 1024), T.tk[:, 512:1024], 3.8)
+    dma("y", "ld2", A("TPI", 0, 512), T.tp[:, 0:512], 4.8)
+    dma("s", "ld3", A("TPI", 512, 1024), T.tp[:, 512:1024], 5.8)
+    dma("y", "ld4", A("LKI"), T.lk[:], 6.2)
+    dma("y", "ld5", A("LII"), T.li[:], 6.6)
+    dma("y", "ld6", A("PNI", 0, 1), T.pn[:], 6.8)
+    dma("y", "ld7", A("DKI"), T.dk[:], 7.6)
+    run("g", [A("PCI", 0, 1)], [], lambda: g.iota(T.PCI[:, 0:1], [[1, 1]], 0, 1), 0.15)
+    run("g", [A("IOTA")], [], lambda: g.iota(T.IOTA[:], [[1, 512]], 0, 0, allow_small_or_imprecise_dtypes=True), 1.2, after=[len(ops) - 1])
+
+    hn = len(on_eng) // 2
+    for h in range(2):
+        act(A("P%d" % h), A("IOTA"), bias=float(own[h] % 2048 - 2048))
+        tt(A("DT", own[h], own[h] + 512), A("TKI", 512 * h, 512 * h + 512), A("P%d" % h), OP.subtract)
+        sent = send("ls%d" % h, [(A("DT", _chunk(r, 2 * h + i), _chunk(r, 2 * h + i) + 256), ro["helpers"][2 * h + i], on_eng[hn * i:hn * i + hn], "hD")
+                                 for i in range(2)])
+    arrive("tabD", 12 * len(off_eng), [A("DT", _chunk(s, 2 * h), _chunk(s, 2 * h) + 512) for s in others for h in range(2)], sent, 13.0)
+    for h in range(2):
+        ts(A("P%d" % (2 + h)), A("TKI", 512 * h, 512 * h + 512), 0.0, OP.is_ge, -0.5, OP.add)
+        ts(A("W1", 512 * h, 512 * h + 512), A("TPI", 512 * h, 512 * h + 512), 2.0, OP.mult, 1.0, OP.add)
+        tt(A("PT", own[h], own[h] + 512), A("W1", 512 * h, 512 * h + 512), A("P%d" % (2 + h)), OP.mult)
+        sent = send("ls%d" % (2 + h), [(A("PT", _chunk(r, 2 * h + i), _chunk(r, 2 * h + i) + 256), ro["helpers"][2 * h + i], on_eng[hn * i:hn * i + hn], "hP")
+                                       for i in range(2)])
+    arrive("tabP", 12 * len(off_eng), [A("PT", _chunk(s, 2 * h), _chunk(s, 2 * h) + 512) for s in others for h in range(2)], sent, 12.0)
+
+    def pc(k):
+        return A("PC", k, k + 1)
+
+    def pi(k):
+        return A("PCI", k, k + 1)
+    PI, PG, W16, B15 = pc(0), pc(1), pc(2), pc(3)
+    ts(pi(1), pi(0), 15, OP.bitwise_and)
+    ts(pi(2), pi(0), 4, OP.arith_shift_right)
+    cp(A("PC", 0, 2), A("PCI", 1, 3))
+    cp(z(0), A("IOTA", 0, 128))
+    ts(A("MI"), z(0), 15, OP.bitwise_and)
+    ts(A("MG"), z(0), 4, OP.arith_shift_right)
+    BO, Ib, Ih, If, XM, CODE = A("BOb"), A("Ib"), A("Ih"), A("If"), A("XM"), A("CODE")
+    ts(BO, A("MG"), PG, OP.is_equal)
+    ts(f(0), A("MG"), PG, OP.not_equal, 32.0, OP.mult)
+    tt(CODE, f(0), A("MI"), OP.add)
+    WTS = [1.0, 2048.0, -1024.0, 1024.0, 2.0, -1.0, 1.0 / 1024]
+    for k, w in enumerate(WTS):
+        ts(A("BOh", 128 * k, 128 * k + 128), BO, w, OP.mult)
+
+    def BOh(w):
+        k = WTS.index(w)
+        return A("BOh", 128 * k, 128 * k + 128)
+
+    def tb(k):
+        return A("TB", 128 * k, 128 * k + 128)
+    ts(A("S16"), A("IOTA", 0, 16), PI, OP.is_equal, 2048.0, OP.mult)
+    for k in range(16):
+        ts(A("SEL", 128 * k, 128 * k + 128), BO, A("S16", k, k + 1), OP.mult)
+        ts(A("REDh", 128 * k, 128 * k + 128), CODE, float(k), OP.is_equal)
+        act(A("REDb", 128 * k, 128 * k + 128), CODE, AF.Abs, -float(k))
+    act(A("REDb"), A("REDb"), AF.Relu, 1.0, -1.0)
+    ts(Ib, CODE, PI, OP.is_equal)
+    ts(Ih, CODE, PI, OP.is_equal)
+    act(If, Ib)
+    ts(tb(0), CODE, PI, OP.is_lt, -1.0, OP.mult)
+    act(tb(1), Ib, scale=-2048.0)
+    tt(XM, tb(0), tb(1), OP.add)
+    act(tb(2), Ib, scale=2.0)
+    tt(tb(3), tb(0), BO, OP.add)
+    tt(tb(4), tb(2), tb(3), OP.subtract)
+    act(A("EMB"), tb(4), scale=BIG)
+    ms(A("RS4"), 1.0)
+    ms(A("RS4", 0, 512, 128), 0.0)
+    ms(A("RS8"), 1.0)
+    ms(A("RS8", 0, 1024, 256), 0.0)
+    ms(A("KB"), 0.0)
+    ts(pi(3), pi(0), 7, OP.bitwise_and)
+    ts(pi(4), pi(0), 4, OP.arith_shift_right, 1, OP.bitwise_and)
+    ts(pi(5), pi(0), 3, OP.arith_shift_right, 1, OP.bitwise_and)
+    tt(pc(4), pi(3), pi(4), OP.subtract)
+    ts(pi(6), pc(4), 1.0, OP.add)
+    ts(pi(7), pi(6), 1, OP.bitwise_and)
+    ts(pc(5), pi(7), 144.0, OP.mult)
+    ts(pc(6), pi(3), 16.0, OP.mult, 16.0, OP.add)
+    tt(pc(7), pc(6), pi(5), OP.add)
+    tt(pc(8), pc(7), pc(5), OP.add)
+    ts(A("PERM"), A("IOTA", 0, 8), 2.0, OP.mult, pc(8), OP.add)
+    ts(A("GS", 0, 8), A("IOTA", 0, 8), PG, OP.is_equal, 32.0, OP.mult)
+    act(A("GS", 8, 16), A("GS", 0, 8), scale=1.0 / 32)
+    ts(W16, PI, 15.0, OP.is_lt, 16.0, OP.mult)
+    act(B15, A("S16", 15, 16), scale=2.0)
+    order = [(r - 1 + k) % N for k in range(N)]
+    act(A("KR"), A("IOTA", 0, 96), bias=95.0, scale=-1.0)
+    act(A("CT", 0, 6), A("IOTA", 0, 6), bias=PI, scale=16.0)
+    for k in range(4):
+        act(A("KW", 96 * k, 96 * k + 96), A("IOTA", 0, 96))
+        act(A("KX", 96 * k, 96 * k + 96), A("IOTA", 0, 96), bias=-2047.0)
+        ts(A("KRW", 96 * k, 96 * k + 96), A("KR"), 96.0 * order[k], OP.add)
+        ts(A("KRC", 6 * k, 6 * k + 6), A("CT", 0, 6), -1.0, OP.mult, 96.0 * order[k] + 95, OP.add)
+        act(A("T256", 6 * k, 6 * k + 6), A("IOTA", 0, 6), bias=256.0 * k, scale=0.0)
+    act(A("IDT"), A("IOTA", 0, 4 * MW), bias=PI, scale=16.0)
+    act(A("DUMP", 0, 24), A("IDT", 0, 24), bias=4096.0)
+    act(A("DUMP", 32, 56), A("IDT", 0, 24), bias=4097.0)
+    ms(A("BD", 56, 64), 0.0)
+    for k, x in enumerate((0.0, 0.0, 0.0, 2048.0)):
+        act(A("XO", 2 * k, 2 * k + 2), A("IDT", 0, 2), bias=x)
+    ms(A("KP"), 0.0)
+    ts(A("CT", 16, 32), A("IOTA", 0, 16), PI, OP.is_le)
+    starts = [SEGT * k + sum(SEG[:m]) for k in range(4) for m in range(6)]
+    for x in starts:
+        act(A("KP", x, x + 16), A("CT", 16, 32))
+    ms(A("CT", 32, 64), 0.0)
+    for m in range(6):
+        ms(A("CT", 32 + m, 56, 6), float(SEG[m]))
+    ms(A("CT", 64, 96), 1.0)
+    scan(A("CT", 96, 128), A("CT", 64, 96), A("CT", 32, 64), -1.0, OP.mult, OP.add)
+    for k in range(2):
+        tt(A("CT", 128 + 16 * k, 144 + 16 * k), A("CT", 96 + 16 * k, 112 + 16 * k), A("S16"), OP.mult)
+        rsum(A("CT", 160 + k, 161 + k), A("CT", 128 + 16 * k, 144 + 16 * k))
+    ts(A("ENDS"), A("CT", 160, 162), 1.0 / 2048, OP.mult)
+    ms(A("TOT"), 0.0)
+    wt = [[0.0] * 32 for k in range(2)]
+    for i in range(16):
+        s = i % 8
+        if s < 4:
+            wt[0][i] = 1.0 if r <= s else 0.0
+        else:
+            wt[1 if r <= s - 4 else 0][i] = 1.0
+    wt[0][16 + r] -= 1.0
+    wt[0][16 + r + 3] += 1.0
+    if r < 3:
+        wt[1][16 + r + 4] -= 1.0
+    for k in range(2):
+        a = 0
+        for i in range(1, 33):
+            if i == 32 or wt[k][i] != wt[k][a]:
+                ms(A("CT", 192 + 32 * k + a, 192 + 32 * k + i), wt[k][a] / 2048)
+                a = i
+        ts(A("CT", 256 + 32 * k, 288 + 32 * k), A("CT", 192 + 32 * k, 224 + 32 * k), A("S16", 7 + 8 * k, 8 + 8 * k), OP.mult)
+    tt(A("WT"), A("CT", 256, 288), A("CT", 288, 320), OP.add)
+    ts(A("PIU"), A("IOTA", 0, 8), 0.0, OP.mult, PI, OP.add)
+    for k in range(2):
+        tt(A("CE", 128 * k, 128 * k + 128), X(A("WT", 16 * k, 16 * k + 16), A("PIU")), BO, OP.mult)
+    ts(pc(9), PI, 8.0, OP.is_ge, 4.0 * MW, OP.mult)
+    ts(pc(10), PI, 11.0, OP.is_equal, -16.0 * MW, OP.mult)
+    ts(pc(11), PI, 15.0, OP.is_lt, pc(9), OP.mult)
+    ms(A("CK", 0, 4), 0.0)
+    ts(A("CK", 4, 8), A("CK", 0, 4), pc(10), OP.add, pc(11), OP.add)
+
+    KEY = A("KB", 16, 144)
+    DW, PW = A("DT", 0, 4096), A("PT", 0, 4096)
+    H1 = A("HT", 0, 128)
+
+    def NV(k):
+        return A("NN", k, k + 1)
+
+    def prep():
+        ts(A("K2"), KEY, 2048.0, OP.add)
+        ts(A("E1"), A("K2"), 11, OP.arith_shift_right)
+        cp(A("EH"), A("E1"))
+        ts(A("Z2"), A("K2"), 4095, OP.bitwise_and)
+        ts(A("HI"), A("K2"), 2047, OP.bitwise_and)
+        tt(f(1), A("Z2"), A("IMG"), OP.is_lt)
+        ts(A("Q"), A("HI"), 9, OP.arith_shift_right)
+        tt(z(0), A("Q"), f(1), OP.add)
+        ts(z(1), z(0), 3, OP.bitwise_and)
+        for d in range(4):
+            ts(A("OG", 128 * d, 128 * d + 128), z(1), float(d), OP.is_equal)
+        scan(A("IG"), A("RS4"), A("OG"), 0.0, OP.mult, OP.add)
+        mm(A("P6"), [(BO, A("IG")), (XM, A("OG"))])
+        act(A("GOB"), A("P6"), AF.Sigmoid, -1407.5 * 256, -256.0)
+        mm(A("P7", 0, 128), [(Ib, A("GOB", 128 * d, 128 * d + 128)) for d in range(4)])
+        act(A("GO"), A("P7", 0, 128))
+        act(f(2), A("P7", 0, 128), bias=64.0, scale=-64.0)
+        for k in range(16):
+            mm(A("P%d" % (k // 4), 128 * (k % 4), 128 * (k % 4) + 128), [(A("SEL", 128 * k, 128 * k + 128), A("EH"))])
+        turn(A("YT", 0, 160), A("KB"))
+        turn(A("YT", 160, 288), KEY)
+        ts(A("KPI"), X(A("YT"), A("PERM")), 2048.0, OP.add)
+        ts(A("ZP"), A("KPI"), 4095, OP.bitwise_and)
+        ts(A("HP"), A("KPI"), 2047, OP.bitwise_and)
+        ts(H1, A("HI"), 1.0, OP.add)
+        for w in (128, 256, 512):
+            act(A("HT", w, 2 * w), A("HT", 0, w))
+        ts(f(3), A("Q"), 2.0, OP.mult)
+        tt(f(4), f(3), f(1), OP.subtract)
+        tt(f(5), f(4), f(2), OP.add)
+
+    cp(KEY, A("LKI"))
+    cp(A("IMG"), A("LII"))
+    cp(NV(0), A("PNI", 0, 1))
+    prep()
+
+    def offsets(t):
+        ts(f(6), A("ZP"), NV(t), OP.is_lt, 2048.0, OP.mult)
+        tt(f(7), f(6), A("HP"), OP.add)
+        cp(A("OFF"), f(7))
+        return len(ops) - 1
+
+    offsets(0)
+    for t in range(RO):
+        last = t == RO - 1
+        n = NV(t)
+        RB = "RB%d" % t
+        m0 = MW * r
+        for c in range(4):
+            a, b, o, P = 512 * c, 512 * c + 512, A("OFF", 32 * c, 32 * c + 32), "P%d" % c
+            act(A("W1", a, b), X(DW, o))
+            if c < 2:
+                tt(A("W2", a, b), A("W1", a, b), A(P), OP.is_equal)
+                tt(A("W3", a, b), X(PW, o), A("W2", a, b), OP.mult)
+            else:
+                act(A("W2", a, b), X(PW, o))
+                tt(A(P), A("W1", a, b), A(P), OP.is_equal)
+                for h in range(2):
+                    tt(A("W3", a + 256 * h, a + 256 * h + 256), A("W2", a + 256 * h, a + 256 * h + 256), A(P, 256 * h, 256 * h + 256), OP.mult)
+            for k in range(4 * c, 4 * c + 4):
+                mm(A("P4", k, 128, 16), [(A("W3", 128 * k, 128 * k + 128), A("GS", 0, 8))])
+        act(A("TS"), A("P4", 0, 128))
+        mm(A("P5", 0, 128), [(A("TS"), If)])
+        ts(f(8), A("Z2"), n, OP.is_lt, 3.0, OP.mult)
+        tt(z(2), f(8), f(5), OP.add)
+        ts(A("CLS"), z(2), 71, OP.bitwise_and)
+        ts(f(9), A("Z2"), n, OP.is_lt, 1024.0, OP.mult)
+        tt(A("ET", 0, 128), f(9), A("E1"), OP.add)
+        for w in (128, 256, 512):
+            act(A("ET", w, 2 * w), A("ET", 0, w))
+        tt(A("CM"), A("P5", 0, 128), A("CLS"), OP.add)
+        for k in range(8):
+            ts(A("OH", 128 * k, 128 * k + 128), A("CM"), float(k), OP.is_equal)
+        scan(A("INC"), A("RS8"), A("OH"), 0.0, OP.mult, OP.add)
+        tt(f(10), A("P5", 0, 128), A("GO"), OP.mult)
+        mm(A("P6", 0, 4), [(A("REDb", 128 * i, 128 * i + 128), A("INC", 16 * i + 15, 1024, 256)) for i in range(16)])
+        mm(A("P7", 0, 64), red("REDb", "INC", 0, 1024))
+        for k in range(4):
+            ts(A("C1", 96 * k, 96 * k + 96), A("IOTA", 0, 96), A("P6", k, k + 1), OP.is_ge, W16, OP.mult)
+        ts(A("BC"), A("P6", 0, 4), 96.0, OP.min)
+        act(A("E2"), A("P7", 0, 64), bias=B15)
+        mm(A("P4", 0, 24), [(Ib, A("T256"))] + red("REDb", "C1", 0, 384))
+        ts(A("O1"), A("P4", 0, 24), 1.0 / 16, OP.mult)
+        for h in range(2):
+            mm(A("P%d" % h), [(BO, A("INC", 512 * h, 512 * h + 512)), (XM, A("OH", 512 * h, 512 * h + 512))])
+            act(A("XS", 512 * h, 512 * h + 512), A("P%d" % h))
+        tt(A("C2"), X(A("E2"), A("O1")), A("KW"), OP.is_le)
+        act(A("VB"), A("P4", 0, 24))
+        mm(A("P4", 0, 24), [(Ib, A("VB"))] + red("REDb", "C2", 0, 384))
+        mm(A("P3", 0, 4), [(A("CE", 0, 128), A("BC"))])
+        mm(A("P3", 4, 8), [(A("CE", 128, 256), A("BC"))])
+        cp(A("O2"), A("P4", 0, 24))
+        tt(A("MK"), X(A("XS"), A("O2")), A("KX"), OP.is_equal)
+        tt(A("MH"), X(A("HT"), A("O2")), A("MK"), OP.mult)
+        mm(A("P2", 0, 24), red("REDh", "MH", 0, 384))
+        tt(A("ME"), X(A("ET"), A("O2")), A("MK"), OP.mult)
+        mm(A("P2", 24, 48), red("REDh", "ME", 0, 384))
+        tt(A(RB, m0 + 48, m0 + 56), A("P3", 0, 8), A("CK"), OP.add)
+        act(A(RB, m0, m0 + 48), A("P2", 0, 48))
+        msg = A(RB, m0, m0 + MW)
+        sent = send("ls%d" % (4 + t), [(msg, R[ro["peer"][0]], off_eng, "m%d" % t)]
+                    + [(msg, x, rest[4 * k:4 * k + 4], "hm%d" % t) for k, x in enumerate(ro["near"])])
+        arrive("m%d" % t, 3 * len(off_eng), [A(RB, MW * s, MW * s + MW) for s in others], sent, 2.5)
+        ts(z(3), A("CLS"), 65, OP.bitwise_and)
+        ts(f(11), z(3), 1.0, OP.is_equal)
+        tt(f(12), f(11), H1, OP.mult)
+        tt(A("IMG"), A("IMG"), f(12), OP.max)
+        tt(f(13), A("DKI", 128 * t, 128 * t + 128), KEY, OP.subtract)
+        tt(f(14), f(13), A("GO"), OP.mult)
+        tt(f(15), f(14), KEY, OP.add)
+        ts(f(16), f(10), 0.0, OP.is_gt, -BIG, OP.mult)
+        act(f(17), f(10), bias=-0.5, scale=1.0 / 32)
+        tt(f(18), f(16), f(15), OP.add)
+        tt(KEY, f(17), f(18), OP.max)
+        if last:
+            dma("y", "st0", T.yl[:], KEY, 2.3)
+            dma("y", "st1", T.yi[:], A("IMG"), 2.3)
+            for h in range(2):
+                act(A("P%d" % h), A("IOTA"), bias=float(own[h] % 2048 - 2048))
+        else:
+            gate.append(sent)
+            prep()
+            gate.pop()
+        ms(A("P6", 96, 388, 97), 0.0)
+        ts(NV(8), n, 32.0, OP.add, 2048.0, OP.min)
+        tt(NV(9), NV(8), n, OP.subtract)
+        ts(A("SG", 0, 2), A("XO", 0, 2), n, OP.add, 2047.0, OP.min)
+        ts(A("SG", 2, 4), A("XO", 0, 2), n, OP.add, 2047.0, OP.min)
+        act(A("SX", 0, 8), A("XO"), bias=n)
+        ts(A("SX", 32, 64), A("IOTA", 0, 32), n, OP.add, -2048.0, OP.add)
+        act(A("SX", 64, 96), A("SX", 32, 64), bias=-1.0, scale=-1.0)
+        act(A("SX", 96, 128), A("SX", 32, 64), bias=-1.0, scale=-1.0)
+        tt(A("ED", 8, 16), A(RB, 48, 56), A(RB, MW + 48, MW + 56), OP.add)
+        tt(A("ED", 16, 24), A(RB, 2 * MW + 48, 2 * MW + 56), A(RB, 3 * MW + 48, 3 * MW + 56), OP.add)
+        tt(A("ED", 0, 8), A("ED", 8, 16), A("ED", 16, 24), OP.add)
+        for k in range(4):
+            x = order[k]
+            ts(A("M1", 96 * k, 96 * k + 96), A("KR"), A("ED", x, x + 1), OP.is_ge, A("ED", 4 + x, 5 + x), OP.mult)
+        mm(A("P4", 0, 384), [(Ih, A("KRW")), (BOh(1.0), A("M1"))])
+        mm(A("P5", 0, 24), [(Ih, A("KRC"))] + red("REDh", "M1", 0, 384))
+        ts(A("O3"), A("P5", 0, 24), -7.5, OP.add, 1.0 / 16, OP.mult)
+        act(A("IX"), A("P4", 0, 384))
+        tt(A("MK"), X(A("IDT"), A("O3")), A("IX"), OP.is_equal)
+        tt(A("MH"), X(A(RB), A("O3")), A("MK"), OP.mult)
+        mm(A("P5", 0, 24), red("REDh", "MH", 0, 384))
+        for k in range(4):
+            mm(A("P6", 97 * k, 97 * k + 96), [(BOh(1.0), A("MH", 96 * k, 96 * k + 96))])
+        tt(A("ME"), X(A(RB, 24, 4 * MW), A("O3")), A("MK"), OP.mult)
+        ts(A("MN"), A("ME"), 1024.0, OP.is_ge, 2048.0, OP.mult)
+        cp(A("BS", 0, 24), A("P5", 0, 24))
+        cp(A("BSH"), A("P5", 0, 24))
+        mm(A("P5", 0, 24), red("REDh", "MN", 0, 384) + [(Ih, A("BSH"))])
+        ts(A("O4"), A("P5", 0, 24), -1.0, OP.add)
+        tt(A("BD", 32, 56), A("P5", 0, 24), A("DUMP", 32, 56), OP.subtract)
+        cols = len(ops) - 1
+        ts(A("MB"), A("MH"), 1025.0, OP.is_ge, 1024.0, OP.mult)
+        w = 192 if last else 384
+        mm(A("P4", 0, w), [(BOh(2048.0), A("ME", 0, w)), (BOh(-1024.0), A("MN", 0, w))], stop=False)
+        act(A("EM"), X(PW, A("O4")), AF.Sigmoid, 0.0, -256.0)
+        mm(A("P5", 0, 24), red("REDb", "EM", 0, 384))
+        mm(A("P4", 0, w), [(A("EMB"), A("EM", 0, w))], start=False)
+        gate.append(len(ops) - 2)
+        mm(A("P7", 0, w), [(BOh(2.0), A("ME", 0, w)), (BOh(-1.0), A("MN", 0, w)), (BOh(1024.0), A("MH", 0, w)),
+                           (BOh(-1024.0), A("MB", 0, w)), (BOh(1.0 / 1024), A("MB", 0, w)), (A("EMB"), A("EM", 0, w))])
+        gate.pop()
+        act(A("W4", 0, w), X(DW, A("O4", 0, w // 16)))
+        act(A("TOT", 0, 24), A("P5", 0, 24))
+        gate.append(len(ops) - 1)
+        act(A("W4", 512, 512 + w), A("P4", 0, w), bias=-BIG)
+        act(A("W4", 1024, 1024 + w), X(PW, A("O4", 0, w // 16)))
+        gate.pop()
+        act(A("W4", 1536, 1536 + w), A("P7", 0, w), bias=-BIG - 1025.5)
+        for k in range(4):
+            for m in range(6):
+                x = starts[6 * k + m]
+                ts(A("NE", x, x + SEG[m]), A("P6", 97 * k + 16 * m, 97 * k + 97), A("BS", 6 * k + m, 6 * k + m + 1), OP.not_equal)
+            gate[:] = [cols]
+        del gate[:]
+        scan(A("SS"), A("NE"), A("KP"), 1.0, OP.min, OP.max)
+        tt(A("OV"), X(A("SS"), A("ENDS")), A("TOT"), OP.is_gt)
+        tt(A("BD", 64, 96), X(A("SS"), A("ENDS")), A("BD", 32, 64), OP.mult)
+        mm(A("P5", 32, 56), [(BO, A("OV", 0, 24))])
+        act(A("TT", 40, 64), A("P5", 32, 56), acc=NV(10))
+        act(NV(11), NV(10), AF.Relu, NV(9), -1.0)
+        act(NV(t + 1), NV(11), AF.Identity, NV(8), -1.0)
+        tt(A("BD", 96, 120), A("BD", 64, 88), A("DUMP", 0, 24), OP.add)
+        cp(A("O5"), A("BD", 96, 120))
+        tt(X(A("DT"), A("O5", 0, w // 16)), A("W4", 0, w), A("W4", 512, 512 + w), OP.max)
+        tt(A("SI", 0, 32), X(DW, A("SG", 0, 2)), A("SX", 32, 64), OP.add)
+        tt(A("SK", 64, 128), X(DW, A("SG")), A("SX", 64, 128), OP.subtract)
+        ts(A("SX", 8, 12), A("SX", 0, 4), NV(t + 1), OP.is_ge, 4096.0, OP.mult)
+        ts(A("SI", 32, 64), A("SI", 0, 32), 0x100800, OP.bitwise_and)
+        tt(A("SX", 12, 16), A("SX", 8, 12), A("SX", 4, 8), OP.add)
+        ts(A("SK", 0, 32), A("SI", 32, 64), 2048.0, OP.not_equal)
+        ts(A("SK", 32, 64), A("SI", 32, 64), 2048.0, OP.is_equal)
+        cp(A("SO"), A("SX", 12, 16))
+        tt(A("SK", 192, 256), A("SK", 0, 64), A("SK", 64, 128), OP.mult)
+        tt(X(A("DT"), A("SO")), A("SK", 192, 256), A("SX", 64, 128), OP.add)
+        if not last:
+            gate.append(len(ops) - 1)
+            gate.append(offsets(t + 1))
+        tt(X(A("PT"), A("O5", 0, w // 16)), A("W4", 1024, 1024 + w), A("W4", 1536, 1536 + w), OP.max)
+        del gate[:]
+        act(A("SK", 128, 192), X(PW, A("SG")), bias=0.5)
+        tt(A("SK", 256, 320), A("SK", 0, 64), A("SK", 128, 192), OP.mult)
+        ts(X(A("PT"), A("SO")), A("SK", 256, 320), 1.0, OP.mult, -0.5, OP.add)
+
+    dma("y", "st2", T.yn[:], NV(RO), 2.0)
+    done = len(ops) - 2
+    for h in range(2):
+        a, b = 512 * h, 512 * h + 512
+        gate.append(done)
+        tt(A("W1", a, b), A("DT", own[h], own[h] + 512), A("P%d" % h), OP.add)
+        gate.pop()
+        dma("y", "st%d" % (3 + h), T.yk[:, a:b], A("W1", a, b), 2.9)
+        for k in range(2):
+            c, P = a + 256 * k, A("P%d" % (2 + 2 * h + k), 0, 256, p=8)
+            act(A("W2", c, c + 256), A("PT", own[h] + 256 * k, own[h] + 256 * k + 256), AF.Abs)
+            ts(A("W3", c, c + 256), A("W2", c, c + 256), -0.5, OP.add)
+            mm(P, [(A("GS", 8, 16), A("W3", c, c + 256))])
+            if h:
+                cp(A("YS", c, c + 256, p=8), P)
+            else:
+                act(A("YS", c, c + 256, p=8), P)
+    dma("s", "st5", T.ys[:], A("YS", p=8), 2.0)
+    _issue(T, Q, ops)

@@ -2,11 +2,9 @@ from concourse.bass import DstId, RemoteDMATransfer
 from concourse.mybir import AluOpType as OP, AxisListType, ActivationFunctionType as AF
 
 N, RO, NCORES = 4, 3, 256
-MW = 56
+LW, YW, OW = 160, 64, 280
 TW = 8256
 BIG = float(2 ** 22)
-SEG = [97 - 16 * m for m in range(6)]
-SEGT = sum(SEG)
 F, H, B, I, U = "float32", "float16", "bfloat16", "int32", "uint16"
 
 
@@ -15,34 +13,32 @@ def _sb(w, d):
 
 
 SCRATCH = {
-    "DT": _sb(TW, F), "PT": _sb(TW, F), "RB0": _sb(4 * MW, F), "RB1": _sb(4 * MW, F), "RB2": _sb(4 * MW, F),
-    "TKI": _sb(1024, I), "TPI": _sb(1024, I), "LKI": _sb(128, I), "LII": _sb(128, I), "DKI": _sb(384, I), "PNI": _sb(4, I),
-    "W1": _sb(2048, F), "W2": _sb(2048, F), "W3": _sb(2048, F), "W4": _sb(2048, F), "TM": _sb(128 * 20, F), "TN": _sb(128 * 8, I),
-    "IOTA": _sb(512, F), "PCI": _sb(8, I), "PC": _sb(24, F), "MI": _sb(128, I), "MG": _sb(128, I), "CODE": _sb(128, B),
-    "BOb": _sb(128, B), "BOh": _sb(1024, H), "Ib": _sb(128, B), "Ih": _sb(128, H), "If": _sb(128, F), "XM": _sb(128, B),
-    "EMB": _sb(128, B), "CE": _sb(256, B), "SEL": _sb(2048, H), "REDb": _sb(2048, B), "REDh": _sb(2048, H), "TB": _sb(1024, B),
-    "GS": _sb(16, F), "S16": _sb(16, F), "CK": _sb(8, F), "RS8": _sb(1024, B), "RS4": _sb(512, B), "KW": _sb(384, F),
-    "KX": _sb(384, F), "KR": _sb(96, F), "KRW": _sb(384, H), "KRC": _sb(24, H), "T256": _sb(24, B), "IDT": _sb(4 * MW, F),
-    "KP": _sb(4 * SEGT, B), "ENDS": _sb(2, U), "PERM": _sb(8, U), "PIU": _sb(8, U), "DUMP": _sb(64, F), "XO": _sb(8, F),
-    "VB": _sb(24, B), "BSH": _sb(24, H), "CT": _sb(384, F), "WT": _sb(32, F),
-    "KB": _sb(160, F), "YT": _sb(288, F), "IMG": _sb(128, F), "K2": _sb(128, I), "Z2": _sb(128, I), "HI": _sb(128, I),
-    "E1": _sb(128, I), "EH": _sb(128, H), "Q": _sb(128, I), "OG": _sb(512, B), "IG": _sb(512, B),
-    "OH": _sb(1024, B), "INC": _sb(1024, B), "GOB": _sb(512, B), "GO": _sb(128, F), "KPI": _sb(128, I),
-    "ZP": _sb(128, I), "HP": _sb(128, I), "OFF": _sb(128, U), "CLS": _sb(128, I), "TS": _sb(128, F), "CM": _sb(128, B),
-    "HT": _sb(1024, F), "ET": _sb(1024, F), "XS": _sb(1024, F), "E2": _sb(64, F), "BC": _sb(4, B), "C1": _sb(384, B),
-    "C2": _sb(384, B), "O1": _sb(24, U), "O2": _sb(24, U), "O3": _sb(24, U), "O4": _sb(24, U), "O5": _sb(24, U),
-    "MK": _sb(384, F), "MH": _sb(384, H), "ME": _sb(384, H), "MN": _sb(384, H), "MB": _sb(384, H), "M1": _sb(384, H),
-    "ED": _sb(24, F), "IX": _sb(384, F), "BS": _sb(32, F), "BD": _sb(128, F), "NE": _sb(4 * SEGT, B), "SS": _sb(4 * SEGT, B),
-    "EM": _sb(384, B), "TOT": _sb(32, F), "OV": _sb(32, B), "TT": _sb(64, F), "NN": _sb(32, F), "SG": _sb(4, U), "SO": _sb(4, U),
-    "SX": _sb(256, F), "SI": _sb(64, I), "SK": _sb(320, F), "YS": _sb(1024, F),
+    "KT": _sb(TW, F), "PT": _sb(TW, F), "TKI": _sb(1024, I), "TPI": _sb(1024, I), "KS": _sb(1024, F), "PS": _sb(1024, F),
+    "LS": _sb(N * LW, I), "LL": _sb(N * LW, I), "LN": _sb(640, I), "PNI": _sb(4, I), "YS": _sb(N * YW, F), "YL": _sb(N * YW, F),
+    "OS": _sb(N * OW, F), "OL": _sb(N * OW, F), "YP": _sb(1024, F), "YI": _sb(128, F),
+    "W1": _sb(2048, F), "W2": _sb(2048, F), "W3": _sb(2048, F), "TM": _sb(128 * 8, F), "TN": _sb(128 * 8, I),
+    "IOTA": _sb(512, F), "PCI": _sb(16, I), "PC": _sb(32, F), "MI": _sb(128, I), "MG": _sb(128, I), "CODE": _sb(128, B),
+    "BOb": _sb(128, B), "BOh": _sb(768, H), "Ib": _sb(128, B), "If": _sb(128, F), "XM": _sb(128, B), "FO": _sb(128, B),
+    "EMB": _sb(128, B), "SEL": _sb(2048, H), "REDb": _sb(2048, B), "REDh": _sb(2048, H), "TB": _sb(1024, B),
+    "MVb": _sb(512, B), "MVh": _sb(512, H), "MVf": _sb(512, F), "GS": _sb(16, F), "S16": _sb(16, F), "RS4": _sb(512, B),
+    "C128": _sb(1024, B), "KR": _sb(96, F), "KX": _sb(96, F), "KP": _sb(582, B), "PERM": _sb(8, U), "CT": _sb(64, F),
+    "XO": _sb(8, F), "OK": _sb(64, U), "OY": _sb(64, U),
+    "KB": _sb(128, F), "OB": _sb(160, F), "YT": _sb(288, F), "IMG": _sb(128, F), "K2": _sb(128, I), "Z2": _sb(128, I), "HI": _sb(128, I),
+    "E1": _sb(128, I), "EH": _sb(256, H), "Q": _sb(128, I), "TO": _sb(256, B), "OG": _sb(512, B), "IG": _sb(512, B),
+    "GOB": _sb(512, B), "GO": _sb(128, F), "OFF": _sb(128, U), "CLS": _sb(128, I), "TS": _sb(128, F), "CM": _sb(128, B),
+    "HM": _sb(1024, F), "EM": _sb(1024, F), "OH": _sb(1024, B), "INC": _sb(1024, B), "E2": _sb(64, F), "JK": _sb(64, B),
+    "AC": _sb(8, F), "VB": _sb(8, B), "C2": _sb(96, B), "G2": _sb(192, B), "G3": _sb(192, F), "MH": _sb(96, H), "ME": _sb(96, H),
+    "MB": _sb(96, H), "O1": _sb(8, U), "O2": _sb(8, U), "O3": _sb(8, U), "O4": _sb(8, U), "O5": _sb(24, U), "BS": _sb(64, F),
+    "NE": _sb(582, B), "SS": _sb(582, B), "EE": _sb(96, B), "OLD": _sb(192, F), "NEW": _sb(192, F), "SC": _sb(768, F),
+    "OV": _sb(8, B), "TT": _sb(8, F), "NN": _sb(32, F), "SG": _sb(4, U), "SO": _sb(4, U),
+    "SX": _sb(64, F), "SI": _sb(64, I), "SK": _sb(320, F),
 }
 for _b in range(8):
     SCRATCH["P%d" % _b] = ("psum", [128, 512], F)
-SEMAPHORES = (["cv", "cs", "ct", "cg", "tabD", "tabP", "hD", "hP", "rl0", "rl1", "rl2", "lo"] + ["m%d" % t for t in range(RO)]
-              + ["hm%d" % t for t in range(RO)] + ["ls%d" % i for i in range(7)] + ["ld%d" % i for i in range(8)]
-              + ["st%d" % i for i in range(8)])
+SEMAPHORES = (["cv", "cs", "ct", "cg", "tabK", "tabP", "lan", "ylan", "hL", "hT", "hl", "hd", "he", "hY", "hO", "lo"]
+              + ["o%d" % s for s in range(N)] + ["ls%d" % i for i in range(8)] + ["d%d" % i for i in range(40)])
 ROUTES = []
-CYC, PEC, WAKE = 1.0e-3, 0.6e-3, 0.12
+CYC, PEC, WAKE = 1.0e-3, 0.5e-3, 0.12
 
 
 def _mask(engines):
@@ -53,24 +49,18 @@ def _routes(T, topo):
     R = list(T.cores)
     out = []
     for s, c in enumerate(R):
-        peer = [d for d in range(N) if d != s and topo.may_write(c, R[d])]
-        cross = [d for d in range(N) if d != s and d not in peer]
-        helpers = [h for h in topo.cores_of(c) if h != c and all(topo.may_write(h, R[d]) for d in cross)]
-        slot = {h: [y for y in helpers if topo.die(y) == topo.die(h)].index(h) for h in helpers}
-        helpers.sort(key=lambda h: (slot[h], topo.die(h)))
-        near = [h for h in helpers if topo.die(h) == topo.die(c)]
-        relay = {}
-        for d in cross:
-            srcs = [x for x in range(N) if x != d and not topo.may_write(R[x], R[d])]
-            for h in helpers:
-                cand = [x for x in range(NCORES) if topo.mates(x, R[d]) and topo.may_write(x, R[d]) and topo.die(x) == topo.die(h)]
-                relay[(h, d)] = (cand[srcs.index(s)], slot[h])
-        out.append({"peer": peer, "cross": cross, "helpers": helpers, "near": near, "relay": relay})
+        peer = [d for d in range(N) if d != s and topo.may_write(c, R[d])][0]
+        cross = [d for d in range(N) if d != s and d != peer]
+        rest = [h for h in topo.cores_of(c) if h != c]
+        ports = [h for h in rest if all(topo.may_write(h, R[d]) for d in cross)]
+        same = [h for h in rest if topo.die(h) == topo.die(c)]
+        out.append({"peer": peer, "cross": cross, "near": [h for h in ports if h in same], "far": [h for h in ports if h not in same],
+                    "side": [h for h in same if h not in ports][0], "plain": [h for h in rest if h not in ports and h not in same]})
     return out
 
 
-def _chunk(s, i):
-    return (512 * s if i < 2 else 2048 + 512 * ((s - 1) % N)) + 256 * (i % 2)
+def _high(s):
+    return 2048 + 512 * ((s - 1) % N)
 
 
 def _dst(topo, d, c):
@@ -80,60 +70,59 @@ def _dst(topo, d, c):
 
 def helper_program(g, core, T, topo, routes):
     R = list(T.cores)
-    total = 0
-    for s in range(N):
-        ro = routes[s]
-        if core in ro["helpers"]:
-            i = ro["helpers"].index(core)
-            a = _chunk(s, i)
-            eng = topo.engines(core, R[ro["peer"][0]])
-            half = len(eng) // 2
-            got = len(topo.engines(R[s], core))
-            g.wait_ge(T.sem.hD, got // 2)
-            ap = T.DT[:, a:a + 256]
-            g.remote_dma_fused([RemoteDMATransfer(dst_ids=[_dst(topo, ro["relay"][(core, d)][0], core)], dma_engine_mask=_mask(eng[k * half:(k + 1) * half]),
-                                                  remote_sem=T.sem["rl%d" % ro["relay"][(core, d)][1]], src=ap, dst=ap)
-                                for k, d in enumerate(ro["cross"])], local_sem=T.sem.lo)
-            rid, pid = topo.addr(R[ro["peer"][0]], core)
-            g.remote_dma(ap, ap, T.sem.tabD, T.sem.lo, pid, rid, _mask(eng))
-            g.wait_ge(T.sem.hP, got // 2)
-            ap = T.PT[:, a:a + 256]
-            if ro["relay"][(core, ro["cross"][0])][1] == 0:
-                g.remote_dma_fused([RemoteDMATransfer(dst_ids=[_dst(topo, ro["relay"][(core, d)][0], core)], dma_engine_mask=_mask(eng[k * half:(k + 1) * half]),
-                                                      remote_sem=T.sem.rl2, src=ap, dst=ap) for k, d in enumerate(ro["cross"])], local_sem=T.sem.lo)
-                g.remote_dma(ap, ap, T.sem.tabP, T.sem.lo, pid, rid, _mask(eng))
-                total += 4 * len(eng)
-            else:
-                ds = ro["cross"] + ro["peer"]
-                g.remote_dma_fused([RemoteDMATransfer(dst_ids=[_dst(topo, R[d], core) for d in ds], dma_engine_mask=_mask(eng),
-                                                      remote_sem=T.sem.tabP, srcs=[ap], dsts=[ap for d in ds])], local_sem=T.sem.lo)
-                total += 3 * len(eng)
-            if core in ro["near"]:
-                d = R[ro["cross"][ro["near"].index(core)]]
-                rid, pid = topo.addr(d, core)
-                for t in range(RO):
-                    g.wait_ge(T.sem["hm%d" % t], got // 4)
-                    ap = T["RB%d" % t][:, MW * s:MW * (s + 1)]
-                    g.remote_dma(ap, ap, T.sem["m%d" % t], T.sem.lo, pid, rid, _mask(eng))
-                    total += len(eng)
-        for (h, d), (x, slot) in sorted(ro["relay"].items(), key=lambda e: e[1][1]):
-            if x == core:
-                a = _chunk(s, ro["helpers"].index(h))
-                eng = topo.engines(core, R[d])
-                rid, pid = topo.addr(R[d], core)
-                g.wait_ge(T.sem["rl%d" % slot], len(eng) // 2)
-                ap = T.DT[:, a:a + 256]
-                g.remote_dma(ap, ap, T.sem.tabD, T.sem.lo, pid, rid, _mask(eng))
-                total += len(eng)
-        for (h, d), (x, slot) in ro["relay"].items():
-            if x == core and slot == 0:
-                a = _chunk(s, ro["helpers"].index(h))
-                g.wait_ge(T.sem.rl2, len(eng) // 2)
-                ap = T.PT[:, a:a + 256]
-                g.remote_dma(ap, ap, T.sem.tabP, T.sem.lo, pid, rid, _mask(eng))
-                total += len(eng)
-    if total:
-        g.wait_ge(T.sem.lo, total)
+    home = [s for s in range(N) if core in topo.cores_of(R[s])]
+    if not home:
+        return
+    s = home[0]
+    ro = routes[s]
+    on = topo.engines(core, R[s])
+    total = [0]
+
+    def hand(sem, src, dst, to, rsem):
+        eng = topo.engines(core, to)
+        rid, pid = topo.addr(to, core)
+        g.wait_ge(T.sem[sem[0]], sem[1])
+        g.remote_dma(dst, src, T.sem[rsem], T.sem.lo, pid, rid, _mask(eng))
+        total[0] += len(eng)
+
+    def spread(sem, src, rep, done, table, owner):
+        for q in (g.sync, g.scalar):
+            q.wait_ge(T.sem[sem[0]], sem[1])
+        for u in range(N):
+            (g.sync, g.scalar)[u % 2].dma_start(rep[32 * u:32 * u + 32, 0:1024], src).then_inc(T.sem[done], 16)
+        g.wait_ge(T.sem[done], 64)
+        hn = len(on) // 2
+        g.remote_dma_fused([RemoteDMATransfer(dst_ids=[_dst(topo, R[s], core)], dma_engine_mask=_mask(on[hn * h:hn * h + hn]), remote_sem=T.sem["tab" + table[0]],
+                                              src=rep[:, 512 * h:512 * h + 512], dst=T[table][:, a:a + 512])
+                            for h, a in enumerate((512 * owner, _high(owner)))], local_sem=T.sem.lo)
+        total[0] += len(on)
+
+    q4 = len(on) // 4
+    off = len(topo.engines(R[s], R[ro["peer"]]))
+    hin, land = T.KS[:, 0:256], T.PS[:, 0:256]
+    for kind, table in (("near", "KT"), ("far", "PT")):
+        if core in ro[kind]:
+            d = ro["cross"][ro[kind].index(core)]
+            if kind == "near":
+                ap = T.LL[:, LW * s:LW * s + LW]
+                hand(("hL", q4), ap, ap, R[d], "lan")
+            hand(("hT", q4), hin, land, routes[d][kind][routes[d]["cross"].index(s)], "hl")
+            spread(("hl", off), land, T.W1, "hd", table, d)
+            if kind == "near":
+                ap = T.YL[:, YW * s:YW * s + YW]
+                hand(("hY", q4), ap, ap, R[d], "ylan")
+            a = OW * s + (OW // 2 if kind == "near" else 0)
+            ap = T.OL[:, a:a + OW // 2]
+            hand(("hO", 2 * q4), ap, ap, R[d], "o%d" % s)
+    if core == ro["side"]:
+        spread(("hT", q4), hin, T.W1, "hd", "KT", s)
+        spread(("hl", q4), land, T.W2, "he", "PT", s)
+    if core == ro["plain"][0]:
+        spread(("hl", q4), land, T.W1, "hd", "KT", ro["peer"])
+    if core == ro["plain"][1]:
+        hand(("hT", q4), hin, land, routes[ro["peer"]]["plain"][1], "hl")
+        spread(("hl", off), land, T.W1, "hd", "PT", ro["peer"])
+    g.wait_ge(T.sem.lo, total[0])
 
 
 def _issue(T, Q, ops):
@@ -227,12 +216,12 @@ def rank_program(g, core, T, topo):
         return
     R = list(T.cores)
     ro = routes[r]
-    ops, hist, bank, gate = [], {}, {}, []
+    ops, hist, gate = [], {}, []
 
-    def A(n, a=0, b=None, st=1, p=128):
+    def A(n, a=0, b=None, st=1, p=128, p0=0):
         if b is None:
             b = SCRATCH[n][1][1]
-        return (T[n][0:p, a:b:st] if st > 1 else T[n][0:p, a:b], [(n, a, b, st)], (b - a + st - 1) // st, False)
+        return (T[n][p0:p0 + p, a:b:st] if st > 1 else T[n][p0:p0 + p, a:b], [(n, a, b, st, p0, p0 + p)], (b - a + st - 1) // st, False)
 
     def X(win, off):
         return (win[0].indirect(off[0]), win[1] + off[1], 16 * off[2], True)
@@ -246,25 +235,23 @@ def rank_program(g, core, T, topo):
                 rd.extend(x[1][1:])
         me, dep, aft = len(ops), set(), set(after) | set(gate)
         for spans, w in ((rd, False), (wr, True)):
-            for n, a, b, st in spans:
+            for n, a, b, st, p, e in spans:
                 ps = SCRATCH[n][0] == "psum"
-                if ps and n in bank:
-                    aft.add(bank[n])
-                for a2, b2, s2, w2, q2, j in hist.get(n, []):
+                for a2, b2, s2, p2, e2, w2, q2, j in hist.get(n, []):
+                    meet = a < b2 and a2 < b and p < e2 and p2 < e
                     if ps and q2 != q:
                         dep.add(j)
                     elif q == "t" and q2 == "t":
-                        continue
-                    elif (w or w2) and a < b2 and a2 < b and (st == 1 or st != s2 or (a - a2) % st == 0):
+                        if ps and meet:
+                            aft.add(j)
+                    elif (w or w2) and meet and (st == 1 or st != s2 or (a - a2) % st == 0):
                         dep.add(j)
         for spans, w in ((rd, False), (wr, True)):
-            for n, a, b, st in spans:
+            for n, a, b, st, p, e in spans:
                 h = hist.setdefault(n, [])
-                if w and st == 1:
-                    h[:] = [e for e in h if not (a <= e[0] and e[1] <= b)]
-                h.append((a, b, st, w, q, me))
-                if SCRATCH[n][0] == "psum":
-                    bank[n] = me
+                if w and st == 1 and SCRATCH[n][0] != "psum":
+                    h[:] = [x for x in h if not (a <= x[0] and x[1] <= b and p <= x[3] and x[4] <= e)]
+                h.append((a, b, st, p, e, w, q, me))
         ops.append({"q": q, "fn": fn, "dep": dep, "after": aft - dep, "cost": cost, "busy": cost if busy is None else busy, "sem": sem, "val": val})
         return me
 
@@ -302,19 +289,16 @@ def rank_program(g, core, T, topo):
     def turn(o, i):
         run("v", [o], [i], lambda: g.vector.transpose(o[0], i[0]), cyc(o, [i]))
 
-    def rsum(o, i):
-        run("v", [o], [i], lambda: g.vector.tensor_reduce(o[0], i[0], AxisListType.X, OP.add), cyc(i, [i]))
-
     def act(o, i, f=AF.Identity, bias=0.0, scale=1.0, acc=None):
         if acc is None:
             run("s", [o], [i, bias], lambda: g.scalar.activation(o[0], i[0], f, bias=ap(bias), scale=scale), cyc(o, [i]))
         else:
-            run("s", [o, acc], [i, bias], lambda: g.scalar.activation(o[0], i[0], f, bias=ap(bias), scale=scale, accum_out=acc[0]), cyc(o, [i]))
+            run("s", [o, acc], [i, bias], lambda: g.scalar.activation(o[0], i[0], f, bias=ap(bias), scale=scale, accum_out=acc[0]), cyc(o, [i]) + 0.02)
 
-    def mm(o, terms, start=True, stop=True):
+    def mm(o, terms):
         def fn():
             for k, (l, x) in enumerate(terms):
-                last = g.tensor.matmul(o[0], l[0], x[0], start and k == 0, stop and k == len(terms) - 1)
+                last = g.tensor.matmul(o[0], l[0], x[0], k == 0, k == len(terms) - 1)
             return last
         c = sum(max(min(64, l[2]), x[2]) * (4 if SCRATCH[l[1][0][0]][2] == F else 1) for l, x in terms) * PEC
         run("t", [o], [x for tm in terms for x in tm], fn, c)
@@ -323,16 +307,27 @@ def rank_program(g, core, T, topo):
         return [(A(mat, 128 * i, 128 * i + 128), A(n, a + i, b, 16)) for i in range(16)]
 
     Q = {"v": g.vector, "s": g.scalar, "t": g.tensor, "g": g, "y": g.sync}
-    dmas = {"s": [], "y": []}
+    dmas = {"s": [], "y": [], "g": []}
+    nd = [0]
 
-    def dma(q, sem, o, i, cost):
-        dmas[q].append(run(q, [o], [i], lambda: Q[q].dma_start(ap(o), ap(i)).then_inc(T.sem[sem], 16), cost, 0.1, sem, 16, dmas[q][-1:]))
+    def dma(q, pairs, cost):
+        sem = "d%d" % nd[0]
+        nd[0] += 1
 
-    def send(ls, items):
-        return run("g", [], [x for x, d, e, sem in items],
+        def fn():
+            for o, i in pairs:
+                Q[q].dma_start(ap(o), ap(i)).then_inc(T.sem[sem], 16)
+        dmas[q].append(run(q, [o for o, i in pairs], [i for o, i in pairs], fn, cost, 0.08 * len(pairs), sem, 16 * len(pairs), dmas[q][-1:]))
+
+    ns = [0]
+
+    def send(items):
+        ls = "ls%d" % ns[0]
+        ns[0] += 1
+        return run("g", [], [x for x, y, d, e, sem in items],
                    lambda: g.remote_dma_fused([RemoteDMATransfer(dst_ids=[_dst(topo, d, core)], dma_engine_mask=_mask(e), remote_sem=T.sem[sem],
-                                                                 src=x[0], dst=x[0]) for x, d, e, sem in items], local_sem=T.sem[ls]),
-                   2.5, 0.6, ls, sum(len(e) for x, d, e, sem in items))
+                                                                 src=x[0], dst=y[0]) for x, y, d, e, sem in items], local_sem=T.sem[ls]),
+                   2.5, 0.6, ls, sum(len(e) for x, y, d, e, sem in items))
 
     def arrive(sem, val, outs, after, cost):
         run("a", outs, [], None, cost, 0.0, sem, val, [after])
@@ -343,72 +338,90 @@ def rank_program(g, core, T, topo):
     def z(k):
         return A("TN", 128 * k, 128 * k + 128)
 
-    off_eng = topo.engines(core, R[ro["peer"][0]])
-    on_eng = topo.engines(core, ro["helpers"][0])
-    rest = [e for e in on_eng if e not in off_eng]
-    others = [s for s in range(N) if s != r]
-    own = (_chunk(r, 0), _chunk(r, 2))
+    def v(k):
+        return A("P7", 128 * k, 128 * k + 128)
 
-    dma("y", "ld0", A("TKI", 0, 512), T.tk[:, 0:512], 2.8)
-    dma("s", "ld1", A("TKI", 512, 1024), T.tk[:, 512:1024], 3.8)
-    dma("y", "ld2", A("TPI", 0, 512), T.tp[:, 0:512], 4.8)
-    dma("s", "ld3", A("TPI", 512, 1024), T.tp[:, 512:1024], 5.8)
-    dma("y", "ld4", A("LKI"), T.lk[:], 6.2)
-    dma("y", "ld5", A("LII"), T.li[:], 6.6)
-    dma("y", "ld6", A("PNI", 0, 1), T.pn[:], 6.8)
-    dma("y", "ld7", A("DKI"), T.dk[:], 7.6)
+    def blk(n, w, k, a=0, b=None):
+        return A(n, w * k + a, w * k + (w if b is None else b))
+
+    peer, cross = ro["peer"], ro["cross"]
+    off_eng = topo.engines(core, R[peer])
+    on_eng = topo.engines(core, ro["side"])
+    rest = [e for e in on_eng if e not in off_eng]
+    q4 = len(on_eng) // 4
+    quart = [(off_eng + rest)[q4 * k:q4 * k + q4] for k in range(4)]
+    others = cross + [peer]
+
+    def rows(x, d):
+        return x[32 * d:32 * d + 32, :]
+    for d in others:
+        dma("s", [(blk("LS", LW, d, 0, 32), rows(T.lk, d)), (blk("LS", LW, d, 32, 64), rows(T.li, d)), (blk("LS", LW, d, 64, LW), rows(T.dk, d))], 2.0)
+    for d in others + [r]:
+        dma("y", [(blk("TKI", 256, d), rows(T.tk, d))], 2.4)
+    for d in others + [r]:
+        dma("y", [(blk("TPI", 256, d), rows(T.tp, d))], 3.6)
+    dma("s", [(A("LN", 0, 128, p0=32 * r, p=32), rows(T.lk, r)), (A("LN", 128, 256, p0=32 * r, p=32), rows(T.li, r)),
+              (A("LN", 256, 640, p0=32 * r, p=32), rows(T.dk, r))] + [(A("PNI", 0, 1, p0=32 * u, p=32), rows(T.pn, r)) for u in range(N)], 4.0)
     run("g", [A("PCI", 0, 1)], [], lambda: g.iota(T.PCI[:, 0:1], [[1, 1]], 0, 1), 0.15)
     run("g", [A("IOTA")], [], lambda: g.iota(T.IOTA[:], [[1, 512]], 0, 0, allow_small_or_imprecise_dtypes=True), 1.2, after=[len(ops) - 1])
 
-    hn = len(on_eng) // 2
-    for h in range(2):
-        act(A("P%d" % h), A("IOTA"), bias=float(own[h] % 2048 - 2048))
-        tt(A("DT", own[h], own[h] + 512), A("TKI", 512 * h, 512 * h + 512), A("P%d" % h), OP.subtract)
-        sent = send("ls%d" % h, [(A("DT", _chunk(r, 2 * h + i), _chunk(r, 2 * h + i) + 256), ro["helpers"][2 * h + i], on_eng[hn * i:hn * i + hn], "hD")
-                                 for i in range(2)])
-    arrive("tabD", 12 * len(off_eng), [A("DT", _chunk(s, 2 * h), _chunk(s, 2 * h) + 512) for s in others for h in range(2)], sent, 13.0)
-    for h in range(2):
-        ts(A("P%d" % (2 + h)), A("TKI", 512 * h, 512 * h + 512), 0.0, OP.is_ge, -0.5, OP.add)
-        ts(A("W1", 512 * h, 512 * h + 512), A("TPI", 512 * h, 512 * h + 512), 2.0, OP.mult, 1.0, OP.add)
-        tt(A("PT", own[h], own[h] + 512), A("W1", 512 * h, 512 * h + 512), A("P%d" % (2 + h)), OP.mult)
-        sent = send("ls%d" % (2 + h), [(A("PT", _chunk(r, 2 * h + i), _chunk(r, 2 * h + i) + 256), ro["helpers"][2 * h + i], on_eng[hn * i:hn * i + hn], "hP")
-                                       for i in range(2)])
-    arrive("tabP", 12 * len(off_eng), [A("PT", _chunk(s, 2 * h), _chunk(s, 2 * h) + 512) for s in others for h in range(2)], sent, 12.0)
+    sent = send([(blk("LS", LW, peer), blk("LL", LW, r), R[peer], off_eng, "lan")]
+                + [(blk("LS", LW, d), blk("LL", LW, r), ro["near"][k], quart[2 + k], "hL") for k, d in enumerate(cross)])
+    arrive("lan", 3 * len(off_eng), [blk("LL", LW, s) for s in others], sent, 3.5)
+    for k, s in enumerate(others):
+        dma("ys"[k % 2], [(A("LN", 0, 128, p0=32 * s, p=32), blk("LL", LW, s, 0, 32)), (A("LN", 128, 256, p0=32 * s, p=32), blk("LL", LW, s, 32, 64)),
+                          (A("LN", 256, 640, p0=32 * s, p=32), blk("LL", LW, s, 64, LW))], 2.0)
+
+    hin, land = A("KS", 0, 256), A("PS", 0, 256)
+    for d in others + [r]:
+        cp(blk("KS", 256, d), blk("TKI", 256, d))
+    sent = send([(blk("KS", 256, peer), land, routes[peer]["plain"][0], quart[0], "hl"), (blk("KS", 256, r), hin, ro["side"], quart[1], "hT")]
+                + [(blk("KS", 256, d), hin, ro["near"][k], quart[2 + k], "hT") for k, d in enumerate(cross)])
+    arrive("tabK", N * len(on_eng), [A("KT", 0, 4096)], sent, 9.0)
+    for k, d in enumerate(others + [r]):
+        P = A("P%d" % k, 0, 256)
+        ts(P, blk("TKI", 256, d), 0.0, OP.is_ge, -0.5, OP.add)
+        tt(P, blk("TPI", 256, d), P, OP.mult)
+        act(blk("PS", 256, d), P, bias=1.0, scale=2.0)
+    sent = send([(blk("PS", 256, peer), hin, ro["plain"][1], quart[0], "hT"), (blk("PS", 256, r), land, ro["side"], quart[1], "hl")]
+                + [(blk("PS", 256, d), hin, ro["far"][k], quart[2 + k], "hT") for k, d in enumerate(cross)])
+    arrive("tabP", N * len(on_eng), [A("PT", 0, 4096)], sent, 9.0)
 
     def pc(k):
         return A("PC", k, k + 1)
 
     def pi(k):
         return A("PCI", k, k + 1)
-    PI, PG, W16, B15 = pc(0), pc(1), pc(2), pc(3)
+    PI, PG, PU, PF, PP, B15 = pc(0), pc(1), pc(2), pc(3), pc(12), pc(13)
     ts(pi(1), pi(0), 15, OP.bitwise_and)
     ts(pi(2), pi(0), 4, OP.arith_shift_right)
-    cp(A("PC", 0, 2), A("PCI", 1, 3))
+    ts(pi(3), pi(0), 5, OP.arith_shift_right)
+    ts(pi(4), pi(0), 4, OP.arith_shift_right, 1, OP.bitwise_and)
+    cp(A("PC", 0, 4), A("PCI", 1, 5))
+    cp(PP, pi(0))
     cp(z(0), A("IOTA", 0, 128))
     ts(A("MI"), z(0), 15, OP.bitwise_and)
     ts(A("MG"), z(0), 4, OP.arith_shift_right)
-    BO, Ib, Ih, If, XM, CODE = A("BOb"), A("Ib"), A("Ih"), A("If"), A("XM"), A("CODE")
+    BO, Ib, If, XM, CODE = A("BOb"), A("Ib"), A("If"), A("XM"), A("CODE")
     ts(BO, A("MG"), PG, OP.is_equal)
     ts(f(0), A("MG"), PG, OP.not_equal, 32.0, OP.mult)
     tt(CODE, f(0), A("MI"), OP.add)
-    WTS = [1.0, 2048.0, -1024.0, 1024.0, 2.0, -1.0, 1.0 / 1024]
+    WTS = [1.0, 2048.0, -1024.0, 1024.0, 2.0, 1.0 / 1024]
     for k, w in enumerate(WTS):
-        ts(A("BOh", 128 * k, 128 * k + 128), BO, w, OP.mult)
+        ts(blk("BOh", 128, k), BO, w, OP.mult)
 
     def BOh(w):
-        k = WTS.index(w)
-        return A("BOh", 128 * k, 128 * k + 128)
+        return blk("BOh", 128, WTS.index(w))
 
     def tb(k):
-        return A("TB", 128 * k, 128 * k + 128)
-    ts(A("S16"), A("IOTA", 0, 16), PI, OP.is_equal, 2048.0, OP.mult)
+        return blk("TB", 128, k)
+    ts(A("S16"), A("IOTA", 0, 16), PI, OP.is_equal, 64.0, OP.mult)
     for k in range(16):
-        ts(A("SEL", 128 * k, 128 * k + 128), BO, A("S16", k, k + 1), OP.mult)
-        ts(A("REDh", 128 * k, 128 * k + 128), CODE, float(k), OP.is_equal)
-        act(A("REDb", 128 * k, 128 * k + 128), CODE, AF.Abs, -float(k))
+        ts(blk("SEL", 128, k), BO, A("S16", k, k + 1), OP.mult)
+        ts(blk("REDh", 128, k), CODE, float(k), OP.is_equal)
+        act(blk("REDb", 128, k), CODE, AF.Abs, -float(k))
     act(A("REDb"), A("REDb"), AF.Relu, 1.0, -1.0)
     ts(Ib, CODE, PI, OP.is_equal)
-    ts(Ih, CODE, PI, OP.is_equal)
     act(If, Ib)
     ts(tb(0), CODE, PI, OP.is_lt, -1.0, OP.mult)
     act(tb(1), Ib, scale=-2048.0)
@@ -417,143 +430,146 @@ def rank_program(g, core, T, topo):
     tt(tb(3), tb(0), BO, OP.add)
     tt(tb(4), tb(2), tb(3), OP.subtract)
     act(A("EMB"), tb(4), scale=BIG)
+    ts(z(1), z(0), 31, OP.bitwise_and)
+    for s in range(N):
+        ts(blk("MVb", 128, s), z(1), 32.0 * s, OP.add, PP, OP.is_equal)
+    cp(A("MVh"), A("MVb"))
+    act(A("MVf"), A("MVb"))
+    ts(z(2), A("MG"), 1, OP.bitwise_and)
+    ts(A("FO"), z(2), PF, OP.is_equal)
     ms(A("RS4"), 1.0)
     ms(A("RS4", 0, 512, 128), 0.0)
-    ms(A("RS8"), 1.0)
-    ms(A("RS8", 0, 1024, 256), 0.0)
-    ms(A("KB"), 0.0)
-    ts(pi(3), pi(0), 7, OP.bitwise_and)
-    ts(pi(4), pi(0), 4, OP.arith_shift_right, 1, OP.bitwise_and)
-    ts(pi(5), pi(0), 3, OP.arith_shift_right, 1, OP.bitwise_and)
-    tt(pc(4), pi(3), pi(4), OP.subtract)
-    ts(pi(6), pc(4), 1.0, OP.add)
-    ts(pi(7), pi(6), 1, OP.bitwise_and)
-    ts(pc(5), pi(7), 144.0, OP.mult)
-    ts(pc(6), pi(3), 16.0, OP.mult, 16.0, OP.add)
-    tt(pc(7), pc(6), pi(5), OP.add)
+    ms(A("C128"), 128.0)
+    ms(A("OB"), 0.0)
+    ms(A("NE"), 0.0)
+    for d in range(N):
+        ms(blk("OS", OW, d, 272), 0.0)
+    ts(pi(5), pi(0), 7, OP.bitwise_and)
+    ts(pi(6), pi(0), 3, OP.arith_shift_right, 1, OP.bitwise_and)
+    tt(pc(4), pi(5), pi(4), OP.subtract)
+    ts(pi(7), pc(4), 1.0, OP.add)
+    ts(pi(8), pi(7), 1, OP.bitwise_and)
+    ts(pc(5), pi(8), 144.0, OP.mult)
+    ts(pc(6), pi(5), 16.0, OP.mult, 16.0, OP.add)
+    tt(pc(7), pc(6), pi(6), OP.add)
     tt(pc(8), pc(7), pc(5), OP.add)
     ts(A("PERM"), A("IOTA", 0, 8), 2.0, OP.mult, pc(8), OP.add)
     ts(A("GS", 0, 8), A("IOTA", 0, 8), PG, OP.is_equal, 32.0, OP.mult)
-    act(A("GS", 8, 16), A("GS", 0, 8), scale=1.0 / 32)
-    ts(W16, PI, 15.0, OP.is_lt, 16.0, OP.mult)
-    act(B15, A("S16", 15, 16), scale=2.0)
-    order = [(r - 1 + k) % N for k in range(N)]
+    ts(pc(9), PF, 4.0, OP.mult, PU, OP.add)
+    ts(A("GS", 8, 16), A("IOTA", 0, 8), pc(9), OP.is_equal)
+    act(B15, A("S16", 15, 16), scale=64.0)
+    C0, C1, SGN, LIM = pc(14), pc(15), pc(16), pc(17)
+    ts(C0, PU, 2.0, OP.mult)
+    ts(C1, PU, 2.0, OP.mult, 1.0, OP.add)
+    ts(SGN, PU, 0.0, OP.is_gt, 2.0, OP.mult)
+    ts(SGN, SGN, -1.0, OP.add)
+    ts(LIM, PU, 512.0, OP.mult, 1.0, OP.add)
+    ms(A("PC", 17, 18, p=32), -1536.0)
     act(A("KR"), A("IOTA", 0, 96), bias=95.0, scale=-1.0)
-    act(A("CT", 0, 6), A("IOTA", 0, 6), bias=PI, scale=16.0)
-    for k in range(4):
-        act(A("KW", 96 * k, 96 * k + 96), A("IOTA", 0, 96))
-        act(A("KX", 96 * k, 96 * k + 96), A("IOTA", 0, 96), bias=-2047.0)
-        ts(A("KRW", 96 * k, 96 * k + 96), A("KR"), 96.0 * order[k], OP.add)
-        ts(A("KRC", 6 * k, 6 * k + 6), A("CT", 0, 6), -1.0, OP.mult, 96.0 * order[k] + 95, OP.add)
-        act(A("T256", 6 * k, 6 * k + 6), A("IOTA", 0, 6), bias=256.0 * k, scale=0.0)
-    act(A("IDT"), A("IOTA", 0, 4 * MW), bias=PI, scale=16.0)
-    act(A("DUMP", 0, 24), A("IDT", 0, 24), bias=4096.0)
-    act(A("DUMP", 32, 56), A("IDT", 0, 24), bias=4097.0)
-    ms(A("BD", 56, 64), 0.0)
-    for k, x in enumerate((0.0, 0.0, 0.0, 2048.0)):
-        act(A("XO", 2 * k, 2 * k + 2), A("IDT", 0, 2), bias=x)
-    ms(A("KP"), 0.0)
-    ts(A("CT", 16, 32), A("IOTA", 0, 16), PI, OP.is_le)
-    starts = [SEGT * k + sum(SEG[:m]) for k in range(4) for m in range(6)]
-    for x in starts:
-        act(A("KP", x, x + 16), A("CT", 16, 32))
-    ms(A("CT", 32, 64), 0.0)
+    act(A("KX"), A("IOTA", 0, 96), bias=95.0 - 2047.0, scale=-1.0)
+    act(A("CT", 0, 16), A("IOTA", 0, 16), bias=PI, scale=16.0)
+    act(A("CT", 16, 22), A("CT", 0, 6), bias=95.5, scale=-1.0)
+    ts(pc(18), PU, 96.0, OP.mult, 4096.0, OP.add)
+    DUMP = A("CT", 24, 30)
+    act(DUMP, A("CT", 0, 6), bias=pc(18))
     for m in range(6):
-        ms(A("CT", 32 + m, 56, 6), float(SEG[m]))
-    ms(A("CT", 64, 96), 1.0)
-    scan(A("CT", 96, 128), A("CT", 64, 96), A("CT", 32, 64), -1.0, OP.mult, OP.add)
-    for k in range(2):
-        tt(A("CT", 128 + 16 * k, 144 + 16 * k), A("CT", 96 + 16 * k, 112 + 16 * k), A("S16"), OP.mult)
-        rsum(A("CT", 160 + k, 161 + k), A("CT", 128 + 16 * k, 144 + 16 * k))
-    ts(A("ENDS"), A("CT", 160, 162), 1.0 / 2048, OP.mult)
-    ms(A("TOT"), 0.0)
-    wt = [[0.0] * 32 for k in range(2)]
-    for i in range(16):
-        s = i % 8
-        if s < 4:
-            wt[0][i] = 1.0 if r <= s else 0.0
-        else:
-            wt[1 if r <= s - 4 else 0][i] = 1.0
-    wt[0][16 + r] -= 1.0
-    wt[0][16 + r + 3] += 1.0
-    if r < 3:
-        wt[1][16 + r + 4] -= 1.0
-    for k in range(2):
-        a = 0
-        for i in range(1, 33):
-            if i == 32 or wt[k][i] != wt[k][a]:
-                ms(A("CT", 192 + 32 * k + a, 192 + 32 * k + i), wt[k][a] / 2048)
-                a = i
-        ts(A("CT", 256 + 32 * k, 288 + 32 * k), A("CT", 192 + 32 * k, 224 + 32 * k), A("S16", 7 + 8 * k, 8 + 8 * k), OP.mult)
-    tt(A("WT"), A("CT", 256, 288), A("CT", 288, 320), OP.add)
-    ts(A("PIU"), A("IOTA", 0, 8), 0.0, OP.mult, PI, OP.add)
-    for k in range(2):
-        tt(A("CE", 128 * k, 128 * k + 128), X(A("WT", 16 * k, 16 * k + 16), A("PIU")), BO, OP.mult)
-    ts(pc(9), PI, 8.0, OP.is_ge, 4.0 * MW, OP.mult)
-    ts(pc(10), PI, 11.0, OP.is_equal, -16.0 * MW, OP.mult)
-    ts(pc(11), PI, 15.0, OP.is_lt, pc(9), OP.mult)
-    ms(A("CK", 0, 4), 0.0)
-    ts(A("CK", 4, 8), A("CK", 0, 4), pc(10), OP.add, pc(11), OP.add)
+        ts(blk("KP", 97, m), A("IOTA", 0, 97), A("CT", m, m + 1), OP.is_le)
+    for k, x in enumerate((0.0, 0.0, 0.0, 2048.0)):
+        act(blk("XO", 2, k), A("CT", 0, 2), bias=x)
+    ts(pc(19), PU, 256.0, OP.mult)
+    ts(pc(20), PU, 2.0, OP.is_ge)
+    ts(pc(21), PI, 8.0, OP.mult, C0, OP.add)
+    for h in range(2):
+        ts(A("CT", 32 + 8 * h, 40 + 8 * h), A("IOTA", 0, 8), 128.0, OP.mult, pc(21), OP.add)
+    for d in range(N):
+        step = float(_high(d) - 512 - 512 * d)
+        if d != r:
+            ts(pc(22), pc(20), step, OP.mult, 512.0 * d, OP.add)
+            tt(pc(23), pc(22), pc(19), OP.add)
+            ts(blk("OK", 16, d), A("CT", 0, 16), pc(23), OP.add)
+        for h in range(2):
+            for x in range(2):
+                a = 8 * h + 4 * x
+                ts(blk("OY", 16, d, a, a + 4), A("CT", 32 + a, 36 + a), 512.0 * d + h + step * x, OP.add)
 
-    KEY = A("KB", 16, 144)
-    DW, PW = A("DT", 0, 4096), A("PT", 0, 4096)
-    H1 = A("HT", 0, 128)
+    KEY, IMG, HI = A("KB"), A("IMG"), A("HI")
+    KW, PW = A("KT", 0, 4096), A("PT", 0, 4096)
 
     def NV(k):
         return A("NN", k, k + 1)
 
-    def prep():
+    def prep(t):
         ts(A("K2"), KEY, 2048.0, OP.add)
-        ts(A("E1"), A("K2"), 11, OP.arith_shift_right)
-        cp(A("EH"), A("E1"))
         ts(A("Z2"), A("K2"), 4095, OP.bitwise_and)
-        ts(A("HI"), A("K2"), 2047, OP.bitwise_and)
-        tt(f(1), A("Z2"), A("IMG"), OP.is_lt)
-        ts(A("Q"), A("HI"), 9, OP.arith_shift_right)
-        tt(z(0), A("Q"), f(1), OP.add)
-        ts(z(1), z(0), 3, OP.bitwise_and)
-        for d in range(4):
-            ts(A("OG", 128 * d, 128 * d + 128), z(1), float(d), OP.is_equal)
+        ts(HI, A("K2"), 2047, OP.bitwise_and)
+        ts(A("E1"), A("K2"), 11, OP.arith_shift_right)
+        ts(A("Q"), A("K2"), 9, OP.arith_shift_right, 3, OP.bitwise_and)
+        ts(v(2), A("Z2"), NV(max(t - 1, 0)), OP.is_lt, 2048.0, OP.mult)
+        tt(A("OB", 16, 144), HI, v(2), OP.add)
+        turn(A("YT", 0, 160), A("OB"))
+        turn(A("YT", 160, 288), A("OB", 16, 144))
+        cp(A("OFF"), X(A("YT"), A("PERM")))
+        ts(A("EH", 0, 128), A("E1"), -1.0, OP.add, 32.0, OP.mult)
+        ts(A("EH", 128, 256), HI, 1.0 / 64, OP.mult)
+        tt(v(0), A("Z2"), IMG, OP.is_le)
+        tt(A("TO", 0, 128), A("Q"), v(0), OP.add)
+        act(A("TO", 128, 256), A("TO", 0, 128), AF.Abs, -2.0)
+        ts(A("OG", 0, 128), A("TO", 128, 256), 2.0, OP.is_equal)
+        for d in range(1, 4):
+            ts(blk("OG", 128, d), A("TO", 0, 128), float(d), OP.is_equal)
         scan(A("IG"), A("RS4"), A("OG"), 0.0, OP.mult, OP.add)
         mm(A("P6"), [(BO, A("IG")), (XM, A("OG"))])
         act(A("GOB"), A("P6"), AF.Sigmoid, -1407.5 * 256, -256.0)
-        mm(A("P7", 0, 128), [(Ib, A("GOB", 128 * d, 128 * d + 128)) for d in range(4)])
-        act(A("GO"), A("P7", 0, 128))
-        act(f(2), A("P7", 0, 128), bias=64.0, scale=-64.0)
-        for k in range(16):
-            mm(A("P%d" % (k // 4), 128 * (k % 4), 128 * (k % 4) + 128), [(A("SEL", 128 * k, 128 * k + 128), A("EH"))])
-        turn(A("YT", 0, 160), A("KB"))
-        turn(A("YT", 160, 288), KEY)
-        ts(A("KPI"), X(A("YT"), A("PERM")), 2048.0, OP.add)
-        ts(A("ZP"), A("KPI"), 4095, OP.bitwise_and)
-        ts(A("HP"), A("KPI"), 2047, OP.bitwise_and)
-        ts(H1, A("HI"), 1.0, OP.add)
-        for w in (128, 256, 512):
-            act(A("HT", w, 2 * w), A("HT", 0, w))
-        ts(f(3), A("Q"), 2.0, OP.mult)
-        tt(f(4), f(3), f(1), OP.subtract)
-        tt(f(5), f(4), f(2), OP.add)
+        mm(A("P4", 128, 256), [(Ib, blk("GOB", 128, d)) for d in range(4)])
+        act(A("GO"), A("P4", 128, 256))
+        act(f(2), A("P4", 128, 256), scale=-64.0)
+        ts(v(1), A("Q"), 3.0, OP.mult, 64.0, OP.add)
+        tt(v(1), v(1), A("TO", 0, 128), OP.subtract)
+        tt(v(1), v(1), f(2), OP.add)
+        tt(v(0), A("LN", 256 + 128 * t, 384 + 128 * t), KEY, OP.subtract)
+        tt(v(0), v(0), A("GO"), OP.mult)
+        tt(f(3), v(0), KEY, OP.add)
+        for k, (n, w) in enumerate((("EM", 1.0 / 32), ("HM", 64.0))):
+            for s in range(N):
+                mm(blk("P6", 128, s), [(blk("MVh", 128, s), blk("EH", 128, k))])
+            act(blk(n, 512, t % 2), A("P6"), bias=1.0, scale=w)
 
-    cp(KEY, A("LKI"))
-    cp(A("IMG"), A("LII"))
+    def spread(c):
+        for k in range(4 * c, 4 * c + 4):
+            mm(blk("P%d" % c, 128, k % 4), [(blk("SEL", 128, k), blk("EH", 128, h)) for h in range(2)])
+
+    def split(t):
+        n = NV(t)
+        ts(A("SG", 0, 2), A("XO", 0, 2), n, OP.add, 2047.0, OP.min)
+        ts(A("SG", 2, 4), A("XO", 0, 2), n, OP.add, 2047.0, OP.min)
+        act(A("SX", 0, 8), A("XO"), bias=n)
+        ts(A("SX", 8, 12), A("SX", 0, 4), NV(t + 1), OP.is_ge, 4096.0, OP.mult)
+        tt(A("SX", 12, 16), A("SX", 8, 12), A("SX", 4, 8), OP.add)
+        cp(A("SO"), A("SX", 12, 16))
+        cp(A("SI", 0, 32), X(KW, A("SG", 0, 2)))
+        act(A("SK", 64, 128), X(KW, A("SG")), bias=1.0)
+        act(A("SK", 128, 192), X(PW, A("SG")), bias=-1.0)
+        ts(A("SI", 32, 64), A("SI", 0, 32), 0x200800, OP.bitwise_and)
+        ts(A("SK", 0, 32), A("SI", 32, 64), 2048.0, OP.not_equal)
+        ts(A("SK", 32, 64), A("SI", 32, 64), 2048.0, OP.is_equal)
+        tt(A("SK", 192, 256), A("SK", 0, 64), A("SK", 64, 128), OP.mult)
+        ts(X(A("KT"), A("SO")), A("SK", 192, 256), 1.0, OP.mult, -1.0, OP.add)
+        tt(A("SK", 256, 320), A("SK", 0, 64), A("SK", 128, 192), OP.mult)
+        ts(X(A("PT"), A("SO")), A("SK", 256, 320), 1.0, OP.mult, 1.0, OP.add)
+
+    cp(KEY, A("LN", 0, 128))
+    ts(IMG, A("LN", 128, 256), -1.0, OP.add)
     cp(NV(0), A("PNI", 0, 1))
-    prep()
+    prep(0)
+    for c in range(4):
+        spread(c)
 
-    def offsets(t):
-        ts(f(6), A("ZP"), NV(t), OP.is_lt, 2048.0, OP.mult)
-        tt(f(7), f(6), A("HP"), OP.add)
-        cp(A("OFF"), f(7))
-        return len(ops) - 1
-
-    offsets(0)
     for t in range(RO):
         last = t == RO - 1
         n = NV(t)
-        RB = "RB%d" % t
-        m0 = MW * r
         for c in range(4):
             a, b, o, P = 512 * c, 512 * c + 512, A("OFF", 32 * c, 32 * c + 32), "P%d" % c
-            act(A("W1", a, b), X(DW, o))
+            act(A("W1", a, b), X(KW, o))
             if c < 2:
                 tt(A("W2", a, b), A("W1", a, b), A(P), OP.is_equal)
                 tt(A("W3", a, b), X(PW, o), A("W2", a, b), OP.mult)
@@ -563,169 +579,136 @@ def rank_program(g, core, T, topo):
                 for h in range(2):
                     tt(A("W3", a + 256 * h, a + 256 * h + 256), A("W2", a + 256 * h, a + 256 * h + 256), A(P, 256 * h, 256 * h + 256), OP.mult)
             for k in range(4 * c, 4 * c + 4):
-                mm(A("P4", k, 128, 16), [(A("W3", 128 * k, 128 * k + 128), A("GS", 0, 8))])
+                mm(A("P4", k, 128, 16), [(blk("W3", 128, k), A("GS", 0, 8))])
         act(A("TS"), A("P4", 0, 128))
         mm(A("P5", 0, 128), [(A("TS"), If)])
-        ts(f(8), A("Z2"), n, OP.is_lt, 3.0, OP.mult)
-        tt(z(2), f(8), f(5), OP.add)
+        ts(f(0), A("Z2"), n, OP.is_lt, 3.0, OP.mult)
+        tt(z(2), f(0), v(1), OP.add)
         ts(A("CLS"), z(2), 71, OP.bitwise_and)
-        ts(f(9), A("Z2"), n, OP.is_lt, 1024.0, OP.mult)
-        tt(A("ET", 0, 128), f(9), A("E1"), OP.add)
-        for w in (128, 256, 512):
-            act(A("ET", w, 2 * w), A("ET", 0, w))
-        tt(A("CM"), A("P5", 0, 128), A("CLS"), OP.add)
-        for k in range(8):
-            ts(A("OH", 128 * k, 128 * k + 128), A("CM"), float(k), OP.is_equal)
-        scan(A("INC"), A("RS8"), A("OH"), 0.0, OP.mult, OP.add)
-        tt(f(10), A("P5", 0, 128), A("GO"), OP.mult)
-        mm(A("P6", 0, 4), [(A("REDb", 128 * i, 128 * i + 128), A("INC", 16 * i + 15, 1024, 256)) for i in range(16)])
-        mm(A("P7", 0, 64), red("REDb", "INC", 0, 1024))
-        for k in range(4):
-            ts(A("C1", 96 * k, 96 * k + 96), A("IOTA", 0, 96), A("P6", k, k + 1), OP.is_ge, W16, OP.mult)
-        ts(A("BC"), A("P6", 0, 4), 96.0, OP.min)
-        act(A("E2"), A("P7", 0, 64), bias=B15)
-        mm(A("P4", 0, 24), [(Ib, A("T256"))] + red("REDb", "C1", 0, 384))
-        ts(A("O1"), A("P4", 0, 24), 1.0 / 16, OP.mult)
-        for h in range(2):
-            mm(A("P%d" % h), [(BO, A("INC", 512 * h, 512 * h + 512)), (XM, A("OH", 512 * h, 512 * h + 512))])
-            act(A("XS", 512 * h, 512 * h + 512), A("P%d" % h))
-        tt(A("C2"), X(A("E2"), A("O1")), A("KW"), OP.is_le)
-        act(A("VB"), A("P4", 0, 24))
-        mm(A("P4", 0, 24), [(Ib, A("VB"))] + red("REDb", "C2", 0, 384))
-        mm(A("P3", 0, 4), [(A("CE", 0, 128), A("BC"))])
-        mm(A("P3", 4, 8), [(A("CE", 128, 256), A("BC"))])
-        cp(A("O2"), A("P4", 0, 24))
-        tt(A("MK"), X(A("XS"), A("O2")), A("KX"), OP.is_equal)
-        tt(A("MH"), X(A("HT"), A("O2")), A("MK"), OP.mult)
-        mm(A("P2", 0, 24), red("REDh", "MH", 0, 384))
-        tt(A("ME"), X(A("ET"), A("O2")), A("MK"), OP.mult)
-        mm(A("P2", 24, 48), red("REDh", "ME", 0, 384))
-        tt(A(RB, m0 + 48, m0 + 56), A("P3", 0, 8), A("CK"), OP.add)
-        act(A(RB, m0, m0 + 48), A("P2", 0, 48))
-        msg = A(RB, m0, m0 + MW)
-        sent = send("ls%d" % (4 + t), [(msg, R[ro["peer"][0]], off_eng, "m%d" % t)]
-                    + [(msg, x, rest[4 * k:4 * k + 4], "hm%d" % t) for k, x in enumerate(ro["near"])])
-        arrive("m%d" % t, 3 * len(off_eng), [A(RB, MW * s, MW * s + MW) for s in others], sent, 2.5)
-        ts(z(3), A("CLS"), 65, OP.bitwise_and)
-        ts(f(11), z(3), 1.0, OP.is_equal)
-        tt(f(12), f(11), H1, OP.mult)
-        tt(A("IMG"), A("IMG"), f(12), OP.max)
-        tt(f(13), A("DKI", 128 * t, 128 * t + 128), KEY, OP.subtract)
-        tt(f(14), f(13), A("GO"), OP.mult)
-        tt(f(15), f(14), KEY, OP.add)
-        ts(f(16), f(10), 0.0, OP.is_gt, -BIG, OP.mult)
-        act(f(17), f(10), bias=-0.5, scale=1.0 / 32)
-        tt(f(18), f(16), f(15), OP.add)
-        tt(KEY, f(17), f(18), OP.max)
-        if last:
-            dma("y", "st0", T.yl[:], KEY, 2.3)
-            dma("y", "st1", T.yi[:], A("IMG"), 2.3)
-            for h in range(2):
-                act(A("P%d" % h), A("IOTA"), bias=float(own[h] % 2048 - 2048))
-        else:
-            gate.append(sent)
-            prep()
-            gate.pop()
-        ms(A("P6", 96, 388, 97), 0.0)
         ts(NV(8), n, 32.0, OP.add, 2048.0, OP.min)
         tt(NV(9), NV(8), n, OP.subtract)
-        ts(A("SG", 0, 2), A("XO", 0, 2), n, OP.add, 2047.0, OP.min)
-        ts(A("SG", 2, 4), A("XO", 0, 2), n, OP.add, 2047.0, OP.min)
-        act(A("SX", 0, 8), A("XO"), bias=n)
-        ts(A("SX", 32, 64), A("IOTA", 0, 32), n, OP.add, -2048.0, OP.add)
-        act(A("SX", 64, 96), A("SX", 32, 64), bias=-1.0, scale=-1.0)
-        act(A("SX", 96, 128), A("SX", 32, 64), bias=-1.0, scale=-1.0)
-        tt(A("ED", 8, 16), A(RB, 48, 56), A(RB, MW + 48, MW + 56), OP.add)
-        tt(A("ED", 16, 24), A(RB, 2 * MW + 48, 2 * MW + 56), A(RB, 3 * MW + 48, 3 * MW + 56), OP.add)
-        tt(A("ED", 0, 8), A("ED", 8, 16), A("ED", 16, 24), OP.add)
-        for k in range(4):
-            x = order[k]
-            ts(A("M1", 96 * k, 96 * k + 96), A("KR"), A("ED", x, x + 1), OP.is_ge, A("ED", 4 + x, 5 + x), OP.mult)
-        mm(A("P4", 0, 384), [(Ih, A("KRW")), (BOh(1.0), A("M1"))])
-        mm(A("P5", 0, 24), [(Ih, A("KRC"))] + red("REDh", "M1", 0, 384))
-        ts(A("O3"), A("P5", 0, 24), -7.5, OP.add, 1.0 / 16, OP.mult)
-        act(A("IX"), A("P4", 0, 384))
-        tt(A("MK"), X(A("IDT"), A("O3")), A("IX"), OP.is_equal)
-        tt(A("MH"), X(A(RB), A("O3")), A("MK"), OP.mult)
-        mm(A("P5", 0, 24), red("REDh", "MH", 0, 384))
-        for k in range(4):
-            mm(A("P6", 97 * k, 97 * k + 96), [(BOh(1.0), A("MH", 96 * k, 96 * k + 96))])
-        tt(A("ME"), X(A(RB, 24, 4 * MW), A("O3")), A("MK"), OP.mult)
-        ts(A("MN"), A("ME"), 1024.0, OP.is_ge, 2048.0, OP.mult)
-        cp(A("BS", 0, 24), A("P5", 0, 24))
-        cp(A("BSH"), A("P5", 0, 24))
-        mm(A("P5", 0, 24), red("REDh", "MN", 0, 384) + [(Ih, A("BSH"))])
-        ts(A("O4"), A("P5", 0, 24), -1.0, OP.add)
-        tt(A("BD", 32, 56), A("P5", 0, 24), A("DUMP", 32, 56), OP.subtract)
-        cols = len(ops) - 1
+        if t:
+            split(t - 1)
+        tt(A("CM"), A("P5", 0, 128), A("CLS"), OP.add)
+        for s in range(N):
+            mm(blk("P0", 128, s), [(blk("MVb", 128, s), A("CM"))])
+        tt(f(1), A("P5", 0, 128), A("GO"), OP.mult)
+        ts(A("OH", 0, 512), A("P0"), C0, OP.is_equal)
+        ts(A("OH", 512, 1024), A("P0"), C1, OP.is_equal)
+        scan(A("INC"), A("OH"), A("C128"), 0.0, OP.add, OP.min)
+        mm(A("P1", 0, 64), [(BO, A("INC", 15, 1024, 16))])
+        mm(A("P2", 0, 64), red("REDb", "INC", 0, 1024))
+        for m in range(6):
+            act(A("JK", 0, 63), A("P1", 0, 63), AF.Sign, A("CT", 16 + m, 17 + m), -1.0, acc=A("AC", m, m + 1))
+        act(A("E2"), A("P2", 0, 64), bias=B15)
+        AC = A("AC", 0, 6)
+        ts(A("O1", 0, 6), AC, 0.5, OP.mult, 31.5, OP.add)
+        ts(A("VB", 0, 6), AC, 8.0, OP.mult, 504.0, OP.add)
+        ts(A("BS", 8, 14), AC, 0.0, OP.is_gt, -512.0, OP.mult)
+        tt(A("C2"), X(A("E2"), A("O1", 0, 6)), A("KR"), OP.is_le)
+        mm(A("P1", 64, 70), [(Ib, A("VB", 0, 6))] + red("REDb", "C2", 0, 96))
+        cp(A("O2", 0, 6), A("P1", 64, 70))
+        tt(A("BS", 16, 22), A("P1", 64, 70), A("BS", 8, 14), OP.add)
+        cp(A("G2", 0, 96), X(A("INC"), A("O2", 0, 6)))
+        act(A("G2", 96, 192), X(A("OH"), A("O2", 0, 6)))
+        cp(A("O3", 0, 6), A("BS", 16, 22))
+        mm(A("P3", 0, 96), [(BO, A("G2", 0, 96)), (XM, A("G2", 96, 192))])
+        act(A("G3", 0, 96), X(blk("HM", 512, t % 2), A("O3", 0, 6)))
+        act(A("G3", 96, 192), X(blk("EM", 512, t % 2), A("O3", 0, 6)))
+        tt(A("P3", 0, 96), A("P3", 0, 96), A("KX"), OP.is_equal)
+        tt(A("MH"), A("P3", 0, 96), A("G3", 0, 96), OP.mult)
+        tt(A("ME"), A("P3", 0, 96), A("G3", 96, 192), OP.mult)
+        ts(z(3), A("CLS"), 65, OP.bitwise_and)
+        ts(v(3), z(3), 1.0, OP.not_equal, -4096.0, OP.mult)
+        tt(v(3), v(3), HI, OP.add)
+        tt(IMG, v(3), IMG, OP.max)
+        ts(v(2), f(1), 0.0, OP.is_gt, -BIG, OP.mult)
+        act(f(4), f(1), bias=-1.0, scale=1.0 / 32)
+        tt(v(2), v(2), f(3), OP.add)
+        tt(KEY, v(2), f(4), OP.max)
+        if last:
+            act(A("YI"), IMG, bias=1.0)
+            for k, d in enumerate(others):
+                dma("y", [(blk("YS", YW, d, 0, 32), A("KB", p0=32 * d, p=32)), (blk("YS", YW, d, 32, 64), A("YI", p0=32 * d, p=32))], 2.0)
+            dma("y", [(rows(T.yl, r), A("KB", p0=32 * r, p=32)), (rows(T.yi, r), A("YI", p0=32 * r, p=32))], 2.0)
+            sent = send([(blk("YS", YW, peer), blk("YL", YW, r), R[peer], off_eng, "ylan")]
+                        + [(blk("YS", YW, d), blk("YL", YW, r), ro["near"][k], quart[2 + k], "hY") for k, d in enumerate(cross)])
+            arrive("ylan", 3 * len(off_eng), [blk("YL", YW, s) for s in others], sent, 3.0)
+            dma("y", [x for s in others for x in ((rows(T.yl, s), blk("YL", YW, s, 0, 32)), (rows(T.yi, s), blk("YL", YW, s, 32, 64)))], 2.0)
+        else:
+            prep(t + 1)
+        mm(A("P1", 80, 86), red("REDh", "MH", 0, 96))
+        ms(A("P0", 96, 97), 0.0)
+        mm(A("P0", 0, 96), [(BOh(1.0), A("MH"))])
+        BS, BO4 = A("BS", 0, 6), A("BS", 40, 46)
+        cp(BS, A("P1", 80, 86))
+        ts(A("BS", 24, 30), A("P1", 80, 86), SGN, OP.mult, LIM, OP.is_lt)
+        ts(A("BS", 32, 38), A("BS", 24, 30), 2048.0, OP.mult, -1.0, OP.add)
+        tt(BO4, A("P1", 80, 86), A("BS", 32, 38), OP.add)
+        cp(A("O4", 0, 6), BO4)
+        O4 = A("O4", 0, 6)
+        act(A("EE"), X(KW, O4), AF.Relu, 0.0, -1.0)
+        ts(A("OLD", 0, 96), X(KW, O4), BIG + 2049.0, OP.add)
+        act(A("OLD", 96, 192), X(PW, O4), bias=BIG + 1025.0)
         ts(A("MB"), A("MH"), 1025.0, OP.is_ge, 1024.0, OP.mult)
-        w = 192 if last else 384
-        mm(A("P4", 0, w), [(BOh(2048.0), A("ME", 0, w)), (BOh(-1024.0), A("MN", 0, w))], stop=False)
-        act(A("EM"), X(PW, A("O4")), AF.Sigmoid, 0.0, -256.0)
-        mm(A("P5", 0, 24), red("REDb", "EM", 0, 384))
-        mm(A("P4", 0, w), [(A("EMB"), A("EM", 0, w))], start=False)
-        gate.append(len(ops) - 2)
-        mm(A("P7", 0, w), [(BOh(2.0), A("ME", 0, w)), (BOh(-1.0), A("MN", 0, w)), (BOh(1024.0), A("MH", 0, w)),
-                           (BOh(-1024.0), A("MB", 0, w)), (BOh(1.0 / 1024), A("MB", 0, w)), (A("EMB"), A("EM", 0, w))])
-        gate.pop()
-        act(A("W4", 0, w), X(DW, A("O4", 0, w // 16)))
-        act(A("TOT", 0, 24), A("P5", 0, 24))
-        gate.append(len(ops) - 1)
-        act(A("W4", 512, 512 + w), A("P4", 0, w), bias=-BIG)
-        act(A("W4", 1024, 1024 + w), X(PW, A("O4", 0, w // 16)))
-        gate.pop()
-        act(A("W4", 1536, 1536 + w), A("P7", 0, w), bias=-BIG - 1025.5)
-        for k in range(4):
-            for m in range(6):
-                x = starts[6 * k + m]
-                ts(A("NE", x, x + SEG[m]), A("P6", 97 * k + 16 * m, 97 * k + 97), A("BS", 6 * k + m, 6 * k + m + 1), OP.not_equal)
-            gate[:] = [cols]
-        del gate[:]
+        mm(A("P2", 0, 96), [(BOh(2048.0), A("ME")), (BOh(1.0), A("MH")), (A("EMB"), A("EE"))])
+        tt(A("NEW", 0, 96), A("P2", 0, 96), A("OLD", 0, 96), OP.max)
+        for s in range(N):
+            mm(blk("P5", 96, s), [(blk("MVf", 128, s), A("NEW", 0, 96))])
+        act(A("SC", 0, 384), A("P5", 0, 384), bias=-BIG - 2049.0)
+        for m in range(6):
+            ts(blk("NE", 97, m, 16 * m), A("P0", 16 * m, 97), A("BS", m, m + 1), OP.not_equal)
         scan(A("SS"), A("NE"), A("KP"), 1.0, OP.min, OP.max)
-        tt(A("OV"), X(A("SS"), A("ENDS")), A("TOT"), OP.is_gt)
-        tt(A("BD", 64, 96), X(A("SS"), A("ENDS")), A("BD", 32, 64), OP.mult)
-        mm(A("P5", 32, 56), [(BO, A("OV", 0, 24))])
-        act(A("TT", 40, 64), A("P5", 32, 56), acc=NV(10))
+        TRY = A("SS", 96, 582, 97)
+        tt(A("BS", 48, 54), BO4, DUMP, OP.subtract)
+        tt(A("BS", 48, 54), A("BS", 48, 54), TRY, OP.mult)
+        tt(A("BS", 56, 62), A("BS", 48, 54), DUMP, OP.add)
+        for s in range(N):
+            mm(blk("P3", 6, s), [(blk("MVf", 128, s), A("BS", 56, 62))])
+        cp(A("O5"), A("P3", 0, 24))
+        cp(X(A("KT"), A("O5")), A("SC", 0, 384))
+        mm(A("P2", 128, 224), [(BOh(2.0), A("ME")), (BOh(1024.0), A("MH")), (BOh(-1024.0), A("MB")), (BOh(1.0 / 1024), A("MB")), (A("EMB"), A("EE"))])
+        tt(A("NEW", 96, 192), A("P2", 128, 224), A("OLD", 96, 192), OP.max)
+        for s in range(N):
+            mm(blk("P6", 96, s), [(blk("MVf", 128, s), A("NEW", 96, 192))])
+        act(A("SC", 384, 768), A("P6", 0, 384), bias=-BIG - 1025.0)
+        cp(X(A("PT"), A("O5")), A("SC", 384, 768))
+        mm(A("P3", 32, 38), red("REDb", "EE", 0, 96))
+        tt(A("OV", 0, 6), A("P3", 32, 38), TRY, OP.is_lt)
+        mm(A("P3", 48, 54), [(A("FO"), A("OV", 0, 6))])
+        act(A("TT", 0, 6), A("P3", 48, 54), acc=NV(10))
         act(NV(11), NV(10), AF.Relu, NV(9), -1.0)
         act(NV(t + 1), NV(11), AF.Identity, NV(8), -1.0)
-        tt(A("BD", 96, 120), A("BD", 64, 88), A("DUMP", 0, 24), OP.add)
-        cp(A("O5"), A("BD", 96, 120))
-        tt(X(A("DT"), A("O5", 0, w // 16)), A("W4", 0, w), A("W4", 512, 512 + w), OP.max)
-        tt(A("SI", 0, 32), X(DW, A("SG", 0, 2)), A("SX", 32, 64), OP.add)
-        tt(A("SK", 64, 128), X(DW, A("SG")), A("SX", 64, 128), OP.subtract)
-        ts(A("SX", 8, 12), A("SX", 0, 4), NV(t + 1), OP.is_ge, 4096.0, OP.mult)
-        ts(A("SI", 32, 64), A("SI", 0, 32), 0x100800, OP.bitwise_and)
-        tt(A("SX", 12, 16), A("SX", 8, 12), A("SX", 4, 8), OP.add)
-        ts(A("SK", 0, 32), A("SI", 32, 64), 2048.0, OP.not_equal)
-        ts(A("SK", 32, 64), A("SI", 32, 64), 2048.0, OP.is_equal)
-        cp(A("SO"), A("SX", 12, 16))
-        tt(A("SK", 192, 256), A("SK", 0, 64), A("SK", 64, 128), OP.mult)
-        tt(X(A("DT"), A("SO")), A("SK", 192, 256), A("SX", 64, 128), OP.add)
         if not last:
-            gate.append(len(ops) - 1)
-            gate.append(offsets(t + 1))
-        tt(X(A("PT"), A("O5", 0, w // 16)), A("W4", 1024, 1024 + w), A("W4", 1536, 1536 + w), OP.max)
-        del gate[:]
-        act(A("SK", 128, 192), X(PW, A("SG")), bias=0.5)
-        tt(A("SK", 256, 320), A("SK", 0, 64), A("SK", 128, 192), OP.mult)
-        ts(X(A("PT"), A("SO")), A("SK", 256, 320), 1.0, OP.mult, -0.5, OP.add)
+            for c in range(4):
+                spread(c)
+    split(RO - 1)
 
-    dma("y", "st2", T.yn[:], NV(RO), 2.0)
-    done = len(ops) - 2
-    for h in range(2):
-        a, b = 512 * h, 512 * h + 512
-        gate.append(done)
-        tt(A("W1", a, b), A("DT", own[h], own[h] + 512), A("P%d" % h), OP.add)
-        gate.pop()
-        dma("y", "st%d" % (3 + h), T.yk[:, a:b], A("W1", a, b), 2.9)
-        for k in range(2):
-            c, P = a + 256 * k, A("P%d" % (2 + 2 * h + k), 0, 256, p=8)
-            act(A("W2", c, c + 256), A("PT", own[h] + 256 * k, own[h] + 256 * k + 256), AF.Abs)
-            ts(A("W3", c, c + 256), A("W2", c, c + 256), -0.5, OP.add)
-            mm(P, [(A("GS", 8, 16), A("W3", c, c + 256))])
-            if h:
-                cp(A("YS", c, c + 256, p=8), P)
-            else:
-                act(A("YS", c, c + 256, p=8), P)
-    dma("s", "st5", T.ys[:], A("YS", p=8), 2.0)
+    def stores(q, s, n):
+        x = OW * s
+        y = [(T.ys[2 * s + h, :], A(n, x + 256 + 8 * h, x + 264 + 8 * h)) for h in range(2)] + [(rows(T.yn, s), A(n, x + 272, x + 273, p=32))]
+        if s != r:
+            y += [(T.yk[32 * s:32 * s + 32, 256 * u:256 * u + 256], A(n, x, x + 256, p0=32 * u, p=32)) for u in range(N)]
+        dma(q, y, 2.5)
+
+    for k, d in enumerate(others + [r]):
+        if d != r:
+            cp(blk("OS", OW, d, 0, 256), X(KW, blk("OK", 16, d)))
+        act(blk("YP", 256, d), X(PW, blk("OY", 16, d)), AF.Abs, -1.0)
+        P = "P%d" % k
+        for h in range(2):
+            mm(A(P, h, 16, 2), [(blk("YP", 256, d, 128 * h, 128 * h + 128), A("GS", 8, 16))])
+        cp(blk("OS", OW, d, 256, 272), A(P, 0, 16))
+        cp(blk("OS", OW, d, 272, 273), NV(RO))
+        hw = OW // 2
+        if d in cross:
+            sent = send([(blk("OS", OW, d, hw * h, hw * h + hw), blk("OL", OW, r, hw * h, hw * h + hw), ro[kind][k], (rest, off_eng)[h], "hO")
+                         for h, kind in enumerate(("far", "near"))])
+        elif d == peer:
+            sent = send([(blk("OS", OW, d), blk("OL", OW, r), R[peer], off_eng, "o%d" % r)])
+    dma("y", [(T.yk[32 * r:32 * r + 32, 512 * h:512 * h + 512], A("KT", a, a + 512, p=32)) for h, a in enumerate((512 * r, _high(r)))], 2.5)
+    stores("y", r, "OS")
+    for k, s in enumerate([peer] + cross):
+        arrive("o%d" % s, len(off_eng) * (1 if s == peer else 2), [blk("OL", OW, s)], sent, 2.0 + k)
+        stores("sy"[k % 2], s, "OL")
     _issue(T, Q, ops)

@@ -2,7 +2,7 @@ from concourse.bass import DstId, RemoteDMATransfer
 from concourse.mybir import AluOpType as OP, AxisListType, ActivationFunctionType as AF
 
 N, RO, NCORES = 4, 3, 256
-LW, YW, OW = 160, 64, 280
+LW, DW, OW = 32, 96, 280
 TW = 8256
 BIG = float(2 ** 22)
 F, H, B, I, U = "float32", "float16", "bfloat16", "int32", "uint16"
@@ -12,21 +12,27 @@ def _sb(w, d):
     return ("sbuf", [128, w], d)
 
 
+def _dr(w, d):
+    return ("dram", [128 * N, w], d)
+
+
 SCRATCH = {
-    "KT": _sb(TW, F), "PT": _sb(TW, F), "TKI": _sb(1024, I), "TPI": _sb(1024, I), "KS": _sb(1024, F), "PS": _sb(1024, F),
-    "LS": _sb(N * LW, I), "LL": _sb(N * LW, I), "LN": _sb(640, I), "PNI": _sb(4, I), "YS": _sb(N * YW, F), "YL": _sb(N * YW, F),
+    "KT": _sb(TW, F), "PT": _sb(TW, F), "TKI": _sb(1024, I), "TPI": _sb(1024, I), "KS": _sb(2048, H), "PS": _sb(2048, H),
+    "KL": _sb(2048, H), "PL": _sb(2048, H), "DS": _dr(DW, I), "DL": _dr(DW, I), "QM": _sb(512, B),
+    "LS0": _dr(LW, I), "LL0": _dr(LW, I), "LS1": _dr(LW, I), "LL1": _dr(LW, I), "LN": _sb(640, I), "PNI": _sb(4, I),
+    "YS0": _dr(LW, F), "YL0": _dr(LW, F), "YS1": _dr(LW, F), "YL1": _dr(LW, F), "OF": _sb(128, F),
     "OS": _sb(N * OW, F), "OL": _sb(N * OW, F), "YP": _sb(1024, F), "YI": _sb(128, F),
     "W1": _sb(2048, F), "W2": _sb(2048, F), "W3": _sb(2048, F), "TM": _sb(128 * 8, F), "TN": _sb(128 * 8, I),
-    "IOTA": _sb(512, F), "PCI": _sb(16, I), "PC": _sb(32, F), "MI": _sb(128, I), "MG": _sb(128, I), "CODE": _sb(128, B),
-    "BOb": _sb(128, B), "BOh": _sb(768, H), "Ib": _sb(128, B), "If": _sb(128, F), "XM": _sb(128, B), "FO": _sb(128, B),
-    "EMB": _sb(128, B), "SEL": _sb(2048, H), "REDb": _sb(2048, B), "REDh": _sb(2048, H), "TB": _sb(1024, B),
-    "MVb": _sb(512, B), "MVh": _sb(512, H), "MVf": _sb(512, F), "GS": _sb(16, F), "S16": _sb(16, F), "RS4": _sb(512, B),
+    "IOTA": _sb(128, F), "PCI": _sb(16, I), "PC": _sb(32, F), "MI": _sb(128, I), "MG": _sb(128, I), "CODE": _sb(128, B),
+    "BOb": _sb(128, B), "BOh": _sb(896, B), "Ib": _sb(128, B), "If": _sb(128, F), "XM": _sb(128, B), "FO": _sb(128, B),
+    "EMB": _sb(128, B), "SEL": _sb(2048, B), "REDb": _sb(2048, B), "TB": _sb(1024, B),
+    "MVb": _sb(512, B), "MVf": _sb(512, F), "GS": _sb(16, F), "S16": _sb(16, F), "RS4": _sb(512, B),
     "C128": _sb(1024, B), "KR": _sb(96, F), "KX": _sb(96, F), "KP": _sb(582, B), "PERM": _sb(8, U), "CT": _sb(64, F),
     "XO": _sb(8, F), "OK": _sb(64, U), "OY": _sb(64, U),
     "KB": _sb(128, F), "OB": _sb(160, F), "YT": _sb(288, F), "IMG": _sb(128, F), "K2": _sb(128, I), "Z2": _sb(128, I), "HI": _sb(128, I),
     "E1": _sb(128, I), "EH": _sb(256, H), "Q": _sb(128, I), "TO": _sb(256, B), "OG": _sb(512, B), "IG": _sb(512, B),
     "GOB": _sb(512, B), "GO": _sb(128, F), "OFF": _sb(128, U), "CLS": _sb(128, I), "TS": _sb(128, F), "CM": _sb(128, B),
-    "HM": _sb(1024, F), "EM": _sb(1024, F), "OH": _sb(1024, B), "INC": _sb(1024, B), "E2": _sb(64, F), "JK": _sb(64, B),
+    "HM": _sb(512, F), "NW": _sb(128, B), "RX": _sb(48, F), "AM": _sb(128, F), "PK": _sb(8, F), "EM": _sb(1024, F), "OH": _sb(1024, B), "INC": _sb(1024, B), "E2": _sb(64, F), "JK": _sb(384, B),
     "AC": _sb(8, F), "VB": _sb(8, B), "C2": _sb(96, B), "G2": _sb(192, B), "G3": _sb(192, F), "MH": _sb(96, H), "ME": _sb(96, H),
     "MB": _sb(96, H), "O1": _sb(8, U), "O2": _sb(8, U), "O3": _sb(8, U), "O4": _sb(8, U), "O5": _sb(24, U), "BS": _sb(64, F),
     "NE": _sb(582, B), "SS": _sb(582, B), "EE": _sb(96, B), "OLD": _sb(192, F), "NEW": _sb(192, F), "SC": _sb(768, F),
@@ -35,10 +41,12 @@ SCRATCH = {
 }
 for _b in range(8):
     SCRATCH["P%d" % _b] = ("psum", [128, 512], F)
-SEMAPHORES = (["cv", "cs", "ct", "cg", "tabK", "tabP", "lan", "ylan", "hL", "hT", "hl", "hd", "he", "hY", "hO", "lo"]
-              + ["o%d" % s for s in range(N)] + ["ls%d" % i for i in range(8)] + ["d%d" % i for i in range(40)])
+SEMAPHORES = (["cv", "cs", "ct", "cg", "lan", "drawn", "ylan", "lo"] + [a + "%d" % s for a in "kpo" for s in range(N)]
+              + [a + b for a in "hl" for b in ("L", "K", "P", "D", "Y", "O0", "O1", "O2")] + ["d%d" % i for i in range(40)])
 ROUTES = []
-CYC, PEC, WAKE = 1.0e-3, 0.5e-3, 0.12
+CYC, PEC, WAKE = 0.9e-3, 0.45e-3, 0.17
+LATE = (3.0, 3.0)
+MIX = 2
 
 
 def _mask(engines):
@@ -68,61 +76,65 @@ def _dst(topo, d, c):
     return DstId(rid=rid, pnc=pid)
 
 
+def _shares(engines, n):
+    k = len(engines) // n
+    return [engines[k * j:k * j + k] for j in range(n)]
+
+
+def _messages(T, topo, routes, s):
+    R = list(T.cores)
+    ro = routes[s]
+    peer, cross = ro["peer"], ro["cross"]
+    off = topo.engines(R[s], R[peer])
+    rest = [e for e in topo.engines(R[s], ro["side"]) if e not in off]
+    half = [rest[:len(rest) // 2], rest[len(rest) // 2:]]
+    out = []
+
+    def call(name, bufs, w, sem, vias):
+        for d, via, eng in zip([peer] + cross, vias, [off] + half):
+            for buf, e in zip(bufs, _shares(eng, len(bufs))):
+                out.append((name, buf, 0, w, d, via, e, sem))
+    die = [(k + routes[d]["cross"].index(s)) % 2 for k, d in enumerate(cross)]
+    call("L", ["LL0", "LL1"], LW, "lan", [None] + ro["near"])
+    call("K", ["KL"], 512, "k%d" % s, [None] + [ro[("near", "far")[die[k]]][0] for k in range(2)])
+    call("P", ["PL"], 512, "p%d" % s, [ro["plain"][0]] + [ro[("far", "near")[die[k]]][1] for k in range(2)])
+    call("D", ["DL"], DW, "drawn", [None] + ro["near"])
+    call("Y", ["YL0", "YL1"], LW, "ylan", [None] + ro["near"])
+    for k, d in enumerate(cross + [peer]):
+        vias = (ro["far"][k], ro["near"][k]) if d != peer else (ro["plain"][0], None)
+        for h in range(2):
+            out.append(("O%d" % k, "OL", OW // 2 * h, OW // 2, d, vias[h], (rest, off)[h], "o%d" % s))
+    return out
+
+
+def _slot(buf, k, a, w):
+    where, shape, dtype = SCRATCH[buf]
+    return (128 * k, 0) if where == "dram" else (0, shape[1] // N * k + a)
+
+
 def helper_program(g, core, T, topo, routes):
     R = list(T.cores)
     home = [s for s in range(N) if core in topo.cores_of(R[s])]
     if not home:
         return
     s = home[0]
-    ro = routes[s]
-    on = topo.engines(core, R[s])
-    total = [0]
-
-    def hand(sem, src, dst, to, rsem):
-        eng = topo.engines(core, to)
-        rid, pid = topo.addr(to, core)
-        g.wait_ge(T.sem[sem[0]], sem[1])
-        g.remote_dma(dst, src, T.sem[rsem], T.sem.lo, pid, rid, _mask(eng))
-        total[0] += len(eng)
-
-    def spread(sem, src, rep, done, table, owner):
-        for q in (g.sync, g.scalar):
-            q.wait_ge(T.sem[sem[0]], sem[1])
-        for u in range(N):
-            (g.sync, g.scalar)[u % 2].dma_start(rep[32 * u:32 * u + 32, 0:1024], src).then_inc(T.sem[done], 16)
-        g.wait_ge(T.sem[done], 64)
-        hn = len(on) // 2
-        g.remote_dma_fused([RemoteDMATransfer(dst_ids=[_dst(topo, R[s], core)], dma_engine_mask=_mask(on[hn * h:hn * h + hn]), remote_sem=T.sem["tab" + table[0]],
-                                              src=rep[:, 512 * h:512 * h + 512], dst=T[table][:, a:a + 512])
-                            for h, a in enumerate((512 * owner, _high(owner)))], local_sem=T.sem.lo)
-        total[0] += len(on)
-
-    q4 = len(on) // 4
-    off = len(topo.engines(R[s], R[ro["peer"]]))
-    hin, land = T.KS[:, 0:256], T.PS[:, 0:256]
-    for kind, table in (("near", "KT"), ("far", "PT")):
-        if core in ro[kind]:
-            d = ro["cross"][ro[kind].index(core)]
-            if kind == "near":
-                ap = T.LL[:, LW * s:LW * s + LW]
-                hand(("hL", q4), ap, ap, R[d], "lan")
-            hand(("hT", q4), hin, land, routes[d][kind][routes[d]["cross"].index(s)], "hl")
-            spread(("hl", off), land, T.W1, "hd", table, d)
-            if kind == "near":
-                ap = T.YL[:, YW * s:YW * s + YW]
-                hand(("hY", q4), ap, ap, R[d], "ylan")
-            a = OW * s + (OW // 2 if kind == "near" else 0)
-            ap = T.OL[:, a:a + OW // 2]
-            hand(("hO", 2 * q4), ap, ap, R[d], "o%d" % s)
-    if core == ro["side"]:
-        spread(("hT", q4), hin, T.W1, "hd", "KT", s)
-        spread(("hl", q4), land, T.W2, "he", "PT", s)
-    if core == ro["plain"][0]:
-        spread(("hl", q4), land, T.W1, "hd", "KT", ro["peer"])
-    if core == ro["plain"][1]:
-        hand(("hT", q4), hin, land, routes[ro["peer"]]["plain"][1], "hl")
-        spread(("hl", off), land, T.W1, "hd", "PT", ro["peer"])
-    g.wait_ge(T.sem.lo, total[0])
+    total = 0
+    calls = {}
+    for m in _messages(T, topo, routes, s):
+        if m[5] == core:
+            calls.setdefault(m[0], []).append(m)
+    for name, items in calls.items():
+        out = topo.engines(core, R[items[0][4]])
+        moves = []
+        for (n, buf, a, w, d, via, eng, sem), e in zip(items, _shares(out, len(items))):
+            p, c = _slot(buf, s, a, w)
+            ap = T[buf][p:p + 128, c:c + w]
+            moves.append(RemoteDMATransfer(dst_ids=[_dst(topo, R[d], core)], dma_engine_mask=_mask(e), remote_sem=T.sem[sem], src=ap, dst=ap))
+        g.wait_ge(T.sem["h" + name], sum(len(m[6]) for m in items))
+        g.remote_dma_fused(moves, local_sem=T.sem.lo)
+        total += len(out)
+    if total:
+        g.wait_ge(T.sem.lo, total)
 
 
 def _issue(T, Q, ops):
@@ -291,7 +303,7 @@ def rank_program(g, core, T, topo):
 
     def act(o, i, f=AF.Identity, bias=0.0, scale=1.0, acc=None):
         if acc is None:
-            run("s", [o], [i, bias], lambda: g.scalar.activation(o[0], i[0], f, bias=ap(bias), scale=scale), cyc(o, [i]))
+            run("s", [o], [i, bias, scale], lambda: g.scalar.activation(o[0], i[0], f, bias=ap(bias), scale=ap(scale)), cyc(o, [i]))
         else:
             run("s", [o, acc], [i, bias], lambda: g.scalar.activation(o[0], i[0], f, bias=ap(bias), scale=scale, accum_out=acc[0]), cyc(o, [i]) + 0.02)
 
@@ -319,15 +331,23 @@ def rank_program(g, core, T, topo):
                 Q[q].dma_start(ap(o), ap(i)).then_inc(T.sem[sem], 16)
         dmas[q].append(run(q, [o for o, i in pairs], [i for o, i in pairs], fn, cost, 0.08 * len(pairs), sem, 16 * len(pairs), dmas[q][-1:]))
 
-    ns = [0]
+    def piece(buf, k, a, w):
+        p, c = _slot(buf, k, a, w)
+        return A(buf, c, c + w, p0=p)
 
-    def send(items):
-        ls = "ls%d" % ns[0]
-        ns[0] += 1
-        return run("g", [], [x for x, y, d, e, sem in items],
-                   lambda: g.remote_dma_fused([RemoteDMATransfer(dst_ids=[_dst(topo, d, core)], dma_engine_mask=_mask(e), remote_sem=T.sem[sem],
-                                                                 src=x[0], dst=y[0]) for x, y, d, e, sem in items], local_sem=T.sem[ls]),
-                   2.5, 0.6, ls, sum(len(e) for x, y, d, e, sem in items))
+    sends = []
+
+    def send(name):
+        items = [(piece(buf[0] + "S" + buf[2:], d, a, w), piece(buf, r, a, w), R[d] if via is None else via, e, sem if via is None else "h" + name)
+                 for n, buf, a, w, d, via, e, sem in _messages(T, topo, routes, r) if n == name]
+        sends.append(run("g", [], [x[0] for x in items],
+                         lambda: g.remote_dma_fused([RemoteDMATransfer(dst_ids=[_dst(topo, d, core)], dma_engine_mask=_mask(e), remote_sem=T.sem[sem],
+                                                                       src=x[0], dst=y[0]) for x, y, d, e, sem in items], local_sem=T.sem["l" + name]),
+                         3.0 if sends else 5.0, 0.6 if sends else 2.8, "l" + name, sum(len(x[3]) for x in items), sends[-1:]))
+        return sends[-1]
+
+    def whole(buf):
+        return A(buf, p=128 * N)
 
     def arrive(sem, val, outs, after, cost):
         run("a", outs, [], None, cost, 0.0, sem, val, [after])
@@ -345,47 +365,61 @@ def rank_program(g, core, T, topo):
         return A(n, w * k + a, w * k + (w if b is None else b))
 
     peer, cross = ro["peer"], ro["cross"]
-    off_eng = topo.engines(core, R[peer])
-    on_eng = topo.engines(core, ro["side"])
-    rest = [e for e in on_eng if e not in off_eng]
-    q4 = len(on_eng) // 4
-    quart = [(off_eng + rest)[q4 * k:q4 * k + q4] for k in range(4)]
+    off = len(topo.engines(core, R[peer]))
     others = cross + [peer]
 
     def rows(x, d):
         return x[32 * d:32 * d + 32, :]
+    for h, x in enumerate((T.lk, T.li)):
+        dma("sy"[h], [(whole("LS%d" % h), x[:])], 1.6)
+    for k, d in enumerate(others):
+        dma("sy"[k % 2], [(blk("TKI", 256, d), rows(T.tk, d))], 1.9 + 0.4 * k)
+    for k, d in enumerate(others):
+        dma("ys"[k % 2], [(blk("TPI", 256, d), rows(T.tp, d))], 3.1 + 0.4 * k)
+    dma("y", [(piece("LL%d" % h, r, 0, LW), rows(x, r)) for h, x in enumerate((T.lk, T.li))] + [(A("PNI", 0, 1), T.pn[:])], 4.2)
+    dma("y", [(blk("TKI", 256, r), rows(T.tk, r)), (blk("TPI", 256, r), rows(T.tp, r))], 4.6)
+    dma("y", [(whole("DS"), T.dk[:]), (piece("DL", r, 0, DW), rows(T.dk, r))], 5.0)
+
+    def iota(o, pattern, base, step=0):
+        run("g", [o], [], lambda: g.iota(o[0], pattern, base, step, allow_small_or_imprecise_dtypes=True), 0.13 + 2 * o[2] * CYC)
+    iota(A("PCI", 0, 1), [[1, 1]], 0, 1)
+    iota(A("IOTA"), [[1, 128]], 0)
+
+    sent = send("L")
+    arrive("lan", 3 * off, [piece("LL%d" % h, s, 0, LW) for s in others for h in range(2)], sent, LATE[0])
+    dma("y", [(A("LN", 128 * h, 128 * h + 128), whole("LL%d" % h)) for h in range(2)], 1.6)
+
+    def parts(n, d, x):
+        cp(blk(n, 512, d, 0, 256), x)
+        tt(blk(n, 512, d, 256), x, blk(n, 512, d, 0, 256), OP.subtract)
+
+    def keys(d):
+        x = A("P%d" % (d // 2), 256 * (d % 2), 256 * (d % 2) + 256)
+        ts(x, blk("TKI", 256, d), 1.0 / 32, OP.mult)
+        parts("KS" if d != r else "KL", d, x)
+
+    def pays(d):
+        x = A("P%d" % (d // 2), 256 * (d % 2), 256 * (d % 2) + 256)
+        ts(x, x, 1.0 / 64, OP.add, 1.0 / 64, OP.min)
+        tt(x, x, blk("TPI", 256, d), OP.mult)
+        parts("PS" if d != r else "PL", d, x)
     for d in others:
-        dma("s", [(blk("LS", LW, d, 0, 32), rows(T.lk, d)), (blk("LS", LW, d, 32, 64), rows(T.li, d)), (blk("LS", LW, d, 64, LW), rows(T.dk, d))], 2.0)
-    for d in others + [r]:
-        dma("y", [(blk("TKI", 256, d), rows(T.tk, d))], 2.4)
-    for d in others + [r]:
-        dma("y", [(blk("TPI", 256, d), rows(T.tp, d))], 3.6)
-    dma("s", [(A("LN", 0, 128, p0=32 * r, p=32), rows(T.lk, r)), (A("LN", 128, 256, p0=32 * r, p=32), rows(T.li, r)),
-              (A("LN", 256, 640, p0=32 * r, p=32), rows(T.dk, r))] + [(A("PNI", 0, 1, p0=32 * u, p=32), rows(T.pn, r)) for u in range(N)], 4.0)
-    run("g", [A("PCI", 0, 1)], [], lambda: g.iota(T.PCI[:, 0:1], [[1, 1]], 0, 1), 0.15)
-    run("g", [A("IOTA")], [], lambda: g.iota(T.IOTA[:], [[1, 512]], 0, 0, allow_small_or_imprecise_dtypes=True), 1.2, after=[len(ops) - 1])
-
-    sent = send([(blk("LS", LW, peer), blk("LL", LW, r), R[peer], off_eng, "lan")]
-                + [(blk("LS", LW, d), blk("LL", LW, r), ro["near"][k], quart[2 + k], "hL") for k, d in enumerate(cross)])
-    arrive("lan", 3 * len(off_eng), [blk("LL", LW, s) for s in others], sent, 3.5)
-    for k, s in enumerate(others):
-        dma("ys"[k % 2], [(A("LN", 0, 128, p0=32 * s, p=32), blk("LL", LW, s, 0, 32)), (A("LN", 128, 256, p0=32 * s, p=32), blk("LL", LW, s, 32, 64)),
-                          (A("LN", 256, 640, p0=32 * s, p=32), blk("LL", LW, s, 64, LW))], 2.0)
-
-    hin, land = A("KS", 0, 256), A("PS", 0, 256)
-    for d in others + [r]:
-        cp(blk("KS", 256, d), blk("TKI", 256, d))
-    sent = send([(blk("KS", 256, peer), land, routes[peer]["plain"][0], quart[0], "hl"), (blk("KS", 256, r), hin, ro["side"], quart[1], "hT")]
-                + [(blk("KS", 256, d), hin, ro["near"][k], quart[2 + k], "hT") for k, d in enumerate(cross)])
-    arrive("tabK", N * len(on_eng), [A("KT", 0, 4096)], sent, 9.0)
-    for k, d in enumerate(others + [r]):
-        P = A("P%d" % k, 0, 256)
-        ts(P, blk("TKI", 256, d), 0.0, OP.is_ge, -0.5, OP.add)
-        tt(P, blk("TPI", 256, d), P, OP.mult)
-        act(blk("PS", 256, d), P, bias=1.0, scale=2.0)
-    sent = send([(blk("PS", 256, peer), hin, ro["plain"][1], quart[0], "hT"), (blk("PS", 256, r), land, ro["side"], quart[1], "hl")]
-                + [(blk("PS", 256, d), hin, ro["far"][k], quart[2 + k], "hT") for k, d in enumerate(cross)])
-    arrive("tabP", N * len(on_eng), [A("PT", 0, 4096)], sent, 9.0)
+        keys(d)
+    sentK = send("K")
+    gate.append(len(ops) - 2)
+    for d in others:
+        pays(d)
+    sentP = send("P")
+    gate.append(len(ops) - 2)
+    keys(r)
+    pays(r)
+    del gate[:]
+    sent = send("D")
+    arrive("drawn", 3 * off, [piece("DL", s, 0, DW) for s in others], sent, LATE[1])
+    dma("y", [(A("LN", 256, 640), whole("DL"))], 1.8)
+    for k, s in enumerate([peer] + cross):
+        arrive("k%d" % s, off, [blk("KL", 512, s)], sentK, LATE[1] if k else 0.5)
+        arrive("p%d" % s, off, [blk("PL", 512, s)], sentP, LATE[1])
 
     def pc(k):
         return A("PC", k, k + 1)
@@ -406,9 +440,19 @@ def rank_program(g, core, T, topo):
     ts(BO, A("MG"), PG, OP.is_equal)
     ts(f(0), A("MG"), PG, OP.not_equal, 32.0, OP.mult)
     tt(CODE, f(0), A("MI"), OP.add)
-    WTS = [1.0, 2048.0, -1024.0, 1024.0, 2.0, 1.0 / 1024]
+    WTS = [1.0, 2048.0, -2048.0, 1024.0, 2.0]
     for k, w in enumerate(WTS):
-        ts(blk("BOh", 128, k), BO, w, OP.mult)
+        act(blk("BOh", 128, k), BO, scale=w)
+    mid = [(512.0 * u + _high(u) + 512) / 2 for u in range(N)]
+    bit = [((512 * u) // 1024, (_high(u) - 2048) // 1024) for u in range(N)]
+    rest = [1024.0 * mid[u] - (2.0 ** 20 - 1) * bit[u][0] + 1 for u in range(N)]
+    MID, NEG, FK, FP = [A("PK", k, k + 1) for k in range(4)]
+    for u in range(N):
+        d = bit[u][1] - bit[u][0]
+        for k, x in enumerate((mid[u], -mid[u], BIG - mid[u], BIG - rest[u], -2.0 ** 21 - 2.0 ** 20 * d, float(d))):
+            ms(A("PK", k, k + 1, p0=32 * u, p=32), x)
+    for k in range(2):
+        act(blk("BOh", 128, 5 + k), BO, scale=A("PK", 4 + k, 5 + k))
 
     def BOh(w):
         return blk("BOh", 128, WTS.index(w))
@@ -417,10 +461,37 @@ def rank_program(g, core, T, topo):
         return blk("TB", 128, k)
     ts(A("S16"), A("IOTA", 0, 16), PI, OP.is_equal, 64.0, OP.mult)
     for k in range(16):
-        ts(blk("SEL", 128, k), BO, A("S16", k, k + 1), OP.mult)
-        ts(blk("REDh", 128, k), CODE, float(k), OP.is_equal)
-        act(blk("REDb", 128, k), CODE, AF.Abs, -float(k))
-    act(A("REDb"), A("REDb"), AF.Relu, 1.0, -1.0)
+        act(blk("SEL", 128, k), BO, scale=A("S16", k, k + 1))
+    gate.append(sent)
+    iota(A("C128"), [[0, 1024]], 128)
+    for k in range(16):
+        run("g", [blk("REDb", 128, k)], [BO], lambda k=k: g.affine_select(blk("REDb", 128, k)[0], BO[0], [[0, 8], [1, 16]], OP.is_equal, 0.0, -k, 0),
+            0.17 + 256 * CYC)
+    iota(A("NE"), [[0, 582]], 0)
+    gate.pop()
+    ts(z(1), z(0), 31, OP.bitwise_and)
+    ts(tb(5), z(1), 4.0, OP.mult, PP, OP.subtract)
+    for q in range(4):
+        ts(blk("QM", 128, q), tb(5), -float(q), OP.is_equal)
+    banks = [0]
+
+    def table(n, src, s, w, c):
+        for h, a in enumerate((512 * s, _high(s))):
+            P = "P%d" % (2 + banks[0] % 4)
+            for q in range(2):
+                mm(blk(P, 256, q), [(blk("QM", 128, 2 * h + q), blk(src, 512, s, 256 * x, 256 * x + 256)) for x in range(2)])
+            if banks[0] % 2 and s in cross:
+                ts(A(n, a, a + 512), A(P), w, OP.mult, c, OP.add)
+            else:
+                act(A(n, a, a + 512), A(P), bias=c, scale=w)
+            banks[0] += 1
+    for s in [r, peer]:
+        table("KT", "KL", s, 32.0, 0.0)
+        table("PT", "PL", s, 64.0, 1.0)
+    for s in cross:
+        table("KT", "KL", s, 32.0, 0.0)
+    for s in cross:
+        table("PT", "PL", s, 64.0, 1.0)
     ts(Ib, CODE, PI, OP.is_equal)
     act(If, Ib)
     ts(tb(0), CODE, PI, OP.is_lt, -1.0, OP.mult)
@@ -430,20 +501,17 @@ def rank_program(g, core, T, topo):
     tt(tb(3), tb(0), BO, OP.add)
     tt(tb(4), tb(2), tb(3), OP.subtract)
     act(A("EMB"), tb(4), scale=BIG)
-    ts(z(1), z(0), 31, OP.bitwise_and)
+    cp(tb(6), z(1))
     for s in range(N):
-        ts(blk("MVb", 128, s), z(1), 32.0 * s, OP.add, PP, OP.is_equal)
-    cp(A("MVh"), A("MVb"))
+        ts(blk("MVb", 128, s), tb(6), 32.0 * s, OP.add, PP, OP.is_equal)
     act(A("MVf"), A("MVb"))
     ts(z(2), A("MG"), 1, OP.bitwise_and)
     ts(A("FO"), z(2), PF, OP.is_equal)
     ms(A("RS4"), 1.0)
     ms(A("RS4", 0, 512, 128), 0.0)
-    ms(A("C128"), 128.0)
     ms(A("OB"), 0.0)
-    ms(A("NE"), 0.0)
     for d in range(N):
-        ms(blk("OS", OW, d, 272), 0.0)
+        act(blk("OS", OW, d, 272), A("IOTA", 0, 8), scale=0.0)
     ts(pi(5), pi(0), 7, OP.bitwise_and)
     ts(pi(6), pi(0), 3, OP.arith_shift_right, 1, OP.bitwise_and)
     tt(pc(4), pi(5), pi(4), OP.subtract)
@@ -458,39 +526,43 @@ def rank_program(g, core, T, topo):
     ts(pc(9), PF, 4.0, OP.mult, PU, OP.add)
     ts(A("GS", 8, 16), A("IOTA", 0, 8), pc(9), OP.is_equal)
     act(B15, A("S16", 15, 16), scale=64.0)
-    C0, C1, SGN, LIM = pc(14), pc(15), pc(16), pc(17)
-    ts(C0, PU, 2.0, OP.mult)
-    ts(C1, PU, 2.0, OP.mult, 1.0, OP.add)
-    ts(SGN, PU, 0.0, OP.is_gt, 2.0, OP.mult)
-    ts(SGN, SGN, -1.0, OP.add)
-    ts(LIM, PU, 512.0, OP.mult, 1.0, OP.add)
-    ms(A("PC", 17, 18, p=32), -1536.0)
+    C0, C1 = pc(14), pc(15)
+    act(C0, PU, scale=2.0)
+    act(C1, PU, bias=1.0, scale=2.0)
     act(A("KR"), A("IOTA", 0, 96), bias=95.0, scale=-1.0)
     act(A("KX"), A("IOTA", 0, 96), bias=95.0 - 2047.0, scale=-1.0)
     act(A("CT", 0, 16), A("IOTA", 0, 16), bias=PI, scale=16.0)
     act(A("CT", 16, 22), A("CT", 0, 6), bias=95.5, scale=-1.0)
-    ts(pc(18), PU, 96.0, OP.mult, 4096.0, OP.add)
+    act(pc(18), PU, bias=4096.0, scale=96.0)
+    act(pc(16), PI, bias=4096.0)
     DUMP = A("CT", 24, 30)
     act(DUMP, A("CT", 0, 6), bias=pc(18))
+    act(A("CT", 56, 62), DUMP, bias=MID, scale=-1.0)
+    act(A("RX", 0, 24), A("IOTA", 0, 24), scale=0.0)
+    act(A("RX", 24, 48), A("IOTA", 0, 24), bias=pc(16), scale=16.0)
+    ts(pi(9), pi(0), 31, OP.bitwise_and)
+    cp(pc(17), pi(9))
+    ts(A("AM"), tb(6), pc(17), OP.is_equal)
+    act(A("CT", 48, 54), A("CT", 0, 6), bias=0.5)
     for m in range(6):
-        ts(blk("KP", 97, m), A("IOTA", 0, 97), A("CT", m, m + 1), OP.is_le)
+        act(blk("KP", 97, m), A("IOTA", 0, 97), AF.Sign, A("CT", 48 + m, 49 + m), -1.0)
     for k, x in enumerate((0.0, 0.0, 0.0, 2048.0)):
         act(blk("XO", 2, k), A("CT", 0, 2), bias=x)
-    ts(pc(19), PU, 256.0, OP.mult)
-    ts(pc(20), PU, 2.0, OP.is_ge)
-    ts(pc(21), PI, 8.0, OP.mult, C0, OP.add)
-    for h in range(2):
-        ts(A("CT", 32 + 8 * h, 40 + 8 * h), A("IOTA", 0, 8), 128.0, OP.mult, pc(21), OP.add)
+    act(pc(19), PU, scale=256.0)
+    act(pc(20), PU, AF.Sign, -1.5)
+    act(pc(21), PI, bias=C0, scale=8.0)
+    act(A("CT", 32, 40), A("IOTA", 0, 8), bias=pc(21), scale=128.0)
     for d in range(N):
         step = float(_high(d) - 512 - 512 * d)
-        if d != r:
-            ts(pc(22), pc(20), step, OP.mult, 512.0 * d, OP.add)
-            tt(pc(23), pc(22), pc(19), OP.add)
-            ts(blk("OK", 16, d), A("CT", 0, 16), pc(23), OP.add)
+        act(pc(22 + d), pc(20), bias=512.0 * d + step / 2, scale=step / 2)
+        act(pc(26 + d), pc(22 + d), bias=pc(19))
+        act(blk("OF", 16, d), A("CT", 0, 16), bias=pc(26 + d))
         for h in range(2):
             for x in range(2):
-                a = 8 * h + 4 * x
-                ts(blk("OY", 16, d, a, a + 4), A("CT", 32 + a, 36 + a), 512.0 * d + h + step * x, OP.add)
+                a = 64 + 16 * d + 8 * h + 4 * x
+                act(A("OF", a, a + 4), A("CT", 32 + 4 * x, 36 + 4 * x), bias=512.0 * d + h + step * x)
+    cp(A("OK"), A("OF", 0, 64))
+    cp(A("OY"), A("OF", 64, 128))
 
     KEY, IMG, HI = A("KB"), A("IMG"), A("HI")
     KW, PW = A("KT", 0, 4096), A("PT", 0, 4096)
@@ -519,20 +591,19 @@ def rank_program(g, core, T, topo):
             ts(blk("OG", 128, d), A("TO", 0, 128), float(d), OP.is_equal)
         scan(A("IG"), A("RS4"), A("OG"), 0.0, OP.mult, OP.add)
         mm(A("P6"), [(BO, A("IG")), (XM, A("OG"))])
-        act(A("GOB"), A("P6"), AF.Sigmoid, -1407.5 * 256, -256.0)
+        act(A("GOB"), A("P6"), AF.Sign, -1407.5, -1.0)
         mm(A("P4", 128, 256), [(Ib, blk("GOB", 128, d)) for d in range(4)])
-        act(A("GO"), A("P4", 128, 256))
-        act(f(2), A("P4", 128, 256), scale=-64.0)
+        act(A("GO"), A("P4", 128, 256), bias=2.0, scale=0.5)
+        act(f(2), A("P4", 128, 256), bias=-128.0, scale=-32.0)
         ts(v(1), A("Q"), 3.0, OP.mult, 64.0, OP.add)
         tt(v(1), v(1), A("TO", 0, 128), OP.subtract)
         tt(v(1), v(1), f(2), OP.add)
         tt(v(0), A("LN", 256 + 128 * t, 384 + 128 * t), KEY, OP.subtract)
         tt(v(0), v(0), A("GO"), OP.mult)
         tt(f(3), v(0), KEY, OP.add)
-        for k, (n, w) in enumerate((("EM", 1.0 / 32), ("HM", 64.0))):
-            for s in range(N):
-                mm(blk("P6", 128, s), [(blk("MVh", 128, s), blk("EH", 128, k))])
-            act(blk(n, 512, t % 2), A("P6"), bias=1.0, scale=w)
+        for s in range(N):
+            mm(blk("P6", 128, s), [(blk("MVb", 128, s), blk("EH", 128, 0))])
+        act(blk("EM", 512, t % 2), A("P6"), scale=1.0 / 32)
 
     def spread(c):
         for k in range(4 * c, 4 * c + 4):
@@ -559,7 +630,9 @@ def rank_program(g, core, T, topo):
 
     cp(KEY, A("LN", 0, 128))
     ts(IMG, A("LN", 128, 256), -1.0, OP.add)
-    cp(NV(0), A("PNI", 0, 1))
+    cp(NV(12), A("PNI", 0, 1))
+    mm(A("P6", 0, 1), [(blk("MVf", 128, r), NV(12))])
+    act(NV(0), A("P6", 0, 1))
     prep(0)
     for c in range(4):
         spread(c)
@@ -570,7 +643,7 @@ def rank_program(g, core, T, topo):
         for c in range(4):
             a, b, o, P = 512 * c, 512 * c + 512, A("OFF", 32 * c, 32 * c + 32), "P%d" % c
             act(A("W1", a, b), X(KW, o))
-            if c < 2:
+            if c < MIX:
                 tt(A("W2", a, b), A("W1", a, b), A(P), OP.is_equal)
                 tt(A("W3", a, b), X(PW, o), A("W2", a, b), OP.mult)
             else:
@@ -585,6 +658,10 @@ def rank_program(g, core, T, topo):
         ts(f(0), A("Z2"), n, OP.is_lt, 3.0, OP.mult)
         tt(z(2), f(0), v(1), OP.add)
         ts(A("CLS"), z(2), 71, OP.bitwise_and)
+        ts(A("NW"), A("Z2"), n, OP.is_lt, 32.0, OP.mult)
+        for s in range(N):
+            mm(blk("P6", 128, s), [(blk("MVb", 128, s), blk("EH", 128, 1)), (blk("MVb", 128, s), A("NW"))])
+        act(A("HM"), A("P6"), bias=NEG, scale=64.0)
         ts(NV(8), n, 32.0, OP.add, 2048.0, OP.min)
         tt(NV(9), NV(8), n, OP.subtract)
         if t:
@@ -599,7 +676,7 @@ def rank_program(g, core, T, topo):
         mm(A("P1", 0, 64), [(BO, A("INC", 15, 1024, 16))])
         mm(A("P2", 0, 64), red("REDb", "INC", 0, 1024))
         for m in range(6):
-            act(A("JK", 0, 63), A("P1", 0, 63), AF.Sign, A("CT", 16 + m, 17 + m), -1.0, acc=A("AC", m, m + 1))
+            act(blk("JK", 64, m, 0, 63), A("P1", 0, 63), AF.Sign, A("CT", 16 + m, 17 + m), -1.0, acc=A("AC", m, m + 1))
         act(A("E2"), A("P2", 0, 64), bias=B15)
         AC = A("AC", 0, 6)
         ts(A("O1", 0, 6), AC, 0.5, OP.mult, 31.5, OP.add)
@@ -613,7 +690,7 @@ def rank_program(g, core, T, topo):
         act(A("G2", 96, 192), X(A("OH"), A("O2", 0, 6)))
         cp(A("O3", 0, 6), A("BS", 16, 22))
         mm(A("P3", 0, 96), [(BO, A("G2", 0, 96)), (XM, A("G2", 96, 192))])
-        act(A("G3", 0, 96), X(blk("HM", 512, t % 2), A("O3", 0, 6)))
+        act(A("G3", 0, 96), X(A("HM"), A("O3", 0, 6)))
         act(A("G3", 96, 192), X(blk("EM", 512, t % 2), A("O3", 0, 6)))
         tt(A("P3", 0, 96), A("P3", 0, 96), A("KX"), OP.is_equal)
         tt(A("MH"), A("P3", 0, 96), A("G3", 0, 96), OP.mult)
@@ -628,55 +705,55 @@ def rank_program(g, core, T, topo):
         tt(KEY, v(2), f(4), OP.max)
         if last:
             act(A("YI"), IMG, bias=1.0)
-            for k, d in enumerate(others):
-                dma("y", [(blk("YS", YW, d, 0, 32), A("KB", p0=32 * d, p=32)), (blk("YS", YW, d, 32, 64), A("YI", p0=32 * d, p=32))], 2.0)
-            dma("y", [(rows(T.yl, r), A("KB", p0=32 * r, p=32)), (rows(T.yi, r), A("YI", p0=32 * r, p=32))], 2.0)
-            sent = send([(blk("YS", YW, peer), blk("YL", YW, r), R[peer], off_eng, "ylan")]
-                        + [(blk("YS", YW, d), blk("YL", YW, r), ro["near"][k], quart[2 + k], "hY") for k, d in enumerate(cross)])
-            arrive("ylan", 3 * len(off_eng), [blk("YL", YW, s) for s in others], sent, 3.0)
-            dma("y", [x for s in others for x in ((rows(T.yl, s), blk("YL", YW, s, 0, 32)), (rows(T.yi, s), blk("YL", YW, s, 32, 64)))], 2.0)
+            dma("y", [(whole("YS%d" % h), A(x)) for h, x in enumerate(("KB", "YI"))], 2.0)
+            dma("y", [(piece("YL%d" % h, r, 0, LW), A(x, p0=32 * r, p=32)) for h, x in enumerate(("KB", "YI"))], 2.0)
+            sent = send("Y")
+            arrive("ylan", 3 * off, [piece("YL%d" % h, s, 0, LW) for s in others for h in range(2)], sent, 3.0)
+            dma("y", [(x[:], whole("YL%d" % h)) for h, x in enumerate((T.yl, T.yi))], 2.0)
         else:
             prep(t + 1)
-        mm(A("P1", 80, 86), red("REDh", "MH", 0, 96))
+        mm(A("P1", 80, 86), red("REDb", "MH", 0, 96))
         ms(A("P0", 96, 97), 0.0)
         mm(A("P0", 0, 96), [(BOh(1.0), A("MH"))])
-        BS, BO4 = A("BS", 0, 6), A("BS", 40, 46)
-        cp(BS, A("P1", 80, 86))
-        ts(A("BS", 24, 30), A("P1", 80, 86), SGN, OP.mult, LIM, OP.is_lt)
-        ts(A("BS", 32, 38), A("BS", 24, 30), 2048.0, OP.mult, -1.0, OP.add)
-        tt(BO4, A("P1", 80, 86), A("BS", 32, 38), OP.add)
-        cp(A("O4", 0, 6), BO4)
         O4 = A("O4", 0, 6)
+        ts(O4, A("P1", 80, 86), MID, OP.add)
+        cp(A("BS", 0, 6), A("P1", 80, 86))
+        tt(A("BS", 48, 54), A("P1", 80, 86), A("CT", 56, 62), OP.add)
         act(A("EE"), X(KW, O4), AF.Relu, 0.0, -1.0)
-        ts(A("OLD", 0, 96), X(KW, O4), BIG + 2049.0, OP.add)
-        act(A("OLD", 96, 192), X(PW, O4), bias=BIG + 1025.0)
-        ts(A("MB"), A("MH"), 1025.0, OP.is_ge, 1024.0, OP.mult)
-        mm(A("P2", 0, 96), [(BOh(2048.0), A("ME")), (BOh(1.0), A("MH")), (A("EMB"), A("EE"))])
+        ts(A("OLD", 0, 96), X(KW, O4), FK, OP.add)
+        act(A("OLD", 96, 192), X(PW, O4), bias=FP)
+        ts(A("MB"), A("MH"), 0.0, OP.is_gt)
+        mm(A("P2", 0, 96), [(BOh(2048.0), A("ME")), (BOh(1.0), A("MH")), (BOh(-2048.0), A("MB")), (A("EMB"), A("EE"))])
+        mm(A("P3", 128, 224), [(BOh(2.0), A("ME")), (BOh(1024.0), A("MH")), (blk("BOh", 128, 5), A("MB")), (blk("BOh", 128, 6), A("MB")), (A("EMB"), A("EE"))])
+        gate.append(len(ops) - 1)
         tt(A("NEW", 0, 96), A("P2", 0, 96), A("OLD", 0, 96), OP.max)
+        gate.pop()
+        tt(A("NEW", 96, 192), A("P3", 128, 224), A("OLD", 96, 192), OP.max)
+        ready = len(ops) - 1
         for s in range(N):
             mm(blk("P5", 96, s), [(blk("MVf", 128, s), A("NEW", 0, 96))])
-        act(A("SC", 0, 384), A("P5", 0, 384), bias=-BIG - 2049.0)
+        for s in range(N):
+            act(blk("SC", 96, s), blk("P5", 96, s), bias=mid[s] - BIG)
         for m in range(6):
             ts(blk("NE", 97, m, 16 * m), A("P0", 16 * m, 97), A("BS", m, m + 1), OP.not_equal)
         scan(A("SS"), A("NE"), A("KP"), 1.0, OP.min, OP.max)
         TRY = A("SS", 96, 582, 97)
-        tt(A("BS", 48, 54), BO4, DUMP, OP.subtract)
-        tt(A("BS", 48, 54), A("BS", 48, 54), TRY, OP.mult)
-        tt(A("BS", 56, 62), A("BS", 48, 54), DUMP, OP.add)
         for s in range(N):
-            mm(blk("P3", 6, s), [(blk("MVf", 128, s), A("BS", 56, 62))])
-        cp(A("O5"), A("P3", 0, 24))
+            tt(A("RX", 6 * s, 6 * s + 6, p0=32 * s, p=32), A("BS", 48, 54, p0=32 * s, p=32), A("SS", 96, 582, 97, p0=32 * s, p=32), OP.mult)
+        mm(A("P2", 128, 152), [(A("AM"), A("RX", 0, 24)), (If, A("RX", 24, 48))])
+        cp(A("O5"), A("P2", 128, 152))
+        gate.append(ready)
         cp(X(A("KT"), A("O5")), A("SC", 0, 384))
-        mm(A("P2", 128, 224), [(BOh(2.0), A("ME")), (BOh(1024.0), A("MH")), (BOh(-1024.0), A("MB")), (BOh(1.0 / 1024), A("MB")), (A("EMB"), A("EE"))])
-        tt(A("NEW", 96, 192), A("P2", 128, 224), A("OLD", 96, 192), OP.max)
+        gate.pop()
         for s in range(N):
             mm(blk("P6", 96, s), [(blk("MVf", 128, s), A("NEW", 96, 192))])
-        act(A("SC", 384, 768), A("P6", 0, 384), bias=-BIG - 1025.0)
+        for s in range(N):
+            act(blk("SC", 96, N + s), blk("P6", 96, s), bias=rest[s] - BIG)
         cp(X(A("PT"), A("O5")), A("SC", 384, 768))
-        mm(A("P3", 32, 38), red("REDb", "EE", 0, 96))
-        tt(A("OV", 0, 6), A("P3", 32, 38), TRY, OP.is_lt)
-        mm(A("P3", 48, 54), [(A("FO"), A("OV", 0, 6))])
-        act(A("TT", 0, 6), A("P3", 48, 54), acc=NV(10))
+        mm(A("P4", 256, 262), red("REDb", "EE", 0, 96))
+        tt(A("OV", 0, 6), A("P4", 256, 262), TRY, OP.is_lt)
+        mm(A("P4", 272, 278), [(A("FO"), A("OV", 0, 6))])
+        act(A("TT", 0, 6), A("P4", 272, 278), acc=NV(10))
         act(NV(11), NV(10), AF.Relu, NV(9), -1.0)
         act(NV(t + 1), NV(11), AF.Identity, NV(8), -1.0)
         if not last:
@@ -689,7 +766,8 @@ def rank_program(g, core, T, topo):
         y = [(T.ys[2 * s + h, :], A(n, x + 256 + 8 * h, x + 264 + 8 * h)) for h in range(2)] + [(rows(T.yn, s), A(n, x + 272, x + 273, p=32))]
         if s != r:
             y += [(T.yk[32 * s:32 * s + 32, 256 * u:256 * u + 256], A(n, x, x + 256, p0=32 * u, p=32)) for u in range(N)]
-        dma(q, y, 2.5)
+        dma(q[0], y[0::2], 2.5)
+        dma(q[1], y[1::2], 2.5)
 
     for k, d in enumerate(others + [r]):
         if d != r:
@@ -700,15 +778,11 @@ def rank_program(g, core, T, topo):
             mm(A(P, h, 16, 2), [(blk("YP", 256, d, 128 * h, 128 * h + 128), A("GS", 8, 16))])
         cp(blk("OS", OW, d, 256, 272), A(P, 0, 16))
         cp(blk("OS", OW, d, 272, 273), NV(RO))
-        hw = OW // 2
-        if d in cross:
-            sent = send([(blk("OS", OW, d, hw * h, hw * h + hw), blk("OL", OW, r, hw * h, hw * h + hw), ro[kind][k], (rest, off_eng)[h], "hO")
-                         for h, kind in enumerate(("far", "near"))])
-        elif d == peer:
-            sent = send([(blk("OS", OW, d), blk("OL", OW, r), R[peer], off_eng, "o%d" % r)])
+        if d != r:
+            sent = send("O%d" % k)
     dma("y", [(T.yk[32 * r:32 * r + 32, 512 * h:512 * h + 512], A("KT", a, a + 512, p=32)) for h, a in enumerate((512 * r, _high(r)))], 2.5)
-    stores("y", r, "OS")
+    stores("sy", r, "OS")
     for k, s in enumerate([peer] + cross):
-        arrive("o%d" % s, len(off_eng) * (1 if s == peer else 2), [blk("OL", OW, s)], sent, 2.0 + k)
-        stores("sy"[k % 2], s, "OL")
+        arrive("o%d" % s, 2 * off, [blk("OL", OW, s)], sent, 2.0 + k)
+        stores(("sy", "ys")[k % 2], s, "OL")
     _issue(T, Q, ops)

@@ -4,7 +4,7 @@ from concourse.mybir import AluOpType as OP, AxisListType, ActivationFunctionTyp
 N, RO, NCORES = 4, 3, 256
 LW, DW, OW = 32, 96, 280
 TW = 8256
-BIG = float(2 ** 22)
+BIG, LIFT = float(2 ** 22), float(2 ** 21)
 F, H, B, I, U = "float32", "float16", "bfloat16", "int32", "uint16"
 
 
@@ -22,21 +22,25 @@ SCRATCH = {
     "LS0": _dr(LW, I), "LL0": _dr(LW, I), "LS1": _dr(LW, I), "LL1": _dr(LW, I), "LN": _sb(640, I), "PNI": _sb(4, I),
     "YS0": _dr(LW, F), "YL0": _dr(LW, F), "YS1": _dr(LW, F), "YL1": _dr(LW, F), "OF": _sb(128, F),
     "OS": _sb(N * OW, F), "OL": _sb(N * OW, F), "YP": _sb(1024, F), "YI": _sb(128, F),
-    "W1": _sb(2048, F), "W2": _sb(2048, F), "W3": _sb(2048, F), "TM": _sb(128 * 8, F), "TN": _sb(128 * 8, I),
+    "W1": _sb(2048, F), "EQ": _sb(2048, B), "GB": _sb(32, B), "W3": _sb(2048, F),
+    "TM": _sb(128 * 8, F), "TN": _sb(128 * 8, I),
     "IOTA": _sb(128, F), "PCI": _sb(16, I), "PC": _sb(32, F), "MI": _sb(128, I), "MG": _sb(128, I), "CODE": _sb(128, B),
-    "BOb": _sb(128, B), "BOh": _sb(896, B), "Ib": _sb(128, B), "If": _sb(128, F), "XM": _sb(128, B), "FO": _sb(128, B),
-    "EMB": _sb(128, B), "SEL": _sb(2048, B), "REDb": _sb(2048, B), "TB": _sb(1024, B),
-    "MVb": _sb(512, B), "MVf": _sb(512, F), "GS": _sb(16, F), "S16": _sb(16, F), "RS4": _sb(512, B),
-    "C128": _sb(1024, B), "KR": _sb(96, F), "KX": _sb(96, F), "KP": _sb(582, B), "PERM": _sb(8, U), "CT": _sb(64, F),
+    "BOb": _sb(128, B), "SUM": _sb(512 * 6, B), "Ib": _sb(128, B), "If": _sb(128, F), "XM": _sb(128, B), "FO": _sb(128, B),
+    "EMB": _sb(512, B), "SEL": _sb(2048, B), "REDb": _sb(2048, B), "TB": _sb(1024, B),
+    "MVb": _sb(512, B), "MVf": _sb(128, F), "GS": _sb(16, F), "TF": _sb(512, B), "PB": _sb(256, B), "LV": _sb(1152, B),
+    "S16": _sb(16, F), "RS4": _sb(512, B),
+    "C128": _sb(1024, B), "KR": _sb(192, F), "KP": _sb(582, B), "PERM": _sb(8, U), "CT": _sb(96, F),
     "XO": _sb(8, F), "OK": _sb(64, U), "OY": _sb(64, U),
-    "KB": _sb(128, F), "OB": _sb(160, F), "YT": _sb(288, F), "IMG": _sb(128, F), "K2": _sb(128, I), "Z2": _sb(128, I), "HI": _sb(128, I),
+    "KB": _sb(128, F), "OB": _sb(160, F), "YT": _sb(288, F), "K2": _sb(128, I), "Z2": _sb(128, I), "HI": _sb(128, I),
     "E1": _sb(128, I), "EH": _sb(256, H), "Q": _sb(128, I), "TO": _sb(256, B), "OG": _sb(512, B), "IG": _sb(512, B),
-    "GOB": _sb(512, B), "GO": _sb(128, F), "OFF": _sb(128, U), "CLS": _sb(128, I), "TS": _sb(128, F), "CM": _sb(128, B),
-    "HM": _sb(512, F), "NW": _sb(128, B), "RX": _sb(48, F), "AM": _sb(128, F), "PK": _sb(8, F), "EM": _sb(1024, F), "OH": _sb(1024, B), "INC": _sb(1024, B), "E2": _sb(64, F), "JK": _sb(384, B),
-    "AC": _sb(8, F), "VB": _sb(8, B), "C2": _sb(96, B), "G2": _sb(192, B), "G3": _sb(192, F), "MH": _sb(96, H), "ME": _sb(96, H),
-    "MB": _sb(96, H), "O1": _sb(8, U), "O2": _sb(8, U), "O3": _sb(8, U), "O4": _sb(8, U), "O5": _sb(24, U), "BS": _sb(64, F),
-    "NE": _sb(582, B), "SS": _sb(582, B), "EE": _sb(96, B), "OLD": _sb(192, F), "NEW": _sb(192, F), "SC": _sb(768, F),
-    "OV": _sb(8, B), "TT": _sb(8, F), "NN": _sb(32, F), "SG": _sb(4, U), "SO": _sb(4, U),
+    "GOB": _sb(512, B), "FL": _sb(384, B), "OFF": _sb(128, U), "IDS": _sb(128 * 10, B), "DF": _sb(384, F),
+    "TS": _sb(128, F), "CM": _sb(128, B),
+    "HM": _sb(512, F), "NW": _sb(128, B), "RX": _sb(72, F), "AM": _sb(128, F), "PK": _sb(16, F), "EM": _sb(1024, F),
+    "OH": _sb(1024, B), "INC": _sb(1024, B), "E2": _sb(64, F), "JK": _sb(384, B),
+    "AC": _sb(8, F), "VB": _sb(8, B), "C2": _sb(96, B), "XS": _sb(1024, F), "MK": _sb(96, F), "MH": _sb(96, H), "ME": _sb(96, H),
+    "MB": _sb(96, H), "O1": _sb(16, U), "O3": _sb(8, U), "O4": _sb(8, U), "O5": _sb(24, U), "BS": _sb(64, F),
+    "NE": _sb(582, B), "SS": _sb(582, B), "EE": _sb(96, B), "OLD": _sb(768, F), "O6": _sb(24, U), "SC": _sb(768, F),
+    "OV": _sb(8, B), "BH": _sb(8, H), "NN": _sb(32, F), "SG": _sb(4, U), "SO": _sb(4, U),
     "SX": _sb(64, F), "SI": _sb(64, I), "SK": _sb(320, F),
 }
 for _b in range(8):
@@ -44,9 +48,8 @@ for _b in range(8):
 SEMAPHORES = (["cv", "cs", "ct", "cg", "lan", "drawn", "ylan", "lo"] + [a + "%d" % s for a in "kpo" for s in range(N)]
               + [a + b for a in "hl" for b in ("L", "K", "P", "D", "Y", "O0", "O1", "O2")] + ["d%d" % i for i in range(40)])
 ROUTES = []
-CYC, PEC, WAKE = 0.9e-3, 0.45e-3, 0.17
-LATE = (3.0, 3.0)
-MIX = 2
+CYC, PEC, WAKE = 0.87e-3, 0.435e-3, 0.2
+LATE = (2.0, 2.3)
 
 
 def _mask(engines):
@@ -90,16 +93,17 @@ def _messages(T, topo, routes, s):
     half = [rest[:len(rest) // 2], rest[len(rest) // 2:]]
     out = []
 
-    def call(name, bufs, w, sem, vias):
-        for d, via, eng in zip([peer] + cross, vias, [off] + half):
-            for buf, e in zip(bufs, _shares(eng, len(bufs))):
-                out.append((name, buf, 0, w, d, via, e, sem))
+    def call(name, bufs, w, sem, *ways):
+        for k, (d, eng) in enumerate(zip([peer] + cross, [off] + half)):
+            for buf, vias, e in zip(bufs, ways, _shares(eng, len(bufs))):
+                out.append((name, buf, 0, w, d, vias[k], e, sem))
     die = [(k + routes[d]["cross"].index(s)) % 2 for k, d in enumerate(cross)]
-    call("L", ["LL0", "LL1"], LW, "lan", [None] + ro["near"])
+    here, there = [None] + ro["near"], ro["plain"][:1] + ro["far"]
+    call("L", ["LL0", "LL1"], LW, "lan", here, there)
     call("K", ["KL"], 512, "k%d" % s, [None] + [ro[("near", "far")[die[k]]][0] for k in range(2)])
     call("P", ["PL"], 512, "p%d" % s, [ro["plain"][0]] + [ro[("far", "near")[die[k]]][1] for k in range(2)])
-    call("D", ["DL"], DW, "drawn", [None] + ro["near"])
-    call("Y", ["YL0", "YL1"], LW, "ylan", [None] + ro["near"])
+    call("D", ["DL"], DW, "drawn", there)
+    call("Y", ["YL0", "YL1"], LW, "ylan", here, there)
     for k, d in enumerate(cross + [peer]):
         vias = (ro["far"][k], ro["near"][k]) if d != peer else (ro["plain"][0], None)
         for h in range(2):
@@ -137,56 +141,69 @@ def helper_program(g, core, T, topo, routes):
         g.wait_ge(T.sem.lo, total)
 
 
-def _issue(T, Q, ops):
+def _order(ops):
     n = len(ops)
+    pred = [[(j, ops[j]["cost"] + WAKE) for j in o["dep"]] + [(j, ops[j]["cost" if o["q"] == "a" else "busy"]) for j in o["after"]] for o in ops]
     succ = [[] for o in ops]
-    for i, o in enumerate(ops):
-        for j in o["dep"] | o["after"]:
-            succ[j].append(i)
+    for i in range(n):
+        for j, lag in pred[i]:
+            succ[j].append((i, lag))
+
+    def pack(key, back):
+        before, behind = (succ, pred) if back else (pred, succ)
+        left = [len(x) for x in before]
+        at = [0.0] * n
+        spans = {}
+        pool = [i for i in range(n) if not left[i]]
+        while pool:
+            i = min(pool, key=lambda k: (key[k], k))
+            pool.remove(i)
+            o = ops[i]
+            if back:
+                t = max([o["cost"]] + [at[k] + lag for k, lag in succ[i]]) - o["busy"]
+            else:
+                t = max([0.0] + [at[j] + lag for j, lag in pred[i]])
+            if o["q"] != "a":
+                busy = spans.setdefault(o["q"], [])
+                x = 0
+                for x, (a, b) in enumerate(busy + [(1e9, 1e9)]):
+                    if b <= t:
+                        continue
+                    if t + o["busy"] <= a + 1e-9:
+                        break
+                    t = b
+                busy.insert(x, (t, t + o["busy"]))
+            at[i] = t + o["busy"] if back else t
+            for k, lag in behind[i]:
+                left[k] -= 1
+                if not left[k]:
+                    pool.append(k)
+        return at
+
     level = [0.0] * n
     for i in range(n - 1, -1, -1):
-        level[i] = ops[i]["cost"] + max([level[k] + (WAKE if i in ops[k]["dep"] else 0.0) for k in succ[i]] + [0.0])
-    for i, o in enumerate(ops):
-        if o["sem"] is not None and not o["dep"]:
-            level[i] += 1000.0
-    left = [len(o["dep"] | o["after"]) for o in ops]
-    ready = [0.0] * n
-    cand = {q: [] for q in list(Q) + ["a"]}
-    free = {q: 0.0 for q in cand}
-    for i, o in enumerate(ops):
-        if not left[i]:
-            cand[o["q"]].append(i)
-    clock = {q: {} for q in cand}
-    count = {q: 0 for q in cand}
-    event = [None] * n
+        level[i] = max([ops[i]["cost"]] + [level[k] + lag for k, lag in succ[i]])
+    best = None
+    for turn in range(60):
+        at = pack([-x for x in level], False)
+        end = max(at[i] + ops[i]["cost"] for i in range(n))
+        if best is None or end < best[0]:
+            best = (end, at)
+        if turn % 2:
+            at = [x + 0.3 * (((i + 1) * (turn + 7) * 2654435761 >> 7) % 1000) / 1000.0 for i, x in enumerate(best[1])]
+        level = pack([-(at[i] + ops[i]["busy"]) for i in range(n)], True)
+    return best[1]
+
+
+def _issue(T, Q, ops):
+    at = _order(ops)
+    clock = {q: {} for q in Q}
+    count = {q: 0 for q in Q}
+    event = [None] * len(ops)
     final = {}
-    for step in range(n):
-        pick = None
-        for q, c in cand.items():
-            if not c:
-                continue
-            t = free[q]
-            best = max(c, key=lambda i: (level[i], -i))
-            if ready[best] > t:
-                fill = [i for i in c if max(ready[i], t) + ops[i]["busy"] <= ready[best] + 0.05 and i != best]
-                if fill:
-                    best = min(fill, key=lambda i: (max(ready[i], t), -level[i]))
-            st = max(t, ready[best])
-            if pick is None or st < pick[0]:
-                pick = (st, best)
-        st, i = pick
+    for i in sorted(range(len(ops)), key=lambda k: (at[k], k)):
         o = ops[i]
         q = o["q"]
-        cand[q].remove(i)
-        free[q] = st + o["busy"]
-        for k in succ[i]:
-            if i in ops[k]["dep"]:
-                ready[k] = max(ready[k], st + o["cost"] + WAKE)
-            else:
-                ready[k] = max(ready[k], st + (o["cost"] if ops[k]["q"] == "a" else o["busy"]))
-            left[k] -= 1
-            if not left[k]:
-                cand[ops[k]["q"]].append(k)
         if q == "a":
             event[i] = (o["sem"], o["val"], {o["sem"]: o["val"]})
             final[o["sem"]] = o["val"]
@@ -307,13 +324,13 @@ def rank_program(g, core, T, topo):
         else:
             run("s", [o, acc], [i, bias], lambda: g.scalar.activation(o[0], i[0], f, bias=ap(bias), scale=scale, accum_out=acc[0]), cyc(o, [i]) + 0.02)
 
-    def mm(o, terms):
+    def mm(o, terms, start=True, stop=True):
         def fn():
-            for k, (l, x) in enumerate(terms):
-                last = g.tensor.matmul(o[0], l[0], x[0], k == 0, k == len(terms) - 1)
+            for k, x in enumerate(terms):
+                last = g.tensor.matmul((x + (o,))[2][0], x[0][0], x[1][0], start and k == 0, stop and k == len(terms) - 1)
             return last
-        c = sum(max(min(64, l[2]), x[2]) * (4 if SCRATCH[l[1][0][0]][2] == F else 1) for l, x in terms) * PEC
-        run("t", [o], [x for tm in terms for x in tm], fn, c)
+        c = sum(max(min(64, x[0][2]), x[1][2]) * (4 if SCRATCH[x[0][1][0][0]][2] == F else 1) for x in terms) * PEC
+        run("t", [o], [y for x in terms for y in x[:2]], fn, c)
 
     def red(mat, n, a, b):
         return [(A(mat, 128 * i, 128 * i + 128), A(n, a + i, b, 16)) for i in range(16)]
@@ -386,7 +403,7 @@ def rank_program(g, core, T, topo):
     iota(A("IOTA"), [[1, 128]], 0)
 
     sent = send("L")
-    arrive("lan", 3 * off, [piece("LL%d" % h, s, 0, LW) for s in others for h in range(2)], sent, LATE[0])
+    arrive("lan", 5 * off + off // 2, [piece("LL%d" % h, s, 0, LW) for s in others for h in range(2)], sent, LATE[0])
     dma("y", [(A("LN", 128 * h, 128 * h + 128), whole("LL%d" % h)) for h in range(2)], 1.6)
 
     def parts(n, d, x):
@@ -394,12 +411,12 @@ def rank_program(g, core, T, topo):
         tt(blk(n, 512, d, 256), x, blk(n, 512, d, 0, 256), OP.subtract)
 
     def keys(d):
-        x = A("P%d" % (d // 2), 256 * (d % 2), 256 * (d % 2) + 256)
+        x = blk("P%d" % (d // 2), 256, d % 2)
         ts(x, blk("TKI", 256, d), 1.0 / 32, OP.mult)
         parts("KS" if d != r else "KL", d, x)
 
     def pays(d):
-        x = A("P%d" % (d // 2), 256 * (d % 2), 256 * (d % 2) + 256)
+        x = blk("P%d" % (d // 2), 256, d % 2)
         ts(x, x, 1.0 / 64, OP.add, 1.0 / 64, OP.min)
         tt(x, x, blk("TPI", 256, d), OP.mult)
         parts("PS" if d != r else "PL", d, x)
@@ -414,9 +431,6 @@ def rank_program(g, core, T, topo):
     keys(r)
     pays(r)
     del gate[:]
-    sent = send("D")
-    arrive("drawn", 3 * off, [piece("DL", s, 0, DW) for s in others], sent, LATE[1])
-    dma("y", [(A("LN", 256, 640), whole("DL"))], 1.8)
     for k, s in enumerate([peer] + cross):
         arrive("k%d" % s, off, [blk("KL", 512, s)], sentK, LATE[1] if k else 0.5)
         arrive("p%d" % s, off, [blk("PL", 512, s)], sentP, LATE[1])
@@ -440,31 +454,29 @@ def rank_program(g, core, T, topo):
     ts(BO, A("MG"), PG, OP.is_equal)
     ts(f(0), A("MG"), PG, OP.not_equal, 32.0, OP.mult)
     tt(CODE, f(0), A("MI"), OP.add)
-    WTS = [1.0, 2048.0, -2048.0, 1024.0, 2.0]
-    for k, w in enumerate(WTS):
-        act(blk("BOh", 128, k), BO, scale=w)
     mid = [(512.0 * u + _high(u) + 512) / 2 for u in range(N)]
     bit = [((512 * u) // 1024, (_high(u) - 2048) // 1024) for u in range(N)]
     rest = [1024.0 * mid[u] - (2.0 ** 20 - 1) * bit[u][0] + 1 for u in range(N)]
-    MID, NEG, FK, FP = [A("PK", k, k + 1) for k in range(4)]
+    MID, NEG = A("PK", 0, 1), A("PK", 1, 2)
+    ts(A("PK", 8, 8 + N), A("IOTA", 0, N), PU, OP.is_equal)
     for u in range(N):
-        d = bit[u][1] - bit[u][0]
-        for k, x in enumerate((mid[u], -mid[u], BIG - mid[u], BIG - rest[u], -2.0 ** 21 - 2.0 ** 20 * d, float(d))):
-            ms(A("PK", k, k + 1, p0=32 * u, p=32), x)
-    for k in range(2):
-        act(blk("BOh", 128, 5 + k), BO, scale=A("PK", 4 + k, 5 + k))
-
-    def BOh(w):
-        return blk("BOh", 128, WTS.index(w))
+        ms(A("PK", 0, 1, p0=32 * u, p=32), mid[u])
+    act(NEG, MID, scale=-1.0)
 
     def tb(k):
         return blk("TB", 128, k)
     ts(A("S16"), A("IOTA", 0, 16), PI, OP.is_equal, 64.0, OP.mult)
     for k in range(16):
         act(blk("SEL", 128, k), BO, scale=A("S16", k, k + 1))
-    gate.append(sent)
+    gate.append(sentP)
     iota(A("C128"), [[0, 1024]], 128)
     for k in range(16):
+        gate[:] = [len(ops) - 1]
+        if k == 2:
+            sent = send("D")
+            arrive("drawn", 3 * off, [piece("DL", s, 0, DW) for s in others], sent, LATE[1] + 4.0)
+            dma("y", [(A("LN", 256, 640), whole("DL"))], 1.8)
+            gate[:] = [sent]
         run("g", [blk("REDb", 128, k)], [BO], lambda k=k: g.affine_select(blk("REDb", 128, k)[0], BO[0], [[0, 8], [1, 16]], OP.is_equal, 0.0, -k, 0),
             0.17 + 256 * CYC)
     iota(A("NE"), [[0, 582]], 0)
@@ -485,33 +497,24 @@ def rank_program(g, core, T, topo):
             else:
                 act(A(n, a, a + 512), A(P), bias=c, scale=w)
             banks[0] += 1
-    for s in [r, peer]:
-        table("KT", "KL", s, 32.0, 0.0)
-        table("PT", "PL", s, 64.0, 1.0)
-    for s in cross:
-        table("KT", "KL", s, 32.0, 0.0)
-    for s in cross:
-        table("PT", "PL", s, 64.0, 1.0)
+    for n, s in [("K", r), ("K", peer), ("P", r), ("K", cross[0]), ("K", cross[1]), ("P", peer), ("P", cross[0]), ("P", cross[1])]:
+        table(n + "T", n + "L", s, 32.0 if n == "K" else 64.0, 0.0 if n == "K" else 1.0)
     ts(Ib, CODE, PI, OP.is_equal)
     act(If, Ib)
     ts(tb(0), CODE, PI, OP.is_lt, -1.0, OP.mult)
     act(tb(1), Ib, scale=-2048.0)
     tt(XM, tb(0), tb(1), OP.add)
-    act(tb(2), Ib, scale=2.0)
-    tt(tb(3), tb(0), BO, OP.add)
-    tt(tb(4), tb(2), tb(3), OP.subtract)
-    act(A("EMB"), tb(4), scale=BIG)
     cp(tb(6), z(1))
     for s in range(N):
         ts(blk("MVb", 128, s), tb(6), 32.0 * s, OP.add, PP, OP.is_equal)
-    act(A("MVf"), A("MVb"))
+    act(A("MVf"), blk("MVb", 128, r))
     ts(z(2), A("MG"), 1, OP.bitwise_and)
     ts(A("FO"), z(2), PF, OP.is_equal)
     ms(A("RS4"), 1.0)
     ms(A("RS4", 0, 512, 128), 0.0)
     ms(A("OB"), 0.0)
     for d in range(N):
-        act(blk("OS", OW, d, 272), A("IOTA", 0, 8), scale=0.0)
+        ms(blk("OS", OW, d, 272), 0.0)
     ts(pi(5), pi(0), 7, OP.bitwise_and)
     ts(pi(6), pi(0), 3, OP.arith_shift_right, 1, OP.bitwise_and)
     tt(pc(4), pi(5), pi(4), OP.subtract)
@@ -523,14 +526,17 @@ def rank_program(g, core, T, topo):
     tt(pc(8), pc(7), pc(5), OP.add)
     ts(A("PERM"), A("IOTA", 0, 8), 2.0, OP.mult, pc(8), OP.add)
     ts(A("GS", 0, 8), A("IOTA", 0, 8), PG, OP.is_equal, 32.0, OP.mult)
+    iota(A("CT", 64, 96), [[2, N], [0, N], [1, 2]], 0)
+    ts(A("GB"), A("CT", 64, 96), PG, OP.is_equal, 32.0, OP.mult)
     ts(pc(9), PF, 4.0, OP.mult, PU, OP.add)
     ts(A("GS", 8, 16), A("IOTA", 0, 8), pc(9), OP.is_equal)
     act(B15, A("S16", 15, 16), scale=64.0)
     C0, C1 = pc(14), pc(15)
     act(C0, PU, scale=2.0)
     act(C1, PU, bias=1.0, scale=2.0)
-    act(A("KR"), A("IOTA", 0, 96), bias=95.0, scale=-1.0)
-    act(A("KX"), A("IOTA", 0, 96), bias=95.0 - 2047.0, scale=-1.0)
+    KR, KX = A("KR", 0, 96), A("KR", 96, 192)
+    act(KR, A("IOTA", 0, 96), bias=95.0, scale=-1.0)
+    act(KX, A("IOTA", 0, 96), bias=95.0 - 2047.0, scale=-1.0)
     act(A("CT", 0, 16), A("IOTA", 0, 16), bias=PI, scale=16.0)
     act(A("CT", 16, 22), A("CT", 0, 6), bias=95.5, scale=-1.0)
     act(pc(18), PU, bias=4096.0, scale=96.0)
@@ -543,35 +549,64 @@ def rank_program(g, core, T, topo):
     ts(pi(9), pi(0), 31, OP.bitwise_and)
     cp(pc(17), pi(9))
     ts(A("AM"), tb(6), pc(17), OP.is_equal)
-    act(A("CT", 48, 54), A("CT", 0, 6), bias=0.5)
+    for u in range(N):
+        ms(A("RX", 48 + 6 * u, 54 + 6 * u), mid[u])
+    rise = [float(b - a) for a, b in bit]
+    for u in range(N):
+        act(blk("SUM", 128, u), A("FO"), scale=A("PK", 8 + u, 9 + u))
+    up, down = 8 + rise.index(1.0), 8 + rise.index(-1.0)
+    ts(A("PK", 2, 3), A("PK", down, down + 1), A("PK", up, up + 1), OP.subtract)
+    ts(A("PK", 3, 4), A("PK", 2, 3), -2.0 ** 20, OP.mult, 2.0 ** 21, OP.add)
+    for k, w in enumerate((2048.0, 2.0, 1024.0, A("PK", 2, 3), A("PK", 3, 4))):
+        act(blk("SUM", 512, k + 1), blk("SUM", 512, 0), scale=w)
+
+    def SUM(u, k):
+        return blk("SUM", 128, N * k + u)
+    ts(tb(2), A("MI"), PI, OP.is_ge, -BIG, OP.mult)
+    ts(tb(3), A("MI"), PI, OP.is_equal, 2 * BIG, OP.mult)
+    tt(tb(4), tb(2), tb(3), OP.add)
+    tt(tb(2), tb(4), A("FO"), OP.mult)
+    for u in range(N):
+        act(blk("EMB", 128, u), tb(2), scale=A("PK", 8 + u, 9 + u))
+    for u in range(N):
+        for k, x in enumerate((mid[u], rest[u] - rest[u] % 1024, rest[u] % 1024)):
+            ms(A("LV", 384 * k + 96 * u, 384 * k + 96 * u + 96), x)
+    newkey = [[(SUM(u, 1), A("ME")), (SUM(u, 0), A("MH")), (SUM(u, 1), A("MB"))] for u in range(N)]
+    newpay = [[(SUM(u, 2), A("ME")), (SUM(u, 3), A("MH")), (SUM(u, 5), A("MB"))] + ([(SUM(u, 4), A("MB"))] if rise[u] else []) for u in range(N)]
     for m in range(6):
-        act(blk("KP", 97, m), A("IOTA", 0, 97), AF.Sign, A("CT", 48 + m, 49 + m), -1.0)
+        ts(blk("KP", 97, m), A("IOTA", 0, 97), A("CT", m, m + 1), OP.is_le)
     for k, x in enumerate((0.0, 0.0, 0.0, 2048.0)):
         act(blk("XO", 2, k), A("CT", 0, 2), bias=x)
-    act(pc(19), PU, scale=256.0)
-    act(pc(20), PU, AF.Sign, -1.5)
-    act(pc(21), PI, bias=C0, scale=8.0)
-    act(A("CT", 32, 40), A("IOTA", 0, 8), bias=pc(21), scale=128.0)
+    gate.append(sent)
+    iota(A("OF", 0, 64), [[512, N], [16, 16]], 0)
     for d in range(N):
-        step = float(_high(d) - 512 - 512 * d)
-        act(pc(22 + d), pc(20), bias=512.0 * d + step / 2, scale=step / 2)
-        act(pc(26 + d), pc(22 + d), bias=pc(19))
-        act(blk("OF", 16, d), A("CT", 0, 16), bias=pc(26 + d))
-        for h in range(2):
-            for x in range(2):
-                a = 64 + 16 * d + 8 * h + 4 * x
-                act(A("OF", a, a + 4), A("CT", 32 + 4 * x, 36 + 4 * x), bias=512.0 * d + h + step * x)
-    cp(A("OK"), A("OF", 0, 64))
-    cp(A("OY"), A("OF", 64, 128))
+        iota(blk("OF", 16, N + d), [[1, 2], [_high(d) - 512 * d, 2], [128, 4]], 512 * d)
+    gate.pop()
+    ts(pc(20), PU, 2.0, OP.is_ge)
+    ts(pc(19), PU, 256.0, OP.mult, PI, OP.add)
+    for k, ds in enumerate(([0], [1, 2, 3])):
+        ts(pc(22 + k), pc(20), float(_high(ds[0]) - 512 - 512 * ds[0]), OP.mult, pc(19), OP.add)
+        ts(A("OK", 16 * ds[0], 16 * ds[-1] + 16), A("OF", 16 * ds[0], 16 * ds[-1] + 16), pc(22 + k), OP.add)
+    ts(pc(21), PI, 8.0, OP.mult, C0, OP.add)
+    ts(A("OY"), A("OF", 64, 128), pc(21), OP.add)
 
-    KEY, IMG, HI = A("KB"), A("IMG"), A("HI")
+    KEY, IMG, HI = A("KB"), v(3), A("HI")
     KW, PW = A("KT", 0, 4096), A("PT", 0, 4096)
+    OLD, WAITS = A("FL", 0, 128), A("FL", 128, 256)
+    scaled = {}
+
+    def ID(w):
+        if w not in scaled:
+            scaled[w] = blk("IDS", 128, len(scaled))
+            ts(scaled[w], Ib, w, OP.mult)
+        return scaled[w]
+    cp(A("DF"), A("LN", 256, 640))
 
     def NV(k):
         return A("NN", k, k + 1)
 
     def prep(t):
-        ts(A("K2"), KEY, 2048.0, OP.add)
+        ts(A("K2"), KEY, 2048.0 - LIFT * t, OP.add)
         ts(A("Z2"), A("K2"), 4095, OP.bitwise_and)
         ts(HI, A("K2"), 2047, OP.bitwise_and)
         ts(A("E1"), A("K2"), 11, OP.arith_shift_right)
@@ -583,8 +618,9 @@ def rank_program(g, core, T, topo):
         cp(A("OFF"), X(A("YT"), A("PERM")))
         ts(A("EH", 0, 128), A("E1"), -1.0, OP.add, 32.0, OP.mult)
         ts(A("EH", 128, 256), HI, 1.0 / 64, OP.mult)
-        tt(v(0), A("Z2"), IMG, OP.is_le)
+        tt(v(0), IMG, A("Z2"), OP.is_ge)
         tt(A("TO", 0, 128), A("Q"), v(0), OP.add)
+        cp(OLD, v(0))
         act(A("TO", 128, 256), A("TO", 0, 128), AF.Abs, -2.0)
         ts(A("OG", 0, 128), A("TO", 128, 256), 2.0, OP.is_equal)
         for d in range(1, 4):
@@ -593,14 +629,7 @@ def rank_program(g, core, T, topo):
         mm(A("P6"), [(BO, A("IG")), (XM, A("OG"))])
         act(A("GOB"), A("P6"), AF.Sign, -1407.5, -1.0)
         mm(A("P4", 128, 256), [(Ib, blk("GOB", 128, d)) for d in range(4)])
-        act(A("GO"), A("P4", 128, 256), bias=2.0, scale=0.5)
-        act(f(2), A("P4", 128, 256), bias=-128.0, scale=-32.0)
-        ts(v(1), A("Q"), 3.0, OP.mult, 64.0, OP.add)
-        tt(v(1), v(1), A("TO", 0, 128), OP.subtract)
-        tt(v(1), v(1), f(2), OP.add)
-        tt(v(0), A("LN", 256 + 128 * t, 384 + 128 * t), KEY, OP.subtract)
-        tt(v(0), v(0), A("GO"), OP.mult)
-        tt(f(3), v(0), KEY, OP.add)
+        act(WAITS, A("P4", 128, 256), bias=-1.0, scale=-0.5)
         for s in range(N):
             mm(blk("P6", 128, s), [(blk("MVb", 128, s), blk("EH", 128, 0))])
         act(blk("EM", 512, t % 2), A("P6"), scale=1.0 / 32)
@@ -611,27 +640,24 @@ def rank_program(g, core, T, topo):
 
     def split(t):
         n = NV(t)
-        ts(A("SG", 0, 2), A("XO", 0, 2), n, OP.add, 2047.0, OP.min)
-        ts(A("SG", 2, 4), A("XO", 0, 2), n, OP.add, 2047.0, OP.min)
+        ts(A("SG"), A("XO", 0, 4), n, OP.add, 2047.0, OP.min)
         act(A("SX", 0, 8), A("XO"), bias=n)
         ts(A("SX", 8, 12), A("SX", 0, 4), NV(t + 1), OP.is_ge, 4096.0, OP.mult)
         tt(A("SX", 12, 16), A("SX", 8, 12), A("SX", 4, 8), OP.add)
         cp(A("SO"), A("SX", 12, 16))
         cp(A("SI", 0, 32), X(KW, A("SG", 0, 2)))
-        act(A("SK", 64, 128), X(KW, A("SG")), bias=1.0)
-        act(A("SK", 128, 192), X(PW, A("SG")), bias=-1.0)
         ts(A("SI", 32, 64), A("SI", 0, 32), 0x200800, OP.bitwise_and)
-        ts(A("SK", 0, 32), A("SI", 32, 64), 2048.0, OP.not_equal)
-        ts(A("SK", 32, 64), A("SI", 32, 64), 2048.0, OP.is_equal)
-        tt(A("SK", 192, 256), A("SK", 0, 64), A("SK", 64, 128), OP.mult)
-        ts(X(A("KT"), A("SO")), A("SK", 192, 256), 1.0, OP.mult, -1.0, OP.add)
-        tt(A("SK", 256, 320), A("SK", 0, 64), A("SK", 128, 192), OP.mult)
-        ts(X(A("PT"), A("SO")), A("SK", 256, 320), 1.0, OP.mult, 1.0, OP.add)
+        for k in range(3):
+            ts(blk("SK", 32, k), A("SI", 32, 64), 2048.0, (OP.not_equal, OP.is_equal)[k % 2])
+        tt(A("SK", 128, 192), X(KW, A("SG")), A("SK", 0, 64), OP.mult)
+        tt(X(A("KT"), A("SO")), A("SK", 128, 192), A("SK", 32, 96), OP.subtract)
+        tt(A("SK", 192, 256), X(PW, A("SG")), A("SK", 0, 64), OP.mult)
+        tt(X(A("PT"), A("SO")), A("SK", 192, 256), A("SK", 32, 96), OP.add)
 
     cp(KEY, A("LN", 0, 128))
     ts(IMG, A("LN", 128, 256), -1.0, OP.add)
     cp(NV(12), A("PNI", 0, 1))
-    mm(A("P6", 0, 1), [(blk("MVf", 128, r), NV(12))])
+    mm(A("P6", 0, 1), [(A("MVf"), NV(12))])
     act(NV(0), A("P6", 0, 1))
     prep(0)
     for c in range(4):
@@ -641,24 +667,32 @@ def rank_program(g, core, T, topo):
         last = t == RO - 1
         n = NV(t)
         for c in range(4):
-            a, b, o, P = 512 * c, 512 * c + 512, A("OFF", 32 * c, 32 * c + 32), "P%d" % c
-            act(A("W1", a, b), X(KW, o))
-            if c < MIX:
-                tt(A("W2", a, b), A("W1", a, b), A(P), OP.is_equal)
-                tt(A("W3", a, b), X(PW, o), A("W2", a, b), OP.mult)
-            else:
-                act(A("W2", a, b), X(PW, o))
-                tt(A(P), A("W1", a, b), A(P), OP.is_equal)
-                for h in range(2):
-                    tt(A("W3", a + 256 * h, a + 256 * h + 256), A("W2", a + 256 * h, a + 256 * h + 256), A(P, 256 * h, 256 * h + 256), OP.mult)
+            act(blk("W1", 512, c), X(KW, blk("OFF", 32, c)))
+            if c == 3:
+                ts(A("NW"), A("Z2"), n, OP.is_lt, 32.0, OP.mult)
+                ts(NV(10), n, 1536.0, OP.min)
+                ts(A("FL", 256, 384), A("Z2"), NV(10), OP.is_lt)
+                gate.extend([len(ops) - 1, len(ops) - 3])
+                mm(A("P6", 0, 128), [(ID(2.0), A("TO", 0, 128)), (ID(-3.0), OLD), (ID(64.0), WAITS), (ID(-5.0 / 32), A("NW")), (ID(8.0), A("FL", 256, 384))])
+                mm(A("P6", 128, 256), [(ID(64.0), blk("EH", 128, 1)), (ID(128.0), A("NW")), (ID(-4096.0), OLD), (ID(-4096.0), WAITS)])
+                act(A("CM"), A("P6", 0, 128))
+                act(f(5), A("P6", 128, 256), bias=-4096.0)
+            tt(blk("EQ", 512, c), blk("W1", 512, c), A("P%d" % c), OP.is_equal)
+            del gate[:]
+            for k in range(4 * c, 4 * c + 4):
+                mm(A("P4", k, 512, 16), [(blk("EQ", 128, k), A("GB"))])
+        for h in range(2):
+            act(blk("TF", 256, h), blk("P4", 256, h))
+        for c in range(4):
+            tt(blk("W3", 512, c), X(PW, blk("OFF", 32, c)), blk("EQ", 512, c), OP.mult)
             for k in range(4 * c, 4 * c + 4):
                 mm(A("P4", k, 128, 16), [(blk("W3", 128, k), A("GS", 0, 8))])
         act(A("TS"), A("P4", 0, 128))
-        mm(A("P5", 0, 128), [(A("TS"), If)])
-        ts(f(0), A("Z2"), n, OP.is_lt, 3.0, OP.mult)
-        tt(z(2), f(0), v(1), OP.add)
-        ts(A("CLS"), z(2), 71, OP.bitwise_and)
-        ts(A("NW"), A("Z2"), n, OP.is_lt, 32.0, OP.mult)
+        mm(A("P5", 128, 256), [(If, blk("DF", 128, t)), (ID(-LIFT), WAITS)])
+        act(f(2), A("P5", 128, 256), bias=LIFT * (t + 1))
+        mm(A("P5", 256, 384), [(If, KEY), (ID(LIFT), WAITS)])
+        tt(f(3), A("P5", 256, 384), f(2), OP.max)
+        mm(A("P5", 0, 128), [(A("TS"), If), (ID(-32 * LIFT), WAITS)])
         for s in range(N):
             mm(blk("P6", 128, s), [(blk("MVb", 128, s), blk("EH", 128, 1)), (blk("MVb", 128, s), A("NW"))])
         act(A("HM"), A("P6"), bias=NEG, scale=64.0)
@@ -666,96 +700,81 @@ def rank_program(g, core, T, topo):
         tt(NV(9), NV(8), n, OP.subtract)
         if t:
             split(t - 1)
-        tt(A("CM"), A("P5", 0, 128), A("CLS"), OP.add)
         for s in range(N):
-            mm(blk("P0", 128, s), [(blk("MVb", 128, s), A("CM"))])
-        tt(f(1), A("P5", 0, 128), A("GO"), OP.mult)
-        ts(A("OH", 0, 512), A("P0"), C0, OP.is_equal)
-        ts(A("OH", 512, 1024), A("P0"), C1, OP.is_equal)
+            mm(blk("P%d" % (s // 2), 128, s % 2), [(blk("MVb", 128, s), A("CM")), (blk("TF", 128, s), Ib)])
+        act(A("PB"), A("P1", 0, 256))
+        for h, x in enumerate((A("P0", 0, 256), A("PB"))):
+            for k, c in enumerate((C0, C1)):
+                ts(blk("OH", 256, 2 * k + h), x, c, OP.is_equal)
         scan(A("INC"), A("OH"), A("C128"), 0.0, OP.add, OP.min)
         mm(A("P1", 0, 64), [(BO, A("INC", 15, 1024, 16))])
         mm(A("P2", 0, 64), red("REDb", "INC", 0, 1024))
         for m in range(6):
             act(blk("JK", 64, m, 0, 63), A("P1", 0, 63), AF.Sign, A("CT", 16 + m, 17 + m), -1.0, acc=A("AC", m, m + 1))
         act(A("E2"), A("P2", 0, 64), bias=B15)
+        for h, P in enumerate(("P0", "P3")):
+            mm(A(P), [(BO, blk("INC", 512, h)), (XM, blk("OH", 512, h))])
+            act(blk("XS", 512, h), A(P))
         AC = A("AC", 0, 6)
         ts(A("O1", 0, 6), AC, 0.5, OP.mult, 31.5, OP.add)
         ts(A("VB", 0, 6), AC, 8.0, OP.mult, 504.0, OP.add)
         ts(A("BS", 8, 14), AC, 0.0, OP.is_gt, -512.0, OP.mult)
-        tt(A("C2"), X(A("E2"), A("O1", 0, 6)), A("KR"), OP.is_le)
+        tt(A("C2"), X(A("E2"), A("O1", 0, 6)), KR, OP.is_le)
         mm(A("P1", 64, 70), [(Ib, A("VB", 0, 6))] + red("REDb", "C2", 0, 96))
-        cp(A("O2", 0, 6), A("P1", 64, 70))
+        cp(A("O1", 8, 14), A("P1", 64, 70))
         tt(A("BS", 16, 22), A("P1", 64, 70), A("BS", 8, 14), OP.add)
-        cp(A("G2", 0, 96), X(A("INC"), A("O2", 0, 6)))
-        act(A("G2", 96, 192), X(A("OH"), A("O2", 0, 6)))
+        tt(A("MK"), X(A("XS"), A("O1", 8, 14)), KX, OP.is_equal)
         cp(A("O3", 0, 6), A("BS", 16, 22))
-        mm(A("P3", 0, 96), [(BO, A("G2", 0, 96)), (XM, A("G2", 96, 192))])
-        act(A("G3", 0, 96), X(A("HM"), A("O3", 0, 6)))
-        act(A("G3", 96, 192), X(blk("EM", 512, t % 2), A("O3", 0, 6)))
-        tt(A("P3", 0, 96), A("P3", 0, 96), A("KX"), OP.is_equal)
-        tt(A("MH"), A("P3", 0, 96), A("G3", 0, 96), OP.mult)
-        tt(A("ME"), A("P3", 0, 96), A("G3", 96, 192), OP.mult)
-        ts(z(3), A("CLS"), 65, OP.bitwise_and)
-        ts(v(3), z(3), 1.0, OP.not_equal, -4096.0, OP.mult)
-        tt(v(3), v(3), HI, OP.add)
-        tt(IMG, v(3), IMG, OP.max)
-        ts(v(2), f(1), 0.0, OP.is_gt, -BIG, OP.mult)
-        act(f(4), f(1), bias=-1.0, scale=1.0 / 32)
+        tt(A("MH"), X(A("HM"), A("O3", 0, 6)), A("MK"), OP.mult)
+        tt(A("ME"), X(blk("EM", 512, t % 2), A("O3", 0, 6)), A("MK"), OP.mult)
+        tt(IMG, IMG, f(5), OP.max)
+        act(f(4), A("P5", 0, 128), bias=LIFT * (t + 1) - 1.0, scale=1.0 / 32)
+        ts(v(2), A("P5", 0, 128), 0.0, OP.is_gt, -LIFT, OP.mult)
         tt(v(2), v(2), f(3), OP.add)
         tt(KEY, v(2), f(4), OP.max)
         if last:
-            act(A("YI"), IMG, bias=1.0)
+            ts(A("YI"), IMG, 1.0, OP.add)
+            act(KEY, KEY, bias=-LIFT * RO)
             dma("y", [(whole("YS%d" % h), A(x)) for h, x in enumerate(("KB", "YI"))], 2.0)
             dma("y", [(piece("YL%d" % h, r, 0, LW), A(x, p0=32 * r, p=32)) for h, x in enumerate(("KB", "YI"))], 2.0)
             sent = send("Y")
-            arrive("ylan", 3 * off, [piece("YL%d" % h, s, 0, LW) for s in others for h in range(2)], sent, 3.0)
+            arrive("ylan", 5 * off + off // 2, [piece("YL%d" % h, s, 0, LW) for s in others for h in range(2)], sent, 3.0)
             dma("y", [(x[:], whole("YL%d" % h)) for h, x in enumerate((T.yl, T.yi))], 2.0)
         else:
             prep(t + 1)
         mm(A("P1", 80, 86), red("REDb", "MH", 0, 96))
         ms(A("P0", 96, 97), 0.0)
-        mm(A("P0", 0, 96), [(BOh(1.0), A("MH"))])
+        mm(A("P0", 0, 96), [(BO, A("MH"))])
         O4 = A("O4", 0, 6)
         ts(O4, A("P1", 80, 86), MID, OP.add)
-        cp(A("BS", 0, 6), A("P1", 80, 86))
+        cp(A("BH", 0, 6), A("P1", 80, 86))
         tt(A("BS", 48, 54), A("P1", 80, 86), A("CT", 56, 62), OP.add)
         act(A("EE"), X(KW, O4), AF.Relu, 0.0, -1.0)
-        ts(A("OLD", 0, 96), X(KW, O4), FK, OP.add)
-        act(A("OLD", 96, 192), X(PW, O4), bias=FP)
-        ts(A("MB"), A("MH"), 0.0, OP.is_gt)
-        mm(A("P2", 0, 96), [(BOh(2048.0), A("ME")), (BOh(1.0), A("MH")), (BOh(-2048.0), A("MB")), (A("EMB"), A("EE"))])
-        mm(A("P3", 128, 224), [(BOh(2.0), A("ME")), (BOh(1024.0), A("MH")), (blk("BOh", 128, 5), A("MB")), (blk("BOh", 128, 6), A("MB")), (A("EMB"), A("EE"))])
-        gate.append(len(ops) - 1)
-        tt(A("NEW", 0, 96), A("P2", 0, 96), A("OLD", 0, 96), OP.max)
-        gate.pop()
-        tt(A("NEW", 96, 192), A("P3", 128, 224), A("OLD", 96, 192), OP.max)
-        ready = len(ops) - 1
-        for s in range(N):
-            mm(blk("P5", 96, s), [(blk("MVf", 128, s), A("NEW", 0, 96))])
-        for s in range(N):
-            act(blk("SC", 96, s), blk("P5", 96, s), bias=mid[s] - BIG)
+        ts(A("MB"), A("MH"), 0.0, OP.is_gt, -1.0, OP.mult)
+        mm(A("P2", 0, 24), [(If, A("RX", 48, 72))] + [(blk("MVb", 128, s), A("BH", 0, 6), blk("P2", 6, s)) for s in range(N)])
+        cp(A("O6"), A("P2", 0, 24))
+        act(A("OLD", 0, 384), X(KW, A("O6")))
+        act(A("OLD", 384, 768), X(PW, A("O6")))
+        for P, terms, c, k in (("P5", newkey, [0], 0), ("P3", newpay, [1, 2], 1)):
+            mm(A(P, 0, 384), [(Ib, blk("LV", 384, x)) for x in c] + [x + (blk(P, 96, s),) for s in range(N) for x in terms[s]], stop=False)
+            mm(A(P, 0, 384), [(blk("EMB", 128, s), A("EE"), blk(P, 96, s)) for s in range(N)], start=False)
+            act(blk("SC", 384, k), A(P, 0, 384), bias=-BIG)
+        mm(A("P4", 0, 6), red("REDb", "EE", 0, 96))
         for m in range(6):
-            ts(blk("NE", 97, m, 16 * m), A("P0", 16 * m, 97), A("BS", m, m + 1), OP.not_equal)
+            ts(blk("NE", 97, m, 16 * m), A("P0", 16 * m, 97), A("P1", 80 + m, 81 + m), OP.not_equal)
         scan(A("SS"), A("NE"), A("KP"), 1.0, OP.min, OP.max)
         TRY = A("SS", 96, 582, 97)
         for s in range(N):
             tt(A("RX", 6 * s, 6 * s + 6, p0=32 * s, p=32), A("BS", 48, 54, p0=32 * s, p=32), A("SS", 96, 582, 97, p0=32 * s, p=32), OP.mult)
         mm(A("P2", 128, 152), [(A("AM"), A("RX", 0, 24)), (If, A("RX", 24, 48))])
         cp(A("O5"), A("P2", 128, 152))
-        gate.append(ready)
-        cp(X(A("KT"), A("O5")), A("SC", 0, 384))
-        gate.pop()
-        for s in range(N):
-            mm(blk("P6", 96, s), [(blk("MVf", 128, s), A("NEW", 96, 192))])
-        for s in range(N):
-            act(blk("SC", 96, N + s), blk("P6", 96, s), bias=rest[s] - BIG)
-        cp(X(A("PT"), A("O5")), A("SC", 384, 768))
-        mm(A("P4", 256, 262), red("REDb", "EE", 0, 96))
-        tt(A("OV", 0, 6), A("P4", 256, 262), TRY, OP.is_lt)
-        mm(A("P4", 272, 278), [(A("FO"), A("OV", 0, 6))])
-        act(A("TT", 0, 6), A("P4", 272, 278), acc=NV(10))
-        act(NV(11), NV(10), AF.Relu, NV(9), -1.0)
-        act(NV(t + 1), NV(11), AF.Identity, NV(8), -1.0)
+        tt(A("OV", 0, 6), A("P4", 0, 6), TRY, OP.is_lt)
+        mm(A("P4", 16, 17), [(A("FO"), A("OV", m, m + 1)) for m in range(6)])
+        ts(NV(t + 1), A("P4", 16, 17), NV(9), OP.min, n, OP.add)
+        gate.extend([len(ops) - 1] if last else [])
+        tt(X(A("KT"), A("O5")), A("OLD", 0, 384), A("SC", 0, 384), OP.max)
+        del gate[:]
+        tt(X(A("PT"), A("O5")), A("OLD", 384, 768), A("SC", 384, 768), OP.max)
         if not last:
             for c in range(4):
                 spread(c)
@@ -777,12 +796,12 @@ def rank_program(g, core, T, topo):
         for h in range(2):
             mm(A(P, h, 16, 2), [(blk("YP", 256, d, 128 * h, 128 * h + 128), A("GS", 8, 16))])
         cp(blk("OS", OW, d, 256, 272), A(P, 0, 16))
-        cp(blk("OS", OW, d, 272, 273), NV(RO))
+        act(blk("OS", OW, d, 272, 273), NV(RO))
         if d != r:
             sent = send("O%d" % k)
     dma("y", [(T.yk[32 * r:32 * r + 32, 512 * h:512 * h + 512], A("KT", a, a + 512, p=32)) for h, a in enumerate((512 * r, _high(r)))], 2.5)
     stores("sy", r, "OS")
-    for k, s in enumerate([peer] + cross):
-        arrive("o%d" % s, 2 * off, [blk("OL", OW, s)], sent, 2.0 + k)
+    for k, s in enumerate(cross + [peer]):
+        arrive("o%d" % s, 2 * off, [blk("OL", OW, s)], sent, 0.5 + 0.5 * k)
         stores(("sy", "ys")[k % 2], s, "OL")
     _issue(T, Q, ops)

@@ -6,6 +6,11 @@ LW, DW, OW = 32, 96, 280
 TW = 8256
 BIG, LIFT = float(2 ** 22), float(2 ** 21)
 F, H, B, I, U = "float32", "float16", "bfloat16", "int32", "uint16"
+OPT = {"ehs": 1, "emd": 0, "ohs": 0, "fuse": [(), (), ()], "wheel": 2500, "wcase": 0, "wheat": 0.3, "wmoves": 1, "ll": 2.6, "lk": 3.5, "lp": 4.5, "tabs": 4.0, "kh": 0, "kp": 0, "pp": 1, "oh": 0, "op": 0, "oss": (), "loads": (None, None, None), "by": ("sv", "sv", "sv", "vv", "vv"), "early": 6.0, "gob": "P4", "tail": 11.0, "period": 13.2, "plate": 1, "eq": (2.2, 3.4, 3.85, 4.4), "oh0": 6.3,
+       "w3": (2.7, 4.85, 5.55, 7.45), "vbs": 0, "cut": 0.0, "tf": 1, "ppe": "", "pt0": 2.3, "pt1": 0.25, "w30": (5.0, 5.7, 7.45, 8.2), "ins": 10.9, "ws": (4.6, 5.95, 6.4, 8.5), "pg": 9, "mean": 0.0, "pb": "56", "ids": 3, "selg": 16, "dat": 1.0, "made": "", "e2": "P4", "ig": 12.45, "k2": 10.45, "shake": 0.3, "turns": 1, "steps": 6000, "heat": 0.1,
+       "fuse": [(0,), (0, 1), (0, 1)], "eq": (1.4, 2.1, 2.85, 3.3), "w3": (4.95, 5.65, 7.45, 8.2), "ws": (5.95, 6.4, 8.3, 8.9), "cut": 1.1, "oh": 1,
+       "by": ("vs", "sv", "sv", "vv", "vs"), "pg": 11, "pt0": 1.5, "lp": 4.5, "scv": 0, "tiny": 64, "tiny0": 128, "made": "", "share": 1.0, "loads": (None, 4, 7), "jk": 0, "seed": 5, "ids": 10,
+       "wheel": 3000, "steps": 12000}
 
 
 def _sb(w, d):
@@ -20,35 +25,39 @@ SCRATCH = {
     "KT": _sb(TW, F), "PT": _sb(TW, F), "TKI": _sb(1024, I), "TPI": _sb(1024, I), "KS": _sb(2048, H), "PS": _sb(2048, H),
     "KL": _sb(2048, H), "PL": _sb(2048, H), "DS": _dr(DW, I), "DL": _dr(DW, I), "QM": _sb(512, B),
     "LS0": _dr(LW, I), "LL0": _dr(LW, I), "LS1": _dr(LW, I), "LL1": _dr(LW, I), "LN": _sb(640, I), "PNI": _sb(4, I),
-    "YS0": _dr(LW, F), "YL0": _dr(LW, F), "YS1": _dr(LW, F), "YL1": _dr(LW, F), "OF": _sb(128, F),
+    "YS0": _dr(LW, F), "YL0": _dr(LW, F), "YS1": _dr(LW, F), "YL1": _dr(LW, F), "OF": _sb(192, F),
     "OS": _sb(N * OW, F), "OL": _sb(N * OW, F), "YP": _sb(1024, F), "YI": _sb(128, F),
     "W1": _sb(2048, F), "EQ": _sb(2048, B), "GB": _sb(32, B), "W3": _sb(2048, F),
     "TM": _sb(128 * 8, F), "TN": _sb(128 * 8, I),
-    "IOTA": _sb(128, F), "PCI": _sb(16, I), "PC": _sb(32, F), "MI": _sb(128, I), "MG": _sb(128, I), "CODE": _sb(128, B),
-    "BOb": _sb(128, B), "SUM": _sb(512 * 6, B), "Ib": _sb(128, B), "If": _sb(128, F), "XM": _sb(128, B), "FO": _sb(128, B),
-    "EMB": _sb(512, B), "SEL": _sb(2048, B), "REDb": _sb(2048, B), "TB": _sb(1024, B),
-    "MVb": _sb(512, B), "MVf": _sb(128, F), "GS": _sb(16, F), "TF": _sb(512, B), "PB": _sb(256, B), "LV": _sb(1152, B),
-    "S16": _sb(16, F), "RS4": _sb(512, B),
-    "C128": _sb(1024, B), "KR": _sb(192, F), "KP": _sb(582, B), "PERM": _sb(8, U), "CT": _sb(96, F),
+    "IOTA": _sb(144, F), "PCI": _sb(16, I), "PC": _sb(32, F), "MI": _sb(128, I), "MG": _sb(128, I),
+    "BOb": _sb(256, B), "SUM": _sb(512 * 2, B), "Ib": _sb(128, B), "If": _sb(128, F), "XM": _sb(128, B), "FO": _sb(128, B),
+    "EMB": _sb(512, B), "SEL": _sb(2048, B), "RED": _sb(144, B), "TB": _sb(1024, B),
+    "MVb": _sb(512, B), "GS": _sb(32, F), "TF": _sb(512, B), "PB": _sb(512, B), "LV": _sb(24, B),
+    "RS4": _sb(512, B),
+    "C128": _sb(1024, B), "KR": _sb(192, F), "KP": _sb(582, B), "PERM": _sb(10, U), "CT": _sb(96, F),
     "XO": _sb(8, F), "OK": _sb(64, U), "OY": _sb(64, U),
-    "KB": _sb(128, F), "OB": _sb(160, F), "YT": _sb(288, F), "K2": _sb(128, I), "Z2": _sb(128, I), "HI": _sb(128, I),
-    "E1": _sb(128, I), "EH": _sb(256, H), "Q": _sb(128, I), "TO": _sb(256, B), "OG": _sb(512, B), "IG": _sb(512, B),
-    "GOB": _sb(512, B), "FL": _sb(384, B), "OFF": _sb(128, U), "IDS": _sb(128 * 10, B), "DF": _sb(384, F),
-    "TS": _sb(128, F), "CM": _sb(128, B),
-    "HM": _sb(512, F), "NW": _sb(128, B), "RX": _sb(72, F), "AM": _sb(128, F), "PK": _sb(16, F), "EM": _sb(1024, F),
-    "OH": _sb(1024, B), "INC": _sb(1024, B), "E2": _sb(64, F), "JK": _sb(384, B),
-    "AC": _sb(8, F), "VB": _sb(8, B), "C2": _sb(96, B), "XS": _sb(1024, F), "MK": _sb(96, F), "MH": _sb(96, H), "ME": _sb(96, H),
-    "MB": _sb(96, H), "O1": _sb(16, U), "O3": _sb(8, U), "O4": _sb(8, U), "O5": _sb(24, U), "BS": _sb(64, F),
+    "KB": _sb(128, F), "YT": _sb(288, F), "K2": _sb(128, I), "Z2": _sb(128, I), "HI": _sb(128, I),
+    "E1": _sb(128, I), "EH": _sb(256, H), "TO": _sb(256, B), "OG": _sb(512, B), "IG": _sb(512, B),
+    "GOB": _sb(512, B), "FL": _sb(512, B), "OFF": _sb(128, U), "IDS": _sb(128 * 15, B), "DF": _sb(384, F),
+    "TPF": _sb(1024, F), "SUP": _sb(128 * 10, B), "SN": _sb(256, B),
+    "TS": _sb(128, F), "CM": _sb(128, B), "MVn": _sb(1024, B), "NG": _sb(128, B),
+    "HM": _sb(512, F), "NW": _sb(128, B), "RX": _sb(96, F), "PK": _sb(16, F), "EM": _sb(1024, I if OPT["emd"] else F),
+    "OH": _sb(1024, B), "INC": _sb(1024, B), "E2": _sb(64, F), "JK": _sb(1152, B),
+    "PLC": _sb(384, B), "VB": _sb(8, B), "C2": _sb(96, B), "XS": _sb(1024, F), "MK": _sb(96, F), "MH": _sb(98, H), "ME": _sb(96, H),
+    "MB": _sb(96, H), "O1": _sb(16, U), "O3": _sb(8, U), "O4": _sb(8, U), "O5": _sb(40, U), "BS": _sb(64, F),
     "NE": _sb(582, B), "SS": _sb(582, B), "EE": _sb(96, B), "OLD": _sb(768, F), "O6": _sb(24, U), "SC": _sb(768, F),
-    "OV": _sb(8, B), "BH": _sb(8, H), "NN": _sb(32, F), "SG": _sb(4, U), "SO": _sb(4, U),
+    "OV": _sb(8, B), "BH": _sb(8, H), "NN": _sb(32, F), "SG": _sb(8, U),
     "SX": _sb(64, F), "SI": _sb(64, I), "SK": _sb(320, F),
 }
 for _b in range(8):
     SCRATCH["P%d" % _b] = ("psum", [128, 512], F)
 SEMAPHORES = (["cv", "cs", "ct", "cg", "lan", "drawn", "ylan", "lo"] + [a + "%d" % s for a in "kpo" for s in range(N)]
-              + [a + b for a in "hl" for b in ("L", "K", "P", "D", "Y", "O0", "O1", "O2")] + ["d%d" % i for i in range(40)])
-ROUTES = []
-CYC, PEC, WAKE = 0.87e-3, 0.435e-3, 0.2
+              + [a + b for a in "hl" for b in ("L", "K", "P", "D", "Y", "O0", "O1", "O2", "Kp", "Pp", "O", "Op")] + ["d%d" % i for i in range(48)])
+ROUTES, PLAN = [], []
+CYC = 0.87e-3
+CASES = [{"cycle": 0.83e-3, "v": 0.0, "s": 0.05, "gather": 1.56, "scatter": 3.8, "wake": 0.18, "same": 0.18, "pe_out": 0.03, "pe": 0.55, "dma": 1.0, "weight": 1.0},
+         {"cycle": 1.1e-3, "v": 0.0, "s": 0.14, "gather": 1.9, "scatter": 5.0, "wake": 0.3, "same": 0.3, "pe_out": 0.03, "pe": 0.5, "dma": 1.5, "weight": 0.6},
+         {"cycle": 0.85e-3, "v": 0.0, "s": 0.07, "gather": 1.25, "scatter": 2.6, "wake": 0.27, "same": 0.27, "pe_out": 0.05, "pe": 0.5, "dma": 0.9, "weight": 1.0}]
 LATE = (2.0, 2.3)
 
 
@@ -100,15 +109,42 @@ def _messages(T, topo, routes, s):
     die = [(k + routes[d]["cross"].index(s)) % 2 for k, d in enumerate(cross)]
     here, there = [None] + ro["near"], ro["plain"][:1] + ro["far"]
     call("L", ["LL0", "LL1"], LW, "lan", here, there)
-    call("K", ["KL"], 512, "k%d" % s, [None] + [ro[("near", "far")[die[k]]][0] for k in range(2)])
-    call("P", ["PL"], 512, "p%d" % s, [ro["plain"][0]] + [ro[("far", "near")[die[k]]][1] for k in range(2)])
+    def halves(name, buf, w, sem, way):
+        for k, d in enumerate(cross):
+            for h in range(2):
+                out.append((name, buf, w // 2 * h, w // 2, d, ro[("near", "far")[h]][k], _shares(off + rest, 4)[2 * k + h], sem))
+        if way == 2:
+            for h in range(2):
+                out.append((name + "p", buf, w // 2 * h, w // 2, peer, (None, ro["plain"][0])[h], (off, rest)[h], sem))
+        else:
+            out.append((name + "p", buf, 0, w, peer, ro["plain"][0] if way else None, off + rest if way else off, sem))
+    if OPT["kh"]:
+        halves("K", "KL", 512, "k%d" % s, OPT["kp"])
+        halves("P", "PL", 512, "p%d" % s, OPT["pp"])
+    else:
+        call("K", ["KL"], 512, "k%d" % s, [None] + [ro[("near", "far")[die[k]]][0] for k in range(2)])
+        call("P", ["PL"], 512, "p%d" % s, [ro["plain"][0]] + [ro[("far", "near")[die[k]]][1] for k in range(2)])
     call("D", ["DL"], DW, "drawn", there)
     call("Y", ["YL0", "YL1"], LW, "ylan", here, there)
-    for k, d in enumerate(cross + [peer]):
-        vias = (ro["far"][k], ro["near"][k]) if d != peer else (ro["plain"][0], None)
-        for h in range(2):
-            out.append(("O%d" % k, "OL", OW // 2 * h, OW // 2, d, vias[h], (rest, off)[h], "o%d" % s))
+    if OPT["oh"]:
+        halves("O", "OL", OW, "o%d" % s, OPT["op"])
+    else:
+        for k, d in enumerate(cross + [peer]):
+            vias = (ro["far"][k], ro["near"][k]) if d != peer else (ro["plain"][0], None)
+            for h in range(2):
+                out.append(("O%d" % k, "OL", OW // 2 * h, OW // 2, d, vias[h], (rest, off)[h], "o%d" % s))
     return out
+
+
+def _landing(T, topo, routes, r, sem):
+    R = list(T.cores)
+    total = 0
+    for s in range(N):
+        mine = _messages(T, topo, routes, s)
+        for n, buf, a, w, d, via, e, x in mine:
+            if d == r and x == sem:
+                total += len(e) if via is None else len(topo.engines(via, R[r])) // len([m for m in mine if m[0] == n and m[5] == via])
+    return total
 
 
 def _slot(buf, k, a, w):
@@ -142,66 +178,229 @@ def helper_program(g, core, T, topo, routes):
 
 
 def _order(ops):
+    if OPT.get("cases"):
+        CASES[:] = OPT["cases"]
     n = len(ops)
-    pred = [[(j, ops[j]["cost"] + WAKE) for j in o["dep"]] + [(j, ops[j]["cost" if o["q"] == "a" else "busy"]) for j in o["after"]] for o in ops]
-    succ = [[] for o in ops]
-    for i in range(n):
-        for j, lag in pred[i]:
-            succ[j].append((i, lag))
+    qs = [o["q"] for o in ops]
+    banks = [o["banks"] for o in ops]
+    cases = []
+    for c in CASES:
+        cost = [_cost(o["q"], o["cost"], c) for o in ops]
+        busy = [cost[i] if o["busy"] is None else o["busy"] for i, o in enumerate(ops)]
+        done = [cost[i] + (c["pe_out"] if qs[i] == "t" else 0.0) for i in range(n)]
+        pred = [[(j, done[j] + (c["same"] if qs[j] == qs[i] else c["wake"])) for j in o["dep"]]
+                + [(j, cost[j] if qs[i] == "a" else busy[j]) for j in o["after"]] for i, o in enumerate(ops)]
+        succ = [[] for o in ops]
+        for i in range(n):
+            for j, lag in pred[i]:
+                succ[j].append((i, lag))
+        cases.append((cost, busy, done, pred, succ, c["wake"]))
 
-    def pack(key, back):
+    def gap(spans, t, w, pad, q):
+        x = max(0, len(spans) - 1)
+        while x and spans[x - 1][1] + pad > t:
+            x -= 1
+        for a, b, p in spans[x:]:
+            if p == q and pad:
+                continue
+            if b + pad <= t:
+                continue
+            if t + w + pad <= a + 1e-9:
+                break
+            t = b + pad
+        return t
+
+    def put(spans, span):
+        x = len(spans)
+        while x and spans[x - 1] > span:
+            x -= 1
+        spans.insert(x, span)
+
+    def pack(case, key, back):
+        cost, busy, done, pred, succ, wake = case
         before, behind = (succ, pred) if back else (pred, succ)
         left = [len(x) for x in before]
         at = [0.0] * n
         spans = {}
         pool = [i for i in range(n) if not left[i]]
         while pool:
-            i = min(pool, key=lambda k: (key[k], k))
+            i = min(pool, key=key.get)
             pool.remove(i)
-            o = ops[i]
             if back:
-                t = max([o["cost"]] + [at[k] + lag for k, lag in succ[i]]) - o["busy"]
+                t = max([cost[i]] + [at[k] + lag for k, lag in succ[i]]) - busy[i]
             else:
                 t = max([0.0] + [at[j] + lag for j, lag in pred[i]])
-            if o["q"] != "a":
-                busy = spans.setdefault(o["q"], [])
-                x = 0
-                for x, (a, b) in enumerate(busy + [(1e9, 1e9)]):
-                    if b <= t:
-                        continue
-                    if t + o["busy"] <= a + 1e-9:
+            if qs[i] != "a":
+                mine = spans.setdefault(qs[i], [])
+                while True:
+                    t = t0 = gap(mine, t, busy[i], 0.0, "")
+                    for b in banks[i]:
+                        t = gap(spans.setdefault(b, []), t, busy[i], wake, qs[i])
+                    if t == t0:
                         break
-                    t = b
-                busy.insert(x, (t, t + o["busy"]))
-            at[i] = t + o["busy"] if back else t
+                put(mine, (t, t + busy[i], ""))
+                for b in banks[i]:
+                    put(spans[b], (t, t + busy[i], qs[i]))
+            at[i] = t + busy[i] if back else t
             for k, lag in behind[i]:
                 left[k] -= 1
                 if not left[k]:
                     pool.append(k)
         return at
 
-    level = [0.0] * n
-    for i in range(n - 1, -1, -1):
-        level[i] = max([ops[i]["cost"]] + [level[k] + lag for k, lag in succ[i]])
+    held = [[b + qs[i] for b in banks[i]] for i in range(n)]
+    rivals = [[b + p for b in banks[i] for p in "vst" if p != qs[i]] for i in range(n)]
+    idle = {k: (0.0, -1) for x in held + rivals + [qs] for k in x}
+
+    def replay(case, order):
+        cost, busy, done, pred, succ, wake = case
+        at, why, turn = [0.0] * n, [-1] * n, [False] * n
+        free = dict(idle)
+        end, last = 0.0, 0
+        for i in order:
+            t, w = free[qs[i]]
+            for k in rivals[i]:
+                if free[k][0] > t:
+                    t, w = free[k]
+            turn[i] = True
+            for j, lag in pred[i]:
+                if at[j] + lag >= t:
+                    t, w, turn[i] = at[j] + lag, j, False
+            at[i], why[i] = t, w
+            if qs[i] != "a":
+                free[qs[i]] = (t + busy[i], i)
+            for k in held[i]:
+                free[k] = (t + done[i] + wake, i)
+            if t + cost[i] > end:
+                end, last = t + cost[i], i
+        turns = []
+        while last >= 0:
+            if turn[last] and why[last] >= 0:
+                turns.append((why[last], last))
+            last = why[last]
+        return end + OPT["mean"] * sum(at) / n, turns
+
+    def score(order):
+        runs = [replay(c, order) for c in cases]
+        return sum(x[0] * w["weight"] for x, w in zip(runs, CASES)), [x[1] for x in runs]
+
+    def mend(order, steps):
+        need = [set(j for j, lag in p) for p in cases[0][3]]
+        end, turns = score(order)
+        seed = 1
+        for step in range(steps):
+            seed = (seed * 1103515245 + 12345) % 2 ** 31
+            chain = turns[(seed >> 8) % len(turns)]
+            if not chain:
+                continue
+            a, b = chain[(seed >> 12) % len(chain)]
+            x, y = order.index(a), order.index(b)
+            if seed >> 28 & 1:
+                x = max(0, x - (seed >> 20) % 24)
+                part = {b}
+                for k in reversed(order[x:y]):
+                    if any(k in need[j] for j in part):
+                        part.add(k)
+                if a in part:
+                    continue
+                new = order[:x] + [k for k in order[x:y + 1] if k in part] + [k for k in order[x:y + 1] if k not in part] + order[y + 1:]
+            else:
+                y = min(n - 1, y + (seed >> 20) % 24)
+                part = {a}
+                for k in order[x + 1:y + 1]:
+                    if need[k] & part:
+                        part.add(k)
+                if b in part:
+                    continue
+                new = order[:x] + [k for k in order[x:y + 1] if k not in part] + [k for k in order[x:y + 1] if k in part] + order[y + 1:]
+            e, tn = score(new)
+            if e <= end + OPT["heat"] * (1.0 - step / steps):
+                order, end, turns = new, e, tn
+        return order
+
     best = None
-    for turn in range(60):
-        at = pack([-x for x in level], False)
-        end = max(at[i] + ops[i]["cost"] for i in range(n))
-        if best is None or end < best[0]:
-            best = (end, at)
-        if turn % 2:
-            at = [x + 0.3 * (((i + 1) * (turn + 7) * 2654435761 >> 7) % 1000) / 1000.0 for i, x in enumerate(best[1])]
-        level = pack([-(at[i] + ops[i]["busy"]) for i in range(n)], True)
-    return best[1]
+    big = [i for i in range(n) if ops[i]["cost"] == ("gather", 512)][0]
+    PLAN.append(n)
+    for start, case in enumerate(cases):
+        cost, busy, done, pred, succ, wake = case
+        level = [0.0] * n
+        for i in range(n - 1, -1, -1):
+            level[i] = ops[i]["due"] * cost[big] / cases[0][0][big] if "due" in ops[i] else max([cost[i]] + [level[k] + lag for k, lag in succ[i]])
+        mine = None
+        for turn in range(OPT["turns"]):
+            at = pack(case, {i: (-level[i], i) for i in range(n)}, False)
+            order = sorted(range(n), key=lambda k: (at[k], k))
+            end = score(order)[0]
+            if mine is None or end < mine[0]:
+                mine = (end, at, order)
+            if turn % 2:
+                at = [x + OPT["shake"] * (((i + 1) * (turn + 7) * 2654435761 >> 7) % 1000) / 1000.0 for i, x in enumerate(mine[1])]
+            level = pack(case, {i: (-(at[i] + busy[i]), i) for i in range(n)}, True)
+        if best is None or mine[0] < best[0]:
+            best = mine
+    if OPT["wheel"]:
+        case = cases[OPT["wcase"]]
+        cost, busy, done, pred, succ, wake = case
+        key = list(best[1])
+        seed = OPT["seed"]
+        for turn in range(OPT["wheel"]):
+            want = list(key)
+            for i in range(n - 1, -1, -1):
+                want[i] = min([want[i]] + [want[k] - lag for k, lag in succ[i]])
+            at = pack(case, {i: (want[i], i) for i in range(n)}, False)
+            order = sorted(range(n), key=lambda k: (at[k], k))
+            end, turns = score(order)
+            if end < best[0]:
+                best = (end, at, order)
+            if not turn or end < best[0] + OPT["wheat"] * (1.0 - turn / OPT["wheel"]) or end < here:
+                here = end
+                base, chains = at, turns
+            key = list(base)
+            for x in range(OPT["wmoves"]):
+                seed = (seed * 1103515245 + 12345) % 2 ** 31
+                chain = chains[(seed >> 8) % len(chains)]
+                if chain:
+                    a, b = chain[(seed >> 12) % len(chain)]
+                    if (seed >> 26) % 3 == 2:
+                        near = [k for k in range(n) if qs[k] == qs[a] and base[a] - 3.0 < base[k] <= base[a] and busy[k] > 0.1]
+                        if near:
+                            a = near[(seed >> 4) % len(near)]
+                        key[a] = base[a] - 0.2 - ((seed >> 20) % 16) * 0.15
+                    elif (seed >> 26) % 3:
+                        key[b] = base[a] - 0.01 - ((seed >> 20) % 16) * 0.1
+                    else:
+                        key[a] = base[b] + 0.01 + ((seed >> 20) % 16) * 0.1
+        PLAN.append(["wheel", best[0]])
+    order = mend(best[2], OPT["steps"])
+    PLAN.append([replay(c, order)[0] for c in cases])
+    return order
+
+
+def _cost(q, x, c):
+    if isinstance(x, list):
+        return sum(_cost(q, y, c) for y in x)
+    kind, size = x if isinstance(x, tuple) else ("us", x)
+    if kind == "us":
+        return size * c["dma"]
+    if kind == "pe":
+        return size * c["cycle"] * c["pe"]
+    if kind == "plain":
+        return c["s"] + size * c["cycle"] if q == "s" else c["v"] + max(64, size) * c["cycle"]
+    return max(0.05, c[q]) + c[kind] * size * c["cycle"]
 
 
 def _issue(T, Q, ops):
-    at = _order(ops)
+    if not PLAN:
+        PLAN.insert(0, _order(ops))
     clock = {q: {} for q in Q}
     count = {q: 0 for q in Q}
     event = [None] * len(ops)
     final = {}
-    for i in sorted(range(len(ops)), key=lambda k: (at[k], k)):
+    holder = {}
+    left = list(PLAN[0])
+    while left:
+        i = [k for k in left if all(event[j] for j in ops[k]["dep"] | ops[k]["after"])][0] if any(not event[j] for j in ops[left[0]]["dep"] | ops[left[0]]["after"]) else left[0]
+        left.remove(i)
         o = ops[i]
         q = o["q"]
         if q == "a":
@@ -210,7 +409,11 @@ def _issue(T, Q, ops):
             continue
         ck = clock[q]
         want = {}
-        for j in o["dep"]:
+        dep = set(o["dep"])
+        for b in o["banks"]:
+            dep.update(j for p, j in holder.setdefault(b, {}).items() if p != q)
+            holder[b][q] = i
+        for j in dep:
             ev = event[j]
             if ev[1] > want.get(ev[0], (0, 0))[1]:
                 want[ev[0]] = ev
@@ -222,9 +425,10 @@ def _issue(T, Q, ops):
                         ck[k] = x
         ins = o["fn"]()
         if o["sem"] is None:
-            count[q] += 1
+            for x in ins if isinstance(ins, list) else [ins]:
+                count[q] += 1
+                x.then_inc(T.sem["c" + q], 1)
             sem, val = "c" + q, count[q]
-            ins.then_inc(T.sem[sem], 1)
         else:
             sem, val = o["sem"], o["val"]
         c2 = dict(ck)
@@ -265,36 +469,39 @@ def rank_program(g, core, T, topo):
         me, dep, aft = len(ops), set(), set(after) | set(gate)
         for spans, w in ((rd, False), (wr, True)):
             for n, a, b, st, p, e in spans:
-                ps = SCRATCH[n][0] == "psum"
                 for a2, b2, s2, p2, e2, w2, q2, j in hist.get(n, []):
                     meet = a < b2 and a2 < b and p < e2 and p2 < e
-                    if ps and q2 != q:
-                        dep.add(j)
-                    elif q == "t" and q2 == "t":
-                        if ps and meet:
-                            aft.add(j)
-                    elif (w or w2) and meet and (st == 1 or st != s2 or (a - a2) % st == 0):
-                        dep.add(j)
+                    if (w or w2) and meet and (st == 1 or st != s2 or (a - a2) % st == 0):
+                        (aft if q == "t" and q2 == "t" else dep).add(j)
         for spans, w in ((rd, False), (wr, True)):
             for n, a, b, st, p, e in spans:
                 h = hist.setdefault(n, [])
-                if w and st == 1 and SCRATCH[n][0] != "psum":
+                if w and st == 1:
                     h[:] = [x for x in h if not (a <= x[0] and x[1] <= b and p <= x[3] and x[4] <= e)]
                 h.append((a, b, st, p, e, w, q, me))
-        ops.append({"q": q, "fn": fn, "dep": dep, "after": aft - dep, "cost": cost, "busy": cost if busy is None else busy, "sem": sem, "val": val})
+        ops.append({"q": q, "fn": fn, "dep": dep, "after": aft - dep, "cost": cost, "busy": busy, "sem": sem, "val": val,
+                    "banks": sorted(set(x[0] for x in rd + wr if SCRATCH[x[0]][0] == "psum"))})
         return me
+
+    def join(first):
+        part = ops[first:]
+        del ops[first + 1:]
+        ops[first] = dict(part[0], fn=lambda: [o["fn"]() for o in part], cost=[o["cost"] for o in part], banks=sorted(set(b for o in part for b in o["banks"])),
+                          dep=set(j for o in part for j in o["dep"] if j < first), after=set(j for o in part for j in o["after"] if j < first))
+        for h in hist.values():
+            h[:] = [x[:7] + (min(x[7], first),) for x in h]
 
     def ap(x):
         return x[0] if isinstance(x, tuple) else x
 
     def cyc(o, ins, f=1.0):
         if o[3]:
-            return 0.05 + 3.8 * o[2] * CYC
+            return ("scatter", o[2])
         if ins[0][3]:
-            return 0.05 + 1.56 * o[2] * CYC
+            return ("gather", o[2])
         if f == 0.5 and not all(SCRATCH[x[1][0][0]][2] in (H, B, U) for x in [o] + ins):
             f = 1.0
-        return max(64, f * o[2]) * CYC
+        return ("plain", f * o[2])
 
     def ts(o, i, s1, op0, s2=None, op1=None):
         if op1 is None:
@@ -318,22 +525,30 @@ def rank_program(g, core, T, topo):
     def turn(o, i):
         run("v", [o], [i], lambda: g.vector.transpose(o[0], i[0]), cyc(o, [i]))
 
+    short = [OPT["tiny0"]]
+
     def act(o, i, f=AF.Identity, bias=0.0, scale=1.0, acc=None):
-        if acc is None:
+        if f == AF.Identity and o[2] <= short[0] and not i[3]:
+            ts(o, i, scale, OP.mult, bias, OP.add)
+        elif acc is None:
             run("s", [o], [i, bias, scale], lambda: g.scalar.activation(o[0], i[0], f, bias=ap(bias), scale=ap(scale)), cyc(o, [i]))
         else:
-            run("s", [o, acc], [i, bias], lambda: g.scalar.activation(o[0], i[0], f, bias=ap(bias), scale=scale, accum_out=acc[0]), cyc(o, [i]) + 0.02)
+            run("s", [o, acc], [i, bias], lambda: g.scalar.activation(o[0], i[0], f, bias=ap(bias), scale=scale, accum_out=acc[0]), ("plain", o[2] + 24))
 
     def mm(o, terms, start=True, stop=True):
         def fn():
             for k, x in enumerate(terms):
                 last = g.tensor.matmul((x + (o,))[2][0], x[0][0], x[1][0], start and k == 0, stop and k == len(terms) - 1)
             return last
-        c = sum(max(min(64, x[0][2]), x[1][2]) * (4 if SCRATCH[x[0][1][0][0]][2] == F else 1) for x in terms) * PEC
-        run("t", [o], [y for x in terms for y in x[:2]], fn, c)
+        c = sum(max(min(64, x[0][2]), x[1][2]) * (4 if SCRATCH[x[0][1][0][0]][2] == F else 1) for x in terms)
+        run("t", [o if start and stop else A(o[1][0][0])], [y for x in terms for y in x[:2]], fn, ("pe", c))
 
     def red(mat, n, a, b):
-        return [(A(mat, 128 * i, 128 * i + 128), A(n, a + i, b, 16)) for i in range(16)]
+        return [(A("RED", 15 - i, 143 - i), A(n, a + i, b, 16)) for i in range(16)]
+
+    def move(mat, x, u):
+        n, a = mat[1][0][:2]
+        return (A(n, a + 128 * u, a + 128 * u + 128), x)
 
     Q = {"v": g.vector, "s": g.scalar, "t": g.tensor, "g": g, "y": g.sync}
     dmas = {"s": [], "y": [], "g": []}
@@ -391,49 +606,82 @@ def rank_program(g, core, T, topo):
         dma("sy"[h], [(whole("LS%d" % h), x[:])], 1.6)
     for k, d in enumerate(others):
         dma("sy"[k % 2], [(blk("TKI", 256, d), rows(T.tk, d))], 1.9 + 0.4 * k)
+    def behind(k):
+        if k is not None:
+            ops[-1]["dep"].add(k)
+    w = OPT["loads"]
     for k, d in enumerate(others):
-        dma("ys"[k % 2], [(blk("TPI", 256, d), rows(T.tp, d))], 3.1 + 0.4 * k)
-    dma("y", [(piece("LL%d" % h, r, 0, LW), rows(x, r)) for h, x in enumerate((T.lk, T.li))] + [(A("PNI", 0, 1), T.pn[:])], 4.2)
-    dma("y", [(blk("TKI", 256, r), rows(T.tk, r)), (blk("TPI", 256, r), rows(T.tp, r))], 4.6)
-    dma("y", [(whole("DS"), T.dk[:]), (piece("DL", r, 0, DW), rows(T.dk, r))], 5.0)
+        dma("y", [(blk("TPI", 256, d), rows(T.tp, d))], 1.9 + 0.4 * k)
+        behind(w[0])
+    dma("y", [(piece("LL%d" % h, r, 0, LW), rows(x, r)) for h, x in enumerate((T.lk, T.li))]
+        + [(A("PNI", 0, 1, p0=32 * u, p=32), rows(T.pn, r)) for u in range(N)], 2.8)
+    dma("y", [(blk("TKI", 256, r), rows(T.tk, r)), (blk("TPI", 256, r), rows(T.tp, r))], 2.2)
+    behind(w[1])
+    dma("y", [(whole("DS"), T.dk[:]), (piece("DL", r, 0, DW), rows(T.dk, r))], 2.2)
+    behind(w[2])
 
     def iota(o, pattern, base, step=0):
         run("g", [o], [], lambda: g.iota(o[0], pattern, base, step, allow_small_or_imprecise_dtypes=True), 0.13 + 2 * o[2] * CYC)
     iota(A("PCI", 0, 1), [[1, 1]], 0, 1)
-    iota(A("IOTA"), [[1, 128]], 0)
+    iota(A("IOTA"), [[1, 144]], 0)
 
     sent = send("L")
-    arrive("lan", 5 * off + off // 2, [piece("LL%d" % h, s, 0, LW) for s in others for h in range(2)], sent, LATE[0])
+    arrive("lan", _landing(T, topo, routes, r, "lan"), [piece("LL%d" % h, s, 0, LW) for s in others for h in range(2)], sent, OPT["ll"])
     dma("y", [(A("LN", 128 * h, 128 * h + 128), whole("LL%d" % h)) for h in range(2)], 1.6)
 
     def parts(n, d, x):
-        cp(blk(n, 512, d, 0, 256), x)
+        if n[0] == "K":
+            act(blk(n, 512, d, 0, 256), blk("TKI", 256, d), scale=1.0 / 32)
+        else:
+            act(blk(n, 512, d, 0, 256), x)
         tt(blk(n, 512, d, 256), x, blk(n, 512, d, 0, 256), OP.subtract)
 
+    def stage(d):
+        return A("P%d" % (0, 1, 6, 7)[(others + [r]).index(d)], 256, 512)
+
     def keys(d):
-        x = blk("P%d" % (d // 2), 256, d % 2)
+        x = stage(d)
         ts(x, blk("TKI", 256, d), 1.0 / 32, OP.mult)
         parts("KS" if d != r else "KL", d, x)
 
     def pays(d):
-        x = blk("P%d" % (d // 2), 256, d % 2)
+        x = stage(d)
         ts(x, x, 1.0 / 64, OP.add, 1.0 / 64, OP.min)
-        tt(x, x, blk("TPI", 256, d), OP.mult)
+        act(blk("TPF", 256, d), blk("TPI", 256, d), bias=0.5)
+        tt(x, x, blk("TPF", 256, d), OP.mult)
         parts("PS" if d != r else "PL", d, x)
     for d in others:
         keys(d)
+    gate.append(len(ops) - 1)
     sentK = send("K")
-    gate.append(len(ops) - 2)
+    ops[-1]["due"] = OPT["tail"] + OPT["period"] * RO + 14.0
+    if OPT["kh"]:
+        sentKp = send("Kp")
+
+    def select(o, i, pattern, op, fill):
+        run("g", [o], [i], lambda: g.affine_select(o[0], i[0], pattern, op, fill, 0, 1), 0.17 + 2 * o[2] * CYC)
+        gate[:] = [len(ops) - 1]
     for d in others:
         pays(d)
+    gate.append(len(ops) - 1)
+    sending = [i for i in range(len(ops)) if ops[i]["q"] == "v"]
     sentP = send("P")
-    gate.append(len(ops) - 2)
+    ops[-1]["due"] = OPT["tail"] + OPT["period"] * RO + 12.0
+    if OPT["kh"]:
+        sentPp = send("Pp")
     keys(r)
     pays(r)
     del gate[:]
     for k, s in enumerate([peer] + cross):
-        arrive("k%d" % s, off, [blk("KL", 512, s)], sentK, LATE[1] if k else 0.5)
-        arrive("p%d" % s, off, [blk("PL", 512, s)], sentP, LATE[1])
+        arrive("k%d" % s, _landing(T, topo, routes, r, "k%d" % s), [blk("KL", 512, s)], sentK, OPT["lk"] if k else 1.0)
+        arrive("p%d" % s, _landing(T, topo, routes, r, "p%d" % s), [blk("PL", 512, s)], sentP, OPT["lp"] if k else 1.5)
+    if OPT["kh"]:
+        sentP = sentPp
+
+    consts = len(ops)
+
+    def early():
+        ops[-1]["due"] = OPT["tail"] + OPT["period"] * RO + OPT["early"]
 
     def pc(k):
         return A("PC", k, k + 1)
@@ -450,71 +698,98 @@ def rank_program(g, core, T, topo):
     cp(z(0), A("IOTA", 0, 128))
     ts(A("MI"), z(0), 15, OP.bitwise_and)
     ts(A("MG"), z(0), 4, OP.arith_shift_right)
-    BO, Ib, If, XM, CODE = A("BOb"), A("Ib"), A("If"), A("XM"), A("CODE")
+    BO, Ib, If, XM = A("BOb", 0, 128), A("Ib"), A("If"), A("XM")
     ts(BO, A("MG"), PG, OP.is_equal)
-    ts(f(0), A("MG"), PG, OP.not_equal, 32.0, OP.mult)
-    tt(CODE, f(0), A("MI"), OP.add)
     mid = [(512.0 * u + _high(u) + 512) / 2 for u in range(N)]
     bit = [((512 * u) // 1024, (_high(u) - 2048) // 1024) for u in range(N)]
-    rest = [1024.0 * mid[u] - (2.0 ** 20 - 1) * bit[u][0] + 1 for u in range(N)]
+    rest = [1024.0 * mid[u] - (2.0 ** 20 - 1) * bit[u][0] + LIFT - 2 for u in range(N)]
     MID, NEG = A("PK", 0, 1), A("PK", 1, 2)
     ts(A("PK", 8, 8 + N), A("IOTA", 0, N), PU, OP.is_equal)
-    for u in range(N):
-        ms(A("PK", 0, 1, p0=32 * u, p=32), mid[u])
-    act(NEG, MID, scale=-1.0)
+    ts(A("PK", 13, 14), PU, mid[2] - mid[1], OP.mult, 2 * mid[1] - mid[2], OP.add)
+    ts(MID, A("PK", 8, 9), mid[0] - 2 * mid[1] + mid[2], OP.mult, A("PK", 13, 14), OP.add)
+    act(NEG, MID, bias=1024.0, scale=-1.0)
+    act(A("PK", 12, 13), MID, bias=-257.0, scale=1.0 / 2048)
 
     def tb(k):
         return blk("TB", 128, k)
-    ts(A("S16"), A("IOTA", 0, 16), PI, OP.is_equal, 64.0, OP.mult)
-    for k in range(16):
-        act(blk("SEL", 128, k), BO, scale=A("S16", k, k + 1))
-    gate.append(sentP)
-    iota(A("C128"), [[0, 1024]], 128)
-    for k in range(16):
-        gate[:] = [len(ops) - 1]
-        if k == 2:
-            sent = send("D")
-            arrive("drawn", 3 * off, [piece("DL", s, 0, DW) for s in others], sent, LATE[1] + 4.0)
-            dma("y", [(A("LN", 256, 640), whole("DL"))], 1.8)
-            gate[:] = [sent]
-        run("g", [blk("REDb", 128, k)], [BO], lambda k=k: g.affine_select(blk("REDb", 128, k)[0], BO[0], [[0, 8], [1, 16]], OP.is_equal, 0.0, -k, 0),
-            0.17 + 256 * CYC)
-    iota(A("NE"), [[0, 582]], 0)
-    gate.pop()
+    ms(A("C128"), 128.0)
+    ops[-1]["due"] = OPT["tail"] + OPT["period"] * RO + 20.0
+    ms(A("OH", 0, 512), 0.0)
+    early()
+    feeds = [len(ops) - 1]
+    ts(Ib, z(0), PP, OP.is_equal)
     ts(z(1), z(0), 31, OP.bitwise_and)
     ts(tb(5), z(1), 4.0, OP.mult, PP, OP.subtract)
     for q in range(4):
         ts(blk("QM", 128, q), tb(5), -float(q), OP.is_equal)
-    banks = [0]
+    ts(A("CT", 32, 48), A("IOTA", 0, 16), PI, OP.is_equal, 128.0, OP.mult)
+    for k in range(OPT["selg"], 16):
+        (ts(blk("SEL", 128, k), BO, A("CT", 32 + k, 33 + k), OP.mult) if k % 2 else act(blk("SEL", 128, k), BO, scale=A("CT", 32 + k, 33 + k)))
+    gate.append(sentP)
+    for h in range(OPT["selg"] // 8):
+        run("g", [blk("SEL", 1024, h)], [A("C128")],
+            lambda h=h: g.affine_select(blk("SEL", 1024, h)[0], A("C128")[0], [[-1, 8], [-16, 8], [0, 16]], OP.is_equal, 0.0, -8 * h, 1), 0.17 + 2048 * CYC)
+        gate[:] = [len(ops) - 1]
+    hold = gate[:]
+    del gate[:]
+    act(A("NG"), BO, scale=-1.0)
+    early()
+    feeds.append(len(ops) - 1)
+    gate[:] = hold
+    select(XM, A("NG"), [[-1, 128]], OP.is_gt, 0.0)
+    select(XM, XM, [[-1, 128]], OP.not_equal, -2048.0)
+    sent = send("D")
+    arrive("drawn", 3 * off, [piece("DL", s, 0, DW) for s in others], sent, LATE[1] + 2.0)
+    dma("y", [(A("LN", 256, 640), whole("DL"))], 1.8)
+    gate[:] = [sent]
+    scaled = {}
 
-    def table(n, src, s, w, c):
+    def ID(w):
+        return scaled[w]
+    for k, w in enumerate((128.0, 1024.0, 512.0, 16.0, 32.0, 48.0, -2048.0, 2048.0, -LIFT, LIFT, 0.75 * LIFT, -0.25 * LIFT, 2.0 ** 17, 0.125, -2.0 ** 20)):
+        scaled[w] = blk("IDS", 128, k)
+        if 3 <= k < OPT["ids"]:
+            select(ID(w), A("OH", 0, 128), [[-1, 128]], OP.not_equal, w)
+    MV, MVn = A("MVb"), A("MVn", 0, 512)
+    for x, w in ((MV, 1.0), (A("MVn", 512, 1024), 16.0), (MVn, -8192.0)):
+        select(x, A("OH", 0, 512), [[-32, N], [0, N], [-1, 32]], OP.not_equal, w)
+    sent = gate[0]
+    iota(A("NE"), [[0, 582]], 0)
+    gate.pop()
+    for k, w in enumerate(scaled):
+        if not 3 <= k < OPT["ids"]:
+            ts(ID(w), Ib, w, OP.mult)
+    ts(pc(18), PG, 16.0, OP.mult, 15.0, OP.add)
+    ts(A("RED"), A("IOTA", 0, 144), pc(18), OP.is_equal)
+
+    def table(n, s, banks, by):
+        w, c = (32.0, 0.0) if n == "K" else (64.0, LIFT)
         for h, a in enumerate((512 * s, _high(s))):
-            P = "P%d" % (2 + banks[0] % 4)
-            for q in range(2):
-                mm(blk(P, 256, q), [(blk("QM", 128, 2 * h + q), blk(src, 512, s, 256 * x, 256 * x + 256)) for x in range(2)])
-            if banks[0] % 2 and s in cross:
-                ts(A(n, a, a + 512), A(P), w, OP.mult, c, OP.add)
+            P = "P" + banks[h]
+            mm(A(P), [(blk("QM", 128, 2 * h + q), blk(n + "L", 512, s, 256 * x, 256 * x + 256), blk(P, 256, q)) for q in range(2) for x in range(2)])
+            if by[h] == "v":
+                ts(A(n + "T", a, a + 512), A(P), w, OP.mult, c, OP.add)
             else:
-                act(A(n, a, a + 512), A(P), bias=c, scale=w)
-            banks[0] += 1
-    for n, s in [("K", r), ("K", peer), ("P", r), ("K", cross[0]), ("K", cross[1]), ("P", peer), ("P", cross[0]), ("P", cross[1])]:
-        table(n + "T", n + "L", s, 32.0 if n == "K" else 64.0, 0.0 if n == "K" else 1.0)
-    ts(Ib, CODE, PI, OP.is_equal)
+                act(A(n + "T", a, a + 512), A(P), bias=c, scale=w)
+    tables = len(ops)
+    table("K", r, "45", "ss")
+    table("K", peer, "23", "ss")
+    table("P", r, "01", "ss")
+    for o in ops[tables:]:
+        o["due"] = OPT["tail"] + OPT["period"] * RO + OPT["tabs"]
+    if OPT["ppe"]:
+        first = len(ops)
+        table("P", peer, OPT["ppe"], OPT["by"][0])
+        for o in ops[first:]:
+            o["due"] = OPT["tail"] + OPT["period"] * RO + 2.5
+    tables = range(tables, len(ops))
     act(If, Ib)
-    ts(tb(0), CODE, PI, OP.is_lt, -1.0, OP.mult)
-    act(tb(1), Ib, scale=-2048.0)
-    tt(XM, tb(0), tb(1), OP.add)
-    cp(tb(6), z(1))
-    for s in range(N):
-        ts(blk("MVb", 128, s), tb(6), 32.0 * s, OP.add, PP, OP.is_equal)
-    act(A("MVf"), blk("MVb", 128, r))
+    ts(A("MH", 96, 98), A("IOTA", 0, 2), 0.0, OP.mult)
     ts(z(2), A("MG"), 1, OP.bitwise_and)
     ts(A("FO"), z(2), PF, OP.is_equal)
     ms(A("RS4"), 1.0)
     ms(A("RS4", 0, 512, 128), 0.0)
-    ms(A("OB"), 0.0)
-    for d in range(N):
-        ms(blk("OS", OW, d, 272), 0.0)
+    later = [(blk("OS", OW, d, 272), 0) for d in range(N)]
     ts(pi(5), pi(0), 7, OP.bitwise_and)
     ts(pi(6), pi(0), 3, OP.arith_shift_right, 1, OP.bitwise_and)
     tt(pc(4), pi(5), pi(4), OP.subtract)
@@ -524,217 +799,364 @@ def rank_program(g, core, T, topo):
     ts(pc(6), pi(5), 16.0, OP.mult, 16.0, OP.add)
     tt(pc(7), pc(6), pi(6), OP.add)
     tt(pc(8), pc(7), pc(5), OP.add)
-    ts(A("PERM"), A("IOTA", 0, 8), 2.0, OP.mult, pc(8), OP.add)
-    ts(A("GS", 0, 8), A("IOTA", 0, 8), PG, OP.is_equal, 32.0, OP.mult)
+    ts(A("PERM", 0, 8), A("IOTA", 0, 8), 2.0, OP.mult, pc(8), OP.add)
+    ts(A("GS", 0, 8), A("IOTA", 0, 8), PG, OP.is_equal)
     iota(A("CT", 64, 96), [[2, N], [0, N], [1, 2]], 0)
-    ts(A("GB"), A("CT", 64, 96), PG, OP.is_equal, 32.0, OP.mult)
-    ts(pc(9), PF, 4.0, OP.mult, PU, OP.add)
-    ts(A("GS", 8, 16), A("IOTA", 0, 8), pc(9), OP.is_equal)
-    act(B15, A("S16", 15, 16), scale=64.0)
+    ts(A("GB"), A("CT", 64, 96), PG, OP.is_equal, 64.0, OP.mult)
+    act(A("GS", 8, 16), A("GS", 0, 8), scale=4.0)
+    for h, op in enumerate((OP.is_lt, OP.is_ge)):
+        ts(pc(29 + h), PI, 8.0, op)
+        act(blk("GS", 8, 2 + h), A("GS", 0, 8), scale=pc(29 + h))
+    act(pc(9), A("PK", 8, 9), bias=-12.0, scale=24.0)
+    ts(pc(24), PI, 6.0, OP.is_ge, pc(9), OP.mult)
+    act(pc(25), PU, bias=PI, scale=6.0)
+    ts(A("PERM", 8, 9), pc(25), pc(24), OP.add, 23.0, OP.min)
+    act(pc(26), PG, bias=2.0)
+    act(pc(27), A("PK", 8 + N - 1, 8 + N), bias=pc(26), scale=-8.0)
+    ts(A("BOb", 128, 256), A("MG"), pc(27), OP.is_equal)
+    ts(B15, PI, 15.0, OP.is_equal, 4096.0, OP.mult)
     C0, C1 = pc(14), pc(15)
-    act(C0, PU, scale=2.0)
-    act(C1, PU, bias=1.0, scale=2.0)
+    act(C0, PU, scale=16.0)
+    act(pc(10), PU, bias=2048.0 - 16.0, scale=16.0)
+    act(C1, A("PK", 8, 9), bias=pc(10), scale=16.0 * N)
     KR, KX = A("KR", 0, 96), A("KR", 96, 192)
     act(KR, A("IOTA", 0, 96), bias=95.0, scale=-1.0)
     act(KX, A("IOTA", 0, 96), bias=95.0 - 2047.0, scale=-1.0)
     act(A("CT", 0, 16), A("IOTA", 0, 16), bias=PI, scale=16.0)
-    act(A("CT", 16, 22), A("CT", 0, 6), bias=95.5, scale=-1.0)
-    act(pc(18), PU, bias=4096.0, scale=96.0)
-    act(pc(16), PI, bias=4096.0)
-    DUMP = A("CT", 24, 30)
-    act(DUMP, A("CT", 0, 6), bias=pc(18))
-    act(A("CT", 56, 62), DUMP, bias=MID, scale=-1.0)
-    act(A("RX", 0, 24), A("IOTA", 0, 24), scale=0.0)
-    act(A("RX", 24, 48), A("IOTA", 0, 24), bias=pc(16), scale=16.0)
-    ts(pi(9), pi(0), 31, OP.bitwise_and)
-    cp(pc(17), pi(9))
-    ts(A("AM"), tb(6), pc(17), OP.is_equal)
+    act(A("CT", 16, 22), A("CT", 0, 6), bias=95.0, scale=-1.0)
+    if OPT["jk"]:
+        for m in range(6):
+            ts(blk("PLC", 64, m), A("IOTA", 0, 64), 0.0, OP.mult, A("CT", 16 + m, 17 + m), OP.add)
+        ms(A("PLC", 63, 384, 64), -1.0)
+        ms(A("JK", 768, 1152), 1.0)
+        ms(A("JK", 768, 1152, 64), 0.0)
+    else:
+        act(A("CT", 48, 54), A("CT", 0, 6), bias=95.5, scale=-1.0)
+    act(pc(17), PI, bias=4096.0)
+    act(A("RX", 24, 48), A("IOTA", 0, 24), bias=pc(17), scale=16.0)
     for u in range(N):
-        ms(A("RX", 48 + 6 * u, 54 + 6 * u), mid[u])
+        later.append((blk("LV", 6, u), mid[u]))
     rise = [float(b - a) for a, b in bit]
-    for u in range(N):
-        act(blk("SUM", 128, u), A("FO"), scale=A("PK", 8 + u, 9 + u))
     up, down = 8 + rise.index(1.0), 8 + rise.index(-1.0)
     ts(A("PK", 2, 3), A("PK", down, down + 1), A("PK", up, up + 1), OP.subtract)
     ts(A("PK", 3, 4), A("PK", 2, 3), -2.0 ** 20, OP.mult, 2.0 ** 21, OP.add)
-    for k, w in enumerate((2048.0, 2.0, 1024.0, A("PK", 2, 3), A("PK", 3, 4))):
-        act(blk("SUM", 512, k + 1), blk("SUM", 512, 0), scale=w)
+    for u in range(N):
+        act(blk("SUM", 128, u), A("FO"), scale=A("PK", 8 + u, 9 + u))
+    act(blk("SUM", 512, 1), blk("SUM", 512, 0), scale=2048.0)
+    early()
+    for k, w in enumerate((2.0, 1024.0, A("PK", 3, 4), A("PK", 2, 3))):
+        act(blk("SUP", 256, k), A("BOb"), scale=w)
+        early()
 
-    def SUM(u, k):
-        return blk("SUM", 128, N * k + u)
+    def SUM(u, k, x):
+        return move(blk("SUM", 512, k), x, u)
     ts(tb(2), A("MI"), PI, OP.is_ge, -BIG, OP.mult)
     ts(tb(3), A("MI"), PI, OP.is_equal, 2 * BIG, OP.mult)
     tt(tb(4), tb(2), tb(3), OP.add)
     tt(tb(2), tb(4), A("FO"), OP.mult)
     for u in range(N):
         act(blk("EMB", 128, u), tb(2), scale=A("PK", 8 + u, 9 + u))
+        early()
+    for x in range(2):
+        tt(blk("SUP", 128, 8 + x), tb(4), blk("BOb", 128, x), OP.mult)
     for u in range(N):
-        for k, x in enumerate((mid[u], rest[u] - rest[u] % 1024, rest[u] % 1024)):
-            ms(A("LV", 384 * k + 96 * u, 384 * k + 96 * u + 96), x)
-    newkey = [[(SUM(u, 1), A("ME")), (SUM(u, 0), A("MH")), (SUM(u, 1), A("MB"))] for u in range(N)]
-    newpay = [[(SUM(u, 2), A("ME")), (SUM(u, 3), A("MH")), (SUM(u, 5), A("MB"))] + ([(SUM(u, 4), A("MB"))] if rise[u] else []) for u in range(N)]
+        for x in range(2):
+            ms(A("PK", 6 + x, 7 + x, p0=32 * ((u + x) % N), p=32), rest[u] + 516.5 - mid[u] / 1024 - BIG)
+    later.append((A("PT", 4096, 4096 + 384), 0))
+    MH = A("MH", 0, 96)
+    newkey = [[SUM(u, 1, A("ME")), SUM(u, 0, MH), SUM(u, 1, A("MB"))] for u in range(N)]
+    newpay = [[(blk("SUP", 128, 2 * k + x), y) for k, y in enumerate((A("ME"), MH, A("MB"), A("MB"), A("EE")))] for x in range(2)]
     for m in range(6):
         ts(blk("KP", 97, m), A("IOTA", 0, 97), A("CT", m, m + 1), OP.is_le)
     for k, x in enumerate((0.0, 0.0, 0.0, 2048.0)):
         act(blk("XO", 2, k), A("CT", 0, 2), bias=x)
     gate.append(sent)
+    for x, c in reversed(later):
+        iota(x, [[0, x[2]]], int(c))
     iota(A("OF", 0, 64), [[512, N], [16, 16]], 0)
-    for d in range(N):
-        iota(blk("OF", 16, N + d), [[1, 2], [_high(d) - 512 * d, 2], [128, 4]], 512 * d)
+    iota(A("OF", 64, 128), [[1, 8], [512, 2], [128, 4]], 0)
+    iota(A("OF", 128, 192), [[0, 8], [1, 2], [0, 4]], 0)
     gate.pop()
+    unhurried = len(ops)
     ts(pc(20), PU, 2.0, OP.is_ge)
     ts(pc(19), PU, 256.0, OP.mult, PI, OP.add)
     for k, ds in enumerate(([0], [1, 2, 3])):
         ts(pc(22 + k), pc(20), float(_high(ds[0]) - 512 - 512 * ds[0]), OP.mult, pc(19), OP.add)
         ts(A("OK", 16 * ds[0], 16 * ds[-1] + 16), A("OF", 16 * ds[0], 16 * ds[-1] + 16), pc(22 + k), OP.add)
-    ts(pc(21), PI, 8.0, OP.mult, C0, OP.add)
-    ts(A("OY"), A("OF", 64, 128), pc(21), OP.add)
+    far = [float(_high(u) - 512 - 512 * u) for u in range(N)]
+    act(pc(11), PU, scale=512.0)
+    act(pc(21), PI, bias=pc(11), scale=8.0)
+    act(pc(28), A("PK", 8, 9), bias=far[1], scale=far[0] - far[1])
+    act(A("OF", 128, 192), A("OF", 128, 192), bias=pc(21), scale=pc(28))
+    tt(A("OF", 64, 128), A("OF", 64, 128), A("OF", 128, 192), OP.add)
+    cp(A("OY"), A("OF", 64, 128))
 
-    KEY, IMG, HI = A("KB"), v(3), A("HI")
+    IMG, HI, K2 = v(3), A("HI"), A("K2")
     KW, PW = A("KT", 0, 4096), A("PT", 0, 4096)
-    OLD, WAITS = A("FL", 0, 128), A("FL", 128, 256)
-    scaled = {}
-
-    def ID(w):
-        if w not in scaled:
-            scaled[w] = blk("IDS", 128, len(scaled))
-            ts(scaled[w], Ib, w, OP.mult)
-        return scaled[w]
-    cp(A("DF"), A("LN", 256, 640))
+    OLD, WAITS, B10 = A("FL", 0, 128), A("FL", 128, 256), A("FL", 384, 512)
+    O5, O7, SG, SO = A("O5", 0, 24), A("O5", 24, 36), A("SG", 0, 4), A("SG", 4, 8)
+    act(A("DF"), A("LN", 256, 640), bias=2048.0)
+    ops[-1]["due"] = OPT["tail"] + OPT["period"] * RO - 7.5
+    unhurried = range(unhurried, len(ops))
+    ms(A("P7", 0, 160), 0.0)
+    EH0, EH1, NW = blk("EH", 128, 0), blk("EH", 128, 1), A("NW")
 
     def NV(k):
         return A("NN", k, k + 1)
 
-    def prep(t):
-        ts(A("K2"), KEY, 2048.0 - LIFT * t, OP.add)
-        ts(A("Z2"), A("K2"), 4095, OP.bitwise_and)
-        ts(HI, A("K2"), 2047, OP.bitwise_and)
-        ts(A("E1"), A("K2"), 11, OP.arith_shift_right)
-        ts(A("Q"), A("K2"), 9, OP.arith_shift_right, 3, OP.bitwise_and)
-        ts(v(2), A("Z2"), NV(max(t - 1, 0)), OP.is_lt, 2048.0, OP.mult)
-        tt(A("OB", 16, 144), HI, v(2), OP.add)
-        turn(A("YT", 0, 160), A("OB"))
-        turn(A("YT", 160, 288), A("OB", 16, 144))
-        cp(A("OFF"), X(A("YT"), A("PERM")))
-        ts(A("EH", 0, 128), A("E1"), -1.0, OP.add, 32.0, OP.mult)
-        ts(A("EH", 128, 256), HI, 1.0 / 64, OP.mult)
-        tt(v(0), IMG, A("Z2"), OP.is_ge)
-        tt(A("TO", 0, 128), A("Q"), v(0), OP.add)
-        cp(OLD, v(0))
-        act(A("TO", 128, 256), A("TO", 0, 128), AF.Abs, -2.0)
-        ts(A("OG", 0, 128), A("TO", 128, 256), 2.0, OP.is_equal)
-        for d in range(1, 4):
-            ts(blk("OG", 128, d), A("TO", 0, 128), float(d), OP.is_equal)
-        scan(A("IG"), A("RS4"), A("OG"), 0.0, OP.mult, OP.add)
-        mm(A("P6"), [(BO, A("IG")), (XM, A("OG"))])
-        act(A("GOB"), A("P6"), AF.Sign, -1407.5, -1.0)
-        mm(A("P4", 128, 256), [(Ib, blk("GOB", 128, d)) for d in range(4)])
-        act(WAITS, A("P4", 128, 256), bias=-1.0, scale=-0.5)
-        for s in range(N):
-            mm(blk("P6", 128, s), [(blk("MVb", 128, s), blk("EH", 128, 0))])
-        act(blk("EM", 512, t % 2), A("P6"), scale=1.0 / 32)
+    def OG(d):
+        return blk("OG", 128, d - 1)
 
-    def spread(c):
-        for k in range(4 * c, 4 * c + 4):
-            mm(blk("P%d" % c, 128, k % 4), [(blk("SEL", 128, k), blk("EH", 128, h)) for h in range(2)])
+    def prep(t):
+        ts(A("Z2"), K2, 4095, OP.bitwise_and)
+        ts(HI, K2, 2047, OP.bitwise_and)
+        ts(A("E1"), K2, 11, OP.arith_shift_right, 1023, OP.bitwise_and)
+        if OPT["ehs"]:
+            act(EH0, A("E1"), bias=-16.0, scale=16.0)
+            act(EH1, HI, scale=1.0 / 128)
+        else:
+            ts(EH0, A("E1"), -1.0, OP.add, 16.0, OP.mult)
+            ts(EH1, HI, 1.0 / 128, OP.mult)
+        before = A("FL", 256, 384)
+        below(before, max(t - 1, 0))
+        mm(A("P7", 16, 144), [(ID(128.0), EH1), (ID(1024.0), before)])
+        due(t - 1, OPT["ig"] - (0.4 if t else 1.5))
+        turn(A("YT", 0, 160), A("P7", 0, 160))
+        turn(A("YT", 160, 288), A("P7", 16, 144))
+        join(len(ops) - 2)
+        due(t - 1, OPT["ig"] + (0.1 if t else -1.2))
+        ts(A("OFF"), X(A("YT"), A("PERM", 0, 8)), 1024.0, OP.add)
+        due(t - 1, OPT["ins"] + (1.9 if t else 0.6))
+        ts(B10, EH1, 8.0, OP.is_ge)
+        due(t, 1.9)
+        tt(OLD, IMG, A("Z2"), OP.is_ge)
+        y = A("P4" if t else "P7", 0 if t else 160, 128 if t else 288)
+        mm(y, [(ID(128.0), EH1), (ID(512.0), OLD)])
+        act(A("TO", 0, 128), y, bias=128.5 + 1.0 / 1024, scale=1.0 / 512)
+        due(t - 1, OPT["ins"] + 0.95)
+        for d in range(1, N):
+            ts(OG(d), A("TO", 0, 128), 129.0 + d, OP.is_equal)
+        join(len(ops) - N + 1)
+        due(t - 1, OPT["ig"] - 0.15)
+        act(A("TO", 128, 256), A("TO", 0, 128), AF.Abs, -131.0)
+        due(t - 1, OPT["ins"] + 1.1)
+        ts(OG(N), A("TO", 128, 256), 2.0, OP.is_equal)
+        due(t - 1, OPT["ig"] - 0.1)
+        scan(A("IG"), A("RS4"), A("OG"), 0.0, OP.mult, OP.add)
+        due(t - 1, OPT["ig"])
+        if OPT["gob"] == "P4" and t:
+            go(t)
+        if OPT["emd"]:
+            dma("y", [(A("EM", 512 * (t % 2) + 128 * s, 512 * (t % 2) + 128 * s + 128, p0=32 * u, p=32), A("E1", p0=32 * s, p=32)) for s in range(N) for u in range(N)], 3.0)
+
+    def payloads():
+        tt(X(A("PT"), O7), A("OLD", 384, 576), A("SC", 384, 576), OP.max)
+
+    def due(t, x):
+        ops[-1]["due"] = OPT["tail"] + OPT["period"] * RO - (OPT["period"] - OPT["cut"]) * t - x + OPT["cut"] * ((x > 4.2) + (x > OPT["period"] + 4.2) + (t < 0) * -1)
+
+    def below(o, t):
+        act(o, A("Z2"), AF.Sign, NV(4 + t), -1.0)
+
+    def go(t):
+        P = OPT["gob"]
+        mm(A(P), [(XM, A("OG")), (BO, A("IG"))])
+        act(A("GOB"), A(P), AF.Sign, -1407.5, -1.0)
+        due(t, 0.7 if t else 2.15)
+
+    def spread(t):
+        if OPT["gob"] != "P4" or not t:
+            go(t)
+        for c in range(4):
+            for x in range(2):
+                mm(blk("P%d" % c, 256, x), [(blk("SEL", 128, 4 * c + k), blk("EH", 128, h), blk("P%d" % c, 128, k)) for k in (2 * x, 2 * x + 1) for h in range(2)])
+                if c in OPT["fuse"][t]:
+                    due(t, -0.3 + 0.4 * c)
+            if c in OPT["fuse"][t]:
+                act(blk("W1", 512, c), A("P%d" % c))
+                due(t, 0.2 + 0.5 * c)
 
     def split(t):
         n = NV(t)
-        ts(A("SG"), A("XO", 0, 4), n, OP.add, 2047.0, OP.min)
-        act(A("SX", 0, 8), A("XO"), bias=n)
+        ts(SG, A("XO", 0, 4), n, OP.add)
+        ts(A("SX", 0, 8), A("XO"), n, OP.add)
         ts(A("SX", 8, 12), A("SX", 0, 4), NV(t + 1), OP.is_ge, 4096.0, OP.mult)
         tt(A("SX", 12, 16), A("SX", 8, 12), A("SX", 4, 8), OP.add)
-        cp(A("SO"), A("SX", 12, 16))
+        cp(SO, A("SX", 12, 16))
         cp(A("SI", 0, 32), X(KW, A("SG", 0, 2)))
         ts(A("SI", 32, 64), A("SI", 0, 32), 0x200800, OP.bitwise_and)
         for k in range(3):
             ts(blk("SK", 32, k), A("SI", 32, 64), 2048.0, (OP.not_equal, OP.is_equal)[k % 2])
-        tt(A("SK", 128, 192), X(KW, A("SG")), A("SK", 0, 64), OP.mult)
-        tt(X(A("KT"), A("SO")), A("SK", 128, 192), A("SK", 32, 96), OP.subtract)
-        tt(A("SK", 192, 256), X(PW, A("SG")), A("SK", 0, 64), OP.mult)
-        tt(X(A("PT"), A("SO")), A("SK", 192, 256), A("SK", 32, 96), OP.add)
+        join(len(ops) - 3)
+        tt(A("SK", 128, 192), X(KW, SG), A("SK", 0, 64), OP.mult)
+        due(t + 1, 4.25)
+        tt(X(A("KT"), SO), A("SK", 128, 192), A("SK", 32, 96), OP.subtract)
+        due(t + 1, 8.2 if t < RO - 1 else 2.5)
+        tt(A("SK", 192, 256), X(PW, SG), A("SK", 0, 64), OP.mult)
+        due(t + 1, (10.9, OPT["period"] + 1.6, 2.8)[(1, 0, 2)[t]])
+        ts(A("SK", 256, 320), A("SK", 32, 96), LIFT - 0.5, OP.mult)
+        tt(X(A("PT"), SO), A("SK", 192, 256), A("SK", 256, 320), OP.add)
+        due(t + 1, (12.3, OPT["period"] + 1.9, 3.0)[(1, 0, 2)[t]])
 
-    cp(KEY, A("LN", 0, 128))
+    made = [i for i in range(consts, len(ops)) if i not in tables and ops[i]["q"] in OPT["made"] and i not in unhurried]
+    small = set(x[7] for n in ("PCI", "PC", "TN", "MI", "MG", "FO", "PK", "BOb", "C128") for x in hist[n] if x[5])
+    for i in range(consts, len(ops)):
+        if ops[i]["q"] == "v" and i not in small:
+            ops[i]["after"].update(sending)
+    ahead = len(ops)
+    for q, by in zip(cross, OPT["by"][1:3]):
+        first = len(ops)
+        table("K", q, "46", by)
+        for o in ops[first:]:
+            o["after"].update(i for i in made if ops[i]["q"] == o["q"])
+            o["due"] = OPT["tail"] + OPT["period"] * RO + 1.5
+    ts(K2, A("LN", 0, 128), 2048.0, OP.add)
+    ops[-1]["after"].update(feeds + made[:int(len(made) * OPT["share"])])
+    for i in list(tables) + list(range(ahead, len(ops))):
+        if ops[i]["q"] == "v":
+            ops[i]["after"].update(feeds)
     ts(IMG, A("LN", 128, 256), -1.0, OP.add)
-    cp(NV(12), A("PNI", 0, 1))
-    mm(A("P6", 0, 1), [(A("MVf"), NV(12))])
-    act(NV(0), A("P6", 0, 1))
+    act(NV(4), A("PNI", 0, 1), bias=-0.5)
+    early()
+    act(NV(0), A("PNI", 0, 1))
+    early()
+    short[0] = OPT["tiny"]
     prep(0)
-    for c in range(4):
-        spread(c)
+    spread(0)
 
     for t in range(RO):
         last = t == RO - 1
         n = NV(t)
-        for c in range(4):
-            act(blk("W1", 512, c), X(KW, blk("OFF", 32, c)))
-            if c == 3:
-                ts(A("NW"), A("Z2"), n, OP.is_lt, 32.0, OP.mult)
-                ts(NV(10), n, 1536.0, OP.min)
-                ts(A("FL", 256, 384), A("Z2"), NV(10), OP.is_lt)
-                gate.extend([len(ops) - 1, len(ops) - 3])
-                mm(A("P6", 0, 128), [(ID(2.0), A("TO", 0, 128)), (ID(-3.0), OLD), (ID(64.0), WAITS), (ID(-5.0 / 32), A("NW")), (ID(8.0), A("FL", 256, 384))])
-                mm(A("P6", 128, 256), [(ID(64.0), blk("EH", 128, 1)), (ID(128.0), A("NW")), (ID(-4096.0), OLD), (ID(-4096.0), WAITS)])
-                act(A("CM"), A("P6", 0, 128))
-                act(f(5), A("P6", 128, 256), bias=-4096.0)
-            tt(blk("EQ", 512, c), blk("W1", 512, c), A("P%d" % c), OP.is_equal)
+        if not t:
+            gate.extend([i for i in range(ahead, len(ops)) if ops[i]["q"] == "t"][:OPT["pg"]])
+            first = len(ops)
+            if not OPT["ppe"]:
+                table("P", peer, "56", OPT["by"][0])
+            table("P", cross[0], "56", OPT["by"][3])
+            table("P", cross[1], OPT["pb"], OPT["by"][4])
+            for k, o in enumerate(ops[first:]):
+                o["due"] = OPT["tail"] + OPT["period"] * RO - OPT["pt0"] - OPT["pt1"] * k
             del gate[:]
-            for k in range(4 * c, 4 * c + 4):
-                mm(A("P4", k, 512, 16), [(blk("EQ", 128, k), A("GB"))])
-        for h in range(2):
-            act(blk("TF", 256, h), blk("P4", 256, h))
+        ts(NW, A("Z2"), n, OP.is_lt, 0.5, OP.subtract)
+        x = A("P6", 256, 384) if t else A("P7", 160, 288)
+        mm(A("P7", 160, 288), [(Ib, blk("GOB", 128, d)) for d in range(4)])
+        due(t, 1.3 if t else 2.8)
+        ts(WAITS, A("P7", 160, 288), -1.0, OP.mult, -3.0, OP.add)
+        due(t, 2.0 if t else 3.2)
+        mm(x, [(ID(16.0 * d), OG(d)) for d in range(1, N)] + [(ID(-2048.0), OLD), (ID(LIFT), WAITS), (ID(2048.0), NW)])
+        due(t, 2.5 if t else 3.5)
+        act(A("CM"), x, bias=1024.0 + LIFT)
+        due(t, 4.3)
+        mm(A("P5"), [move(MV, EH0, s) + (blk("P5", 128, s),) for s in range(N)])
+        due(t, 3.2 if t else 5.5)
+        act(blk("EM", 512, t % 2), A("P5"), bias=A("PK", 12, 13), scale=1.0 / 16)
+        due(t, 4.4 if t else 6.0)
+        mm(A("P6", 384, 512), [(ID(128.0), EH1), (ID(-2048.0), OLD), (ID(-2048.0), WAITS), (ID(2048.0), NW)])
+        due(t, 5.3)
+        act(f(5), A("P6", 384, 512), bias=-3072.0)
+        due(t, 5.75)
+        mm(A("P6", 384, 512), [(ID(16.0), A("C128", 0, 128)), (ID(128.0), EH0), (ID(128.0), EH1), (ID(LIFT), WAITS)])
+        due(t, 7.0)
+        tt(f(3), A("P6", 384, 512), blk("DF", 128, t), OP.max)
+        due(t, 8.95)
         for c in range(4):
-            tt(blk("W3", 512, c), X(PW, blk("OFF", 32, c)), blk("EQ", 512, c), OP.mult)
-            for k in range(4 * c, 4 * c + 4):
-                mm(A("P4", k, 128, 16), [(blk("W3", 128, k), A("GS", 0, 8))])
-        act(A("TS"), A("P4", 0, 128))
-        mm(A("P5", 128, 256), [(If, blk("DF", 128, t)), (ID(-LIFT), WAITS)])
-        act(f(2), A("P5", 128, 256), bias=LIFT * (t + 1))
-        mm(A("P5", 256, 384), [(If, KEY), (ID(LIFT), WAITS)])
-        tt(f(3), A("P5", 256, 384), f(2), OP.max)
-        mm(A("P5", 0, 128), [(A("TS"), If), (ID(-32 * LIFT), WAITS)])
-        for s in range(N):
-            mm(blk("P6", 128, s), [(blk("MVb", 128, s), blk("EH", 128, 1)), (blk("MVb", 128, s), A("NW"))])
-        act(A("HM"), A("P6"), bias=NEG, scale=64.0)
+            if c in OPT["fuse"][t]:
+                tt(blk("EQ", 512, c), X(KW, blk("OFF", 32, c)), blk("W1", 512, c), OP.is_equal)
+            else:
+                act(blk("W1", 512, c), X(KW, blk("OFF", 32, c)))
+                due(t, 1.4 + 0.7 * (c - len(OPT["fuse"][t])))
+                tt(blk("EQ", 512, c), blk("W1", 512, c), A("P%d" % c), OP.is_equal)
+            due(t, OPT["eq"][c])
+            mm(A("P4"), [(blk("EQ", 128, k), A("GB"), A("P4", k, 512, 16)) for k in range(4 * c, 4 * c + 4)])
+        for h in range(OPT["tf"]):
+            act(blk("TF", 512 // OPT["tf"], h), blk("P4", 512 // OPT["tf"], h))
+            due(t, 5.1)
+        w = 16 // len(OPT["w3"])
+        for c, x in enumerate(OPT["w3"] if t else OPT["w30"]):
+            tt(blk("W3", 128 * w, c), X(PW, blk("OFF", 8 * w, c)), blk("EQ", 128 * w, c), OP.mult)
+            due(t, x)
+            for x in range(w * c, w * c + w, 2):
+                mm(A("P6", 0, 256), [(blk("W3", 128, k), A("GS", 0, 16), A("P6", k, 256, 16)) for k in (x, x + 1)])
+                due(t, OPT["ws"][c] if t else OPT["w30"][c] + 0.9)
+        act(A("SN"), A("P6", 0, 256), AF.Sign, -LIFT)
+        due(t, 9.07)
+        act(A("TS"), A("P6", 0, 128), bias=2047.5 - LIFT)
+        due(t, 9.3)
+        mm(A("P6", 256, 384), [(ID(-LIFT), WAITS), (blk("SN", 128, 0), ID(LIFT)), (A("TS"), If)])
+        due(t, 9.85)
+        mm(A("P2", 0, 128), [(ID(16.0), A("C128", 0, 128)), (ID(-0.25 * LIFT), WAITS), (ID(2.0 ** 17), EH1), (ID(0.125), EH0), (ID(-2.0 ** 20), B10),
+                             (Ib, B10)], stop=False)
+        due(t, 7.2)
+        mm(A("P2", 0, 128), [(blk("SN", 128, 1), ID(0.75 * LIFT))], start=False)
+        due(t, 9.8)
+        tt(f(4), A("P2", 0, 128), f(3), OP.max)
+        due(t, 10.2)
+        for h in range(2):
+            mm(blk("P5", 256, h), [x + (blk("P5", 128, s),) for s in (2 * h, 2 * h + 1) for x in (move(MV, EH1, s), move(A("MVn", 512, 1024), NW, s))])
+            due(t, 5.0)
+        act(A("HM"), A("P5"), bias=NEG, scale=128.0)
+        due(t, 6.3)
         ts(NV(8), n, 32.0, OP.add, 2048.0, OP.min)
-        tt(NV(9), NV(8), n, OP.subtract)
         if t:
+            if OPT["plate"]:
+                payloads()
+                due(t, 9.0)
             split(t - 1)
-        for s in range(N):
-            mm(blk("P%d" % (s // 2), 128, s % 2), [(blk("MVb", 128, s), A("CM")), (blk("TF", 128, s), Ib)])
-        act(A("PB"), A("P1", 0, 256))
-        for h, x in enumerate((A("P0", 0, 256), A("PB"))):
+        for h in range(2):
+            P = "P%d" % h
+            mm(A(P, 0, 256), [x + (blk(P, 128, s % 2),) for s in (2 * h, 2 * h + 1) for x in (move(MV, A("CM"), s), (blk("TF", 128, s), Ib))])
+        act(A("PB", 256, 512), A("P1", 0, 256))
+        if OPT["ohs"]:
+            act(A("PB", 0, 256), A("P0", 0, 256))
+        for h, x in enumerate((A("PB" if OPT["ohs"] else "P0", 0, 256), A("PB", 256, 512))):
             for k, c in enumerate((C0, C1)):
                 ts(blk("OH", 256, 2 * k + h), x, c, OP.is_equal)
+                due(t, OPT["oh0"])
         scan(A("INC"), A("OH"), A("C128"), 0.0, OP.add, OP.min)
-        mm(A("P1", 0, 64), [(BO, A("INC", 15, 1024, 16))])
-        mm(A("P2", 0, 64), red("REDb", "INC", 0, 1024))
+        due(t, OPT["oh0"] + 0.7)
+        jv = OPT["jk"]
+        mm(A("P1", 256, 320), [(BO, A("INC", 15, 1024, 16))])
+        due(t, OPT["oh0"] + 1.3)
+        mm(A("P4", 384, 448), red("REDb", "INC", 0, 1024))
+        due(t, 7.63)
         for m in range(6):
-            act(blk("JK", 64, m, 0, 63), A("P1", 0, 63), AF.Sign, A("CT", 16 + m, 17 + m), -1.0, acc=A("AC", m, m + 1))
-        act(A("E2"), A("P2", 0, 64), bias=B15)
+            act(blk("JK", 64, m, 0, 63), A("P1", 256, 319), AF.Sign, A("CT", 48 + m, 49 + m), -1.0, acc=A("BS", 32 + m, 33 + m))
+        join(len(ops) - 6)
+        due(t, 7.7)
+        act(A("E2"), A("P4", 384, 448), bias=B15)
+        due(t, 8.2)
         for h, P in enumerate(("P0", "P3")):
             mm(A(P), [(BO, blk("INC", 512, h)), (XM, blk("OH", 512, h))])
+            due(t, (8.05, 8.9)[h])
             act(blk("XS", 512, h), A(P))
-        AC = A("AC", 0, 6)
-        ts(A("O1", 0, 6), AC, 0.5, OP.mult, 31.5, OP.add)
-        ts(A("VB", 0, 6), AC, 8.0, OP.mult, 504.0, OP.add)
-        ts(A("BS", 8, 14), AC, 0.0, OP.is_gt, -512.0, OP.mult)
+            due(t, (8.6, 9.5)[h])
+        if jv:
+            AC = A("JK", 384 + 63, 768, 64)
+            cp(A("O1", 0, 6), AC)
+            ts(A("VB", 0, 6), AC, 16.0, OP.mult)
+            ts(A("BS", 8, 14), AC, 32.0, OP.is_ge, -512.0, OP.mult)
+        else:
+            AC = A("BS", 32, 38)
+            ts(A("O1", 0, 6), AC, 0.5, OP.mult, 31.5, OP.add)
+            ts(A("VB", 0, 6), AC, 8.0, OP.mult, 504.0, OP.add)
+            ts(A("BS", 8, 14), AC, 0.0, OP.is_gt, -512.0, OP.mult)
         tt(A("C2"), X(A("E2"), A("O1", 0, 6)), KR, OP.is_le)
-        mm(A("P1", 64, 70), [(Ib, A("VB", 0, 6))] + red("REDb", "C2", 0, 96))
-        cp(A("O1", 8, 14), A("P1", 64, 70))
-        tt(A("BS", 16, 22), A("P1", 64, 70), A("BS", 8, 14), OP.add)
+        mm(A("P1", 320, 326), [(Ib, A("VB", 0, 6))] + red("REDb", "C2", 0, 96))
+        cp(A("O1", 8, 14), A("P1", 320, 326))
+        tt(A("BS", 16, 22), A("P1", 320, 326), A("BS", 8, 14), OP.add)
         tt(A("MK"), X(A("XS"), A("O1", 8, 14)), KX, OP.is_equal)
         cp(A("O3", 0, 6), A("BS", 16, 22))
-        tt(A("MH"), X(A("HM"), A("O3", 0, 6)), A("MK"), OP.mult)
+        tt(A("MH", 0, 96), X(A("HM"), A("O3", 0, 6)), A("MK"), OP.mult)
+        due(t, OPT["ins"] - 0.35)
         tt(A("ME"), X(blk("EM", 512, t % 2), A("O3", 0, 6)), A("MK"), OP.mult)
+        due(t, OPT["ins"] - 0.1)
         tt(IMG, IMG, f(5), OP.max)
-        act(f(4), A("P5", 0, 128), bias=LIFT * (t + 1) - 1.0, scale=1.0 / 32)
-        ts(v(2), A("P5", 0, 128), 0.0, OP.is_gt, -LIFT, OP.mult)
-        tt(v(2), v(2), f(3), OP.add)
-        tt(KEY, v(2), f(4), OP.max)
+        tt(K2, A("P6", 256, 384), f(4), OP.max)
+        due(t, OPT["k2"])
         if last:
             ts(A("YI"), IMG, 1.0, OP.add)
-            act(KEY, KEY, bias=-LIFT * RO)
+            ts(HI, K2, int(LIFT) - 1, OP.bitwise_and)
+            ts(A("KB"), HI, -2048.0, OP.add)
             dma("y", [(whole("YS%d" % h), A(x)) for h, x in enumerate(("KB", "YI"))], 2.0)
             dma("y", [(piece("YL%d" % h, r, 0, LW), A(x, p0=32 * r, p=32)) for h, x in enumerate(("KB", "YI"))], 2.0)
             sent = send("Y")
@@ -742,66 +1164,108 @@ def rank_program(g, core, T, topo):
             dma("y", [(x[:], whole("YL%d" % h)) for h, x in enumerate((T.yl, T.yi))], 2.0)
         else:
             prep(t + 1)
-        mm(A("P1", 80, 86), red("REDb", "MH", 0, 96))
-        ms(A("P0", 96, 97), 0.0)
-        mm(A("P0", 0, 96), [(BO, A("MH"))])
+        z0 = OPT["ins"]
+        mm(A("P7", 160, 266), [(BO, A("MH", 0, 97), A("P7", 160, 257))] + [x + (A("P7", 260, 266),) for x in red("REDb", "MH", 0, 96)])
+        due(t, z0)
         O4 = A("O4", 0, 6)
-        ts(O4, A("P1", 80, 86), MID, OP.add)
-        cp(A("BH", 0, 6), A("P1", 80, 86))
-        tt(A("BS", 48, 54), A("P1", 80, 86), A("CT", 56, 62), OP.add)
+        cp(A("BH", 0, 6), A("P7", 260, 266))
+        due(t, z0 + 0.55)
+        ts(O4, A("P7", 260, 266), MID, OP.add)
+        due(t, z0 + 0.6)
         act(A("EE"), X(KW, O4), AF.Relu, 0.0, -1.0)
-        ts(A("MB"), A("MH"), 0.0, OP.is_gt, -1.0, OP.mult)
-        mm(A("P2", 0, 24), [(If, A("RX", 48, 72))] + [(blk("MVb", 128, s), A("BH", 0, 6), blk("P2", 6, s)) for s in range(N)])
-        cp(A("O6"), A("P2", 0, 24))
+        due(t, z0 + 0.75)
+        ts(A("MB"), A("MH", 0, 96), 0.0, OP.is_gt, -1.0, OP.mult)
+        due(t, z0 + 0.1)
+        mm(A("P3", 0, 24), [(Ib, A("LV"))] + [move(MV, A("BH", 0, 6), s) + (blk("P3", 6, s),) for s in range(N)])
+        due(t, z0 + 0.75)
+        cp(A("O6"), A("P3", 0, 24))
+        due(t, z0 + 1.05)
+        (act if OPT["vbs"] else cp)(A("RX", 0, 24), A("P3", 0, 24))
+        due(t, z0 + 1.2)
         act(A("OLD", 0, 384), X(KW, A("O6")))
-        act(A("OLD", 384, 768), X(PW, A("O6")))
-        for P, terms, c, k in (("P5", newkey, [0], 0), ("P3", newpay, [1, 2], 1)):
-            mm(A(P, 0, 384), [(Ib, blk("LV", 384, x)) for x in c] + [x + (blk(P, 96, s),) for s in range(N) for x in terms[s]], stop=False)
-            mm(A(P, 0, 384), [(blk("EMB", 128, s), A("EE"), blk(P, 96, s)) for s in range(N)], start=False)
-            act(blk("SC", 384, k), A(P, 0, 384), bias=-BIG)
-        mm(A("P4", 0, 6), red("REDb", "EE", 0, 96))
+        due(t, z0 + 1.25)
+        for h in range(2):
+            mm(A("P5", 0, 384), [x + (blk("P5", 96, s),) for s in (2 * h, 2 * h + 1) for x in newkey[s]], start=not h, stop=False)
+            due(t, z0 + (0.5, 0.9)[h])
+        mm(A("P5", 0, 384), [move(A("EMB"), A("EE"), s) + (blk("P5", 96, s),) for s in range(N)], start=False)
+        due(t, z0 + 1.15)
+        act(A("SC", 0, 384), A("P5", 0, 384), bias=257.0 * 2048 - BIG)
+        due(t, z0 + 1.8)
+        for x in range(2):
+            mm(blk("P6", 96, x), newpay[x])
+            due(t, OPT["period"] - (0.5 if last else -1.5))
+            if OPT["scv"]:
+                ts(blk("SC", 96, N + x), blk("P6", 96, x), A("PK", 6 + x, 7 + x), OP.add)
+            else:
+                act(blk("SC", 96, N + x), blk("P6", 96, x), bias=A("PK", 6 + x, 7 + x))
+            due(t, OPT["period"] + (0.4 if last else 4.1))
+        mm(A("P3", 32, 38), red("REDb", "EE", 0, 96))
+        due(t, z0 + 1.6)
         for m in range(6):
-            ts(blk("NE", 97, m, 16 * m), A("P0", 16 * m, 97), A("P1", 80 + m, 81 + m), OP.not_equal)
+            ts(blk("NE", 97, m, 16 * m), A("P7", 160 + 16 * m, 257), A("P7", 260 + m, 261 + m), OP.not_equal)
+            if m % 3 == 2:
+                join(len(ops) - 3)
+                due(t, z0 + 0.65)
         scan(A("SS"), A("NE"), A("KP"), 1.0, OP.min, OP.max)
+        due(t, z0 + 1.15)
         TRY = A("SS", 96, 582, 97)
-        for s in range(N):
-            tt(A("RX", 6 * s, 6 * s + 6, p0=32 * s, p=32), A("BS", 48, 54, p0=32 * s, p=32), A("SS", 96, 582, 97, p0=32 * s, p=32), OP.mult)
-        mm(A("P2", 128, 152), [(A("AM"), A("RX", 0, 24)), (If, A("RX", 24, 48))])
-        cp(A("O5"), A("P2", 128, 152))
-        tt(A("OV", 0, 6), A("P4", 0, 6), TRY, OP.is_lt)
-        mm(A("P4", 16, 17), [(A("FO"), A("OV", m, m + 1)) for m in range(6)])
-        ts(NV(t + 1), A("P4", 16, 17), NV(9), OP.min, n, OP.add)
-        gate.extend([len(ops) - 1] if last else [])
-        tt(X(A("KT"), A("O5")), A("OLD", 0, 384), A("SC", 0, 384), OP.max)
+        mm(A("P2", 272, 296), [(If, A("RX", 24, 48))] + [move(MVn, TRY, s) + (A("P2", 272 + 6 * s, 278 + 6 * s),) for s in range(N)])
+        due(t, z0 + 1.5)
+        tt(A("RX", 72, 96), A("P2", 272, 296), A("RX", 0, 24), OP.max)
+        due(t, z0 + 1.5)
+        cp(O5, A("RX", 72, 96))
+        due(t, z0 + 1.6)
+        cp(A("O5", 24, 40), X(A("RX", 72, 96), A("PERM", 8, 9)))
+        due(t, z0 + 2.1 if last else OPT["period"] + 1.4)
+        act(A("OLD", 384, 576), X(A("PT", 0, 4096 + 384), O7))
+        due(t, OPT["period"] + (0.1 if last else 7.0))
+        tt(A("OV", 0, 6), A("P3", 32, 38), TRY, OP.is_lt)
+        due(t, z0 + 2.15 if last else OPT["period"] + 1.27)
+        mm(A("P3", 48, 49), [(A("FO"), A("OV", m, m + 1)) for m in range(6)])
+        due(t, OPT["period"] + (0.2 if last else 1.45))
+        ts(NV(t + 1), A("P3", 48, 49), n, OP.add, NV(8), OP.min)
+        due(t, OPT["period"] + (1.27 if last else 1.8))
+        if t < RO - 2:
+            ts(NV(5 + t), NV(t + 1), -0.5, OP.add)
+        tt(X(A("KT"), O5), A("OLD", 0, 384), A("SC", 0, 384), OP.max)
+        due(t, OPT["period"])
+        if not t:
+            for i in unhurried[:-1]:
+                ops[i]["after"].add(len(ops) - 1)
         del gate[:]
-        tt(X(A("PT"), A("O5")), A("OLD", 384, 768), A("SC", 384, 768), OP.max)
+        if last or not OPT["plate"]:
+            payloads()
+            due(t, OPT["period"] + 1.3)
         if not last:
-            for c in range(4):
-                spread(c)
+            spread(t + 1)
     split(RO - 1)
+    short[0] = 0
 
     def stores(q, s, n):
         x = OW * s
         y = [(T.ys[2 * s + h, :], A(n, x + 256 + 8 * h, x + 264 + 8 * h)) for h in range(2)] + [(rows(T.yn, s), A(n, x + 272, x + 273, p=32))]
         if s != r:
-            y += [(T.yk[32 * s:32 * s + 32, 256 * u:256 * u + 256], A(n, x, x + 256, p0=32 * u, p=32)) for u in range(N)]
+            y = [(T.yk[32 * s:32 * s + 32, 256 * u:256 * u + 256], A(n, x, x + 256, p0=32 * u, p=32)) for u in range(N)] + y
         dma(q[0], y[0::2], 2.5)
         dma(q[1], y[1::2], 2.5)
 
+    for c in range(4):
+        act(blk("YP", 256, c), X(PW, blk("OY", 16, c)), AF.Abs, -LIFT)
+        for b in range(2 * c, 2 * c + 2):
+            mm(A("P0", b, 128, 8), [(blk("YP", 128, b), A("GS", 16, 32))])
+    ts(A("BS"), A("P0", 64, 128), -8.0, OP.add)
     for k, d in enumerate(others + [r]):
         if d != r:
-            cp(blk("OS", OW, d, 0, 256), X(KW, blk("OK", 16, d)))
-        act(blk("YP", 256, d), X(PW, blk("OY", 16, d)), AF.Abs, -1.0)
-        P = "P%d" % k
-        for h in range(2):
-            mm(A(P, h, 16, 2), [(blk("YP", 256, d, 128 * h, 128 * h + 128), A("GS", 8, 16))])
-        cp(blk("OS", OW, d, 256, 272), A(P, 0, 16))
+            (act if k in OPT["oss"] else cp)(blk("OS", OW, d, 0, 256), X(KW, blk("OK", 16, d)))
+        tt(blk("OS", OW, d, 256, 272), blk("P0", 16, d), blk("BS", 16, d), OP.add)
         act(blk("OS", OW, d, 272, 273), NV(RO))
-        if d != r:
+        if d != r and not OPT["oh"]:
             sent = send("O%d" % k)
+        elif 0 < k < N - 1:
+            sent = send(("O", "Op")[k - 1])
     dma("y", [(T.yk[32 * r:32 * r + 32, 512 * h:512 * h + 512], A("KT", a, a + 512, p=32)) for h, a in enumerate((512 * r, _high(r)))], 2.5)
     stores("sy", r, "OS")
     for k, s in enumerate(cross + [peer]):
-        arrive("o%d" % s, 2 * off, [blk("OL", OW, s)], sent, 0.5 + 0.5 * k)
+        arrive("o%d" % s, _landing(T, topo, routes, r, "o%d" % s), [blk("OL", OW, s)], sent, 0.5 + 0.5 * k)
         stores(("sy", "ys")[k % 2], s, "OL")
     _issue(T, Q, ops)

from concourse.bass import DstId, RemoteDMATransfer
from concourse.mybir import AluOpType as OP, AxisListType, ActivationFunctionType as AF

N, RO, NCORES = 4, 3, 256
LW, DW, OW = 32, 96, 280
TW = 8256
BIG, LIFT = float(2 ** 22), float(2 ** 21)
F, H, B, I, U = "float32", "float16", "bfloat16", "int32", "uint16"
OPT = {"ehs": 1, "emd": 0, "ohs": 0, "fuse": [(), (), ()], "wheel": 2500, "wcase": 0, "wheat": 0.3, "wmoves": 1, "ll": 2.6, "lk": 3.5, "lp": 4.5, "tabs": 4.0, "kh": 0, "kp": 0, "pp": 1, "oh": 0, "op": 0, "oss": (), "loads": (None, None, None), "by": ("sv", "sv", "sv", "vv", "vv"), "early": 6.0, "gob": "P4", "tail": 11.0, "period": 13.2, "plate": 1, "eq": (2.2, 3.4, 3.85, 4.4), "oh0": 6.3,
       "w3": (2.7, 4.85, 5.55, 7.45), "vbs": 0, "cut": 0.0, "tf": 1, "ppe": "", "pt0": 2.3, "pt1": 0.25, "w30": (5.0, 5.7, 7.45, 8.2), "ins": 10.9, "ws": (4.6, 5.95, 6.4, 8.5), "pg": 9, "mean": 0.0, "pb": "56", "ids": 3, "selg": 16, "dat": 1.0, "made": "", "e2": "P4", "ig": 12.45, "k2": 10.45, "shake": 0.3, "turns": 1, "steps": 6000, "heat": 0.1,
       "fuse": [(0,), (0, 1), (0, 1)], "eq": (1.4, 2.1, 2.85, 3.3), "w3": (4.95, 5.65, 7.45, 8.2), "ws": (5.95, 6.4, 8.3, 8.9), "cut": 1.1, "oh": 1,
       "by": ("vs", "sv", "sv", "vv", "vs"), "pg": 11, "pt0": 1.5, "lp": 4.5, "scv": 0, "tiny": 64, "tiny0": 128, "made": "", "share": 1.0, "loads": (None, 4, 7), "jk": 0, "seed": 5, "ids": 10,
       "wheel": 3000, "steps": 12000}


def _sb(w, d):
    return ("sbuf", [128, w], d)


def _dr(w, d):
    return ("dram", [128 * N, w], d)


SCRATCH = {
    "KT": _sb(TW, F), "PT": _sb(TW, F), "TKI": _sb(1024, I), "TPI": _sb(1024, I), "KS": _sb(2048, H), "PS": _sb(2048, H),
    "KL": _sb(2048, H), "PL": _sb(2048, H), "DS": _dr(DW, I), "DL": _dr(DW, I), "QM": _sb(512, B),
    "LS0": _dr(LW, I), "LL0": _dr(LW, I), "LS1": _dr(LW, I), "LL1": _dr(LW, I), "LN": _sb(640, I), "PNI": _sb(4, I),
    "YS0": _dr(LW, F), "YL0": _dr(LW, F), "YS1": _dr(LW, F), "YL1": _dr(LW, F), "OF": _sb(192, F),
    "OS": _sb(N * OW, F), "OL": _sb(N * OW, F), "YP": _sb(1024, F), "YI": _sb(128, F),
    "W1": _sb(2048, F), "EQ": _sb(2048, B), "GB": _sb(32, B), "W3": _sb(2048, F),
    "TM": _sb(128 * 8, F), "TN": _sb(128 * 8, I),
    "IOTA": _sb(144, F), "PCI": _sb(16, I), "PC": _sb(32, F), "MI": _sb(128, I), "MG": _sb(128, I),
    "BOb": _sb(256, B), "SUM": _sb(512 * 2, B), "Ib": _sb(128, B), "If": _sb(128, F), "XM": _sb(128, B), "FO": _sb(128, B),
    "EMB": _sb(512, B), "SEL": _sb(2048, B), "RED": _sb(144, B), "TB": _sb(1024, B),
    "MVb": _sb(512, B), "GS": _sb(32, F), "TF": _sb(512, B), "PB": _sb(512, B), "LV": _sb(24, B),
    "RS4": _sb(512, B),
    "C128": _sb(1024, B), "KR": _sb(192, F), "KP": _sb(582, B), "PERM": _sb(10, U), "CT": _sb(96, F),
    "XO": _sb(8, F), "OK": _sb(64, U), "OY": _sb(64, U),
    "KB": _sb(128, F), "YT": _sb(288, F), "K2": _sb(128, I), "Z2": _sb(128, I), "HI": _sb(128, I),
    "E1": _sb(128, I), "EH": _sb(256, H), "TO": _sb(256, B), "OG": _sb(512, B), "IG": _sb(512, B),
    "GOB": _sb(512, B), "FL": _sb(512, B), "OFF": _sb(128, U), "IDS": _sb(128 * 15, B), "DF": _sb(384, F),
    "TPF": _sb(1024, F), "SUP": _sb(128 * 10, B), "SN": _sb(256, B),
    "TS": _sb(128, F), "CM": _sb(128, B), "MVn": _sb(1024, B), "NG": _sb(128, B),
    "HM": _sb(512, F), "NW": _sb(128, B), "RX": _sb(96, F), "PK": _sb(16, F), "EM": _sb(1024, I if OPT["emd"] else F),
    "OH": _sb(1024, B), "INC": _sb(1024, B), "E2": _sb(64, F), "JK": _sb(1152, B),
    "PLC": _sb(384, B), "VB": _sb(8, B), "C2": _sb(96, B), "XS": _sb(1024, F), "MK": _sb(96, F), "MH": _sb(98, H), "ME": _sb(96, H),
    "MB": _sb(96, H), "O1": _sb(16, U), "O3": _sb(8, U), "O4": _sb(8, U), "O5": _sb(40, U), "BS": _sb(64, F),
    "NE": _sb(582, B), "SS": _sb(582, B), "EE": _sb(96, B), "OLD": _sb(768, F), "O6": _sb(24, U), "SC": _sb(768, F),
    "OV": _sb(8, B), "BH": _sb(8, H), "NN": _sb(32, F), "SG": _sb(8, U),
    "SX": _sb(64, F), "SI": _sb(64, I), "SK": _sb(320, F),
}
for _b in range(8):
    SCRATCH["P%d" % _b] = ("psum", [128, 512], F)
SEMAPHORES = (["cv", "cs", "ct", "cg", "lan", "drawn", "ylan", "lo"] + [a + "%d" % s for a in "kpo" for s in range(N)]
              + [a + b for a in "hl" for b in ("L", "K", "P", "D", "Y", "O0", "O1", "O2", "Kp", "Pp", "O", "Op")] + ["d%d" % i for i in range(48)])
ROUTES, PLAN = [], []
CYC = 0.87e-3
CASES = [{"cycle": 0.83e-3, "v": 0.0, "s": 0.05, "gather": 1.56, "scatter": 3.8, "wake": 0.18, "same": 0.18, "pe_out": 0.03, "pe": 0.55, "dma": 1.0, "weight": 1.0},
         {"cycle": 1.1e-3, "v": 0.0, "s": 0.14, "gather": 1.9, "scatter": 5.0, "wake": 0.3, "same": 0.3, "pe_out": 0.03, "pe": 0.5, "dma": 1.5, "weight": 0.6},
         {"cycle": 0.85e-3, "v": 0.0, "s": 0.07, "gather": 1.25, "scatter": 2.6, "wake": 0.27, "same": 0.27, "pe_out": 0.05, "pe": 0.5, "dma": 0.9, "weight": 1.0}]
LATE = (2.0, 2.3)


def _mask(engines):
    return sum(1 << e for e in engines)


def _routes(T, topo):
    R = list(T.cores)
    out = []
    for s, c in enumerate(R):
        peer = [d for d in range(N) if d != s and topo.may_write(c, R[d])][0]
        cross = [d for d in range(N) if d != s and d != peer]
        rest = [h for h in topo.cores_of(c) if h != c]
        ports = [h for h in rest if all(topo.may_write(h, R[d]) for d in cross)]
        same = [h for h in rest if topo.die(h) == topo.die(c)]
        out.append({"peer": peer, "cross": cross, "near": [h for h in ports if h in same], "far": [h for h in ports if h not in same],
                    "side": [h for h in same if h not in ports][0], "plain": [h for h in rest if h not in ports and h not in same]})
    return out


def _high(s):
    return 2048 + 512 * ((s - 1) % N)


def _dst(topo, d, c):
    rid, pid = topo.addr(d, c)
    return DstId(rid=rid, pnc=pid)


def _shares(engines, n):
    k = len(engines) // n
    return [engines[k * j:k * j + k] for j in range(n)]


def _messages(T, topo, routes, s):
    R = list(T.cores)
    ro = routes[s]
    peer, cross = ro["peer"], ro["cross"]
    off = topo.engines(R[s], R[peer])
    rest = [e for e in topo.engines(R[s], ro["side"]) if e not in off]
    half = [rest[:len(rest) // 2], rest[len(rest) // 2:]]
    out = []

    def call(name, bufs, w, sem, *ways):
        for k, (d, eng) in enumerate(zip([peer] + cross, [off] + half)):
            for buf, vias, e in zip(bufs, ways, _shares(eng, len(bufs))):
                out.append((name, buf, 0, w, d, vias[k], e, sem))
    die = [(k + routes[d]["cross"].index(s)) % 2 for k, d in enumerate(cross)]
    here, there = [None] + ro["near"], ro["plain"][:1] + ro["far"]
    call("L", ["LL0", "LL1"], LW, "lan", here, there)
    def halves(name, buf, w, sem, way):
        for k, d in enumerate(cross):
            for h in range(2):
                out.append((name, buf, w // 2 * h, w // 2, d, ro[("near", "far")[h]][k], _shares(off + rest, 4)[2 * k + h], sem))
        if way == 2:
            for h in range(2):
                out.append((name + "p", buf, w // 2 * h, w // 2, peer, (None, ro["plain"][0])[h], (off, rest)[h], sem))
        else:
            out.append((name + "p", buf, 0, w, peer, ro["plain"][0] if way else None, off + rest if way else off, sem))
    if OPT["kh"]:
        halves("K", "KL", 512, "k%d" % s, OPT["kp"])
        halves("P", "PL", 512, "p%d" % s, OPT["pp"])
    else:
        call("K", ["KL"], 512, "k%d" % s, [None] + [ro[("near", "far")[die[k]]][0] for k in range(2)])
        call("P", ["PL"], 512, "p%d" % s, [ro["plain"][0]] + [ro[("far", "near")[die[k]]][1] for k in range(2)])
    call("D", ["DL"], DW, "drawn", there)
    call("Y", ["YL0", "YL1"], LW, "ylan", here, there)
    if OPT["oh"]:
        halves("O", "OL", OW, "o%d" % s, OPT["op"])
    else:
        for k, d in enumerate(cross + [peer]):
            vias = (ro["far"][k], ro["near"][k]) if d != peer else (ro["plain"][0], None)
            for h in range(2):
                out.append(("O%d" % k, "OL", OW // 2 * h, OW // 2, d, vias[h], (rest, off)[h], "o%d" % s))
    return out


def _landing(T, topo, routes, r, sem):
    R = list(T.cores)
    total = 0
    for s in range(N):
        mine = _messages(T, topo, routes, s)
        for n, buf, a, w, d, via, e, x in mine:
            if d == r and x == sem:
                total += len(e) if via is None else len(topo.engines(via, R[r])) // len([m for m in mine if m[0] == n and m[5] == via])
    return total


def _slot(buf, k, a, w):
    where, shape, dtype = SCRATCH[buf]
    return (128 * k, 0) if where == "dram" else (0, shape[1] // N * k + a)


def helper_program(g, core, T, topo, routes):
    R = list(T.cores)
    home = [s for s in range(N) if core in topo.cores_of(R[s])]
    if not home:
        return
    s = home[0]
    total = 0
    calls = {}
    for m in _messages(T, topo, routes, s):
        if m[5] == core:
            calls.setdefault(m[0], []).append(m)
    for name, items in calls.items():
        out = topo.engines(core, R[items[0][4]])
        moves = []
        for (n, buf, a, w, d, via, eng, sem), e in zip(items, _shares(out, len(items))):
            p, c = _slot(buf, s, a, w)
            ap = T[buf][p:p + 128, c:c + w]
            moves.append(RemoteDMATransfer(dst_ids=[_dst(topo, R[d], core)], dma_engine_mask=_mask(e), remote_sem=T.sem[sem], src=ap, dst=ap))
        g.wait_ge(T.sem["h" + name], sum(len(m[6]) for m in items))
        g.remote_dma_fused(moves, local_sem=T.sem.lo)
        total += len(out)
    if total:
        g.wait_ge(T.sem.lo, total)


def _order(ops):
    if OPT.get("cases"):
        CASES[:] = OPT["cases"]
    n = len(ops)
    qs = [o["q"] for o in ops]
    banks = [o["banks"] for o in ops]
    cases = []
    for c in CASES:
        cost = [_cost(o["q"], o["cost"], c) for o in ops]
        busy = [cost[i] if o["busy"] is None else o["busy"] for i, o in enumerate(ops)]
        done = [cost[i] + (c["pe_out"] if qs[i] == "t" else 0.0) for i in range(n)]
        pred = [[(j, done[j] + (c["same"] if qs[j] == qs[i] else c["wake"])) for j in o["dep"]]
                + [(j, cost[j] if qs[i] == "a" else busy[j]) for j in o["after"]] for i, o in enumerate(ops)]
        succ = [[] for o in ops]
        for i in range(n):
            for j, lag in pred[i]:
                succ[j].append((i, lag))
        cases.append((cost, busy, done, pred, succ, c["wake"]))

    def gap(spans, t, w, pad, q):
        x = max(0, len(spans) - 1)
        while x and spans[x - 1][1] + pad > t:
            x -= 1
        for a, b, p in spans[x:]:
            if p == q and pad:
                continue
            if b + pad <= t:
                continue
            if t + w + pad <= a + 1e-9:
                break
            t = b + pad
        return t

    def put(spans, span):
        x = len(spans)
        while x and spans[x - 1] > span:
            x -= 1
        spans.insert(x, span)

    def pack(case, key, back):
        cost, busy, done, pred, succ, wake = case
        before, behind = (succ, pred) if back else (pred, succ)
        left = [len(x) for x in before]
        at = [0.0] * n
        spans = {}
        pool = [i for i in range(n) if not left[i]]
        while pool:
            i = min(pool, key=key.get)
            pool.remove(i)
            if back:
                t = max([cost[i]] + [at[k] + lag for k, lag in succ[i]]) - busy[i]
            else:
                t = max([0.0] + [at[j] + lag for j, lag in pred[i]])
            if qs[i] != "a":
                mine = spans.setdefault(qs[i], [])
                while True:
                    t = t0 = gap(mine, t, busy[i], 0.0, "")
                    for b in banks[i]:
                        t = gap(spans.setdefault(b, []), t, busy[i], wake, qs[i])
                    if t == t0:
                        break
                put(mine, (t, t + busy[i], ""))
                for b in banks[i]:
                    put(spans[b], (t, t + busy[i], qs[i]))
            at[i] = t + busy[i] if back else t
            for k, lag in behind[i]:
                left[k] -= 1
                if not left[k]:
                    pool.append(k)
        return at

    held = [[b + qs[i] for b in banks[i]] for i in range(n)]
    rivals = [[b + p for b in banks[i] for p in "vst" if p != qs[i]] for i in range(n)]
    idle = {k: (0.0, -1) for x in held + rivals + [qs] for k in x}

    def replay(case, order):
        cost, busy, done, pred, succ, wake = case
        at, why, turn = [0.0] * n, [-1] * n, [False] * n
        free = dict(idle)
        end, last = 0.0, 0
        for i in order:
            t, w = free[qs[i]]
            for k in rivals[i]:
                if free[k][0] > t:
                    t, w = free[k]
            turn[i] = True
            for j, lag in pred[i]:
                if at[j] + lag >= t:
                    t, w, turn[i] = at[j] + lag, j, False
            at[i], why[i] = t, w
            if qs[i] != "a":
                free[qs[i]] = (t + busy[i], i)
            for k in held[i]:
                free[k] = (t + done[i] + wake, i)
            if t + cost[i] > end:
                end, last = t + cost[i], i
        turns = []
        while last >= 0:
            if turn[last] and why[last] >= 0:
                turns.append((why[last], last))
            last = why[last]
        return end + OPT["mean"] * sum(at) / n, turns

    def score(order):
        runs = [replay(c, order) for c in cases]
        return sum(x[0] * w["weight"] for x, w in zip(runs, CASES)), [x[1] for x in runs]

    def mend(order, steps):
        need = [set(j for j, lag in p) for p in cases[0][3]]
        end, turns = score(order)
        seed = 1
        for step in range(steps):
            seed = (seed * 1103515245 + 12345) % 2 ** 31
            chain = turns[(seed >> 8) % len(turns)]
            if not chain:
                continue
            a, b = chain[(seed >> 12) % len(chain)]
            x, y = order.index(a), order.index(b)
            if seed >> 28 & 1:
                x = max(0, x - (seed >> 20) % 24)
                part = {b}
                for k in reversed(order[x:y]):
                    if any(k in need[j] for j in part):
                        part.add(k)
                if a in part:
                    continue
                new = order[:x] + [k for k in order[x:y + 1] if k in part] + [k for k in order[x:y + 1] if k not in part] + order[y + 1:]
            else:
                y = min(n - 1, y + (seed >> 20) % 24)
                part = {a}
                for k in order[x + 1:y + 1]:
                    if need[k] & part:
                        part.add(k)
                if b in part:
                    continue
                new = order[:x] + [k for k in order[x:y + 1] if k not in part] + [k for k in order[x:y + 1] if k in part] + order[y + 1:]
            e, tn = score(new)
            if e <= end + OPT["heat"] * (1.0 - step / steps):
                order, end, turns = new, e, tn
        return order

    best = None
    big = [i for i in range(n) if ops[i]["cost"] == ("gather", 512)][0]
    PLAN.append(n)
    for start, case in enumerate(cases):
        cost, busy, done, pred, succ, wake = case
        level = [0.0] * n
        for i in range(n - 1, -1, -1):
            level[i] = ops[i]["due"] * cost[big] / cases[0][0][big] if "due" in ops[i] else max([cost[i]] + [level[k] + lag for k, lag in succ[i]])
        mine = None
        for turn in range(OPT["turns"]):
            at = pack(case, {i: (-level[i], i) for i in range(n)}, False)
            order = sorted(range(n), key=lambda k: (at[k], k))
            end = score(order)[0]
            if mine is None or end < mine[0]:
                mine = (end, at, order)
            if turn % 2:
                at = [x + OPT["shake"] * (((i + 1) * (turn + 7) * 2654435761 >> 7) % 1000) / 1000.0 for i, x in enumerate(mine[1])]
            level = pack(case, {i: (-(at[i] + busy[i]), i) for i in range(n)}, True)
        if best is None or mine[0] < best[0]:
            best = mine
    if OPT["wheel"]:
        case = cases[OPT["wcase"]]
        cost, busy, done, pred, succ, wake = case
        key = list(best[1])
        seed = OPT["seed"]
        for turn in range(OPT["wheel"]):
            want = list(key)
            for i in range(n - 1, -1, -1):
                want[i] = min([want[i]] + [want[k] - lag for k, lag in succ[i]])
            at = pack(case, {i: (want[i], i) for i in range(n)}, False)
            order = sorted(range(n), key=lambda k: (at[k], k))
            end, turns = score(order)
            if end < best[0]:
                best = (end, at, order)
            if not turn or end < best[0] + OPT["wheat"] * (1.0 - turn / OPT["wheel"]) or end < here:
                here = end
                base, chains = at, turns
            key = list(base)
            for x in range(OPT["wmoves"]):
                seed = (seed * 1103515245 + 12345) % 2 ** 31
                chain = chains[(seed >> 8) % len(chains)]
                if chain:
                    a, b = chain[(seed >> 12) % len(chain)]
                    if (seed >> 26) % 3 == 2:
                        near = [k for k in range(n) if qs[k] == qs[a] and base[a] - 3.0 < base[k] <= base[a] and busy[k] > 0.1]
                        if near:
                            a = near[(seed >> 4) % len(near)]
                        key[a] = base[a] - 0.2 - ((seed >> 20) % 16) * 0.15
                    elif (seed >> 26) % 3:
                        key[b] = base[a] - 0.01 - ((seed >> 20) % 16) * 0.1
                    else:
                        key[a] = base[b] + 0.01 + ((seed >> 20) % 16) * 0.1
        PLAN.append(["wheel", best[0]])
    order = mend(best[2], OPT["steps"])
    PLAN.append([replay(c, order)[0] for c in cases])
    return order


def _cost(q, x, c):
    if isinstance(x, list):
        return sum(_cost(q, y, c) for y in x)
    kind, size = x if isinstance(x, tuple) else ("us", x)
    if kind == "us":
        return size * c["dma"]
    if kind == "pe":
        return size * c["cycle"] * c["pe"]
    if kind == "plain":
        return c["s"] + size * c["cycle"] if q == "s" else c["v"] + max(64, size) * c["cycle"]
    return max(0.05, c[q]) + c[kind] * size * c["cycle"]


def _issue(T, Q, ops):
    if not PLAN:
        PLAN.insert(0, _order(ops))
    clock = {q: {} for q in Q}
    count = {q: 0 for q in Q}
    event = [None] * len(ops)
    final = {}
    holder = {}
    left = list(PLAN[0])
    while left:
        i = [k for k in left if all(event[j] for j in ops[k]["dep"] | ops[k]["after"])][0] if any(not event[j] for j in ops[left[0]]["dep"] | ops[left[0]]["after"]) else left[0]
        left.remove(i)
        o = ops[i]
        q = o["q"]
        if q == "a":
            event[i] = (o["sem"], o["val"], {o["sem"]: o["val"]})
            final[o["sem"]] = o["val"]
            continue
        ck = clock[q]
        want = {}
        dep = set(o["dep"])
        for b in o["banks"]:
            dep.update(j for p, j in holder.setdefault(b, {}).items() if p != q)
            holder[b][q] = i
        for j in dep:
            ev = event[j]
            if ev[1] > want.get(ev[0], (0, 0))[1]:
                want[ev[0]] = ev
        for ev in sorted(want.values(), key=lambda e: -len(e[2])):
            if ck.get(ev[0], 0) < ev[1]:
                Q[q].wait_ge(T.sem[ev[0]], ev[1])
                for k, x in ev[2].items():
                    if ck.get(k, 0) < x:
                        ck[k] = x
        ins = o["fn"]()
        if o["sem"] is None:
            for x in ins if isinstance(ins, list) else [ins]:
                count[q] += 1
                x.then_inc(T.sem["c" + q], 1)
            sem, val = "c" + q, count[q]
        else:
            sem, val = o["sem"], o["val"]
        c2 = dict(ck)
        c2[sem] = val
        event[i] = (sem, val, c2)
        final[sem] = val
    for sem, val in final.items():
        Q["g"].wait_ge(T.sem[sem], val)


def rank_program(g, core, T, topo):
    if not ROUTES:
        ROUTES.extend(_routes(T, topo))
    routes = ROUTES
    r = T.rank_of(core)
    if r is None:
        helper_program(g, core, T, topo, routes)
        return
    R = list(T.cores)
    ro = routes[r]
    ops, hist, gate = [], {}, []

    def A(n, a=0, b=None, st=1, p=128, p0=0):
        if b is None:
            b = SCRATCH[n][1][1]
        return (T[n][p0:p0 + p, a:b:st] if st > 1 else T[n][p0:p0 + p, a:b], [(n, a, b, st, p0, p0 + p)], (b - a + st - 1) // st, False)

    def X(win, off):
        return (win[0].indirect(off[0]), win[1] + off[1], 16 * off[2], True)

    def run(q, outs, ins, fn, cost, busy=None, sem=None, val=0, after=()):
        rd = [s for x in ins if isinstance(x, tuple) for s in x[1]]
        wr = []
        for x in outs:
            if isinstance(x, tuple):
                wr.append(x[1][0])
                rd.extend(x[1][1:])
        me, dep, aft = len(ops), set(), set(after) | set(gate)
        for spans, w in ((rd, False), (wr, True)):
            for n, a, b, st, p, e in spans:
                for a2, b2, s2, p2, e2, w2, q2, j in hist.get(n, []):
                    meet = a < b2 and a2 < b and p < e2 and p2 < e
                    if (w or w2) and meet and (st == 1 or st != s2 or (a - a2) % st == 0):
                        (aft if q == "t" and q2 == "t" else dep).add(j)
        for spans, w in ((rd, False), (wr, True)):
            for n, a, b, st, p, e in spans:
                h = hist.setdefault(n, [])
                if w and st == 1:
                    h[:] = [x for x in h if not (a <= x[0] and x[1] <= b and p <= x[3] and x[4] <= e)]
                h.append((a, b, st, p, e, w, q, me))
        ops.append({"q": q, "fn": fn, "dep": dep, "after": aft - dep, "cost": cost, "busy": busy, "sem": sem, "val": val,
                    "banks": sorted(set(x[0] for x in rd + wr if SCRATCH[x[0]][0] == "psum"))})
        return me

    def join(first):
        part = ops[first:]
        del ops[first + 1:]
        ops[first] = dict(part[0], fn=lambda: [o["fn"]() for o in part], cost=[o["cost"] for o in part], banks=sorted(set(b for o in part for b in o["banks"])),
                          dep=set(j for o in part for j in o["dep"] if j < first), after=set(j for o in part for j in o["after"] if j < first))
        for h in hist.values():
            h[:] = [x[:7] + (min(x[7], first),) for x in h]

    def ap(x):
        return x[0] if isinstance(x, tuple) else x

    def cyc(o, ins, f=1.0):
        if o[3]:
            return ("scatter", o[2])
        if ins[0][3]:
            return ("gather", o[2])
        if f == 0.5 and not all(SCRATCH[x[1][0][0]][2] in (H, B, U) for x in [o] + ins):
            f = 1.0
        return ("plain", f * o[2])

    def ts(o, i, s1, op0, s2=None, op1=None):
        if op1 is None:
            run("v", [o], [i, s1], lambda: g.vector.tensor_scalar(o[0], i[0], ap(s1), None, op0), cyc(o, [i], 0.5))
        else:
            run("v", [o], [i, s1, s2], lambda: g.vector.tensor_scalar(o[0], i[0], ap(s1), ap(s2), op0, op1), cyc(o, [i], 0.5))

    def tt(o, a, b, op):
        ps = any(SCRATCH[x[1][0][0]][0] == "psum" for x in (a, b))
        run("v", [o], [a, b], lambda: g.vector.tensor_tensor(o[0], a[0], b[0], op), cyc(o, [a], 1.0 if ps else 2.0))

    def cp(o, i):
        run("v", [o], [i], lambda: g.vector.tensor_copy(o[0], i[0]), cyc(o, [i], 0.5))

    def ms(o, c):
        run("v", [o], [], lambda: g.vector.memset(o[0], c), cyc(o, [o], 0.5))

    def scan(o, d0, d1, init, op0, op1):
        run("v", [o], [d0, d1], lambda: g.vector.tensor_tensor_scan(o[0], d0[0], d1[0], init, op0, op1), cyc(o, [d0, d1], 0.5))

    def turn(o, i):
        run("v", [o], [i], lambda: g.vector.transpose(o[0], i[0]), cyc(o, [i]))

    short = [OPT["tiny0"]]

    def act(o, i, f=AF.Identity, bias=0.0, scale=1.0, acc=None):
        if f == AF.Identity and o[2] <= short[0] and not i[3]:
            ts(o, i, scale, OP.mult, bias, OP.add)
        elif acc is None:
            run("s", [o], [i, bias, scale], lambda: g.scalar.activation(o[0], i[0], f, bias=ap(bias), scale=ap(scale)), cyc(o, [i]))
        else:
            run("s", [o, acc], [i, bias], lambda: g.scalar.activation(o[0], i[0], f, bias=ap(bias), scale=scale, accum_out=acc[0]), ("plain", o[2] + 24))

    def mm(o, terms, start=True, stop=True):
        def fn():
            for k, x in enumerate(terms):
                last = g.tensor.matmul((x + (o,))[2][0], x[0][0], x[1][0], start and k == 0, stop and k == len(terms) - 1)
            return last
        c = sum(max(min(64, x[0][2]), x[1][2]) * (4 if SCRATCH[x[0][1][0][0]][2] == F else 1) for x in terms)
        run("t", [o if start and stop else A(o[1][0][0])], [y for x in terms for y in x[:2]], fn, ("pe", c))

    def red(mat, n, a, b):
        return [(A("RED", 15 - i, 143 - i), A(n, a + i, b, 16)) for i in range(16)]

    def move(mat, x, u):
        n, a = mat[1][0][:2]
        return (A(n, a + 128 * u, a + 128 * u + 128), x)

    Q = {"v": g.vector, "s": g.scalar, "t": g.tensor, "g": g, "y": g.sync}
    dmas = {"s": [], "y": [], "g": []}
    nd = [0]

    def dma(q, pairs, cost):
        sem = "d%d" % nd[0]
        nd[0] += 1

        def fn():
            for o, i in pairs:
                Q[q].dma_start(ap(o), ap(i)).then_inc(T.sem[sem], 16)
        dmas[q].append(run(q, [o for o, i in pairs], [i for o, i in pairs], fn, cost, 0.08 * len(pairs), sem, 16 * len(pairs), dmas[q][-1:]))

    def piece(buf, k, a, w):
        p, c = _slot(buf, k, a, w)
        return A(buf, c, c + w, p0=p)

    sends = []

    def send(name):
        items = [(piece(buf[0] + "S" + buf[2:], d, a, w), piece(buf, r, a, w), R[d] if via is None else via, e, sem if via is None else "h" + name)
                 for n, buf, a, w, d, via, e, sem in _messages(T, topo, routes, r) if n == name]
        sends.append(run("g", [], [x[0] for x in items],
                         lambda: g.remote_dma_fused([RemoteDMATransfer(dst_ids=[_dst(topo, d, core)], dma_engine_mask=_mask(e), remote_sem=T.sem[sem],
                                                                       src=x[0], dst=y[0]) for x, y, d, e, sem in items], local_sem=T.sem["l" + name]),
                         3.0 if sends else 5.0, 0.6 if sends else 2.8, "l" + name, sum(len(x[3]) for x in items), sends[-1:]))
        return sends[-1]

    def whole(buf):
        return A(buf, p=128 * N)

    def arrive(sem, val, outs, after, cost):
        run("a", outs, [], None, cost, 0.0, sem, val, [after])

    def f(k):
        return A("TM", 128 * k, 128 * k + 128)

    def z(k):
        return A("TN", 128 * k, 128 * k + 128)

    def v(k):
        return A("P7", 128 * k, 128 * k + 128)

    def blk(n, w, k, a=0, b=None):
        return A(n, w * k + a, w * k + (w if b is None else b))

    peer, cross = ro["peer"], ro["cross"]
    off = len(topo.engines(core, R[peer]))
    others = cross + [peer]

    def rows(x, d):
        return x[32 * d:32 * d + 32, :]
    for h, x in enumerate((T.lk, T.li)):
        dma("sy"[h], [(whole("LS%d" % h), x[:])], 1.6)
    for k, d in enumerate(others):
        dma("sy"[k % 2], [(blk("TKI", 256, d), rows(T.tk, d))], 1.9 + 0.4 * k)
    def behind(k):
        if k is not None:
            ops[-1]["dep"].add(k)
    w = OPT["loads"]
    for k, d in enumerate(others):
        dma("y", [(blk("TPI", 256, d), rows(T.tp, d))], 1.9 + 0.4 * k)
        behind(w[0])
    dma("y", [(piece("LL%d" % h, r, 0, LW), rows(x, r)) for h, x in enumerate((T.lk, T.li))]
        + [(A("PNI", 0, 1, p0=32 * u, p=32), rows(T.pn, r)) for u in range(N)], 2.8)
    dma("y", [(blk("TKI", 256, r), rows(T.tk, r)), (blk("TPI", 256, r), rows(T.tp, r))], 2.2)
    behind(w[1])
    dma("y", [(whole("DS"), T.dk[:]), (piece("DL", r, 0, DW), rows(T.dk, r))], 2.2)
    behind(w[2])

    def iota(o, pattern, base, step=0):
        run("g", [o], [], lambda: g.iota(o[0], pattern, base, step, allow_small_or_imprecise_dtypes=True), 0.13 + 2 * o[2] * CYC)
    iota(A("PCI", 0, 1), [[1, 1]], 0, 1)
    iota(A("IOTA"), [[1, 144]], 0)

    sent = send("L")
    arrive("lan", _landing(T, topo, routes, r, "lan"), [piece("LL%d" % h, s, 0, LW) for s in others for h in range(2)], sent, OPT["ll"])
    dma("y", [(A("LN", 128 * h, 128 * h + 128), whole("LL%d" % h)) for h in range(2)], 1.6)

    def parts(n, d, x):
        if n[0] == "K":
            act(blk(n, 512, d, 0, 256), blk("TKI", 256, d), scale=1.0 / 32)
        else:
            act(blk(n, 512, d, 0, 256), x)
        tt(blk(n, 512, d, 256), x, blk(n, 512, d, 0, 256), OP.subtract)

    def stage(d):
        return A("P%d" % (0, 1, 6, 7)[(others + [r]).index(d)], 256, 512)

    def keys(d):
        x = stage(d)
        ts(x, blk("TKI", 256, d), 1.0 / 32, OP.mult)
        parts("KS" if d != r else "KL", d, x)

    def pays(d):
        x = stage(d)
        ts(x, x, 1.0 / 64, OP.add, 1.0 / 64, OP.min)
        act(blk("TPF", 256, d), blk("TPI", 256, d), bias=0.5)
        tt(x, x, blk("TPF", 256, d), OP.mult)
        parts("PS" if d != r else "PL", d, x)
    for d in others:
        keys(d)
    gate.append(len(ops) - 1)
    sentK = send("K")
    ops[-1]["due"] = OPT["tail"] + OPT["period"] * RO + 14.0
    if OPT["kh"]:
        sentKp = send("Kp")

    def select(o, i, pattern, op, fill):
        run("g", [o], [i], lambda: g.affine_select(o[0], i[0], pattern, op, fill, 0, 1), 0.17 + 2 * o[2] * CYC)
        gate[:] = [len(ops) - 1]
    for d in others:
        pays(d)
    gate.append(len(ops) - 1)
    sending = [i for i in range(len(ops)) if ops[i]["q"] == "v"]
    sentP = send("P")
    ops[-1]["due"] = OPT["tail"] + OPT["period"] * RO + 12.0
    if OPT["kh"]:
        sentPp = send("Pp")
    keys(r)
    pays(r)
    del gate[:]
    for k, s in enumerate([peer] + cross):
        arrive("k%d" % s, _landing(T, topo, routes, r, "k%d" % s), [blk("KL", 512, s)], sentK, OPT["lk"] if k else 1.0)
        arrive("p%d" % s, _landing(T, topo, routes, r, "p%d" % s), [blk("PL", 512, s)], sentP, OPT["lp"] if k else 1.5)
    if OPT["kh"]:
        sentP = sentPp

    consts = len(ops)

    def early():
        ops[-1]["due"] = OPT["tail"] + OPT["period"] * RO + OPT["early"]

    def pc(k):
        return A("PC", k, k + 1)

    def pi(k):
        return A("PCI", k, k + 1)
    PI, PG, PU, PF, PP, B15 = pc(0), pc(1), pc(2), pc(3), pc(12), pc(13)
    ts(pi(1), pi(0), 15, OP.bitwise_and)
    ts(pi(2), pi(0), 4, OP.arith_shift_right)
    ts(pi(3), pi(0), 5, OP.arith_shift_right)
    ts(pi(4), pi(0), 4, OP.arith_shift_right, 1, OP.bitwise_and)
    cp(A("PC", 0, 4), A("PCI", 1, 5))
    cp(PP, pi(0))
    cp(z(0), A("IOTA", 0, 128))
    ts(A("MI"), z(0), 15, OP.bitwise_and)
    ts(A("MG"), z(0), 4, OP.arith_shift_right)
    BO, Ib, If, XM = A("BOb", 0, 128), A("Ib"), A("If"), A("XM")
    ts(BO, A("MG"), PG, OP.is_equal)
    mid = [(512.0 * u + _high(u) + 512) / 2 for u in range(N)]
    bit = [((512 * u) // 1024, (_high(u) - 2048) // 1024) for u in range(N)]
    rest = [1024.0 * mid[u] - (2.0 ** 20 - 1) * bit[u][0] + LIFT - 2 for u in range(N)]
    MID, NEG = A("PK", 0, 1), A("PK", 1, 2)
    ts(A("PK", 8, 8 + N), A("IOTA", 0, N), PU, OP.is_equal)
    ts(A("PK", 13, 14), PU, mid[2] - mid[1], OP.mult, 2 * mid[1] - mid[2], OP.add)
    ts(MID, A("PK", 8, 9), mid[0] - 2 * mid[1] + mid[2], OP.mult, A("PK", 13, 14), OP.add)
    act(NEG, MID, bias=1024.0, scale=-1.0)
    act(A("PK", 12, 13), MID, bias=-257.0, scale=1.0 / 2048)

    def tb(k):
        return blk("TB", 128, k)
    ms(A("C128"), 128.0)
    ops[-1]["due"] = OPT["tail"] + OPT["period"] * RO + 20.0
    ms(A("OH", 0, 512), 0.0)
    early()
    feeds = [len(ops) - 1]
    ts(Ib, z(0), PP, OP.is_equal)
    ts(z(1), z(0), 31, OP.bitwise_and)
    ts(tb(5), z(1), 4.0, OP.mult, PP, OP.subtract)
    for q in range(4):
        ts(blk("QM", 128, q), tb(5), -float(q), OP.is_equal)
    ts(A("CT", 32, 48), A("IOTA", 0, 16), PI, OP.is_equal, 128.0, OP.mult)
    for k in range(OPT["selg"], 16):
        (ts(blk("SEL", 128, k), BO, A("CT", 32 + k, 33 + k), OP.mult) if k % 2 else act(blk("SEL", 128, k), BO, scale=A("CT", 32 + k, 33 + k)))
    gate.append(sentP)
    for h in range(OPT["selg"] // 8):
        run("g", [blk("SEL", 1024, h)], [A("C128")],
            lambda h=h: g.affine_select(blk("SEL", 1024, h)[0], A("C128")[0], [[-1, 8], [-16, 8], [0, 16]], OP.is_equal, 0.0, -8 * h, 1), 0.17 + 2048 * CYC)
        gate[:] = [len(ops) - 1]
    hold = gate[:]
    del gate[:]
    act(A("NG"), BO, scale=-1.0)
    early()
    feeds.append(len(ops) - 1)
    gate[:] = hold
    select(XM, A("NG"), [[-1, 128]], OP.is_gt, 0.0)
    select(XM, XM, [[-1, 128]], OP.not_equal, -2048.0)
    sent = send("D")
    arrive("drawn", 3 * off, [piece("DL", s, 0, DW) for s in others], sent, LATE[1] + 2.0)
    dma("y", [(A("LN", 256, 640), whole("DL"))], 1.8)
    gate[:] = [sent]
    scaled = {}

    def ID(w):
        return scaled[w]
    for k, w in enumerate((128.0, 1024.0, 512.0, 16.0, 32.0, 48.0, -2048.0, 2048.0, -LIFT, LIFT, 0.75 * LIFT, -0.25 * LIFT, 2.0 ** 17, 0.125, -2.0 ** 20)):
        scaled[w] = blk("IDS", 128, k)
        if 3 <= k < OPT["ids"]:
            select(ID(w), A("OH", 0, 128), [[-1, 128]], OP.not_equal, w)
    MV, MVn = A("MVb"), A("MVn", 0, 512)
    for x, w in ((MV, 1.0), (A("MVn", 512, 1024), 16.0), (MVn, -8192.0)):
        select(x, A("OH", 0, 512), [[-32, N], [0, N], [-1, 32]], OP.not_equal, w)
    sent = gate[0]
    iota(A("NE"), [[0, 582]], 0)
    gate.pop()
    for k, w in enumerate(scaled):
        if not 3 <= k < OPT["ids"]:
            ts(ID(w), Ib, w, OP.mult)
    ts(pc(18), PG, 16.0, OP.mult, 15.0, OP.add)
    ts(A("RED"), A("IOTA", 0, 144), pc(18), OP.is_equal)

    def table(n, s, banks, by):
        w, c = (32.0, 0.0) if n == "K" else (64.0, LIFT)
        for h, a in enumerate((512 * s, _high(s))):
            P = "P" + banks[h]
            mm(A(P), [(blk("QM", 128, 2 * h + q), blk(n + "L", 512, s, 256 * x, 256 * x + 256), blk(P, 256, q)) for q in range(2) for x in range(2)])
            if by[h] == "v":
                ts(A(n + "T", a, a + 512), A(P), w, OP.mult, c, OP.add)
            else:
                act(A(n + "T", a, a + 512), A(P), bias=c, scale=w)
    tables = len(ops)
    table("K", r, "45", "ss")
    table("K", peer, "23", "ss")
    table("P", r, "01", "ss")
    for o in ops[tables:]:
        o["due"] = OPT["tail"] + OPT["period"] * RO + OPT["tabs"]
    if OPT["ppe"]:
        first = len(ops)
        table("P", peer, OPT["ppe"], OPT["by"][0])
        for o in ops[first:]:
            o["due"] = OPT["tail"] + OPT["period"] * RO + 2.5
    tables = range(tables, len(ops))
    act(If, Ib)
    ts(A("MH", 96, 98), A("IOTA", 0, 2), 0.0, OP.mult)
    ts(z(2), A("MG"), 1, OP.bitwise_and)
    ts(A("FO"), z(2), PF, OP.is_equal)
    ms(A("RS4"), 1.0)
    ms(A("RS4", 0, 512, 128), 0.0)
    later = [(blk("OS", OW, d, 272), 0) for d in range(N)]
    ts(pi(5), pi(0), 7, OP.bitwise_and)
    ts(pi(6), pi(0), 3, OP.arith_shift_right, 1, OP.bitwise_and)
    tt(pc(4), pi(5), pi(4), OP.subtract)
    ts(pi(7), pc(4), 1.0, OP.add)
    ts(pi(8), pi(7), 1, OP.bitwise_and)
    ts(pc(5), pi(8), 144.0, OP.mult)
    ts(pc(6), pi(5), 16.0, OP.mult, 16.0, OP.add)
    tt(pc(7), pc(6), pi(6), OP.add)
    tt(pc(8), pc(7), pc(5), OP.add)
    ts(A("PERM", 0, 8), A("IOTA", 0, 8), 2.0, OP.mult, pc(8), OP.add)
    ts(A("GS", 0, 8), A("IOTA", 0, 8), PG, OP.is_equal)
    iota(A("CT", 64, 96), [[2, N], [0, N], [1, 2]], 0)
    ts(A("GB"), A("CT", 64, 96), PG, OP.is_equal, 64.0, OP.mult)
    act(A("GS", 8, 16), A("GS", 0, 8), scale=4.0)
    for h, op in enumerate((OP.is_lt, OP.is_ge)):
        ts(pc(29 + h), PI, 8.0, op)
        act(blk("GS", 8, 2 + h), A("GS", 0, 8), scale=pc(29 + h))
    act(pc(9), A("PK", 8, 9), bias=-12.0, scale=24.0)
    ts(pc(24), PI, 6.0, OP.is_ge, pc(9), OP.mult)
    act(pc(25), PU, bias=PI, scale=6.0)
    ts(A("PERM", 8, 9), pc(25), pc(24), OP.add, 23.0, OP.min)
    act(pc(26), PG, bias=2.0)
    act(pc(27), A("PK", 8 + N - 1, 8 + N), bias=pc(26), scale=-8.0)
    ts(A("BOb", 128, 256), A("MG"), pc(27), OP.is_equal)
    ts(B15, PI, 15.0, OP.is_equal, 4096.0, OP.mult)
    C0, C1 = pc(14), pc(15)
    act(C0, PU, scale=16.0)
    act(pc(10), PU, bias=2048.0 - 16.0, scale=16.0)
    act(C1, A("PK", 8, 9), bias=pc(10), scale=16.0 * N)
    KR, KX = A("KR", 0, 96), A("KR", 96, 192)
    act(KR, A("IOTA", 0, 96), bias=95.0, scale=-1.0)
    act(KX, A("IOTA", 0, 96), bias=95.0 - 2047.0, scale=-1.0)
    act(A("CT", 0, 16), A("IOTA", 0, 16), bias=PI, scale=16.0)
    act(A("CT", 16, 22), A("CT", 0, 6), bias=95.0, scale=-1.0)
    if OPT["jk"]:
        for m in range(6):
            ts(blk("PLC", 64, m), A("IOTA", 0, 64), 0.0, OP.mult, A("CT", 16 + m, 17 + m), OP.add)
        ms(A("PLC", 63, 384, 64), -1.0)
        ms(A("JK", 768, 1152), 1.0)
        ms(A("JK", 768, 1152, 64), 0.0)
    else:
        act(A("CT", 48, 54), A("CT", 0, 6), bias=95.5, scale=-1.0)
    act(pc(17), PI, bias=4096.0)
    act(A("RX", 24, 48), A("IOTA", 0, 24), bias=pc(17), scale=16.0)
    for u in range(N):
        later.append((blk("LV", 6, u), mid[u]))
    rise = [float(b - a) for a, b in bit]
    up, down = 8 + rise.index(1.0), 8 + rise.index(-1.0)
    ts(A("PK", 2, 3), A("PK", down, down + 1), A("PK", up, up + 1), OP.subtract)
    ts(A("PK", 3, 4), A("PK", 2, 3), -2.0 ** 20, OP.mult, 2.0 ** 21, OP.add)
    for u in range(N):
        act(blk("SUM", 128, u), A("FO"), scale=A("PK", 8 + u, 9 + u))
    act(blk("SUM", 512, 1), blk("SUM", 512, 0), scale=2048.0)
    early()
    for k, w in enumerate((2.0, 1024.0, A("PK", 3, 4), A("PK", 2, 3))):
        act(blk("SUP", 256, k), A("BOb"), scale=w)
        early()

    def SUM(u, k, x):
        return move(blk("SUM", 512, k), x, u)
    ts(tb(2), A("MI"), PI, OP.is_ge, -BIG, OP.mult)
    ts(tb(3), A("MI"), PI, OP.is_equal, 2 * BIG, OP.mult)
    tt(tb(4), tb(2), tb(3), OP.add)
    tt(tb(2), tb(4), A("FO"), OP.mult)
    for u in range(N):
        act(blk("EMB", 128, u), tb(2), scale=A("PK", 8 + u, 9 + u))
        early()
    for x in range(2):
        tt(blk("SUP", 128, 8 + x), tb(4), blk("BOb", 128, x), OP.mult)
    for u in range(N):
        for x in range(2):
            ms(A("PK", 6 + x, 7 + x, p0=32 * ((u + x) % N), p=32), rest[u] + 516.5 - mid[u] / 1024 - BIG)
    later.append((A("PT", 4096, 4096 + 384), 0))
    MH = A("MH", 0, 96)
    newkey = [[SUM(u, 1, A("ME")), SUM(u, 0, MH), SUM(u, 1, A("MB"))] for u in range(N)]
    newpay = [[(blk("SUP", 128, 2 * k + x), y) for k, y in enumerate((A("ME"), MH, A("MB"), A("MB"), A("EE")))] for x in range(2)]
    for m in range(6):
        ts(blk("KP", 97, m), A("IOTA", 0, 97), A("CT", m, m + 1), OP.is_le)
    for k, x in enumerate((0.0, 0.0, 0.0, 2048.0)):
        act(blk("XO", 2, k), A("CT", 0, 2), bias=x)
    gate.append(sent)
    for x, c in reversed(later):
        iota(x, [[0, x[2]]], int(c))
    iota(A("OF", 0, 64), [[512, N], [16, 16]], 0)
    iota(A("OF", 64, 128), [[1, 8], [512, 2], [128, 4]], 0)
    iota(A("OF", 128, 192), [[0, 8], [1, 2], [0, 4]], 0)
    gate.pop()
    unhurried = len(ops)
    ts(pc(20), PU, 2.0, OP.is_ge)
    ts(pc(19), PU, 256.0, OP.mult, PI, OP.add)
    for k, ds in enumerate(([0], [1, 2, 3])):
        ts(pc(22 + k), pc(20), float(_high(ds[0]) - 512 - 512 * ds[0]), OP.mult, pc(19), OP.add)
        ts(A("OK", 16 * ds[0], 16 * ds[-1] + 16), A("OF", 16 * ds[0], 16 * ds[-1] + 16), pc(22 + k), OP.add)
    far = [float(_high(u) - 512 - 512 * u) for u in range(N)]
    act(pc(11), PU, scale=512.0)
    act(pc(21), PI, bias=pc(11), scale=8.0)
    act(pc(28), A("PK", 8, 9), bias=far[1], scale=far[0] - far[1])
    act(A("OF", 128, 192), A("OF", 128, 192), bias=pc(21), scale=pc(28))
    tt(A("OF", 64, 128), A("OF", 64, 128), A("OF", 128, 192), OP.add)
    cp(A("OY"), A("OF", 64, 128))

    IMG, HI, K2 = v(3), A("HI"), A("K2")
    KW, PW = A("KT", 0, 4096), A("PT", 0, 4096)
    OLD, WAITS, B10 = A("FL", 0, 128), A("FL", 128, 256), A("FL", 384, 512)
    O5, O7, SG, SO = A("O5", 0, 24), A("O5", 24, 36), A("SG", 0, 4), A("SG", 4, 8)
    act(A("DF"), A("LN", 256, 640), bias=2048.0)
    ops[-1]["due"] = OPT["tail"] + OPT["period"] * RO - 7.5
    unhurried = range(unhurried, len(ops))
    ms(A("P7", 0, 160), 0.0)
    EH0, EH1, NW = blk("EH", 128, 0), blk("EH", 128, 1), A("NW")

    def NV(k):
        return A("NN", k, k + 1)

    def OG(d):
        return blk("OG", 128, d - 1)

    def prep(t):
        ts(A("Z2"), K2, 4095, OP.bitwise_and)
        ts(HI, K2, 2047, OP.bitwise_and)
        ts(A("E1"), K2, 11, OP.arith_shift_right, 1023, OP.bitwise_and)
        if OPT["ehs"]:
            act(EH0, A("E1"), bias=-16.0, scale=16.0)
            act(EH1, HI, scale=1.0 / 128)
        else:
            ts(EH0, A("E1"), -1.0, OP.add, 16.0, OP.mult)
            ts(EH1, HI, 1.0 / 128, OP.mult)
        before = A("FL", 256, 384)
        below(before, max(t - 1, 0))
        mm(A("P7", 16, 144), [(ID(128.0), EH1), (ID(1024.0), before)])
        due(t - 1, OPT["ig"] - (0.4 if t else 1.5))
        turn(A("YT", 0, 160), A("P7", 0, 160))
        turn(A("YT", 160, 288), A("P7", 16, 144))
        join(len(ops) - 2)
        due(t - 1, OPT["ig"] + (0.1 if t else -1.2))
        ts(A("OFF"), X(A("YT"), A("PERM", 0, 8)), 1024.0, OP.add)
        due(t - 1, OPT["ins"] + (1.9 if t else 0.6))
        ts(B10, EH1, 8.0, OP.is_ge)
        due(t, 1.9)
        tt(OLD, IMG, A("Z2"), OP.is_ge)
        y = A("P4" if t else "P7", 0 if t else 160, 128 if t else 288)
        mm(y, [(ID(128.0), EH1), (ID(512.0), OLD)])
        act(A("TO", 0, 128), y, bias=128.5 + 1.0 / 1024, scale=1.0 / 512)
        due(t - 1, OPT["ins"] + 0.95)
        for d in range(1, N):
            ts(OG(d), A("TO", 0, 128), 129.0 + d, OP.is_equal)
        join(len(ops) - N + 1)
        due(t - 1, OPT["ig"] - 0.15)
        act(A("TO", 128, 256), A("TO", 0, 128), AF.Abs, -131.0)
        due(t - 1, OPT["ins"] + 1.1)
        ts(OG(N), A("TO", 128, 256), 2.0, OP.is_equal)
        due(t - 1, OPT["ig"] - 0.1)
        scan(A("IG"), A("RS4"), A("OG"), 0.0, OP.mult, OP.add)
        due(t - 1, OPT["ig"])
        if OPT["gob"] == "P4" and t:
            go(t)
        if OPT["emd"]:
            dma("y", [(A("EM", 512 * (t % 2) + 128 * s, 512 * (t % 2) + 128 * s + 128, p0=32 * u, p=32), A("E1", p0=32 * s, p=32)) for s in range(N) for u in range(N)], 3.0)

    def payloads():
        tt(X(A("PT"), O7), A("OLD", 384, 576), A("SC", 384, 576), OP.max)

    def due(t, x):
        ops[-1]["due"] = OPT["tail"] + OPT["period"] * RO - (OPT["period"] - OPT["cut"]) * t - x + OPT["cut"] * ((x > 4.2) + (x > OPT["period"] + 4.2) + (t < 0) * -1)

    def below(o, t):
        act(o, A("Z2"), AF.Sign, NV(4 + t), -1.0)

    def go(t):
        P = OPT["gob"]
        mm(A(P), [(XM, A("OG")), (BO, A("IG"))])
        act(A("GOB"), A(P), AF.Sign, -1407.5, -1.0)
        due(t, 0.7 if t else 2.15)

    def spread(t):
        if OPT["gob"] != "P4" or not t:
            go(t)
        for c in range(4):
            for x in range(2):
                mm(blk("P%d" % c, 256, x), [(blk("SEL", 128, 4 * c + k), blk("EH", 128, h), blk("P%d" % c, 128, k)) for k in (2 * x, 2 * x + 1) for h in range(2)])
                if c in OPT["fuse"][t]:
                    due(t, -0.3 + 0.4 * c)
            if c in OPT["fuse"][t]:
                act(blk("W1", 512, c), A("P%d" % c))
                due(t, 0.2 + 0.5 * c)

    def split(t):
        n = NV(t)
        ts(SG, A("XO", 0, 4), n, OP.add)
        ts(A("SX", 0, 8), A("XO"), n, OP.add)
        ts(A("SX", 8, 12), A("SX", 0, 4), NV(t + 1), OP.is_ge, 4096.0, OP.mult)
        tt(A("SX", 12, 16), A("SX", 8, 12), A("SX", 4, 8), OP.add)
        cp(SO, A("SX", 12, 16))
        cp(A("SI", 0, 32), X(KW, A("SG", 0, 2)))
        ts(A("SI", 32, 64), A("SI", 0, 32), 0x200800, OP.bitwise_and)
        for k in range(3):
            ts(blk("SK", 32, k), A("SI", 32, 64), 2048.0, (OP.not_equal, OP.is_equal)[k % 2])
        join(len(ops) - 3)
        tt(A("SK", 128, 192), X(KW, SG), A("SK", 0, 64), OP.mult)
        due(t + 1, 4.25)
        tt(X(A("KT"), SO), A("SK", 128, 192), A("SK", 32, 96), OP.subtract)
        due(t + 1, 8.2 if t < RO - 1 else 2.5)
        tt(A("SK", 192, 256), X(PW, SG), A("SK", 0, 64), OP.mult)
        due(t + 1, (10.9, OPT["period"] + 1.6, 2.8)[(1, 0, 2)[t]])
        ts(A("SK", 256, 320), A("SK", 32, 96), LIFT - 0.5, OP.mult)
        tt(X(A("PT"), SO), A("SK", 192, 256), A("SK", 256, 320), OP.add)
        due(t + 1, (12.3, OPT["period"] + 1.9, 3.0)[(1, 0, 2)[t]])

    made = [i for i in range(consts, len(ops)) if i not in tables and ops[i]["q"] in OPT["made"] and i not in unhurried]
    small = set(x[7] for n in ("PCI", "PC", "TN", "MI", "MG", "FO", "PK", "BOb", "C128") for x in hist[n] if x[5])
    for i in range(consts, len(ops)):
        if ops[i]["q"] == "v" and i not in small:
            ops[i]["after"].update(sending)
    ahead = len(ops)
    for q, by in zip(cross, OPT["by"][1:3]):
        first = len(ops)
        table("K", q, "46", by)
        for o in ops[first:]:
            o["after"].update(i for i in made if ops[i]["q"] == o["q"])
            o["due"] = OPT["tail"] + OPT["period"] * RO + 1.5
    ts(K2, A("LN", 0, 128), 2048.0, OP.add)
    ops[-1]["after"].update(feeds + made[:int(len(made) * OPT["share"])])
    for i in list(tables) + list(range(ahead, len(ops))):
        if ops[i]["q"] == "v":
            ops[i]["after"].update(feeds)
    ts(IMG, A("LN", 128, 256), -1.0, OP.add)
    act(NV(4), A("PNI", 0, 1), bias=-0.5)
    early()
    act(NV(0), A("PNI", 0, 1))
    early()
    short[0] = OPT["tiny"]
    prep(0)
    spread(0)

    for t in range(RO):
        last = t == RO - 1
        n = NV(t)
        if not t:
            gate.extend([i for i in range(ahead, len(ops)) if ops[i]["q"] == "t"][:OPT["pg"]])
            first = len(ops)
            if not OPT["ppe"]:
                table("P", peer, "56", OPT["by"][0])
            table("P", cross[0], "56", OPT["by"][3])
            table("P", cross[1], OPT["pb"], OPT["by"][4])
            for k, o in enumerate(ops[first:]):
                o["due"] = OPT["tail"] + OPT["period"] * RO - OPT["pt0"] - OPT["pt1"] * k
            del gate[:]
        ts(NW, A("Z2"), n, OP.is_lt, 0.5, OP.subtract)
        x = A("P6", 256, 384) if t else A("P7", 160, 288)
        mm(A("P7", 160, 288), [(Ib, blk("GOB", 128, d)) for d in range(4)])
        due(t, 1.3 if t else 2.8)
        ts(WAITS, A("P7", 160, 288), -1.0, OP.mult, -3.0, OP.add)
        due(t, 2.0 if t else 3.2)
        mm(x, [(ID(16.0 * d), OG(d)) for d in range(1, N)] + [(ID(-2048.0), OLD), (ID(LIFT), WAITS), (ID(2048.0), NW)])
        due(t, 2.5 if t else 3.5)
        act(A("CM"), x, bias=1024.0 + LIFT)
        due(t, 4.3)
        mm(A("P5"), [move(MV, EH0, s) + (blk("P5", 128, s),) for s in range(N)])
        due(t, 3.2 if t else 5.5)
        act(blk("EM", 512, t % 2), A("P5"), bias=A("PK", 12, 13), scale=1.0 / 16)
        due(t, 4.4 if t else 6.0)
        mm(A("P6", 384, 512), [(ID(128.0), EH1), (ID(-2048.0), OLD), (ID(-2048.0), WAITS), (ID(2048.0), NW)])
        due(t, 5.3)
        act(f(5), A("P6", 384, 512), bias=-3072.0)
        due(t, 5.75)
        mm(A("P6", 384, 512), [(ID(16.0), A("C128", 0, 128)), (ID(128.0), EH0), (ID(128.0), EH1), (ID(LIFT), WAITS)])
        due(t, 7.0)
        tt(f(3), A("P6", 384, 512), blk("DF", 128, t), OP.max)
        due(t, 8.95)
        for c in range(4):
            if c in OPT["fuse"][t]:
                tt(blk("EQ", 512, c), X(KW, blk("OFF", 32, c)), blk("W1", 512, c), OP.is_equal)
            else:
                act(blk("W1", 512, c), X(KW, blk("OFF", 32, c)))
                due(t, 1.4 + 0.7 * (c - len(OPT["fuse"][t])))
                tt(blk("EQ", 512, c), blk("W1", 512, c), A("P%d" % c), OP.is_equal)
            due(t, OPT["eq"][c])
            mm(A("P4"), [(blk("EQ", 128, k), A("GB"), A("P4", k, 512, 16)) for k in range(4 * c, 4 * c + 4)])
        for h in range(OPT["tf"]):
            act(blk("TF", 512 // OPT["tf"], h), blk("P4", 512 // OPT["tf"], h))
            due(t, 5.1)
        w = 16 // len(OPT["w3"])
        for c, x in enumerate(OPT["w3"] if t else OPT["w30"]):
            tt(blk("W3", 128 * w, c), X(PW, blk("OFF", 8 * w, c)), blk("EQ", 128 * w, c), OP.mult)
            due(t, x)
            for x in range(w * c, w * c + w, 2):
                mm(A("P6", 0, 256), [(blk("W3", 128, k), A("GS", 0, 16), A("P6", k, 256, 16)) for k in (x, x + 1)])
                due(t, OPT["ws"][c] if t else OPT["w30"][c] + 0.9)
        act(A("SN"), A("P6", 0, 256), AF.Sign, -LIFT)
        due(t, 9.07)
        act(A("TS"), A("P6", 0, 128), bias=2047.5 - LIFT)
        due(t, 9.3)
        mm(A("P6", 256, 384), [(ID(-LIFT), WAITS), (blk("SN", 128, 0), ID(LIFT)), (A("TS"), If)])
        due(t, 9.85)
        mm(A("P2", 0, 128), [(ID(16.0), A("C128", 0, 128)), (ID(-0.25 * LIFT), WAITS), (ID(2.0 ** 17), EH1), (ID(0.125), EH0), (ID(-2.0 ** 20), B10),
                             (Ib, B10)], stop=False)
        due(t, 7.2)
        mm(A("P2", 0, 128), [(blk("SN", 128, 1), ID(0.75 * LIFT))], start=False)
        due(t, 9.8)
        tt(f(4), A("P2", 0, 128), f(3), OP.max)
        due(t, 10.2)
        for h in range(2):
            mm(blk("P5", 256, h), [x + (blk("P5", 128, s),) for s in (2 * h, 2 * h + 1) for x in (move(MV, EH1, s), move(A("MVn", 512, 1024), NW, s))])
            due(t, 5.0)
        act(A("HM"), A("P5"), bias=NEG, scale=128.0)
        due(t, 6.3)
        ts(NV(8), n, 32.0, OP.add, 2048.0, OP.min)
        if t:
            if OPT["plate"]:
                payloads()
                due(t, 9.0)
            split(t - 1)
        for h in range(2):
            P = "P%d" % h
            mm(A(P, 0, 256), [x + (blk(P, 128, s % 2),) for s in (2 * h, 2 * h + 1) for x in (move(MV, A("CM"), s), (blk("TF", 128, s), Ib))])
        act(A("PB", 256, 512), A("P1", 0, 256))
        if OPT["ohs"]:
            act(A("PB", 0, 256), A("P0", 0, 256))
        for h, x in enumerate((A("PB" if OPT["ohs"] else "P0", 0, 256), A("PB", 256, 512))):
            for k, c in enumerate((C0, C1)):
                ts(blk("OH", 256, 2 * k + h), x, c, OP.is_equal)
                due(t, OPT["oh0"])
        scan(A("INC"), A("OH"), A("C128"), 0.0, OP.add, OP.min)
        due(t, OPT["oh0"] + 0.7)
        jv = OPT["jk"]
        mm(A("P1", 256, 320), [(BO, A("INC", 15, 1024, 16))])
        due(t, OPT["oh0"] + 1.3)
        mm(A("P4", 384, 448), red("REDb", "INC", 0, 1024))
        due(t, 7.63)
        for m in range(6):
            act(blk("JK", 64, m, 0, 63), A("P1", 256, 319), AF.Sign, A("CT", 48 + m, 49 + m), -1.0, acc=A("BS", 32 + m, 33 + m))
        join(len(ops) - 6)
        due(t, 7.7)
        act(A("E2"), A("P4", 384, 448), bias=B15)
        due(t, 8.2)
        for h, P in enumerate(("P0", "P3")):
            mm(A(P), [(BO, blk("INC", 512, h)), (XM, blk("OH", 512, h))])
            due(t, (8.05, 8.9)[h])
            act(blk("XS", 512, h), A(P))
            due(t, (8.6, 9.5)[h])
        if jv:
            AC = A("JK", 384 + 63, 768, 64)
            cp(A("O1", 0, 6), AC)
            ts(A("VB", 0, 6), AC, 16.0, OP.mult)
            ts(A("BS", 8, 14), AC, 32.0, OP.is_ge, -512.0, OP.mult)
        else:
            AC = A("BS", 32, 38)
            ts(A("O1", 0, 6), AC, 0.5, OP.mult, 31.5, OP.add)
            ts(A("VB", 0, 6), AC, 8.0, OP.mult, 504.0, OP.add)
            ts(A("BS", 8, 14), AC, 0.0, OP.is_gt, -512.0, OP.mult)
        tt(A("C2"), X(A("E2"), A("O1", 0, 6)), KR, OP.is_le)
        mm(A("P1", 320, 326), [(Ib, A("VB", 0, 6))] + red("REDb", "C2", 0, 96))
        cp(A("O1", 8, 14), A("P1", 320, 326))
        tt(A("BS", 16, 22), A("P1", 320, 326), A("BS", 8, 14), OP.add)
        tt(A("MK"), X(A("XS"), A("O1", 8, 14)), KX, OP.is_equal)
        cp(A("O3", 0, 6), A("BS", 16, 22))
        tt(A("MH", 0, 96), X(A("HM"), A("O3", 0, 6)), A("MK"), OP.mult)
        due(t, OPT["ins"] - 0.35)
        tt(A("ME"), X(blk("EM", 512, t % 2), A("O3", 0, 6)), A("MK"), OP.mult)
        due(t, OPT["ins"] - 0.1)
        tt(IMG, IMG, f(5), OP.max)
        tt(K2, A("P6", 256, 384), f(4), OP.max)
        due(t, OPT["k2"])
        if last:
            ts(A("YI"), IMG, 1.0, OP.add)
            ts(HI, K2, int(LIFT) - 1, OP.bitwise_and)
            ts(A("KB"), HI, -2048.0, OP.add)
            dma("y", [(whole("YS%d" % h), A(x)) for h, x in enumerate(("KB", "YI"))], 2.0)
            dma("y", [(piece("YL%d" % h, r, 0, LW), A(x, p0=32 * r, p=32)) for h, x in enumerate(("KB", "YI"))], 2.0)
            sent = send("Y")
            arrive("ylan", 5 * off + off // 2, [piece("YL%d" % h, s, 0, LW) for s in others for h in range(2)], sent, 3.0)
            dma("y", [(x[:], whole("YL%d" % h)) for h, x in enumerate((T.yl, T.yi))], 2.0)
        else:
            prep(t + 1)
        z0 = OPT["ins"]
        mm(A("P7", 160, 266), [(BO, A("MH", 0, 97), A("P7", 160, 257))] + [x + (A("P7", 260, 266),) for x in red("REDb", "MH", 0, 96)])
        due(t, z0)
        O4 = A("O4", 0, 6)
        cp(A("BH", 0, 6), A("P7", 260, 266))
        due(t, z0 + 0.55)
        ts(O4, A("P7", 260, 266), MID, OP.add)
        due(t, z0 + 0.6)
        act(A("EE"), X(KW, O4), AF.Relu, 0.0, -1.0)
        due(t, z0 + 0.75)
        ts(A("MB"), A("MH", 0, 96), 0.0, OP.is_gt, -1.0, OP.mult)
        due(t, z0 + 0.1)
        mm(A("P3", 0, 24), [(Ib, A("LV"))] + [move(MV, A("BH", 0, 6), s) + (blk("P3", 6, s),) for s in range(N)])
        due(t, z0 + 0.75)
        cp(A("O6"), A("P3", 0, 24))
        due(t, z0 + 1.05)
        (act if OPT["vbs"] else cp)(A("RX", 0, 24), A("P3", 0, 24))
        due(t, z0 + 1.2)
        act(A("OLD", 0, 384), X(KW, A("O6")))
        due(t, z0 + 1.25)
        for h in range(2):
            mm(A("P5", 0, 384), [x + (blk("P5", 96, s),) for s in (2 * h, 2 * h + 1) for x in newkey[s]], start=not h, stop=False)
            due(t, z0 + (0.5, 0.9)[h])
        mm(A("P5", 0, 384), [move(A("EMB"), A("EE"), s) + (blk("P5", 96, s),) for s in range(N)], start=False)
        due(t, z0 + 1.15)
        act(A("SC", 0, 384), A("P5", 0, 384), bias=257.0 * 2048 - BIG)
        due(t, z0 + 1.8)
        for x in range(2):
            mm(blk("P6", 96, x), newpay[x])
            due(t, OPT["period"] - (0.5 if last else -1.5))
            if OPT["scv"]:
                ts(blk("SC", 96, N + x), blk("P6", 96, x), A("PK", 6 + x, 7 + x), OP.add)
            else:
                act(blk("SC", 96, N + x), blk("P6", 96, x), bias=A("PK", 6 + x, 7 + x))
            due(t, OPT["period"] + (0.4 if last else 4.1))
        mm(A("P3", 32, 38), red("REDb", "EE", 0, 96))
        due(t, z0 + 1.6)
        for m in range(6):
            ts(blk("NE", 97, m, 16 * m), A("P7", 160 + 16 * m, 257), A("P7", 260 + m, 261 + m), OP.not_equal)
            if m % 3 == 2:
                join(len(ops) - 3)
                due(t, z0 + 0.65)
        scan(A("SS"), A("NE"), A("KP"), 1.0, OP.min, OP.max)
        due(t, z0 + 1.15)
        TRY = A("SS", 96, 582, 97)
        mm(A("P2", 272, 296), [(If, A("RX", 24, 48))] + [move(MVn, TRY, s) + (A("P2", 272 + 6 * s, 278 + 6 * s),) for s in range(N)])
        due(t, z0 + 1.5)
        tt(A("RX", 72, 96), A("P2", 272, 296), A("RX", 0, 24), OP.max)
        due(t, z0 + 1.5)
        cp(O5, A("RX", 72, 96))
        due(t, z0 + 1.6)
        cp(A("O5", 24, 40), X(A("RX", 72, 96), A("PERM", 8, 9)))
        due(t, z0 + 2.1 if last else OPT["period"] + 1.4)
        act(A("OLD", 384, 576), X(A("PT", 0, 4096 + 384), O7))
        due(t, OPT["period"] + (0.1 if last else 7.0))
        tt(A("OV", 0, 6), A("P3", 32, 38), TRY, OP.is_lt)
        due(t, z0 + 2.15 if last else OPT["period"] + 1.27)
        mm(A("P3", 48, 49), [(A("FO"), A("OV", m, m + 1)) for m in range(6)])
        due(t, OPT["period"] + (0.2 if last else 1.45))
        ts(NV(t + 1), A("P3", 48, 49), n, OP.add, NV(8), OP.min)
        due(t, OPT["period"] + (1.27 if last else 1.8))
        if t < RO - 2:
            ts(NV(5 + t), NV(t + 1), -0.5, OP.add)
        tt(X(A("KT"), O5), A("OLD", 0, 384), A("SC", 0, 384), OP.max)
        due(t, OPT["period"])
        if not t:
            for i in unhurried[:-1]:
                ops[i]["after"].add(len(ops) - 1)
        del gate[:]
        if last or not OPT["plate"]:
            payloads()
            due(t, OPT["period"] + 1.3)
        if not last:
            spread(t + 1)
    split(RO - 1)
    short[0] = 0

    def stores(q, s, n):
        x = OW * s
        y = [(T.ys[2 * s + h, :], A(n, x + 256 + 8 * h, x + 264 + 8 * h)) for h in range(2)] + [(rows(T.yn, s), A(n, x + 272, x + 273, p=32))]
        if s != r:
            y = [(T.yk[32 * s:32 * s + 32, 256 * u:256 * u + 256], A(n, x, x + 256, p0=32 * u, p=32)) for u in range(N)] + y
        dma(q[0], y[0::2], 2.5)
        dma(q[1], y[1::2], 2.5)

    for c in range(4):
        act(blk("YP", 256, c), X(PW, blk("OY", 16, c)), AF.Abs, -LIFT)
        for b in range(2 * c, 2 * c + 2):
            mm(A("P0", b, 128, 8), [(blk("YP", 128, b), A("GS", 16, 32))])
    ts(A("BS"), A("P0", 64, 128), -8.0, OP.add)
    for k, d in enumerate(others + [r]):
        if d != r:
            (act if k in OPT["oss"] else cp)(blk("OS", OW, d, 0, 256), X(KW, blk("OK", 16, d)))
        tt(blk("OS", OW, d, 256, 272), blk("P0", 16, d), blk("BS", 16, d), OP.add)
        act(blk("OS", OW, d, 272, 273), NV(RO))
        if d != r and not OPT["oh"]:
            sent = send("O%d" % k)
        elif 0 < k < N - 1:
            sent = send(("O", "Op")[k - 1])
    dma("y", [(T.yk[32 * r:32 * r + 32, 512 * h:512 * h + 512], A("KT", a, a + 512, p=32)) for h, a in enumerate((512 * r, _high(r)))], 2.5)
    stores("sy", r, "OS")
    for k, s in enumerate(cross + [peer]):
        arrive("o%d" % s, _landing(T, topo, routes, r, "o%d" % s), [blk("OL", OW, s)], sent, 0.5 + 0.5 * k)
        stores(("sy", "ys")[k % 2], s, "OL")
    _issue(T, Q, ops)
